import numpy as np
import ml_dtypes


def mxq(x, axis, fmt="e4m3"):
    dtype, down = {"e4m3": (ml_dtypes.float8_e4m3fn, 7), "e5m2": (ml_dtypes.float8_e5m2, 14)}[fmt]
    v = np.moveaxis(np.asarray(x, np.float32).astype(ml_dtypes.bfloat16).astype(np.float64), axis, -1)
    blocks = v.reshape(v.shape[:-1] + (-1, 32))
    amax = np.abs(blocks).max(-1, keepdims=True)
    byte = np.maximum(np.where(amax > 0, np.frexp(amax)[1] - 1 + 127, 0) - down, 1)
    scale = np.exp2(byte - 127.0)
    codes = (blocks / scale).astype(np.float32).astype(dtype).astype(np.float64)
    return np.moveaxis((codes * scale).reshape(v.shape), -1, axis)


WIDE = False


def mx_kscale(k):
    if not WIDE:
        return np.ones(k)
    levels = np.array([10, -10, 5, -5, 0])
    if k % 512:
        return np.exp2(np.random.permutation(np.resize(levels, k // 32))).repeat(32)
    a = np.empty((k // 512, 16))
    for p in range(k // 512):
        a[p, :8] = np.random.permutation(np.resize(levels, 8))
        for g in range(8):
            far = levels[np.abs(levels - a[p, g]) >= 10]
            a[p, g + 8] = far[np.random.randint(len(far))]
    return np.exp2(a.ravel()).repeat(32)


def f64(x):
    return np.asarray(x).astype(np.float64)


def striped(idx):
    return np.tile(idx.reshape(-1, 16).T, (8, 1)).astype(np.uint16)


def unstriped(offs):
    return offs[:16].T.reshape(-1).astype(np.int64)


E2M1 = np.array([0.0, 0.5, 1.0, 1.5, 2.0, 3.0, 4.0, 6.0, -0.0, -0.5, -1.0, -1.5, -2.0, -3.0, -4.0, -6.0])


def pack_weight(w, fmt):
    k, n = w.shape
    w = f64(np.asarray(w, np.float32).astype(ml_dtypes.bfloat16)).reshape(k // 32, 32, n)
    amax = np.abs(w).max(1)
    if fmt == "e4m3":
        byte = np.frexp(amax)[1] - 1 + 127 - 7
    else:
        mant, ex = np.frexp(amax / 6.0)
        byte = np.where(mant > 0.5, ex, ex - 1) + 127
    byte = np.clip(np.where(amax > 0, byte, 1), 1, 254)
    scaled = (w * np.exp2(127.0 - byte)[:, None, :]).reshape(k, n).astype(np.float32)
    by_word = np.ascontiguousarray(scaled.reshape(k // 512, 128, 4, n).transpose(0, 1, 3, 2))
    if fmt == "e4m3":
        words = by_word.astype(ml_dtypes.float8_e4m3fn).view(np.uint8)
    else:
        c = by_word.astype(ml_dtypes.float4_e2m1fn).view(np.uint8) & 0xF
        words = (c[..., 0::2] | (c[..., 1::2] << 4)).reshape(k // 512, 128, 2 * n)
    return np.ascontiguousarray(words), np.ascontiguousarray(byte.astype(np.uint8).reshape(k // 512, 16, n))


def unpack_weight(words, scales, fmt):
    g, _, n = scales.shape
    words = np.ascontiguousarray(words).reshape(g, 128, n, -1)
    if fmt == "e4m3":
        vals = words.view(ml_dtypes.float8_e4m3fn).astype(np.float64)
    else:
        nib = np.empty((g, 128, n, 4), np.uint8)
        nib[..., 0::2] = words & 0xF
        nib[..., 1::2] = words >> 4
        vals = E2M1[nib]
    vals = vals * np.repeat(np.exp2(scales.astype(np.float64) - 127.0), 8, axis=1)[..., None]
    return vals.transpose(0, 1, 3, 2).reshape(g * 512, n)


def gelu(v):
    return 0.5 * v * (1.0 + np.tanh(np.sqrt(2.0 / np.pi) * (v + 0.044715 * v**3)))


K, H, T, T2, S = 1024, 512, 2048, 2048, 1024

def setup_inputs():
    n = np.random.standard_normal
    s = mx_kscale(K)[:, None]
    u = mx_kscale(H)[:, None]
    tab_words, tab_scales = pack_weight(n((K, T)) * s, "e4m3")
    w4_words, w4_scales = pack_weight(0.7 * n((K, H)) / np.sqrt(K) / s / u.T, "e2m1")
    xT = np.round(16 * n((K, T2))) / 16 * s
    perm = np.random.permutation(T2)
    return {
        "tab_words": tab_words, "tab_scales": tab_scales,
        "offs": striped(np.random.permutation(T)[:S]),
        "xT": xT.astype(np.float32),
        "offs2": striped(perm[:S]), "offs3": striped(perm[-S:]),
        "w4_words": w4_words, "w4_scales": w4_scales,
        "wb": (n((K, H)) / np.sqrt(K) / s / u.T).astype(np.float32),
        "flux": (n((H, S)) / u).astype(np.float32),
        "var": (np.exp(0.3 * n(H)) / u[:, 0] ** 2).astype(np.float32),
        "step": (np.random.uniform(1.0, 3.0, K) * s[:, 0]).astype(np.float32),
    }

def reference(tab_words, tab_scales, offs, xT, offs2, offs3, w4_words, w4_scales, wb, flux, var, step):
    v = unpack_weight(tab_words, tab_scales, "e4m3")[:, unstriped(offs)]
    w4 = unpack_weight(w4_words, w4_scales, "e2m1")
    x = f64(xT)[:, unstriped(offs2)] - f64(xT)[:, unstriped(offs3)]
    model = w4.T @ v + mxq(f64(wb), 0, "e4m3").T @ mxq(x, 0, "e4m3")
    res = f64(flux) - model
    psi = res / (f64(var)[:, None] + np.square(res))
    wbT = f64(wb).T
    back = mxq(wbT, 0, "e4m3").T @ mxq(psi, 0, "e4m3")
    return f64(step)[:, None] * back

@@ -1,0 +1,362 @@
+from contextlib import ExitStack
+
+import concourse.mybir as mybir
+from concourse.masks import make_identity
+
+K, H, T, S = 1024, 512, 2048, 1024
+FLOPS = 2 * (2 * K * H * S + H * K * S)
+
+F32 = mybir.dt.float32
+BF16 = mybir.dt.bfloat16
+I32 = mybir.dt.int32
+U32 = mybir.dt.uint32
+U16 = mybir.dt.uint16
+U8 = mybir.dt.uint8
+FP8X4 = mybir.dt.float8_e4m3fn_x4
+FP4X4 = mybir.dt.float4_e2m1fn_x4
+ACT = mybir.ActivationFunctionType
+ALU = mybir.AluOpType
+
+P = 128
+PACK = 4
+PASSES = K // (P * PACK)
+CHUNK = 256
+UNITS = CHUNK // P
+PER_COL = 16
+M_BANKS, R_BANKS, O_BANKS = 2, 3, 3
+ON_SCALAR = [(0,), (0,), (0, 2), (0, 2)]
+
+
+def tile_list_transit_cauchy_step_kernel(
+    tc, tab_words, tab_scales, offs, xT, offs2, offs3, w4_words, w4_scales, wb, flux, var, step, out
+):
+    nc = tc.nc
+    with ExitStack() as ctx:
+        keep = ctx.enter_context(tc.tile_pool(name="keep", bufs=1))
+        work = ctx.enter_context(tc.tile_pool(name="work", bufs=1))
+        psum = ctx.enter_context(tc.psum_pool(name="psum", bufs=1))
+
+        def entries(lst, j0, n):
+            return lst[:, j0 // PER_COL : (j0 + n) // PER_COL]
+
+        idx = keep.tile([P, S // PER_COL], U16, name="idx")
+        idx2 = keep.tile([P, S // PER_COL], U16, name="idx2")
+        idx3 = keep.tile([P, S // PER_COL], U16, name="idx3")
+        nc.sync.dma_start(idx[:], offs)
+        nc.sync.dma_start(idx3[:], offs3)
+        nc.sync.dma_start(idx2[:], offs2)
+
+        tab_sc = keep.tile([P, T], U8, name="tab_sc")
+        w4_sc = keep.tile([P, PASSES * H], U8, name="w4_sc", align_bytes=64)
+        v_sc0 = keep.tile([P, S], U8, name="v_sc0", align_bytes=64)
+        v_sc1 = keep.tile([P, S], U8, name="v_sc1", align_bytes=64)
+        nc.gpsimd.memset(tab_sc[:].bitcast(I32), 0)
+        nc.gpsimd.memset(w4_sc[:].bitcast(I32), 0)
+        nc.gpsimd.memset(v_sc1[:].bitcast(I32), 0)
+        ident = keep.tile([P, P], F32, name="ident")
+        make_identity(nc, ident[:])
+        for q in range(4):
+            nc.scalar.dma_start(
+                out=tab_sc[32 * q : 32 * q + 8, :].bitcast(I32),
+                in_=tab_scales[:, 4 * q : 4 * q + 4, :].bitcast(I32),
+            )
+
+        x_rows = xT.rearrange("(a p i) t -> a i p t", a=PASSES, i=PACK)
+        planes = {}
+
+        def load_plane(a, i):
+            planes[a, i] = work.tile([P, T], F32, name="plane%d%d" % (a, i), align_bytes=64)
+            nc.sync.dma_start(out=planes[a, i][:], in_=x_rows[a, i])
+
+        wb_raw = {}
+
+        def load_wb(a):
+            wb_raw[a] = work.tile([P, PACK * H], F32, name="wb_raw%d" % a, tag="wb_raw%d" % a)
+            nc.sync.dma_start(
+                out=wb_raw[a][:], in_=wb[a * P * PACK : (a + 1) * P * PACK, :].rearrange("(p j) r -> p (j r)", j=PACK)
+            )
+
+        flux_raw = {}
+
+        def load_flux(c):
+            flux_raw[c] = work.tile([P, PACK, CHUNK], F32, name="flux_raw%d" % c)
+            nc.sync.dma_start(
+                out=flux_raw[c][:],
+                in_=flux[:, c * CHUNK : (c + 1) * CHUNK].rearrange("(p t) j -> p t j", t=PACK),
+            )
+
+        tab_w = {}
+
+        def load_tab(a):
+            tab_w[a] = work.tile([P, T], I32, name="tab_w%d" % a, align_bytes=64)
+            nc.sync.dma_start(out=tab_w[a][:], in_=tab_words[a].rearrange("p t i -> p (t i)").bitcast(I32))
+
+        load_plane(0, 0)
+        load_plane(0, 1)
+        load_plane(0, 2)
+        load_wb(0)
+        load_plane(0, 3)
+        load_wb(1)
+        load_tab(0)
+        load_tab(1)
+        w4_w = keep.tile([P, PASSES, 2 * H], U8, name="w4_w", align_bytes=64)
+        nc.sync.dma_start(out=w4_w[:].bitcast(I32), in_=w4_words.rearrange("a p c -> p a c").bitcast(I32))
+        for q in range(4):
+            nc.sync.dma_start(
+                out=w4_sc[32 * q : 32 * q + 4, :].bitcast(I32).rearrange("p (a c) -> p a c", a=PASSES),
+                in_=w4_scales[:, 4 * q : 4 * q + 4, :].rearrange("a r c -> r a c").bitcast(I32),
+            )
+        load_plane(1, 0)
+        load_flux(0)
+        load_plane(1, 1)
+        load_plane(1, 2)
+        load_plane(1, 3)
+        var_t = keep.tile([P, PACK], F32, name="var_t")
+        nc.sync.dma_start(out=var_t[:], in_=var.rearrange("(p t) -> p t", t=PACK))
+        load_flux(1)
+        step_t = keep.tile([P, PASSES, PACK], F32, name="step_t")
+        nc.sync.dma_start(out=step_t[:], in_=step.rearrange("(a p j) -> p a j", a=PASSES, j=PACK))
+        load_flux(2)
+        load_flux(3)
+
+        nc.vector.tensor_copy(v_sc0[:], tab_sc[:].indirect(idx[:]))
+        nc.scalar.dma_start(out=v_sc1[0:112, :].bitcast(I32), in_=v_sc0[4:116, :].bitcast(I32))
+        v_sc = [v_sc0, v_sc1]
+
+        x_codes = [keep.tile([P, S], U32, name="x_codes%d" % a, align_bytes=64) for a in range(PASSES)]
+        x_sc = [keep.tile([P, S], U8, name="x_sc%d" % a, align_bytes=64) for a in range(PASSES)]
+
+        def round_and_quantise_x(a, j0, n, xf, xb):
+            nc.scalar.copy(xb[:].rearrange("p (j i) -> p j i", i=PACK), xf[:].rearrange("p i j -> p j i"))
+            nc.vector.quantize_mx(
+                out=x_codes[a][:, j0 : j0 + n].bitcast(FP8X4), scales=x_sc[a][:, j0 : j0 + n], in_=xb[:]
+            )
+
+        early = [(0, 2 * CHUNK), (2 * CHUNK, CHUNK)]
+        xf0 = [work.tile([P, PACK, n], F32, name="xf0%d" % h, tag="xf%d" % h) for h, (j0, n) in enumerate(early)]
+        for i in range(PACK):
+            outside = work.tile([P, 3 * CHUNK], F32, name="outside0", bufs=2)
+            for j0, n in early:
+                nc.vector.tensor_copy(outside[:, j0 : j0 + n], planes[0, i][:].indirect(entries(idx3, j0, n)))
+            for h, (j0, n) in enumerate(early):
+                nc.vector.tensor_tensor(
+                    xf0[h][:, i, :],
+                    planes[0, i][:].indirect(entries(idx2, j0, n)),
+                    outside[:, j0 : j0 + n],
+                    ALU.subtract,
+                )
+
+        wb_codes = keep.tile([P, PASSES * H], U32, name="wb_codes", align_bytes=64)
+        wb_sc = keep.tile([P, PASSES * H], U8, name="wb_sc", align_bytes=64)
+        wt_codes = keep.tile([P, K], U32, name="wt_codes", align_bytes=64)
+        wt_sc = keep.tile([P, K], U8, name="wt_sc", align_bytes=64)
+        for a in range(PASSES):
+            wb_b = work.tile([P, H * PACK], BF16, name="wb_b%d" % a, align_bytes=64)
+            nc.scalar.copy(
+                wb_b[:].rearrange("p (r j) -> p r j", j=PACK), wb_raw[a][:].rearrange("p (j r) -> p r j", j=PACK)
+            )
+            nc.vector.quantize_mx(
+                out=wb_codes[:, a * H : (a + 1) * H].bitcast(FP8X4), scales=wb_sc[:, a * H : (a + 1) * H], in_=wb_b[:]
+            )
+            pairs = wb_b[:].bitcast(F32)
+            wt_b = work.tile([P, H * PACK], BF16, name="wt_b%d" % a, align_bytes=64)
+            for u in range(2):
+                bank = psum.tile([P, PACK, P], F32, name="wt_bank", tag="o_bank", bufs=O_BANKS)
+                for t in range(PACK):
+                    nc.tensor.transpose(bank[:, t, :], pairs[:, 2 * t + u : 2 * H : 2 * PACK], ident[:])
+                nc.scalar.copy(
+                    wt_b[:, u * 2 * H : (u + 1) * 2 * H].rearrange("p (e k t) -> p e k t", e=2, t=PACK),
+                    bank[:].rearrange("p t k -> p (t k)").bitcast(BF16).rearrange("p (t k e) -> p e k t", t=PACK, e=2),
+                )
+            nc.vector.quantize_mx(
+                out=wt_codes[:, a * H : (a + 1) * H].bitcast(FP8X4), scales=wt_sc[:, a * H : (a + 1) * H], in_=wt_b[:]
+            )
+
+        flux_t = {}
+
+        def turn_flux(c):
+            if c % 2 == 0:
+                flux_t[c // 2] = work.tile([P, PACK, H], F32, name="flux_t", tag="wb_raw%d" % (c // 2))
+            for u in range(UNITS):
+                g = c * UNITS + u
+                bank = psum.tile([P, PACK, P], F32, name="flux_bank", tag="o_bank", bufs=O_BANKS)
+                for t in range(PACK):
+                    nc.tensor.transpose(bank[:, t, :], flux_raw[c][:, t, u * P : (u + 1) * P], ident[:])
+                nc.scalar.copy(flux_t[g // PACK][:, g % PACK, :], bank[:].rearrange("p t m -> p (t m)"))
+
+        v_words = [keep.tile([P, S], U32, name="v_words%d" % a, align_bytes=64) for a in range(PASSES)]
+        for a in range(PASSES):
+            nc.vector.tensor_copy(v_words[a][:], tab_w[a][:].bitcast(U32).indirect(idx[:]))
+
+        for h, (j0, n) in enumerate(early):
+            xb0 = work.tile([P, n * PACK], BF16, name="xb0%d" % h, align_bytes=64)
+            round_and_quantise_x(0, j0, n, xf0[h], xb0)
+
+        out_rows = out.rearrange("(a p j) s -> a p j s", a=PASSES, j=PACK)
+
+        late = [(1, 0), (1, 1), (1, 2), (0, 3), (1, 3)]
+        xf1 = {}
+
+        def gather_plane(k, h, after):
+            a, c = late[k]
+            j0 = c * CHUNK
+            outside = work.tile([P, 2, CHUNK], F32, name="outside1", tag=after, align_bytes=64)
+            if h == 0:
+                xf1[k] = work.tile([P, PACK, CHUNK], F32, name="xf1", tag="xf%d" % (k % 2))
+            for e in range(2):
+                nc.vector.tensor_copy(outside[:, e, :], planes[a, 2 * h + e][:].indirect(entries(idx3, j0, CHUNK)))
+            for e in range(2):
+                nc.vector.tensor_tensor(
+                    xf1[k][:, 2 * h + e, :],
+                    planes[a, 2 * h + e][:].indirect(entries(idx2, j0, CHUNK)),
+                    outside[:, e, :],
+                    ALU.subtract,
+                )
+
+        def quantise_late(k, after):
+            a, c = late[k]
+            xb = work.tile([P, CHUNK * PACK], BF16, name="xb1", tag=after, align_bytes=64)
+            round_and_quantise_x(a, c * CHUNK, CHUNK, xf1[k], xb)
+
+        psi_b = {}
+
+        held = {}
+
+        def residual(g):
+            cols = slice(g * P, (g + 1) * P)
+            model = psum.tile([P, H], F32, name="model", bufs=M_BANKS)
+            for a in range(PASSES):
+                nc.tensor.matmul_mx(
+                    out=model[:],
+                    lhsT=v_words[a][:, cols].bitcast(FP8X4),
+                    lhsT_scale=v_sc[a][:, cols],
+                    rhs=w4_w[:, a, :].bitcast(FP4X4),
+                    rhs_scale=w4_sc[:, a * H : (a + 1) * H],
+                    start=(a == 0),
+                    stop=False,
+                )
+            for a in range(PASSES):
+                nc.tensor.matmul_mx(
+                    out=model[:],
+                    lhsT=x_codes[a][:, cols].bitcast(FP8X4),
+                    lhsT_scale=x_sc[a][:, cols],
+                    rhs=wb_codes[:, a * H : (a + 1) * H].bitcast(FP8X4),
+                    rhs_scale=wb_sc[:, a * H : (a + 1) * H],
+                    start=False,
+                    stop=(a == PASSES - 1),
+                )
+            neg_model = work.tile([P, PACK, P], F32, name="neg_model", tag="neg%d" % (g % 4), align_bytes=64)
+            nc.scalar.activation(neg_model[:], model[:].rearrange("p (m t) -> p t m", t=PACK), ACT.Copy, scale=-1.0)
+            res = psum.tile([P, PACK, P], F32, name="res", bufs=R_BANKS)
+            for t in range(PACK):
+                nc.tensor.matmul(
+                    res[:, t, :],
+                    lhsT=flux_t[g // PACK][:, g % PACK, t * P : (t + 1) * P],
+                    rhs=ident[:],
+                    is_transpose=True,
+                    start=(t == 0),
+                    stop=False,
+                )
+            for t in range(PACK):
+                nc.tensor.matmul(
+                    res[:, t, :],
+                    lhsT=neg_model[:, t, :],
+                    rhs=ident[:],
+                    is_transpose=True,
+                    start=False,
+                    stop=(t == PACK - 1),
+                )
+            res_sq = work.tile([P, PACK, P], F32, name="res_sq", bufs=3)
+            nc.scalar.activation(res_sq[:], res[:], ACT.Square)
+            held[g] = (res, res_sq)
+
+        def influence(g):
+            c, u = divmod(g, UNITS)
+            res, res_sq = held[g]
+            inv_root = work.tile([P, PACK, P], F32, name="inv_root", bufs=2)
+            for t in range(PACK):
+                nc.scalar.activation(
+                    inv_root[:, t, :], res_sq[:, t, :], ACT.Abs_reciprocal_sqrt, bias=var_t[:, t : t + 1]
+                )
+            inv = work.tile([P, P, PACK], F32, name="inv", tag="inv%d" % (g % 4), align_bytes=64)
+            nc.scalar.activation(inv[:], inv_root[:].rearrange("p t j -> p j t"), ACT.Square)
+            if u == 0:
+                psi_b[c] = work.tile([P, CHUNK * PACK], BF16, name="psi_b", tag="psi%d" % c, align_bytes=64)
+            nc.vector.tensor_tensor(
+                psi_b[c][:, u * P * PACK : (u + 1) * P * PACK].rearrange("p (j t) -> p j t", t=PACK),
+                res[:].rearrange("p t j -> p j t"),
+                inv[:],
+                ALU.mult,
+            )
+
+        def back_through_wb(c, after):
+            j0 = c * CHUNK
+            psi_codes = work.tile([P, CHUNK], U32, name="psi_codes", align_bytes=64, bufs=2)
+            psi_sc = work.tile([P, CHUNK], U8, name="psi_sc", align_bytes=64, bufs=2)
+            nc.vector.quantize_mx(out=psi_codes[:].bitcast(FP8X4), scales=psi_sc[:], in_=psi_b[c][:])
+            staged = work.tile([P, PASSES * PACK, CHUNK], F32, name="staged", tag=after, align_bytes=64)
+            for b in range(PACK):
+                back = psum.tile([P, 2, CHUNK], F32, name="back", tag="o_bank", bufs=O_BANKS)
+                for e in range(2):
+                    n = 2 * b + e
+                    nc.tensor.matmul_mx(
+                        out=back[:, e, :],
+                        lhsT=wt_codes[:, n * P : (n + 1) * P].bitcast(FP8X4),
+                        lhsT_scale=wt_sc[:, n * P : (n + 1) * P],
+                        rhs=psi_codes[:].bitcast(FP8X4),
+                        rhs_scale=psi_sc[:],
+                        start=True,
+                        stop=True,
+                    )
+                for e in range(2):
+                    n = 2 * b + e
+                    factor = step_t[:, n // PACK, n % PACK : n % PACK + 1]
+                    if b in ON_SCALAR[c]:
+                        nc.scalar.activation(staged[:, n, :], back[:, e, :], ACT.Copy, scale=factor)
+                    else:
+                        nc.vector.tensor_scalar(staged[:, n, :], back[:, e, :], factor, None, ALU.mult)
+                if b % 2 == 1:
+                    a = b // 2
+                    nc.sync.dma_start(
+                        out=out_rows[a, :, :, j0 : j0 + CHUNK], in_=staged[:, a * PACK : (a + 1) * PACK, :]
+                    )
+
+        turn_flux(0)
+        gather_plane(0, 0, "o0")
+        gather_plane(0, 1, "o1")
+        quantise_late(0, "xa")
+        gather_plane(1, 0, "o1")
+        gather_plane(1, 1, "xa")
+        turn_flux(1)
+        residual(0)
+        residual(1)
+        quantise_late(1, "neg1")
+        gather_plane(2, 0, "xa")
+        gather_plane(2, 1, "neg1")
+        influence(0)
+        residual(2)
+        residual(3)
+        influence(1)
+        quantise_late(2, "neg3")
+        turn_flux(2)
+        gather_plane(3, 0, "inv1")
+        gather_plane(3, 1, "neg3")
+        back_through_wb(0, "neg3")
+        influence(2)
+        residual(4)
+        residual(5)
+        influence(3)
+        quantise_late(3, "xa")
+        gather_plane(4, 0, "inv2")
+        gather_plane(4, 1, "inv3")
+        turn_flux(3)
+        influence(4)
+        quantise_late(4, "o0")
+        influence(5)
+        back_through_wb(1, "tab_w0")
+        residual(6)
+        residual(7)
+        influence(6)
+        back_through_wb(2, "tab_w1")
+        influence(7)
+        back_through_wb(3, "plane00")

@@ -23,8 +23,9 @@ PASSES = K // (P * PACK)
 CHUNK = 256
 UNITS = CHUNK // P
 PER_COL = 16
+RUN = 4
 M_BANKS, R_BANKS, O_BANKS = 2, 3, 3
-ON_SCALAR = [(0,), (0,), (0, 2), (0, 2)]
+ON_SCALAR = [(), (), (), (0, 2)]
 
 
 def tile_list_transit_cauchy_step_kernel(
@@ -43,23 +44,22 @@ def tile_list_transit_cauchy_step_kernel(
         idx2 = keep.tile([P, S // PER_COL], U16, name="idx2")
         idx3 = keep.tile([P, S // PER_COL], U16, name="idx3")
         nc.sync.dma_start(idx[:], offs)
+        tab_sc = keep.tile([P, T], U8, name="tab_sc")
+        nc.sync.dma_start(
+            out=tab_sc[0:32, :].bitcast(I32), in_=tab_scales.rearrange("a q t -> (a q) t").bitcast(I32)
+        )
         nc.sync.dma_start(idx3[:], offs3)
         nc.sync.dma_start(idx2[:], offs2)
 
-        tab_sc = keep.tile([P, T], U8, name="tab_sc")
         w4_sc = keep.tile([P, PASSES * H], U8, name="w4_sc", align_bytes=64)
-        v_sc0 = keep.tile([P, S], U8, name="v_sc0", align_bytes=64)
-        v_sc1 = keep.tile([P, S], U8, name="v_sc1", align_bytes=64)
-        nc.gpsimd.memset(tab_sc[:].bitcast(I32), 0)
+        v_sc = [keep.tile([P, S], U8, name="v_sc%d" % a, align_bytes=64) for a in range(PASSES)]
+        nc.vector.memset(tab_sc[32:64, :].bitcast(I32), 0)
+        nc.vector.memset(tab_sc[64:128, :].bitcast(I32), 0)
+        for a in range(PASSES):
+            nc.gpsimd.memset(v_sc[a][:].bitcast(I32), 0)
         nc.gpsimd.memset(w4_sc[:].bitcast(I32), 0)
-        nc.gpsimd.memset(v_sc1[:].bitcast(I32), 0)
         ident = keep.tile([P, P], F32, name="ident")
         make_identity(nc, ident[:])
-        for q in range(4):
-            nc.scalar.dma_start(
-                out=tab_sc[32 * q : 32 * q + 8, :].bitcast(I32),
-                in_=tab_scales[:, 4 * q : 4 * q + 4, :].bitcast(I32),
-            )
 
         x_rows = xT.rearrange("(a p i) t -> a i p t", a=PASSES, i=PACK)
         planes = {}
@@ -119,15 +119,25 @@ def tile_list_transit_cauchy_step_kernel(
         load_flux(2)
         load_flux(3)
 
-        nc.vector.tensor_copy(v_sc0[:], tab_sc[:].indirect(idx[:]))
-        nc.scalar.dma_start(out=v_sc1[0:112, :].bitcast(I32), in_=v_sc0[4:116, :].bitcast(I32))
-        v_sc = [v_sc0, v_sc1]
+        picked_sc = keep.tile([P, S], U8, name="picked_sc")
+        nc.vector.tensor_copy(picked_sc[:], tab_sc[:].indirect(idx[:]))
+        for a in range(PASSES):
+            for q in range(4):
+                row = 16 * a + 4 * q
+                nc.gpsimd.dma_start(
+                    out=v_sc[a][32 * q : 32 * q + 4, :].bitcast(I32), in_=picked_sc[row : row + 4, :].bitcast(I32)
+                )
 
         x_codes = [keep.tile([P, S], U32, name="x_codes%d" % a, align_bytes=64) for a in range(PASSES)]
         x_sc = [keep.tile([P, S], U8, name="x_sc%d" % a, align_bytes=64) for a in range(PASSES)]
 
-        def round_and_quantise_x(a, j0, n, xf, xb):
-            nc.scalar.copy(xb[:].rearrange("p (j i) -> p j i", i=PACK), xf[:].rearrange("p i j -> p j i"))
+        def weave(engine_copy, woven, rows):
+            engine_copy(
+                woven.rearrange("p (c e t) -> p c t e", e=RUN, t=PACK), rows.rearrange("p t (c e) -> p c t e", e=RUN)
+            )
+
+        def round_and_quantise_x(a, j0, n, xf, xb, copy=nc.scalar.copy):
+            weave(copy, xb[:], xf[:])
             nc.vector.quantize_mx(
                 out=x_codes[a][:, j0 : j0 + n].bitcast(FP8X4), scales=x_sc[a][:, j0 : j0 + n], in_=xb[:]
             )
@@ -152,9 +162,7 @@ def tile_list_transit_cauchy_step_kernel(
         wt_sc = keep.tile([P, K], U8, name="wt_sc", align_bytes=64)
         for a in range(PASSES):
             wb_b = work.tile([P, H * PACK], BF16, name="wb_b%d" % a, align_bytes=64)
-            nc.scalar.copy(
-                wb_b[:].rearrange("p (r j) -> p r j", j=PACK), wb_raw[a][:].rearrange("p (j r) -> p r j", j=PACK)
-            )
+            weave(nc.scalar.copy, wb_b[:], wb_raw[a][:].rearrange("p (j r) -> p j r", j=PACK))
             nc.vector.quantize_mx(
                 out=wb_codes[:, a * H : (a + 1) * H].bitcast(FP8X4), scales=wb_sc[:, a * H : (a + 1) * H], in_=wb_b[:]
             )
@@ -216,7 +224,7 @@ def tile_list_transit_cauchy_step_kernel(
         def quantise_late(k, after):
             a, c = late[k]
             xb = work.tile([P, CHUNK * PACK], BF16, name="xb1", tag=after, align_bytes=64)
-            round_and_quantise_x(a, c * CHUNK, CHUNK, xf1[k], xb)
+            round_and_quantise_x(a, c * CHUNK, CHUNK, xf1[k], xb, nc.vector.tensor_copy if k == 4 else nc.scalar.copy)
 
         psi_b = {}
 
@@ -246,7 +254,11 @@ def tile_list_transit_cauchy_step_kernel(
                     stop=(a == PASSES - 1),
                 )
             neg_model = work.tile([P, PACK, P], F32, name="neg_model", tag="neg%d" % (g % 4), align_bytes=64)
-            nc.scalar.activation(neg_model[:], model[:].rearrange("p (m t) -> p t m", t=PACK), ACT.Copy, scale=-1.0)
+            by_slot = model[:].rearrange("p (m t) -> p t m", t=PACK)
+            if g == 7:
+                nc.vector.tensor_scalar(neg_model[:], by_slot, -1.0, None, ALU.mult)
+            else:
+                nc.scalar.activation(neg_model[:], by_slot, ACT.Copy, scale=-1.0)
             res = psum.tile([P, PACK, P], F32, name="res", bufs=R_BANKS)
             for t in range(PACK):
                 nc.tensor.matmul(
@@ -289,11 +301,17 @@ def tile_list_transit_cauchy_step_kernel(
                 ALU.mult,
             )
 
+        psi_q = {}
+
+        def quantise_psi(c):
+            codes = work.tile([P, CHUNK], U32, name="psi_codes", align_bytes=64, bufs=4)
+            scales = work.tile([P, CHUNK], U8, name="psi_sc", align_bytes=64, bufs=4)
+            nc.vector.quantize_mx(out=codes[:].bitcast(FP8X4), scales=scales[:], in_=psi_b[c][:])
+            psi_q[c] = (codes, scales)
+
         def back_through_wb(c, after):
             j0 = c * CHUNK
-            psi_codes = work.tile([P, CHUNK], U32, name="psi_codes", align_bytes=64, bufs=2)
-            psi_sc = work.tile([P, CHUNK], U8, name="psi_sc", align_bytes=64, bufs=2)
-            nc.vector.quantize_mx(out=psi_codes[:].bitcast(FP8X4), scales=psi_sc[:], in_=psi_b[c][:])
+            psi_codes, psi_sc = psi_q[c]
             staged = work.tile([P, PASSES * PACK, CHUNK], F32, name="staged", tag=after, align_bytes=64)
             for b in range(PACK):
                 back = psum.tile([P, 2, CHUNK], F32, name="back", tag="o_bank", bufs=O_BANKS)
@@ -339,24 +357,28 @@ def tile_list_transit_cauchy_step_kernel(
         influence(1)
         quantise_late(2, "neg3")
         turn_flux(2)
-        gather_plane(3, 0, "inv1")
-        gather_plane(3, 1, "neg3")
-        back_through_wb(0, "neg3")
-        influence(2)
+        gather_plane(3, 0, "inv0")
+        gather_plane(3, 1, "inv1")
+        quantise_psi(0)
         residual(4)
+        influence(2)
         residual(5)
+        quantise_late(3, "neg0")
         influence(3)
-        quantise_late(3, "xa")
-        gather_plane(4, 0, "inv2")
-        gather_plane(4, 1, "inv3")
         turn_flux(3)
+        gather_plane(4, 0, "neg3")
+        gather_plane(4, 1, "inv2")
+        quantise_late(4, "tab_w1")
+        quantise_psi(1)
         influence(4)
-        quantise_late(4, "o0")
-        influence(5)
-        back_through_wb(1, "tab_w0")
         residual(6)
         residual(7)
+        influence(5)
+        quantise_psi(2)
         influence(6)
-        back_through_wb(2, "tab_w1")
         influence(7)
-        back_through_wb(3, "plane00")
+        quantise_psi(3)
+        back_through_wb(0, "tab_w1")
+        back_through_wb(1, "tab_w0")
+        back_through_wb(2, "plane00")
+        back_through_wb(3, "plane01")

@@ -21,11 +21,11 @@ P = 128
 PACK = 4
 PASSES = K // (P * PACK)
 CHUNK = 256
-UNITS = CHUNK // P
 PER_COL = 16
 RUN = 4
-M_BANKS, R_BANKS, O_BANKS = 2, 3, 3
-ON_SCALAR = [(), (), (), (0, 2)]
+BANK = 512
+EARLY = 3
+UNITS = CHUNK // P
 
 
 def tile_list_transit_cauchy_step_kernel(
@@ -40,84 +40,79 @@ def tile_list_transit_cauchy_step_kernel(
         def entries(lst, j0, n):
             return lst[:, j0 // PER_COL : (j0 + n) // PER_COL]
 
-        idx = keep.tile([P, S // PER_COL], U16, name="idx")
-        idx2 = keep.tile([P, S // PER_COL], U16, name="idx2")
-        idx3 = keep.tile([P, S // PER_COL], U16, name="idx3")
-        nc.sync.dma_start(idx[:], offs)
-        tab_sc = keep.tile([P, T], U8, name="tab_sc")
-        nc.sync.dma_start(
-            out=tab_sc[0:32, :].bitcast(I32), in_=tab_scales.rearrange("a q t -> (a q) t").bitcast(I32)
-        )
-        nc.sync.dma_start(idx3[:], offs3)
-        nc.sync.dma_start(idx2[:], offs2)
-
-        w4_sc = keep.tile([P, PASSES * H], U8, name="w4_sc", align_bytes=64)
-        v_sc = [keep.tile([P, S], U8, name="v_sc%d" % a, align_bytes=64) for a in range(PASSES)]
-        nc.vector.memset(tab_sc[32:64, :].bitcast(I32), 0)
-        nc.vector.memset(tab_sc[64:128, :].bitcast(I32), 0)
-        for a in range(PASSES):
-            nc.gpsimd.memset(v_sc[a][:].bitcast(I32), 0)
-        nc.gpsimd.memset(w4_sc[:].bitcast(I32), 0)
-        ident = keep.tile([P, P], F32, name="ident")
-        make_identity(nc, ident[:])
-
         x_rows = xT.rearrange("(a p i) t -> a i p t", a=PASSES, i=PACK)
         planes = {}
 
         def load_plane(a, i):
-            planes[a, i] = work.tile([P, T], F32, name="plane%d%d" % (a, i), align_bytes=64)
+            planes[a, i] = keep.tile([P, T], F32, name="plane%d%d" % (a, i), align_bytes=64)
             nc.sync.dma_start(out=planes[a, i][:], in_=x_rows[a, i])
 
         wb_raw = {}
 
         def load_wb(a):
-            wb_raw[a] = work.tile([P, PACK * H], F32, name="wb_raw%d" % a, tag="wb_raw%d" % a)
+            wb_raw[a] = work.tile([P, PACK * H], F32, name="wb_raw", tag="big%d" % a, align_bytes=64)
             nc.sync.dma_start(
                 out=wb_raw[a][:], in_=wb[a * P * PACK : (a + 1) * P * PACK, :].rearrange("(p j) r -> p (j r)", j=PACK)
             )
 
-        flux_raw = {}
+        flux_sb = {}
 
-        def load_flux(c):
-            flux_raw[c] = work.tile([P, PACK, CHUNK], F32, name="flux_raw%d" % c)
+        def load_flux(h):
+            flux_sb[h] = work.tile([P, PACK, S // 2], F32, name="flux_sb", tag="big%d" % h, align_bytes=64)
             nc.sync.dma_start(
-                out=flux_raw[c][:],
-                in_=flux[:, c * CHUNK : (c + 1) * CHUNK].rearrange("(p t) j -> p t j", t=PACK),
+                out=flux_sb[h][:],
+                in_=flux[:, h * S // 2 : (h + 1) * S // 2].rearrange("(p t) j -> p t j", t=PACK),
             )
 
         tab_w = {}
 
         def load_tab(a):
-            tab_w[a] = work.tile([P, T], I32, name="tab_w%d" % a, align_bytes=64)
+            tab_w[a] = work.tile([P, T], I32, name="tab_w", tag="big%d" % (2 + a), align_bytes=64)
             nc.sync.dma_start(out=tab_w[a][:], in_=tab_words[a].rearrange("p t i -> p (t i)").bitcast(I32))
 
+        idx = keep.tile([P, S // PER_COL], U16, name="idx")
+        idx2 = keep.tile([P, S // PER_COL], U16, name="idx2")
+        idx3 = keep.tile([P, S // PER_COL], U16, name="idx3")
+        tab_sc = keep.tile([P, T], U8, name="tab_sc")
+        w4_sc_raw = keep.tile([P, PASSES * H], U8, name="w4_sc_raw", align_bytes=64)
+        v_sc = [keep.tile([P, S], U8, name="v_sc%d" % a, align_bytes=64) for a in range(PASSES)]
+        nc.vector.memset(tab_sc[32:64, :].bitcast(I32), 0)
+        nc.vector.memset(tab_sc[64:128, :].bitcast(I32), 0)
+        nc.gpsimd.memset(w4_sc_raw[:].bitcast(I32), 0)
+        for a in range(PASSES):
+            nc.gpsimd.memset(v_sc[a][:].bitcast(I32), 0)
+        ident = keep.tile([P, P], F32, name="ident")
+        make_identity(nc, ident[:])
+
+        nc.sync.dma_start(idx[:], offs)
+        nc.sync.dma_start(
+            out=tab_sc[0:32, :].bitcast(I32), in_=tab_scales.rearrange("a q t -> (a q) t").bitcast(I32)
+        )
         load_plane(0, 0)
+        nc.sync.dma_start(idx3[:], offs3)
+        nc.sync.dma_start(idx2[:], offs2)
         load_plane(0, 1)
-        load_plane(0, 2)
         load_wb(0)
-        load_plane(0, 3)
-        load_wb(1)
-        load_tab(0)
-        load_tab(1)
-        w4_w = keep.tile([P, PASSES, 2 * H], U8, name="w4_w", align_bytes=64)
-        nc.sync.dma_start(out=w4_w[:].bitcast(I32), in_=w4_words.rearrange("a p c -> p a c").bitcast(I32))
+        load_plane(0, 2)
+        w4_raw = keep.tile([P, PASSES, 2 * H], U8, name="w4_raw", align_bytes=64)
+        nc.sync.dma_start(out=w4_raw[:].bitcast(I32), in_=w4_words.rearrange("a p c -> p a c").bitcast(I32))
         for q in range(4):
             nc.sync.dma_start(
-                out=w4_sc[32 * q : 32 * q + 4, :].bitcast(I32).rearrange("p (a c) -> p a c", a=PASSES),
+                out=w4_sc_raw[32 * q : 32 * q + 4, :].bitcast(I32).rearrange("p (a c) -> p a c", a=PASSES),
                 in_=w4_scales[:, 4 * q : 4 * q + 4, :].rearrange("a r c -> r a c").bitcast(I32),
             )
-        load_plane(1, 0)
+        load_wb(1)
+        load_plane(0, 3)
+        load_tab(0)
+        load_tab(1)
         load_flux(0)
-        load_plane(1, 1)
-        load_plane(1, 2)
-        load_plane(1, 3)
+        for i in range(PACK):
+            load_plane(1, i)
         var_t = keep.tile([P, PACK], F32, name="var_t")
         nc.sync.dma_start(out=var_t[:], in_=var.rearrange("(p t) -> p t", t=PACK))
-        load_flux(1)
         step_t = keep.tile([P, PASSES, PACK], F32, name="step_t")
         nc.sync.dma_start(out=step_t[:], in_=step.rearrange("(a p j) -> p a j", a=PASSES, j=PACK))
-        load_flux(2)
-        load_flux(3)
+        load_flux(1)
 
         picked_sc = keep.tile([P, S], U8, name="picked_sc")
         nc.vector.tensor_copy(picked_sc[:], tab_sc[:].indirect(idx[:]))
@@ -128,29 +123,21 @@ def tile_list_transit_cauchy_step_kernel(
                     out=v_sc[a][32 * q : 32 * q + 4, :].bitcast(I32), in_=picked_sc[row : row + 4, :].bitcast(I32)
                 )
 
-        x_codes = [keep.tile([P, S], U32, name="x_codes%d" % a, align_bytes=64) for a in range(PASSES)]
-        x_sc = [keep.tile([P, S], U8, name="x_sc%d" % a, align_bytes=64) for a in range(PASSES)]
-
         def weave(engine_copy, woven, rows):
             engine_copy(
                 woven.rearrange("p (c e t) -> p c t e", e=RUN, t=PACK), rows.rearrange("p t (c e) -> p c t e", e=RUN)
             )
 
-        def round_and_quantise_x(a, j0, n, xf, xb, copy=nc.scalar.copy):
-            weave(copy, xb[:], xf[:])
-            nc.vector.quantize_mx(
-                out=x_codes[a][:, j0 : j0 + n].bitcast(FP8X4), scales=x_sc[a][:, j0 : j0 + n], in_=xb[:]
-            )
-
+        n_early = EARLY * CHUNK
         early = [(0, 2 * CHUNK), (2 * CHUNK, CHUNK)]
-        xf0 = [work.tile([P, PACK, n], F32, name="xf0%d" % h, tag="xf%d" % h) for h, (j0, n) in enumerate(early)]
+        xf_early = work.tile([P, PACK, n_early], F32, name="xf_early", align_bytes=64)
         for i in range(PACK):
-            outside = work.tile([P, 3 * CHUNK], F32, name="outside0", bufs=2)
+            outside = work.tile([P, n_early], F32, name="outside_early", bufs=2)
             for j0, n in early:
                 nc.vector.tensor_copy(outside[:, j0 : j0 + n], planes[0, i][:].indirect(entries(idx3, j0, n)))
-            for h, (j0, n) in enumerate(early):
+            for j0, n in early:
                 nc.vector.tensor_tensor(
-                    xf0[h][:, i, :],
+                    xf_early[:, i, j0 : j0 + n],
                     planes[0, i][:].indirect(entries(idx2, j0, n)),
                     outside[:, j0 : j0 + n],
                     ALU.subtract,
@@ -161,17 +148,20 @@ def tile_list_transit_cauchy_step_kernel(
         wt_codes = keep.tile([P, K], U32, name="wt_codes", align_bytes=64)
         wt_sc = keep.tile([P, K], U8, name="wt_sc", align_bytes=64)
         for a in range(PASSES):
-            wb_b = work.tile([P, H * PACK], BF16, name="wb_b%d" % a, align_bytes=64)
-            weave(nc.scalar.copy, wb_b[:], wb_raw[a][:].rearrange("p (j r) -> p j r", j=PACK))
+            wb_b = work.tile([P, H * PACK], BF16, name="wb_b", tag="mid%d" % a, align_bytes=64)
+            nc.scalar.copy(
+                wb_b[:].rearrange("p (t m j) -> p m t j", t=PACK, j=PACK),
+                wb_raw[a][:].rearrange("p (j m t) -> p m t j", j=PACK, t=PACK),
+            )
             nc.vector.quantize_mx(
                 out=wb_codes[:, a * H : (a + 1) * H].bitcast(FP8X4), scales=wb_sc[:, a * H : (a + 1) * H], in_=wb_b[:]
             )
             pairs = wb_b[:].bitcast(F32)
-            wt_b = work.tile([P, H * PACK], BF16, name="wt_b%d" % a, align_bytes=64)
+            wt_b = work.tile([P, H * PACK], BF16, name="wt_b", tag="mid%d" % (2 + a), align_bytes=64)
             for u in range(2):
-                bank = psum.tile([P, PACK, P], F32, name="wt_bank", tag="o_bank", bufs=O_BANKS)
+                bank = psum.tile([P, PACK, P], F32, name="wt_bank", tag="o_bank", bufs=4)
                 for t in range(PACK):
-                    nc.tensor.transpose(bank[:, t, :], pairs[:, 2 * t + u : 2 * H : 2 * PACK], ident[:])
+                    nc.tensor.transpose(bank[:, t, :], pairs[:, 2 * P * t + u : 2 * P * (t + 1) : 2], ident[:])
                 nc.scalar.copy(
                     wt_b[:, u * 2 * H : (u + 1) * 2 * H].rearrange("p (e k t) -> p e k t", e=2, t=PACK),
                     bank[:].rearrange("p t k -> p (t k)").bitcast(BF16).rearrange("p (t k e) -> p e k t", t=PACK, e=2),
@@ -180,205 +170,240 @@ def tile_list_transit_cauchy_step_kernel(
                 out=wt_codes[:, a * H : (a + 1) * H].bitcast(FP8X4), scales=wt_sc[:, a * H : (a + 1) * H], in_=wt_b[:]
             )
 
-        flux_t = {}
-
-        def turn_flux(c):
-            if c % 2 == 0:
-                flux_t[c // 2] = work.tile([P, PACK, H], F32, name="flux_t", tag="wb_raw%d" % (c // 2))
-            for u in range(UNITS):
-                g = c * UNITS + u
-                bank = psum.tile([P, PACK, P], F32, name="flux_bank", tag="o_bank", bufs=O_BANKS)
-                for t in range(PACK):
-                    nc.tensor.transpose(bank[:, t, :], flux_raw[c][:, t, u * P : (u + 1) * P], ident[:])
-                nc.scalar.copy(flux_t[g // PACK][:, g % PACK, :], bank[:].rearrange("p t m -> p (t m)"))
+        w4_w = keep.tile([P, PASSES * 2 * H], U8, name="w4_w", align_bytes=64)
+        w4_sc = keep.tile([P, PASSES * H], U8, name="w4_sc", align_bytes=64)
+        nc.vector.tensor_copy(
+            w4_w[:].bitcast(U16).rearrange("p (a t m) -> p a m t", a=PASSES, t=PACK),
+            w4_raw[:].rearrange("p a c -> p (a c)").bitcast(U16).rearrange("p (a m t) -> p a m t", a=PASSES, t=PACK),
+        )
+        nc.vector.tensor_copy(
+            w4_sc[:].rearrange("p (a t m) -> p a m t", a=PASSES, t=PACK),
+            w4_sc_raw[:].rearrange("p (a m t) -> p a m t", a=PASSES, t=PACK),
+        )
 
         v_words = [keep.tile([P, S], U32, name="v_words%d" % a, align_bytes=64) for a in range(PASSES)]
         for a in range(PASSES):
             nc.vector.tensor_copy(v_words[a][:], tab_w[a][:].bitcast(U32).indirect(idx[:]))
 
-        for h, (j0, n) in enumerate(early):
-            xb0 = work.tile([P, n * PACK], BF16, name="xb0%d" % h, align_bytes=64)
-            round_and_quantise_x(0, j0, n, xf0[h], xb0)
+        xb = {}
+        for c in range(EARLY):
+            xb[c, 0] = work.tile([P, CHUNK * PACK], BF16, name="xb", tag="xb0%d" % c, align_bytes=64)
+            weave(nc.scalar.copy, xb[c, 0][:], xf_early[:, :, c * CHUNK : (c + 1) * CHUNK])
 
         out_rows = out.rearrange("(a p j) s -> a p j s", a=PASSES, j=PACK)
 
-        late = [(1, 0), (1, 1), (1, 2), (0, 3), (1, 3)]
-        xf1 = {}
+        lanes = [keep.tile([P, 6 * CHUNK], F32, name="lane%d" % k, align_bytes=64) for k in range(5)]
 
-        def gather_plane(k, h, after):
-            a, c = late[k]
-            j0 = c * CHUNK
-            outside = work.tile([P, 2, CHUNK], F32, name="outside1", tag=after, align_bytes=64)
-            if h == 0:
-                xf1[k] = work.tile([P, PACK, CHUNK], F32, name="xf1", tag="xf%d" % (k % 2))
-            for e in range(2):
-                nc.vector.tensor_copy(outside[:, e, :], planes[a, 2 * h + e][:].indirect(entries(idx3, j0, CHUNK)))
-            for e in range(2):
+        def quarter(k, i, n=1):
+            return lanes[k][:, i * CHUNK : (i + n) * CHUNK]
+
+        def by_runs(ap):
+            return ap.rearrange("p (c e t) -> p c t e", e=RUN, t=PACK)
+
+        def weave_flux(c):
+            h, o = divmod(c * CHUNK, S // 2)
+            weave(nc.scalar.copy, quarter(c + 1, 2, 4), flux_sb[h][:, :, o : o + CHUNK])
+
+        def pick_outside(a, c, i, dst):
+            nc.vector.tensor_copy(dst, planes[a, i][:].indirect(entries(idx3, c * CHUNK, CHUNK)))
+
+        def subtract_inside(dst, a, i, j0, n, outside):
+            nc.vector.tensor_tensor(dst, planes[a, i][:].indirect(entries(idx2, j0, n)), outside, ALU.subtract)
+
+        def quantise(name, src, width):
+            codes = work.tile([P, width // PACK], U32, name=name + "_codes", align_bytes=64)
+            scales = work.tile([P, width // PACK], U8, name=name + "_sc", align_bytes=64)
+            nc.vector.quantize_mx(out=codes[:].bitcast(FP8X4), scales=scales[:], in_=src)
+            return codes, scales
+
+        model = {}
+
+        def stage_one(g, x_ops):
+            cols = slice(g * P, (g + 1) * P)
+            model[g] = psum.tile([P, PACK, P], F32, name="model", bufs=4)
+            for t in range(PACK):
+                for a in range(PASSES):
+                    nc.tensor.matmul_mx(
+                        out=model[g][:, t, :],
+                        lhsT=w4_w[:, 2 * (a * H + t * P) : 2 * (a * H + (t + 1) * P)].bitcast(FP4X4),
+                        lhsT_scale=w4_sc[:, a * H + t * P : a * H + (t + 1) * P],
+                        rhs=v_words[a][:, cols].bitcast(FP8X4),
+                        rhs_scale=v_sc[a][:, cols],
+                        start=(t == 0 and a == 0),
+                        stop=False,
+                    )
+            for a in range(PASSES):
+                for t in range(PACK):
+                    nc.tensor.matmul_mx(
+                        out=model[g][:, t, :],
+                        lhsT=wb_codes[:, a * H + t * P : a * H + (t + 1) * P].bitcast(FP8X4),
+                        lhsT_scale=wb_sc[:, a * H + t * P : a * H + (t + 1) * P],
+                        rhs=x_ops[a][0].bitcast(FP8X4),
+                        rhs_scale=x_ops[a][1],
+                        start=False,
+                        stop=(a == PASSES - 1 and t == PACK - 1),
+                    )
+
+        def residual(g0, n, tag):
+            res = work.tile([P, n * PACK], F32, name="res", tag=tag, align_bytes=64)
+            for u in range(n // P):
+                c, o = divmod((g0 + u) * P, CHUNK)
                 nc.vector.tensor_tensor(
-                    xf1[k][:, 2 * h + e, :],
-                    planes[a, 2 * h + e][:].indirect(entries(idx2, j0, CHUNK)),
-                    outside[:, e, :],
+                    res[:, u * P * PACK : (u + 1) * P * PACK].rearrange("p (j t) -> p j t", t=PACK),
+                    quarter(c + 1, 2, 4)[:, o * PACK : (o + P) * PACK].rearrange("p (j t) -> p j t", t=PACK),
+                    model[g0 + u][:].rearrange("p t j -> p j t"),
                     ALU.subtract,
                 )
+            return res
 
-        def quantise_late(k, after):
-            a, c = late[k]
-            xb = work.tile([P, CHUNK * PACK], BF16, name="xb1", tag=after, align_bytes=64)
-            round_and_quantise_x(a, c * CHUNK, CHUNK, xf1[k], xb, nc.vector.tensor_copy if k == 4 else nc.scalar.copy)
+        def square(res, n, tag):
+            res_sq = work.tile([P, PACK, n], F32, name="res_sq", tag=tag, align_bytes=64)
+            nc.scalar.activation(res_sq[:].rearrange("p t (c e) -> p c t e", e=RUN), by_runs(res[:]), ACT.Square)
+            return res_sq
 
-        psi_b = {}
-
-        held = {}
-
-        def residual(g):
-            cols = slice(g * P, (g + 1) * P)
-            model = psum.tile([P, H], F32, name="model", bufs=M_BANKS)
-            for a in range(PASSES):
-                nc.tensor.matmul_mx(
-                    out=model[:],
-                    lhsT=v_words[a][:, cols].bitcast(FP8X4),
-                    lhsT_scale=v_sc[a][:, cols],
-                    rhs=w4_w[:, a, :].bitcast(FP4X4),
-                    rhs_scale=w4_sc[:, a * H : (a + 1) * H],
-                    start=(a == 0),
-                    stop=False,
-                )
-            for a in range(PASSES):
-                nc.tensor.matmul_mx(
-                    out=model[:],
-                    lhsT=x_codes[a][:, cols].bitcast(FP8X4),
-                    lhsT_scale=x_sc[a][:, cols],
-                    rhs=wb_codes[:, a * H : (a + 1) * H].bitcast(FP8X4),
-                    rhs_scale=wb_sc[:, a * H : (a + 1) * H],
-                    start=False,
-                    stop=(a == PASSES - 1),
-                )
-            neg_model = work.tile([P, PACK, P], F32, name="neg_model", tag="neg%d" % (g % 4), align_bytes=64)
-            by_slot = model[:].rearrange("p (m t) -> p t m", t=PACK)
-            if g == 7:
-                nc.vector.tensor_scalar(neg_model[:], by_slot, -1.0, None, ALU.mult)
-            else:
-                nc.scalar.activation(neg_model[:], by_slot, ACT.Copy, scale=-1.0)
-            res = psum.tile([P, PACK, P], F32, name="res", bufs=R_BANKS)
-            for t in range(PACK):
-                nc.tensor.matmul(
-                    res[:, t, :],
-                    lhsT=flux_t[g // PACK][:, g % PACK, t * P : (t + 1) * P],
-                    rhs=ident[:],
-                    is_transpose=True,
-                    start=(t == 0),
-                    stop=False,
-                )
-            for t in range(PACK):
-                nc.tensor.matmul(
-                    res[:, t, :],
-                    lhsT=neg_model[:, t, :],
-                    rhs=ident[:],
-                    is_transpose=True,
-                    start=False,
-                    stop=(t == PACK - 1),
-                )
-            res_sq = work.tile([P, PACK, P], F32, name="res_sq", bufs=3)
-            nc.scalar.activation(res_sq[:], res[:], ACT.Square)
-            held[g] = (res, res_sq)
-
-        def influence(g):
-            c, u = divmod(g, UNITS)
-            res, res_sq = held[g]
-            inv_root = work.tile([P, PACK, P], F32, name="inv_root", bufs=2)
+        def invert(res_sq, n, root_tag, tag):
+            inv_root = work.tile([P, PACK, n], F32, name="inv_root", tag=root_tag, align_bytes=64)
             for t in range(PACK):
                 nc.scalar.activation(
                     inv_root[:, t, :], res_sq[:, t, :], ACT.Abs_reciprocal_sqrt, bias=var_t[:, t : t + 1]
                 )
-            inv = work.tile([P, P, PACK], F32, name="inv", tag="inv%d" % (g % 4), align_bytes=64)
-            nc.scalar.activation(inv[:], inv_root[:].rearrange("p t j -> p j t"), ACT.Square)
-            if u == 0:
-                psi_b[c] = work.tile([P, CHUNK * PACK], BF16, name="psi_b", tag="psi%d" % c, align_bytes=64)
-            nc.vector.tensor_tensor(
-                psi_b[c][:, u * P * PACK : (u + 1) * P * PACK].rearrange("p (j t) -> p j t", t=PACK),
-                res[:].rearrange("p t j -> p j t"),
-                inv[:],
-                ALU.mult,
-            )
+            inv = work.tile([P, n * PACK], F32, name="inv", tag=tag, align_bytes=64)
+            nc.scalar.activation(by_runs(inv[:]), inv_root[:].rearrange("p t (c e) -> p c t e", e=RUN), ACT.Square)
+            return inv
 
-        psi_q = {}
+        def influence(res, inv, n):
+            psi_b = work.tile([P, n * PACK], BF16, name="psi_b", align_bytes=64, bufs=2)
+            nc.vector.tensor_tensor(psi_b[:], res[:], inv[:], ALU.mult)
+            return psi_b
 
-        def quantise_psi(c):
-            codes = work.tile([P, CHUNK], U32, name="psi_codes", align_bytes=64, bufs=4)
-            scales = work.tile([P, CHUNK], U8, name="psi_sc", align_bytes=64, bufs=4)
-            nc.vector.quantize_mx(out=codes[:].bitcast(FP8X4), scales=scales[:], in_=psi_b[c][:])
-            psi_q[c] = (codes, scales)
-
-        def back_through_wb(c, after):
-            j0 = c * CHUNK
-            psi_codes, psi_sc = psi_q[c]
-            staged = work.tile([P, PASSES * PACK, CHUNK], F32, name="staged", tag=after, align_bytes=64)
-            for b in range(PACK):
-                back = psum.tile([P, 2, CHUNK], F32, name="back", tag="o_bank", bufs=O_BANKS)
-                for e in range(2):
-                    n = 2 * b + e
+        def back_through_wb(psi_q, j0, n, on_vector, tag):
+            psi_codes, psi_sc = psi_q
+            per_bank = BANK // n
+            staged = work.tile([P, PASSES * PACK, n], F32, name="staged", tag=tag, align_bytes=64)
+            for b in range(PASSES * PACK // per_bank):
+                back = psum.tile([P, per_bank, n], F32, name="back", tag="o_bank", bufs=4)
+                for e in range(per_bank):
+                    m = b * per_bank + e
                     nc.tensor.matmul_mx(
                         out=back[:, e, :],
-                        lhsT=wt_codes[:, n * P : (n + 1) * P].bitcast(FP8X4),
-                        lhsT_scale=wt_sc[:, n * P : (n + 1) * P],
+                        lhsT=wt_codes[:, m * P : (m + 1) * P].bitcast(FP8X4),
+                        lhsT_scale=wt_sc[:, m * P : (m + 1) * P],
                         rhs=psi_codes[:].bitcast(FP8X4),
                         rhs_scale=psi_sc[:],
                         start=True,
                         stop=True,
                     )
-                for e in range(2):
-                    n = 2 * b + e
-                    factor = step_t[:, n // PACK, n % PACK : n % PACK + 1]
-                    if b in ON_SCALAR[c]:
-                        nc.scalar.activation(staged[:, n, :], back[:, e, :], ACT.Copy, scale=factor)
+                for e in range(per_bank):
+                    m = b * per_bank + e
+                    factor = step_t[:, m // PACK, m % PACK : m % PACK + 1]
+                    if b in on_vector:
+                        nc.vector.tensor_scalar(staged[:, m, :], back[:, e, :], factor, None, ALU.mult)
                     else:
-                        nc.vector.tensor_scalar(staged[:, n, :], back[:, e, :], factor, None, ALU.mult)
-                if b % 2 == 1:
-                    a = b // 2
-                    nc.sync.dma_start(
-                        out=out_rows[a, :, :, j0 : j0 + CHUNK], in_=staged[:, a * PACK : (a + 1) * PACK, :]
-                    )
+                        nc.scalar.activation(staged[:, m, :], back[:, e, :], ACT.Copy, scale=factor)
+                if (b + 1) * per_bank % PACK == 0:
+                    a = b * per_bank // PACK
+                    nc.sync.dma_start(out=out_rows[a, :, :, j0 : j0 + n], in_=staged[:, a * PACK : (a + 1) * PACK, :])
 
-        turn_flux(0)
-        gather_plane(0, 0, "o0")
-        gather_plane(0, 1, "o1")
-        quantise_late(0, "xa")
-        gather_plane(1, 0, "o1")
-        gather_plane(1, 1, "xa")
-        turn_flux(1)
-        residual(0)
-        residual(1)
-        quantise_late(1, "neg1")
-        gather_plane(2, 0, "xa")
-        gather_plane(2, 1, "neg1")
-        influence(0)
-        residual(2)
-        residual(3)
-        influence(1)
-        quantise_late(2, "neg3")
-        turn_flux(2)
-        gather_plane(3, 0, "inv0")
-        gather_plane(3, 1, "inv1")
-        quantise_psi(0)
-        residual(4)
-        influence(2)
-        residual(5)
-        quantise_late(3, "neg0")
-        influence(3)
-        turn_flux(3)
-        gather_plane(4, 0, "neg3")
-        gather_plane(4, 1, "inv2")
-        quantise_late(4, "tab_w1")
-        quantise_psi(1)
-        influence(4)
-        residual(6)
-        residual(7)
-        influence(5)
-        quantise_psi(2)
-        influence(6)
-        influence(7)
-        quantise_psi(3)
-        back_through_wb(0, "tab_w1")
-        back_through_wb(1, "tab_w0")
-        back_through_wb(2, "plane00")
-        back_through_wb(3, "plane01")
+        x_first = {}
+
+        def quantise_second_pass(c):
+            second = quantise("x1%d" % (c % 2), xb[c, 1][:], CHUNK * PACK)
+            for u in range(UNITS):
+                cols = slice(u * P, (u + 1) * P)
+                stage_one(c * UNITS + u, [(codes[:, cols], scales[:, cols]) for codes, scales in (x_first[c], second)])
+
+        last = EARLY
+        res, res_sq, inv, psi, psi_q = {}, {}, {}, {}, {}
+        spare = work.tile([P, PACK * CHUNK], F32, name="spare", align_bytes=64)
+        for c in range(EARLY):
+            x_first[c] = quantise("x0%d" % c, xb[c, 0][:], CHUNK * PACK)
+        weave_flux(0)
+        weave_flux(1)
+
+        def straddle(k):
+            return lanes[k][:, CHUNK // 2 : 3 * CHUNK // 2]
+
+        ahead = work.tile([P, PACK * CHUNK], F32, name="ahead", tag="root", align_bytes=64)
+        for i in range(PACK):
+            room = spare[:, i * CHUNK : (i + 1) * CHUNK] if i < 3 else straddle(1)
+            pick_outside(1, 0, i, room)
+            pick_outside(1, 1, i, ahead[:, i * CHUNK : (i + 1) * CHUNK] if i < 3 else straddle(2))
+            subtract_inside(quarter(0, i), 1, i, 0, CHUNK, room)
+        xb[0, 1] = work.tile([P, CHUNK * PACK], BF16, name="xb", tag="xb10", align_bytes=64)
+        weave(nc.scalar.copy, xb[0, 1][:], quarter(0, 0, 4).rearrange("p (t j) -> p t j", t=PACK))
+        weave_flux(2)
+        for k in range(1, EARLY + 1):
+            a = 1 if k < EARLY else 0
+            if k == 1:
+                room = [ahead[:, 0:CHUNK], ahead[:, CHUNK : 2 * CHUNK]]
+            elif k == 2:
+                room = later
+            else:
+                for i in range(2):
+                    pick_outside(a, k, i, room[i])
+            for i in range(2):
+                subtract_inside(quarter(k, i), a, i, k * CHUNK, CHUNK, room[i])
+            quantise_second_pass(k - 1)
+            if k >= 2:
+                psi[k - 2] = influence(res[k - 2], inv[k - 2], CHUNK)
+            if k == 1:
+                room = [ahead[:, 2 * CHUNK : 3 * CHUNK], straddle(2)]
+                later = [quarter(0, 0), quarter(0, 1)]
+                for i in range(2):
+                    pick_outside(1, 2, i, later[i])
+            else:
+                room = [quarter(k - 1, 0), quarter(k - 1, 1)]
+                for i in range(2):
+                    pick_outside(a, k, 2 + i, room[i])
+            res[k - 1] = residual((k - 1) * UNITS, CHUNK, "mid%d" % (k % 2))
+            res_sq[k - 1] = square(res[k - 1], CHUNK, "res_sq")
+            if k >= 2:
+                psi_q[k - 2] = quantise("psi%d" % (k % 2), psi[k - 2][:], CHUNK * PACK)
+            for i in range(2):
+                subtract_inside(quarter(k, 2 + i), a, 2 + i, k * CHUNK, CHUNK, room[i])
+            xb[k, a] = work.tile([P, CHUNK * PACK], BF16, name="xb", tag="xb1%d" % (k % 2), align_bytes=64)
+            weave(nc.scalar.copy, xb[k, a][:], quarter(k, 0, 4).rearrange("p (t j) -> p t j", t=PACK))
+            inv[k - 1] = invert(res_sq[k - 1], CHUNK, "root", "mid%d" % (2 + k % 2))
+            if k == 1:
+                weave_flux(3)
+            if k == 2:
+                back_through_wb(psi_q[0], 0, CHUNK, (), "big2")
+
+        j_last = last * CHUNK
+        got = list(room)
+        for i in (1, 0):
+            pick_outside(1, last, i, got[i])
+        codes0, scales0 = quantise("x00", xb[last, 0][:], CHUNK * PACK)
+        got = got + [quarter(last, 0), quarter(last, 1)]
+        for i in (3, 2):
+            pick_outside(1, last, i, got[i])
+        xb_unit = {}
+
+        def unit_gather(u, xf, copy):
+            for i in range(PACK):
+                subtract_inside(xf[:, i, :], 1, i, j_last + u * P, P, got[i][:, u * P : (u + 1) * P])
+            xb_unit[u] = work.tile([P, P * PACK], BF16, name="xb_unit", tag="xb0%d" % (1 + u), align_bytes=64)
+            weave(copy, xb_unit[u][:], xf)
+
+        def unit_quantise(u):
+            codes1, scales1 = quantise("x0%d" % (1 + u), xb_unit[u][:], P * PACK)
+            cols = slice(u * P, (u + 1) * P)
+            stage_one(last * UNITS + u, [(codes0[:, cols], scales0[:, cols]), (codes1[:], scales1[:])])
+
+        unit_gather(0, quarter(last, 2, 2).rearrange("p (t j) -> p t j", t=PACK), nc.scalar.copy)
+        back_through_wb(psi_q[1], CHUNK, CHUNK, (), "big3")
+        psi[2] = influence(res[2], inv[2], CHUNK)
+        unit_quantise(0)
+        psi_q[2] = quantise("psi0", psi[2][:], CHUNK * PACK)
+        xf_b = work.tile([P, PACK, P], F32, name="xf_b", tag="root", align_bytes=64)
+        unit_gather(1, xf_b[:], nc.vector.tensor_copy)
+        res_a = residual(last * UNITS, P, "mid0")
+        unit_quantise(1)
+        inv_a = invert(square(res_a, P, "res_sq"), P, "spare", "mid2")
+        res_b = residual(last * UNITS + 1, P, "xb10")
+        inv_b = invert(square(res_b, P, "xb11"), P, "xb00", "xb01")
+        psi_qa = quantise("psi1", influence(res_a, inv_a, P)[:], P * PACK)
+        psi_qb = quantise("psi2", influence(res_b, inv_b, P)[:], P * PACK)
+        back_through_wb(psi_q[2], 2 * CHUNK, CHUNK, (0, 1, 2, 3), "xf_early")
+        back_through_wb(psi_qa, j_last, P, (0,), "big0")
+        back_through_wb(psi_qb, j_last + P, P, (0,), "big1")

@@ -101,27 +101,33 @@ def tile_list_transit_cauchy_step_kernel(
                 out=w4_sc_raw[32 * q : 32 * q + 4, :].bitcast(I32).rearrange("p (a c) -> p a c", a=PASSES),
                 in_=w4_scales[:, 4 * q : 4 * q + 4, :].rearrange("a r c -> r a c").bitcast(I32),
             )
+        picked_sc = keep.tile([P, S], U8, name="picked_sc")
+        nc.vector.tensor_copy(picked_sc[:], tab_sc[:].indirect(idx[:]))
+
+        def move_scale_rows(a):
+            for q in range(4):
+                row = 16 * a + 4 * q
+                nc.sync.dma_start(
+                    out=v_sc[a][32 * q : 32 * q + 4, :].bitcast(I32), in_=picked_sc[row : row + 4, :].bitcast(I32)
+                )
+
         load_wb(1)
+        move_scale_rows(0)
         load_plane(0, 3)
         load_tab(0)
+        move_scale_rows(1)
         load_tab(1)
+        load_plane(1, 0)
+        load_plane(1, 1)
         load_flux(0)
-        for i in range(PACK):
-            load_plane(1, i)
+        load_plane(1, 2)
+        load_plane(1, 3)
         var_t = keep.tile([P, PACK], F32, name="var_t")
         nc.sync.dma_start(out=var_t[:], in_=var.rearrange("(p t) -> p t", t=PACK))
         step_t = keep.tile([P, PASSES, PACK], F32, name="step_t")
         nc.sync.dma_start(out=step_t[:], in_=step.rearrange("(a p j) -> p a j", a=PASSES, j=PACK))
         load_flux(1)
 
-        picked_sc = keep.tile([P, S], U8, name="picked_sc")
-        nc.vector.tensor_copy(picked_sc[:], tab_sc[:].indirect(idx[:]))
-        for a in range(PASSES):
-            for q in range(4):
-                row = 16 * a + 4 * q
-                nc.gpsimd.dma_start(
-                    out=v_sc[a][32 * q : 32 * q + 4, :].bitcast(I32), in_=picked_sc[row : row + 4, :].bitcast(I32)
-                )
 
         def weave(engine_copy, woven, rows):
             engine_copy(
@@ -132,7 +138,7 @@ def tile_list_transit_cauchy_step_kernel(
         early = [(0, 2 * CHUNK), (2 * CHUNK, CHUNK)]
         xf_early = work.tile([P, PACK, n_early], F32, name="xf_early", align_bytes=64)
         for i in range(PACK):
-            outside = work.tile([P, n_early], F32, name="outside_early", bufs=2)
+            outside = work.tile([P, n_early], F32, name="outside_early", tag="oe%d" % (i % 2), align_bytes=64)
             for j0, n in early:
                 nc.vector.tensor_copy(outside[:, j0 : j0 + n], planes[0, i][:].indirect(entries(idx3, j0, n)))
             for j0, n in early:
@@ -192,17 +198,39 @@ def tile_list_transit_cauchy_step_kernel(
 
         out_rows = out.rearrange("(a p j) s -> a p j s", a=PASSES, j=PACK)
 
-        lanes = [keep.tile([P, 6 * CHUNK], F32, name="lane%d" % k, align_bytes=64) for k in range(5)]
+        pitch = 2 * CHUNK + PACK * CHUNK - CHUNK - P
+        lanes = [keep.tile([P, 10 * CHUNK], F32, name="lane%d" % k, align_bytes=64) for k in range(4)]
+        end_lane = keep.tile([P, 2 * PACK * CHUNK], F32, name="end_lane", align_bytes=64)
 
-        def quarter(k, i, n=1):
-            return lanes[k][:, i * CHUNK : (i + n) * CHUNK]
+        def quarter(k, i):
+            o = (i // 2) * pitch + (i % 2) * CHUNK
+            return lanes[k][:, o : o + CHUNK]
+
+        def flux_woven(c):
+            if c == 3:
+                return end_lane[:, PACK * CHUNK : 2 * PACK * CHUNK]
+            return lanes[c + 1][:, 2 * CHUNK : 6 * CHUNK]
+
+        def root_room(c):
+            if c == 2:
+                return end_lane[:, 0 : PACK * CHUNK]
+            return lanes[c + 2][:, 6 * CHUNK : 10 * CHUNK]
+
+        def weave_lane(k, woven):
+            rows = lanes[k][:, 0 : 2 * pitch].rearrange("p (u x) -> p u x", u=2)[:, :, 0 : 2 * CHUNK]
+            nc.scalar.copy(
+                woven.rearrange("p (c e u v) -> p c u v e", e=RUN, u=2, v=2),
+                rows.rearrange("p u (v c e) -> p c u v e", v=2, e=RUN),
+            )
 
         def by_runs(ap):
             return ap.rearrange("p (c e t) -> p c t e", e=RUN, t=PACK)
 
         def weave_flux(c):
             h, o = divmod(c * CHUNK, S // 2)
-            weave(nc.scalar.copy, quarter(c + 1, 2, 4), flux_sb[h][:, :, o : o + CHUNK])
+            for u in range(UNITS):
+                unit = flux_woven(c)[:, u * P * PACK : (u + 1) * P * PACK]
+                weave(nc.scalar.copy, unit, flux_sb[h][:, :, o + u * P : o + (u + 1) * P])
 
         def pick_outside(a, c, i, dst):
             nc.vector.tensor_copy(dst, planes[a, i][:].indirect(entries(idx3, c * CHUNK, CHUNK)))
@@ -250,7 +278,7 @@ def tile_list_transit_cauchy_step_kernel(
                 c, o = divmod((g0 + u) * P, CHUNK)
                 nc.vector.tensor_tensor(
                     res[:, u * P * PACK : (u + 1) * P * PACK].rearrange("p (j t) -> p j t", t=PACK),
-                    quarter(c + 1, 2, 4)[:, o * PACK : (o + P) * PACK].rearrange("p (j t) -> p j t", t=PACK),
+                    flux_woven(c)[:, o * PACK : (o + P) * PACK].rearrange("p (j t) -> p j t", t=PACK),
                     model[g0 + u][:].rearrange("p t j -> p j t"),
                     ALU.subtract,
                 )
@@ -258,17 +286,31 @@ def tile_list_transit_cauchy_step_kernel(
 
         def square(res, n, tag):
             res_sq = work.tile([P, PACK, n], F32, name="res_sq", tag=tag, align_bytes=64)
-            nc.scalar.activation(res_sq[:].rearrange("p t (c e) -> p c t e", e=RUN), by_runs(res[:]), ACT.Square)
+            for o in range(0, n, P):
+                nc.scalar.activation(
+                    res_sq[:, :, o : o + P].rearrange("p t (c e) -> p c t e", e=RUN),
+                    by_runs(res[:, o * PACK : (o + P) * PACK]),
+                    ACT.Square,
+                )
             return res_sq
 
-        def invert(res_sq, n, root_tag, tag):
-            inv_root = work.tile([P, PACK, n], F32, name="inv_root", tag=root_tag, align_bytes=64)
-            for t in range(PACK):
-                nc.scalar.activation(
-                    inv_root[:, t, :], res_sq[:, t, :], ACT.Abs_reciprocal_sqrt, bias=var_t[:, t : t + 1]
-                )
+        def invert(res_sq, n, root, tag, piece):
+            inv_root = root.rearrange("p (t j) -> p t j", t=PACK)
+            for o in range(0, n, piece):
+                for t in range(PACK):
+                    nc.scalar.activation(
+                        inv_root[:, t, o : o + piece],
+                        res_sq[:, t, o : o + piece],
+                        ACT.Abs_reciprocal_sqrt,
+                        bias=var_t[:, t : t + 1],
+                    )
             inv = work.tile([P, n * PACK], F32, name="inv", tag=tag, align_bytes=64)
-            nc.scalar.activation(by_runs(inv[:]), inv_root[:].rearrange("p t (c e) -> p c t e", e=RUN), ACT.Square)
+            for o in range(0, n, piece):
+                nc.scalar.activation(
+                    by_runs(inv[:, o * PACK : (o + piece) * PACK]),
+                    inv_root[:, :, o : o + piece].rearrange("p t (c e) -> p c t e", e=RUN),
+                    ACT.Square,
+                )
             return inv
 
         def influence(res, inv, n):
@@ -279,8 +321,9 @@ def tile_list_transit_cauchy_step_kernel(
         def back_through_wb(psi_q, j0, n, on_vector, tag):
             psi_codes, psi_sc = psi_q
             per_bank = BANK // n
-            staged = work.tile([P, PASSES * PACK, n], F32, name="staged", tag=tag, align_bytes=64)
             for b in range(PASSES * PACK // per_bank):
+                if b * per_bank % PACK == 0:
+                    staged = work.tile([P, PACK, n], F32, name="staged", tag=tag[b * per_bank // PACK], align_bytes=64)
                 back = psum.tile([P, per_bank, n], F32, name="back", tag="o_bank", bufs=4)
                 for e in range(per_bank):
                     m = b * per_bank + e
@@ -297,12 +340,12 @@ def tile_list_transit_cauchy_step_kernel(
                     m = b * per_bank + e
                     factor = step_t[:, m // PACK, m % PACK : m % PACK + 1]
                     if b in on_vector:
-                        nc.vector.tensor_scalar(staged[:, m, :], back[:, e, :], factor, None, ALU.mult)
+                        nc.vector.tensor_scalar(staged[:, m % PACK, :], back[:, e, :], factor, None, ALU.mult)
                     else:
-                        nc.scalar.activation(staged[:, m, :], back[:, e, :], ACT.Copy, scale=factor)
+                        nc.scalar.activation(staged[:, m % PACK, :], back[:, e, :], ACT.Copy, scale=factor)
                 if (b + 1) * per_bank % PACK == 0:
                     a = b * per_bank // PACK
-                    nc.sync.dma_start(out=out_rows[a, :, :, j0 : j0 + n], in_=staged[:, a * PACK : (a + 1) * PACK, :])
+                    nc.sync.dma_start(out=out_rows[a, :, :, j0 : j0 + n], in_=staged[:])
 
         x_first = {}
 
@@ -314,7 +357,7 @@ def tile_list_transit_cauchy_step_kernel(
 
         last = EARLY
         res, res_sq, inv, psi, psi_q = {}, {}, {}, {}, {}
-        spare = work.tile([P, PACK * CHUNK], F32, name="spare", align_bytes=64)
+        spare = work.tile([P, 3 * CHUNK], F32, name="spare", tag="oe0", align_bytes=64)
         for c in range(EARLY):
             x_first[c] = quantise("x0%d" % c, xb[c, 0][:], CHUNK * PACK)
         weave_flux(0)
@@ -323,14 +366,14 @@ def tile_list_transit_cauchy_step_kernel(
         def straddle(k):
             return lanes[k][:, CHUNK // 2 : 3 * CHUNK // 2]
 
-        ahead = work.tile([P, PACK * CHUNK], F32, name="ahead", tag="root", align_bytes=64)
+        ahead = work.tile([P, 3 * CHUNK], F32, name="ahead", tag="oe1", align_bytes=64)
         for i in range(PACK):
             room = spare[:, i * CHUNK : (i + 1) * CHUNK] if i < 3 else straddle(1)
             pick_outside(1, 0, i, room)
             pick_outside(1, 1, i, ahead[:, i * CHUNK : (i + 1) * CHUNK] if i < 3 else straddle(2))
             subtract_inside(quarter(0, i), 1, i, 0, CHUNK, room)
         xb[0, 1] = work.tile([P, CHUNK * PACK], BF16, name="xb", tag="xb10", align_bytes=64)
-        weave(nc.scalar.copy, xb[0, 1][:], quarter(0, 0, 4).rearrange("p (t j) -> p t j", t=PACK))
+        weave_lane(0, xb[0, 1][:])
         weave_flux(2)
         for k in range(1, EARLY + 1):
             a = 1 if k < EARLY else 0
@@ -344,8 +387,6 @@ def tile_list_transit_cauchy_step_kernel(
             for i in range(2):
                 subtract_inside(quarter(k, i), a, i, k * CHUNK, CHUNK, room[i])
             quantise_second_pass(k - 1)
-            if k >= 2:
-                psi[k - 2] = influence(res[k - 2], inv[k - 2], CHUNK)
             if k == 1:
                 room = [ahead[:, 2 * CHUNK : 3 * CHUNK], straddle(2)]
                 later = [quarter(0, 0), quarter(0, 1)]
@@ -357,17 +398,19 @@ def tile_list_transit_cauchy_step_kernel(
                     pick_outside(a, k, 2 + i, room[i])
             res[k - 1] = residual((k - 1) * UNITS, CHUNK, "mid%d" % (k % 2))
             res_sq[k - 1] = square(res[k - 1], CHUNK, "res_sq")
+            subtract_inside(quarter(k, 2), a, 2, k * CHUNK, CHUNK, room[0])
+            if k >= 2:
+                psi[k - 2] = influence(res[k - 2], inv[k - 2], CHUNK)
+            subtract_inside(quarter(k, 3), a, 3, k * CHUNK, CHUNK, room[1])
             if k >= 2:
                 psi_q[k - 2] = quantise("psi%d" % (k % 2), psi[k - 2][:], CHUNK * PACK)
-            for i in range(2):
-                subtract_inside(quarter(k, 2 + i), a, 2 + i, k * CHUNK, CHUNK, room[i])
             xb[k, a] = work.tile([P, CHUNK * PACK], BF16, name="xb", tag="xb1%d" % (k % 2), align_bytes=64)
-            weave(nc.scalar.copy, xb[k, a][:], quarter(k, 0, 4).rearrange("p (t j) -> p t j", t=PACK))
-            inv[k - 1] = invert(res_sq[k - 1], CHUNK, "root", "mid%d" % (2 + k % 2))
+            weave_lane(k, xb[k, a][:])
+            inv[k - 1] = invert(res_sq[k - 1], CHUNK, root_room(k - 1), "mid%d" % (2 + k % 2), P)
             if k == 1:
                 weave_flux(3)
             if k == 2:
-                back_through_wb(psi_q[0], 0, CHUNK, (), "big2")
+                back_through_wb(psi_q[0], 0, CHUNK, (), ["xf_early", "oe1"])
 
         j_last = last * CHUNK
         got = list(room)
@@ -379,9 +422,11 @@ def tile_list_transit_cauchy_step_kernel(
             pick_outside(1, last, i, got[i])
         xb_unit = {}
 
-        def unit_gather(u, xf, copy):
-            for i in range(PACK):
+        def unit_subtract(u, xf, which):
+            for i in which:
                 subtract_inside(xf[:, i, :], 1, i, j_last + u * P, P, got[i][:, u * P : (u + 1) * P])
+
+        def unit_weave(u, xf, copy):
             xb_unit[u] = work.tile([P, P * PACK], BF16, name="xb_unit", tag="xb0%d" % (1 + u), align_bytes=64)
             weave(copy, xb_unit[u][:], xf)
 
@@ -390,20 +435,23 @@ def tile_list_transit_cauchy_step_kernel(
             cols = slice(u * P, (u + 1) * P)
             stage_one(last * UNITS + u, [(codes0[:, cols], scales0[:, cols]), (codes1[:], scales1[:])])
 
-        unit_gather(0, quarter(last, 2, 2).rearrange("p (t j) -> p t j", t=PACK), nc.scalar.copy)
-        back_through_wb(psi_q[1], CHUNK, CHUNK, (), "big3")
+        xf_a = lanes[last][:, pitch : pitch + 2 * CHUNK].rearrange("p (t j) -> p t j", t=PACK)
+        xf_b = end_lane[:, 2 * CHUNK : 4 * CHUNK].rearrange("p (t j) -> p t j", t=PACK)
+        unit_subtract(0, xf_a, range(PACK))
+        unit_weave(0, xf_a, nc.scalar.copy)
+        back_through_wb(psi_q[1], CHUNK, CHUNK, (), ["big2", "big3"])
         psi[2] = influence(res[2], inv[2], CHUNK)
         unit_quantise(0)
         psi_q[2] = quantise("psi0", psi[2][:], CHUNK * PACK)
-        xf_b = work.tile([P, PACK, P], F32, name="xf_b", tag="root", align_bytes=64)
-        unit_gather(1, xf_b[:], nc.vector.tensor_copy)
+        unit_subtract(1, xf_b, range(PACK))
+        unit_weave(1, xf_b, nc.vector.tensor_copy)
         res_a = residual(last * UNITS, P, "mid0")
         unit_quantise(1)
-        inv_a = invert(square(res_a, P, "res_sq"), P, "spare", "mid2")
+        inv_a = invert(square(res_a, P, "res_sq"), P, lanes[0][:, 0 : PACK * P], "mid2", P)
         res_b = residual(last * UNITS + 1, P, "xb10")
-        inv_b = invert(square(res_b, P, "xb11"), P, "xb00", "xb01")
+        inv_b = invert(square(res_b, P, "xb11"), P, lanes[0][:, PACK * P : 2 * PACK * P], "xb01", P)
         psi_qa = quantise("psi1", influence(res_a, inv_a, P)[:], P * PACK)
         psi_qb = quantise("psi2", influence(res_b, inv_b, P)[:], P * PACK)
-        back_through_wb(psi_q[2], 2 * CHUNK, CHUNK, (0, 1, 2, 3), "xf_early")
-        back_through_wb(psi_qa, j_last, P, (0,), "big0")
-        back_through_wb(psi_qb, j_last + P, P, (0,), "big1")
+        back_through_wb(psi_q[2], 2 * CHUNK, CHUNK, (0, 1, 2, 3), ["xf_early", "oe1"])
+        back_through_wb(psi_qa, j_last, P, (), ["big0", "big1"])
+        back_through_wb(psi_qb, j_last + P, P, (0,), ["big2", "big3"])

@@ -117,16 +117,16 @@ def tile_list_transit_cauchy_step_kernel(
         load_tab(0)
         move_scale_rows(1)
         load_tab(1)
+        load_flux(0)
         load_plane(1, 0)
         load_plane(1, 1)
-        load_flux(0)
         load_plane(1, 2)
+        load_flux(1)
         load_plane(1, 3)
         var_t = keep.tile([P, PACK], F32, name="var_t")
         nc.sync.dma_start(out=var_t[:], in_=var.rearrange("(p t) -> p t", t=PACK))
         step_t = keep.tile([P, PASSES, PACK], F32, name="step_t")
         nc.sync.dma_start(out=step_t[:], in_=step.rearrange("(a p j) -> p a j", a=PASSES, j=PACK))
-        load_flux(1)
 
 
         def weave(engine_copy, woven, rows):
@@ -179,12 +179,12 @@ def tile_list_transit_cauchy_step_kernel(
         w4_w = keep.tile([P, PASSES * 2 * H], U8, name="w4_w", align_bytes=64)
         w4_sc = keep.tile([P, PASSES * H], U8, name="w4_sc", align_bytes=64)
         nc.vector.tensor_copy(
-            w4_w[:].bitcast(U16).rearrange("p (a t m) -> p a m t", a=PASSES, t=PACK),
-            w4_raw[:].rearrange("p a c -> p (a c)").bitcast(U16).rearrange("p (a m t) -> p a m t", a=PASSES, t=PACK),
+            w4_w[:].bitcast(U16).rearrange("p (a t m) -> p a t m", a=PASSES, t=PACK),
+            w4_raw[:].rearrange("p a c -> p (a c)").bitcast(U16).rearrange("p (a m t) -> p a t m", a=PASSES, t=PACK),
         )
         nc.vector.tensor_copy(
-            w4_sc[:].rearrange("p (a t m) -> p a m t", a=PASSES, t=PACK),
-            w4_sc_raw[:].rearrange("p (a m t) -> p a m t", a=PASSES, t=PACK),
+            w4_sc[:].rearrange("p (a t m) -> p a t m", a=PASSES, t=PACK),
+            w4_sc_raw[:].rearrange("p (a m t) -> p a t m", a=PASSES, t=PACK),
         )
 
         v_words = [keep.tile([P, S], U32, name="v_words%d" % a, align_bytes=64) for a in range(PASSES)]
@@ -362,6 +362,8 @@ def tile_list_transit_cauchy_step_kernel(
             x_first[c] = quantise("x0%d" % c, xb[c, 0][:], CHUNK * PACK)
         weave_flux(0)
         weave_flux(1)
+        weave_flux(2)
+        weave_flux(3)
 
         def straddle(k):
             return lanes[k][:, CHUNK // 2 : 3 * CHUNK // 2]
@@ -374,7 +376,6 @@ def tile_list_transit_cauchy_step_kernel(
             subtract_inside(quarter(0, i), 1, i, 0, CHUNK, room)
         xb[0, 1] = work.tile([P, CHUNK * PACK], BF16, name="xb", tag="xb10", align_bytes=64)
         weave_lane(0, xb[0, 1][:])
-        weave_flux(2)
         for k in range(1, EARLY + 1):
             a = 1 if k < EARLY else 0
             if k == 1:
@@ -406,9 +407,7 @@ def tile_list_transit_cauchy_step_kernel(
                 psi_q[k - 2] = quantise("psi%d" % (k % 2), psi[k - 2][:], CHUNK * PACK)
             xb[k, a] = work.tile([P, CHUNK * PACK], BF16, name="xb", tag="xb1%d" % (k % 2), align_bytes=64)
             weave_lane(k, xb[k, a][:])
-            inv[k - 1] = invert(res_sq[k - 1], CHUNK, root_room(k - 1), "mid%d" % (2 + k % 2), P)
-            if k == 1:
-                weave_flux(3)
+            inv[k - 1] = invert(res_sq[k - 1], CHUNK, root_room(k - 1), "mid%d" % (2 + k % 2), CHUNK)
             if k == 2:
                 back_through_wb(psi_q[0], 0, CHUNK, (), ["xf_early", "oe1"])
 

@@ -25,6 +25,7 @@ PER_COL = 16
 RUN = 4
 BANK = 512
 EARLY = 3
+TURNED = (0, 1, 2)
 UNITS = CHUNK // P
 
 
@@ -151,8 +152,8 @@ def tile_list_transit_cauchy_step_kernel(
 
         wb_codes = keep.tile([P, PASSES * H], U32, name="wb_codes", align_bytes=64)
         wb_sc = keep.tile([P, PASSES * H], U8, name="wb_sc", align_bytes=64)
-        wt_codes = keep.tile([P, K], U32, name="wt_codes", align_bytes=64)
         wt_sc = keep.tile([P, K], U8, name="wt_sc", align_bytes=64)
+        wt_both = work.tile([P, PASSES * H * PACK], BF16, name="wt_both", tag="mid2", align_bytes=64)
         for a in range(PASSES):
             wb_b = work.tile([P, H * PACK], BF16, name="wb_b", tag="mid%d" % a, align_bytes=64)
             nc.scalar.copy(
@@ -163,7 +164,7 @@ def tile_list_transit_cauchy_step_kernel(
                 out=wb_codes[:, a * H : (a + 1) * H].bitcast(FP8X4), scales=wb_sc[:, a * H : (a + 1) * H], in_=wb_b[:]
             )
             pairs = wb_b[:].bitcast(F32)
-            wt_b = work.tile([P, H * PACK], BF16, name="wt_b", tag="mid%d" % (2 + a), align_bytes=64)
+            wt_b = wt_both[:, a * H * PACK : (a + 1) * H * PACK]
             for u in range(2):
                 bank = psum.tile([P, PACK, P], F32, name="wt_bank", tag="o_bank", bufs=4)
                 for t in range(PACK):
@@ -172,9 +173,6 @@ def tile_list_transit_cauchy_step_kernel(
                     wt_b[:, u * 2 * H : (u + 1) * 2 * H].rearrange("p (e k t) -> p e k t", e=2, t=PACK),
                     bank[:].rearrange("p t k -> p (t k)").bitcast(BF16).rearrange("p (t k e) -> p e k t", t=PACK, e=2),
                 )
-            nc.vector.quantize_mx(
-                out=wt_codes[:, a * H : (a + 1) * H].bitcast(FP8X4), scales=wt_sc[:, a * H : (a + 1) * H], in_=wt_b[:]
-            )
 
         w4_w = keep.tile([P, PASSES * 2 * H], U8, name="w4_w", align_bytes=64)
         w4_sc = keep.tile([P, PASSES * H], U8, name="w4_sc", align_bytes=64)
@@ -187,9 +185,19 @@ def tile_list_transit_cauchy_step_kernel(
             w4_sc_raw[:].rearrange("p (a m t) -> p a t m", a=PASSES, t=PACK),
         )
 
-        v_words = [keep.tile([P, S], U32, name="v_words%d" % a, align_bytes=64) for a in range(PASSES)]
+        half = S // 2
+        v_words = {}
+
+        def gather_words(a, h, tag):
+            v_words[a, h] = work.tile([P, half], U32, name="v_words", tag=tag, align_bytes=64)
+            nc.vector.tensor_copy(v_words[a, h][:], tab_w[a][:].bitcast(U32).indirect(entries(idx, h * half, half)))
+
+        def words_of(a, g):
+            h, o = divmod(g * P, half)
+            return v_words[a, h][:, o : o + P].bitcast(FP8X4)
+
         for a in range(PASSES):
-            nc.vector.tensor_copy(v_words[a][:], tab_w[a][:].bitcast(U32).indirect(idx[:]))
+            gather_words(a, 0, "words%d" % a)
 
         xb = {}
         for c in range(EARLY):
@@ -199,16 +207,21 @@ def tile_list_transit_cauchy_step_kernel(
         out_rows = out.rearrange("(a p j) s -> a p j s", a=PASSES, j=PACK)
 
         pitch = 2 * CHUNK + PACK * CHUNK - CHUNK - P
-        lanes = [keep.tile([P, 10 * CHUNK], F32, name="lane%d" % k, align_bytes=64) for k in range(4)]
+        lanes = [keep.tile([P, 10 * CHUNK], F32, name="lane%d" % k, align_bytes=64) for k in range(1, 4)]
+        lanes.insert(0, keep.tile([P, 2 * PACK * P], F32, name="lane0", align_bytes=64))
+        starts = [2 * CHUNK, 0, 0, 0]
+        homes = [lanes[1], lanes[1], lanes[2], lanes[3]]
         end_lane = keep.tile([P, 2 * PACK * CHUNK], F32, name="end_lane", align_bytes=64)
 
         def quarter(k, i):
-            o = (i // 2) * pitch + (i % 2) * CHUNK
-            return lanes[k][:, o : o + CHUNK]
+            o = (starts[k] if i < 2 else pitch) + (i % 2) * CHUNK
+            return homes[k][:, o : o + CHUNK]
 
         def flux_woven(c):
             if c == 3:
                 return end_lane[:, PACK * CHUNK : 2 * PACK * CHUNK]
+            if c == 0:
+                return lanes[0][:, :]
             return lanes[c + 1][:, 2 * CHUNK : 6 * CHUNK]
 
         def root_room(c):
@@ -217,7 +230,8 @@ def tile_list_transit_cauchy_step_kernel(
             return lanes[c + 2][:, 6 * CHUNK : 10 * CHUNK]
 
         def weave_lane(k, woven):
-            rows = lanes[k][:, 0 : 2 * pitch].rearrange("p (u x) -> p u x", u=2)[:, :, 0 : 2 * CHUNK]
+            step_u = pitch - starts[k]
+            rows = homes[k][:, starts[k] : starts[k] + 2 * step_u].rearrange("p (u x) -> p u x", u=2)[:, :, 0 : 2 * CHUNK]
             nc.scalar.copy(
                 woven.rearrange("p (c e u v) -> p c u v e", e=RUN, u=2, v=2),
                 rows.rearrange("p u (v c e) -> p c u v e", v=2, e=RUN),
@@ -231,6 +245,14 @@ def tile_list_transit_cauchy_step_kernel(
             for u in range(UNITS):
                 unit = flux_woven(c)[:, u * P * PACK : (u + 1) * P * PACK]
                 weave(nc.scalar.copy, unit, flux_sb[h][:, :, o + u * P : o + (u + 1) * P])
+
+        def turn_flux(c):
+            h, o = divmod(c * CHUNK, S // 2)
+            for u in range(UNITS):
+                bank = psum.tile([P, PACK, P], F32, name="flux_bank", tag="o_bank", bufs=4)
+                for t in range(PACK):
+                    nc.tensor.transpose(bank[:, t, :], flux_sb[h][:, t, o + u * P : o + (u + 1) * P], ident[:])
+                nc.scalar.copy(flux_woven(c)[:, u * H : (u + 1) * H], bank[:].rearrange("p t m -> p (t m)"))
 
         def pick_outside(a, c, i, dst):
             nc.vector.tensor_copy(dst, planes[a, i][:].indirect(entries(idx3, c * CHUNK, CHUNK)))
@@ -248,14 +270,14 @@ def tile_list_transit_cauchy_step_kernel(
 
         def stage_one(g, x_ops):
             cols = slice(g * P, (g + 1) * P)
-            model[g] = psum.tile([P, PACK, P], F32, name="model", bufs=4)
+            model[g] = psum.tile([P, PACK, P], F32, name="model", tag="m_bank", bufs=4)
             for t in range(PACK):
                 for a in range(PASSES):
                     nc.tensor.matmul_mx(
                         out=model[g][:, t, :],
                         lhsT=w4_w[:, 2 * (a * H + t * P) : 2 * (a * H + (t + 1) * P)].bitcast(FP4X4),
                         lhsT_scale=w4_sc[:, a * H + t * P : a * H + (t + 1) * P],
-                        rhs=v_words[a][:, cols].bitcast(FP8X4),
+                        rhs=words_of(a, g),
                         rhs_scale=v_sc[a][:, cols],
                         start=(t == 0 and a == 0),
                         stop=False,
@@ -271,6 +293,64 @@ def tile_list_transit_cauchy_step_kernel(
                         start=False,
                         stop=(a == PASSES - 1 and t == PACK - 1),
                     )
+
+        res_bank = {}
+
+        def stage_one_turned(g, x_ops):
+            cols = slice(g * P, (g + 1) * P)
+            turned = psum.tile([P, H], F32, name="turned", tag="m_bank", bufs=4)
+            for a in range(PASSES):
+                nc.tensor.matmul_mx(
+                    out=turned[:],
+                    lhsT=words_of(a, g),
+                    lhsT_scale=v_sc[a][:, cols],
+                    rhs=w4_w[:, 2 * a * H : 2 * (a + 1) * H].bitcast(FP4X4),
+                    rhs_scale=w4_sc[:, a * H : (a + 1) * H],
+                    start=(a == 0),
+                    stop=False,
+                )
+            for a in range(PASSES):
+                nc.tensor.matmul_mx(
+                    out=turned[:],
+                    lhsT=x_ops[a][0].bitcast(FP8X4),
+                    lhsT_scale=x_ops[a][1],
+                    rhs=wb_codes[:, a * H : (a + 1) * H].bitcast(FP8X4),
+                    rhs_scale=wb_sc[:, a * H : (a + 1) * H],
+                    start=False,
+                    stop=(a == PASSES - 1),
+                )
+            negated = work.tile([P, H], F32, name="negated", tag="xb0%d" % (g % 2), align_bytes=64)
+            nc.scalar.activation(negated[:], turned[:], ACT.Copy, scale=-1.0)
+            c, u = divmod(g, UNITS)
+            res_bank[g] = psum.tile([P, PACK, P], F32, name="res_bank", tag="o_bank", bufs=4)
+            for n, src in enumerate((flux_woven(c)[:, u * H : (u + 1) * H], negated[:])):
+                for t in range(PACK):
+                    nc.tensor.matmul(
+                        res_bank[g][:, t, :],
+                        lhsT=src[:, t * P : (t + 1) * P],
+                        rhs=ident[:],
+                        is_transpose=True,
+                        start=(n == 0 and t == 0),
+                        stop=(n == 1 and t == PACK - 1),
+                    )
+
+        def square_turned(c):
+            res_sq = work.tile([P, PACK, CHUNK], F32, name="res_sq", tag="res_sq", align_bytes=64)
+            for u in range(UNITS):
+                nc.scalar.activation(res_sq[:, :, u * P : (u + 1) * P], res_bank[c * UNITS + u][:], ACT.Square)
+            return res_sq
+
+        def influence_turned(c, inv):
+            psi_b = work.tile([P, CHUNK * PACK], BF16, name="psi_b", align_bytes=64, bufs=2)
+            for u in range(UNITS):
+                cols = slice(u * H, (u + 1) * H)
+                nc.vector.tensor_tensor(
+                    psi_b[:, cols].rearrange("p (j t) -> p j t", t=PACK),
+                    res_bank[c * UNITS + u][:].rearrange("p t j -> p j t"),
+                    inv[:, cols].rearrange("p (j t) -> p j t", t=PACK),
+                    ALU.mult,
+                )
+            return psi_b
 
         def residual(g0, n, tag):
             res = work.tile([P, n * PACK], F32, name="res", tag=tag, align_bytes=64)
@@ -353,17 +433,19 @@ def tile_list_transit_cauchy_step_kernel(
             second = quantise("x1%d" % (c % 2), xb[c, 1][:], CHUNK * PACK)
             for u in range(UNITS):
                 cols = slice(u * P, (u + 1) * P)
-                stage_one(c * UNITS + u, [(codes[:, cols], scales[:, cols]) for codes, scales in (x_first[c], second)])
+                (stage_one_turned if c in TURNED else stage_one)(c * UNITS + u, [(codes[:, cols], scales[:, cols]) for codes, scales in (x_first[c], second)])
 
         last = EARLY
         res, res_sq, inv, psi, psi_q = {}, {}, {}, {}, {}
         spare = work.tile([P, 3 * CHUNK], F32, name="spare", tag="oe0", align_bytes=64)
         for c in range(EARLY):
             x_first[c] = quantise("x0%d" % c, xb[c, 0][:], CHUNK * PACK)
-        weave_flux(0)
-        weave_flux(1)
-        weave_flux(2)
+        for c in range(EARLY):
+            (turn_flux if c in TURNED else weave_flux)(c)
         weave_flux(3)
+
+        def chunk_influence(c):
+            return influence_turned(c, inv[c]) if c in TURNED else influence(res[c], inv[c], CHUNK)
 
         def straddle(k):
             return lanes[k][:, CHUNK // 2 : 3 * CHUNK // 2]
@@ -383,11 +465,14 @@ def tile_list_transit_cauchy_step_kernel(
             elif k == 2:
                 room = later
             else:
+                room = room_next
                 for i in range(2):
                     pick_outside(a, k, i, room[i])
             for i in range(2):
                 subtract_inside(quarter(k, i), a, i, k * CHUNK, CHUNK, room[i])
             quantise_second_pass(k - 1)
+            if k == 1:
+                gather_words(0, 1, "xb10")
             if k == 1:
                 room = [ahead[:, 2 * CHUNK : 3 * CHUNK], straddle(2)]
                 later = [quarter(0, 0), quarter(0, 1)]
@@ -397,19 +482,27 @@ def tile_list_transit_cauchy_step_kernel(
                 room = [quarter(k - 1, 0), quarter(k - 1, 1)]
                 for i in range(2):
                     pick_outside(a, k, 2 + i, room[i])
-            res[k - 1] = residual((k - 1) * UNITS, CHUNK, "mid%d" % (k % 2))
-            res_sq[k - 1] = square(res[k - 1], CHUNK, "res_sq")
+                room_next = [straddle(k - 1), homes[k - 1][:, 3 * CHUNK // 2 : 5 * CHUNK // 2]]
+            if k - 1 in TURNED:
+                res_sq[k - 1] = square_turned(k - 1)
+            else:
+                res[k - 1] = residual((k - 1) * UNITS, CHUNK, "mid%d" % (k % 2))
+                res_sq[k - 1] = square(res[k - 1], CHUNK, "res_sq")
             subtract_inside(quarter(k, 2), a, 2, k * CHUNK, CHUNK, room[0])
             if k >= 2:
-                psi[k - 2] = influence(res[k - 2], inv[k - 2], CHUNK)
+                psi[k - 2] = chunk_influence(k - 2)
             subtract_inside(quarter(k, 3), a, 3, k * CHUNK, CHUNK, room[1])
+            if k == 1:
+                wt_codes = work.tile([P, K], U32, name="wt_codes", tag="oe1", align_bytes=64)
+                nc.vector.quantize_mx(out=wt_codes[:].bitcast(FP8X4), scales=wt_sc[:], in_=wt_both[:])
+                gather_words(1, 1, "oe0")
             if k >= 2:
                 psi_q[k - 2] = quantise("psi%d" % (k % 2), psi[k - 2][:], CHUNK * PACK)
-            xb[k, a] = work.tile([P, CHUNK * PACK], BF16, name="xb", tag="xb1%d" % (k % 2), align_bytes=64)
+            xb[k, a] = work.tile([P, CHUNK * PACK], BF16, name="xb", tag="xb01" if k < last else "xb11", align_bytes=64)
             weave_lane(k, xb[k, a][:])
-            inv[k - 1] = invert(res_sq[k - 1], CHUNK, root_room(k - 1), "mid%d" % (2 + k % 2), CHUNK)
+            inv[k - 1] = invert(res_sq[k - 1], CHUNK, root_room(k - 1), "mid%d" % (2 + k % 2), P)
             if k == 2:
-                back_through_wb(psi_q[0], 0, CHUNK, (), ["xf_early", "oe1"])
+                back_through_wb(psi_q[0], 0, CHUNK, (), ["xf_early", "big0"])
 
         j_last = last * CHUNK
         got = list(room)
@@ -439,7 +532,7 @@ def tile_list_transit_cauchy_step_kernel(
         unit_subtract(0, xf_a, range(PACK))
         unit_weave(0, xf_a, nc.scalar.copy)
         back_through_wb(psi_q[1], CHUNK, CHUNK, (), ["big2", "big3"])
-        psi[2] = influence(res[2], inv[2], CHUNK)
+        psi[2] = chunk_influence(2)
         unit_quantise(0)
         psi_q[2] = quantise("psi0", psi[2][:], CHUNK * PACK)
         unit_subtract(1, xf_b, range(PACK))
@@ -447,10 +540,10 @@ def tile_list_transit_cauchy_step_kernel(
         res_a = residual(last * UNITS, P, "mid0")
         unit_quantise(1)
         inv_a = invert(square(res_a, P, "res_sq"), P, lanes[0][:, 0 : PACK * P], "mid2", P)
-        res_b = residual(last * UNITS + 1, P, "xb10")
+        res_b = residual(last * UNITS + 1, P, "xb12")
         inv_b = invert(square(res_b, P, "xb11"), P, lanes[0][:, PACK * P : 2 * PACK * P], "xb01", P)
         psi_qa = quantise("psi1", influence(res_a, inv_a, P)[:], P * PACK)
         psi_qb = quantise("psi2", influence(res_b, inv_b, P)[:], P * PACK)
-        back_through_wb(psi_q[2], 2 * CHUNK, CHUNK, (0, 1, 2, 3), ["xf_early", "oe1"])
-        back_through_wb(psi_qa, j_last, P, (), ["big0", "big1"])
+        back_through_wb(psi_q[2], 2 * CHUNK, CHUNK, (0, 1, 2, 3), ["xf_early", "big0"])
+        back_through_wb(psi_qa, j_last, P, (), ["big1", "xb13"])
         back_through_wb(psi_qb, j_last + P, P, (0,), ["big2", "big3"])

@@ -82,6 +82,9 @@ def tile_list_transit_cauchy_step_kernel(
         nc.gpsimd.memset(w4_sc_raw[:].bitcast(I32), 0)
         for a in range(PASSES):
             nc.gpsimd.memset(v_sc[a][:].bitcast(I32), 0)
+        warm = keep.tile([P, 2], F32, name="warm")
+        nc.vector.memset(warm[:, 0:1], 1.0)
+        nc.scalar.activation(warm[:, 1:2], warm[:, 0:1], ACT.Abs_reciprocal_sqrt)
         ident = keep.tile([P, P], F32, name="ident")
         make_identity(nc, ident[:])
 
@@ -352,24 +355,25 @@ def tile_list_transit_cauchy_step_kernel(
                 )
             return psi_b
 
-        def residual(g0, n, tag):
-            res = work.tile([P, n * PACK], F32, name="res", tag=tag, align_bytes=64)
-            for u in range(n // P):
-                c, o = divmod((g0 + u) * P, CHUNK)
+        def residual(g, tag, piece):
+            res = work.tile([P, P * PACK], F32, name="res", tag=tag, align_bytes=64)
+            c, u = divmod(g, UNITS)
+            for o in range(0, P, piece):
+                cols = slice(o * PACK, (o + piece) * PACK)
                 nc.vector.tensor_tensor(
-                    res[:, u * P * PACK : (u + 1) * P * PACK].rearrange("p (j t) -> p j t", t=PACK),
-                    flux_woven(c)[:, o * PACK : (o + P) * PACK].rearrange("p (j t) -> p j t", t=PACK),
-                    model[g0 + u][:].rearrange("p t j -> p j t"),
+                    res[:, cols].rearrange("p (j t) -> p j t", t=PACK),
+                    flux_woven(c)[:, u * H : (u + 1) * H][:, cols].rearrange("p (j t) -> p j t", t=PACK),
+                    model[g][:, :, o : o + piece].rearrange("p t j -> p j t"),
                     ALU.subtract,
                 )
             return res
 
-        def square(res, n, tag):
+        def square(res, n, tag, piece=P):
             res_sq = work.tile([P, PACK, n], F32, name="res_sq", tag=tag, align_bytes=64)
-            for o in range(0, n, P):
+            for o in range(0, n, piece):
                 nc.scalar.activation(
-                    res_sq[:, :, o : o + P].rearrange("p t (c e) -> p c t e", e=RUN),
-                    by_runs(res[:, o * PACK : (o + P) * PACK]),
+                    res_sq[:, :, o : o + piece].rearrange("p t (c e) -> p c t e", e=RUN),
+                    by_runs(res[:, o * PACK : (o + piece) * PACK]),
                     ACT.Square,
                 )
             return res_sq
@@ -393,14 +397,15 @@ def tile_list_transit_cauchy_step_kernel(
                 )
             return inv
 
-        def influence(res, inv, n):
+        def influence(res, inv, n, piece):
             psi_b = work.tile([P, n * PACK], BF16, name="psi_b", align_bytes=64, bufs=2)
-            nc.vector.tensor_tensor(psi_b[:], res[:], inv[:], ALU.mult)
+            for o in range(0, n * PACK, piece * PACK):
+                cols = slice(o, o + piece * PACK)
+                nc.vector.tensor_tensor(psi_b[:, cols], res[:, cols], inv[:, cols], ALU.mult)
             return psi_b
 
-        def back_through_wb(psi_q, j0, n, on_vector, tag):
+        def back_through_wb(psi_q, j0, n, on_vector, tag, per_bank=2):
             psi_codes, psi_sc = psi_q
-            per_bank = BANK // n
             for b in range(PASSES * PACK // per_bank):
                 if b * per_bank % PACK == 0:
                     staged = work.tile([P, PACK, n], F32, name="staged", tag=tag[b * per_bank // PACK], align_bytes=64)
@@ -537,13 +542,13 @@ def tile_list_transit_cauchy_step_kernel(
         psi_q[2] = quantise("psi0", psi[2][:], CHUNK * PACK)
         unit_subtract(1, xf_b, range(PACK))
         unit_weave(1, xf_b, nc.vector.tensor_copy)
-        res_a = residual(last * UNITS, P, "mid0")
+        res_a = residual(last * UNITS, "mid0", P)
         unit_quantise(1)
-        inv_a = invert(square(res_a, P, "res_sq"), P, lanes[0][:, 0 : PACK * P], "mid2", P)
-        res_b = residual(last * UNITS + 1, P, "xb12")
-        inv_b = invert(square(res_b, P, "xb11"), P, lanes[0][:, PACK * P : 2 * PACK * P], "xb01", P)
-        psi_qa = quantise("psi1", influence(res_a, inv_a, P)[:], P * PACK)
-        psi_qb = quantise("psi2", influence(res_b, inv_b, P)[:], P * PACK)
+        inv_a = invert(square(res_a, P, "res_sq", P // 2), P, lanes[0][:, 0 : PACK * P], "mid2", P // 2)
+        res_b = residual(last * UNITS + 1, "xb12", P // 2)
+        inv_b = invert(square(res_b, P, "xb11", P // 2), P, lanes[0][:, PACK * P : 2 * PACK * P], "xb01", P // 2)
+        psi_qa = quantise("psi1", influence(res_a, inv_a, P, P)[:], P * PACK)
+        psi_qb = quantise("psi2", influence(res_b, inv_b, P, P // 2)[:], P * PACK)
         back_through_wb(psi_q[2], 2 * CHUNK, CHUNK, (0, 1, 2, 3), ["xf_early", "big0"])
-        back_through_wb(psi_qa, j_last, P, (), ["big1", "xb13"])
-        back_through_wb(psi_qb, j_last + P, P, (0,), ["big2", "big3"])
+        back_through_wb(psi_qa, j_last, P, (), ["big1", "xb13"], 4)
+        back_through_wb(psi_qb, j_last + P, P, (0, 2), ["big2", "big3"], 2)

@@ -21,12 +21,13 @@ P = 128
 PACK = 4
 PASSES = K // (P * PACK)
 CHUNK = 256
+UNITS = CHUNK // P
+HALF = S // 2
 PER_COL = 16
 RUN = 4
-BANK = 512
-EARLY = 3
-TURNED = (0, 1, 2)
-UNITS = CHUNK // P
+LAST = S // CHUNK - 1
+BANKS = 4
+TAIL_PIECE = P // 2
 
 
 def tile_list_transit_cauchy_step_kernel(
@@ -42,30 +43,25 @@ def tile_list_transit_cauchy_step_kernel(
             return lst[:, j0 // PER_COL : (j0 + n) // PER_COL]
 
         x_rows = xT.rearrange("(a p i) t -> a i p t", a=PASSES, i=PACK)
-        planes = {}
+        planes, wb_raw, flux_sb, tab_w = {}, {}, {}, {}
 
         def load_plane(a, i):
             planes[a, i] = keep.tile([P, T], F32, name="plane%d%d" % (a, i), align_bytes=64)
             nc.sync.dma_start(out=planes[a, i][:], in_=x_rows[a, i])
 
-        wb_raw = {}
-
         def load_wb(a):
             wb_raw[a] = work.tile([P, PACK * H], F32, name="wb_raw", tag="big%d" % a, align_bytes=64)
             nc.sync.dma_start(
-                out=wb_raw[a][:], in_=wb[a * P * PACK : (a + 1) * P * PACK, :].rearrange("(p j) r -> p (j r)", j=PACK)
+                out=wb_raw[a][:], in_=wb[a * P * PACK : (a + 1) * P * PACK, :].rearrange("(p i) r -> p (i r)", i=PACK)
             )
 
-        flux_sb = {}
-
-        def load_flux(h):
-            flux_sb[h] = work.tile([P, PACK, S // 2], F32, name="flux_sb", tag="big%d" % h, align_bytes=64)
+        def load_flux(c, chunks, tag):
+            rows = work.tile([P, PACK, chunks * CHUNK], F32, name="flux_sb", tag=tag, align_bytes=64)
             nc.sync.dma_start(
-                out=flux_sb[h][:],
-                in_=flux[:, h * S // 2 : (h + 1) * S // 2].rearrange("(p t) j -> p t j", t=PACK),
+                out=rows[:], in_=flux[:, c * CHUNK : (c + chunks) * CHUNK].rearrange("(m t) j -> m t j", t=PACK)
             )
-
-        tab_w = {}
+            for d in range(chunks):
+                flux_sb[c + d] = rows[:, :, d * CHUNK : (d + 1) * CHUNK]
 
         def load_tab(a):
             tab_w[a] = work.tile([P, T], I32, name="tab_w", tag="big%d" % (2 + a), align_bytes=64)
@@ -103,7 +99,7 @@ def tile_list_transit_cauchy_step_kernel(
         for q in range(4):
             nc.sync.dma_start(
                 out=w4_sc_raw[32 * q : 32 * q + 4, :].bitcast(I32).rearrange("p (a c) -> p a c", a=PASSES),
-                in_=w4_scales[:, 4 * q : 4 * q + 4, :].rearrange("a r c -> r a c").bitcast(I32),
+                in_=w4_scales[:, 4 * q : 4 * q + 4, :].rearrange("a s c -> s a c").bitcast(I32),
             )
         picked_sc = keep.tile([P, S], U8, name="picked_sc")
         nc.vector.tensor_copy(picked_sc[:], tab_sc[:].indirect(idx[:]))
@@ -121,31 +117,32 @@ def tile_list_transit_cauchy_step_kernel(
         load_tab(0)
         move_scale_rows(1)
         load_tab(1)
-        load_flux(0)
+        load_flux(0, 2, "big0")
         load_plane(1, 0)
         load_plane(1, 1)
         load_plane(1, 2)
-        load_flux(1)
+        load_flux(2, 1, "big1")
         load_plane(1, 3)
+        load_flux(LAST, 1, "flux3")
         var_t = keep.tile([P, PACK], F32, name="var_t")
-        nc.sync.dma_start(out=var_t[:], in_=var.rearrange("(p t) -> p t", t=PACK))
+        nc.sync.dma_start(out=var_t[:], in_=var.rearrange("(m t) -> m t", t=PACK))
         step_t = keep.tile([P, PASSES, PACK], F32, name="step_t")
-        nc.sync.dma_start(out=step_t[:], in_=step.rearrange("(a p j) -> p a j", a=PASSES, j=PACK))
+        nc.sync.dma_start(out=step_t[:], in_=step.rearrange("(a p i) -> p a i", a=PASSES, i=PACK))
 
+        def by_runs(woven):
+            return woven.rearrange("p (c e t) -> p c t e", e=RUN, t=PACK)
 
         def weave(engine_copy, woven, rows):
-            engine_copy(
-                woven.rearrange("p (c e t) -> p c t e", e=RUN, t=PACK), rows.rearrange("p t (c e) -> p c t e", e=RUN)
-            )
+            engine_copy(by_runs(woven), rows.rearrange("p t (c e) -> p c t e", e=RUN))
 
-        n_early = EARLY * CHUNK
-        early = [(0, 2 * CHUNK), (2 * CHUNK, CHUNK)]
+        n_early = LAST * CHUNK
+        pieces = [(0, 2 * CHUNK), (2 * CHUNK, CHUNK)]
         xf_early = work.tile([P, PACK, n_early], F32, name="xf_early", align_bytes=64)
         for i in range(PACK):
             outside = work.tile([P, n_early], F32, name="outside_early", tag="oe%d" % (i % 2), align_bytes=64)
-            for j0, n in early:
+            for j0, n in pieces:
                 nc.vector.tensor_copy(outside[:, j0 : j0 + n], planes[0, i][:].indirect(entries(idx3, j0, n)))
-            for j0, n in early:
+            for j0, n in pieces:
                 nc.vector.tensor_tensor(
                     xf_early[:, i, j0 : j0 + n],
                     planes[0, i][:].indirect(entries(idx2, j0, n)),
@@ -153,28 +150,30 @@ def tile_list_transit_cauchy_step_kernel(
                     ALU.subtract,
                 )
 
-        wb_codes = keep.tile([P, PASSES * H], U32, name="wb_codes", align_bytes=64)
+        wb_codes = [
+            work.tile([P, H], U32, name="wb_codes", tag=tag, align_bytes=64) for tag in ("wb_codes0", "oe1")
+        ]
         wb_sc = keep.tile([P, PASSES * H], U8, name="wb_sc", align_bytes=64)
         wt_sc = keep.tile([P, K], U8, name="wt_sc", align_bytes=64)
         wt_both = work.tile([P, PASSES * H * PACK], BF16, name="wt_both", tag="mid2", align_bytes=64)
         for a in range(PASSES):
             wb_b = work.tile([P, H * PACK], BF16, name="wb_b", tag="mid%d" % a, align_bytes=64)
             nc.scalar.copy(
-                wb_b[:].rearrange("p (t m j) -> p m t j", t=PACK, j=PACK),
-                wb_raw[a][:].rearrange("p (j m t) -> p m t j", j=PACK, t=PACK),
+                wb_b[:].rearrange("p (t m i) -> p m t i", t=PACK, i=PACK),
+                wb_raw[a][:].rearrange("p (i m t) -> p m t i", i=PACK, t=PACK),
             )
             nc.vector.quantize_mx(
-                out=wb_codes[:, a * H : (a + 1) * H].bitcast(FP8X4), scales=wb_sc[:, a * H : (a + 1) * H], in_=wb_b[:]
+                out=wb_codes[a][:].bitcast(FP8X4), scales=wb_sc[:, a * H : (a + 1) * H], in_=wb_b[:]
             )
             pairs = wb_b[:].bitcast(F32)
             wt_b = wt_both[:, a * H * PACK : (a + 1) * H * PACK]
             for u in range(2):
-                bank = psum.tile([P, PACK, P], F32, name="wt_bank", tag="o_bank", bufs=4)
+                bank = psum.tile([P, PACK, P], F32, name="wt_bank", tag="o_bank", bufs=BANKS)
                 for t in range(PACK):
                     nc.tensor.transpose(bank[:, t, :], pairs[:, 2 * P * t + u : 2 * P * (t + 1) : 2], ident[:])
                 nc.scalar.copy(
-                    wt_b[:, u * 2 * H : (u + 1) * 2 * H].rearrange("p (e k t) -> p e k t", e=2, t=PACK),
-                    bank[:].rearrange("p t k -> p (t k)").bitcast(BF16).rearrange("p (t k e) -> p e k t", t=PACK, e=2),
+                    wt_b[:, u * 2 * H : (u + 1) * 2 * H].rearrange("m (e p t) -> m e p t", e=2, t=PACK),
+                    bank[:].rearrange("m t p -> m (t p)").bitcast(BF16).rearrange("m (t p e) -> m e p t", t=PACK, e=2),
                 )
 
         w4_w = keep.tile([P, PASSES * 2 * H], U8, name="w4_w", align_bytes=64)
@@ -188,80 +187,81 @@ def tile_list_transit_cauchy_step_kernel(
             w4_sc_raw[:].rearrange("p (a m t) -> p a t m", a=PASSES, t=PACK),
         )
 
-        half = S // 2
         v_words = {}
 
         def gather_words(a, h, tag):
-            v_words[a, h] = work.tile([P, half], U32, name="v_words", tag=tag, align_bytes=64)
-            nc.vector.tensor_copy(v_words[a, h][:], tab_w[a][:].bitcast(U32).indirect(entries(idx, h * half, half)))
+            v_words[a, h] = work.tile([P, HALF], U32, name="v_words", tag=tag, align_bytes=64)
+            nc.vector.tensor_copy(v_words[a, h][:], tab_w[a][:].bitcast(U32).indirect(entries(idx, h * HALF, HALF)))
 
         def words_of(a, g):
-            h, o = divmod(g * P, half)
+            h, o = divmod(g * P, HALF)
             return v_words[a, h][:, o : o + P].bitcast(FP8X4)
 
         for a in range(PASSES):
             gather_words(a, 0, "words%d" % a)
 
         xb = {}
-        for c in range(EARLY):
+        for c in range(LAST):
             xb[c, 0] = work.tile([P, CHUNK * PACK], BF16, name="xb", tag="xb0%d" % c, align_bytes=64)
             weave(nc.scalar.copy, xb[c, 0][:], xf_early[:, :, c * CHUNK : (c + 1) * CHUNK])
 
-        out_rows = out.rearrange("(a p j) s -> a p j s", a=PASSES, j=PACK)
-
-        pitch = 2 * CHUNK + PACK * CHUNK - CHUNK - P
-        lanes = [keep.tile([P, 10 * CHUNK], F32, name="lane%d" % k, align_bytes=64) for k in range(1, 4)]
-        lanes.insert(0, keep.tile([P, 2 * PACK * P], F32, name="lane0", align_bytes=64))
-        starts = [2 * CHUNK, 0, 0, 0]
-        homes = [lanes[1], lanes[1], lanes[2], lanes[3]]
+        second_pair = 9 * CHUNK // 2
+        lanes = [keep.tile([P, 10 * CHUNK], F32, name="lane%d" % s, align_bytes=64) for s in range(1, LAST + 1)]
+        lanes.insert(0, keep.tile([P, PACK * CHUNK], F32, name="lane0", align_bytes=64))
         end_lane = keep.tile([P, 2 * PACK * CHUNK], F32, name="end_lane", align_bytes=64)
+        row_lane = [lanes[1], lanes[1], lanes[2], lanes[3]]
+        first_pair = [2 * CHUNK, 0, 0, 0]
 
-        def quarter(k, i):
-            o = (starts[k] if i < 2 else pitch) + (i % 2) * CHUNK
-            return homes[k][:, o : o + CHUNK]
+        def row(s, i):
+            o = (first_pair[s] if i < 2 else second_pair) + (i % 2) * CHUNK
+            return row_lane[s][:, o : o + CHUNK]
 
-        def flux_woven(c):
-            if c == 3:
-                return end_lane[:, PACK * CHUNK : 2 * PACK * CHUNK]
+        def across_rows(s):
+            return lanes[s][:, CHUNK // 2 : 3 * CHUNK // 2]
+
+        def flux_room(c):
             if c == 0:
                 return lanes[0][:, :]
+            if c == LAST:
+                return end_lane[:, PACK * CHUNK : 2 * PACK * CHUNK]
             return lanes[c + 1][:, 2 * CHUNK : 6 * CHUNK]
 
         def root_room(c):
-            if c == 2:
+            if c == LAST - 1:
                 return end_lane[:, 0 : PACK * CHUNK]
             return lanes[c + 2][:, 6 * CHUNK : 10 * CHUNK]
 
-        def weave_lane(k, woven):
-            step_u = pitch - starts[k]
-            rows = homes[k][:, starts[k] : starts[k] + 2 * step_u].rearrange("p (u x) -> p u x", u=2)[:, :, 0 : 2 * CHUNK]
-            nc.scalar.copy(
-                woven.rearrange("p (c e u v) -> p c u v e", e=RUN, u=2, v=2),
-                rows.rearrange("p u (v c e) -> p c u v e", v=2, e=RUN),
+        def weave_rows(engine_copy, s, a, tag):
+            xb[s, a] = work.tile([P, CHUNK * PACK], BF16, name="xb", tag=tag, align_bytes=64)
+            pitch = second_pair - first_pair[s]
+            both = row_lane[s][:, first_pair[s] : first_pair[s] + 2 * pitch].rearrange("p (u x) -> p u x", u=2)
+            engine_copy(
+                xb[s, a][:].rearrange("p (c e u v) -> p c u v e", e=RUN, u=2, v=2),
+                both[:, :, 0 : 2 * CHUNK].rearrange("p u (v c e) -> p c u v e", v=2, e=RUN),
             )
 
-        def by_runs(ap):
-            return ap.rearrange("p (c e t) -> p c t e", e=RUN, t=PACK)
+        def flux_unit(g):
+            c, u = divmod(g, UNITS)
+            return flux_sb[c][:, :, u * P : (u + 1) * P]
 
-        def weave_flux(c):
-            h, o = divmod(c * CHUNK, S // 2)
-            for u in range(UNITS):
-                unit = flux_woven(c)[:, u * P * PACK : (u + 1) * P * PACK]
-                weave(nc.scalar.copy, unit, flux_sb[h][:, :, o + u * P : o + (u + 1) * P])
+        def flux_laid(g):
+            c, u = divmod(g, UNITS)
+            return flux_room(c)[:, u * H : (u + 1) * H]
 
-        def turn_flux(c):
-            h, o = divmod(c * CHUNK, S // 2)
-            for u in range(UNITS):
-                bank = psum.tile([P, PACK, P], F32, name="flux_bank", tag="o_bank", bufs=4)
-                for t in range(PACK):
-                    nc.tensor.transpose(bank[:, t, :], flux_sb[h][:, t, o + u * P : o + (u + 1) * P], ident[:])
-                nc.scalar.copy(flux_woven(c)[:, u * H : (u + 1) * H], bank[:].rearrange("p t m -> p (t m)"))
+        def turn_flux(g):
+            bank = psum.tile([P, PACK, P], F32, name="flux_bank", tag="o_bank", bufs=BANKS)
+            for t in range(PACK):
+                nc.tensor.transpose(bank[:, t, :], flux_unit(g)[:, t, :], ident[:])
+            nc.scalar.copy(flux_laid(g), bank[:].rearrange("j t m -> j (t m)"))
 
-        def pick_outside(a, c, i, dst):
-            nc.vector.tensor_copy(dst, planes[a, i][:].indirect(entries(idx3, c * CHUNK, CHUNK)))
+        def pick_outside(a, c, i, room):
+            nc.vector.tensor_copy(room, planes[a, i][:].indirect(entries(idx3, c * CHUNK, CHUNK)))
 
         def subtract_inside(dst, a, i, j0, n, outside):
             nc.vector.tensor_tensor(dst, planes[a, i][:].indirect(entries(idx2, j0, n)), outside, ALU.subtract)
+
+        def subtract_row(s, a, i, outside):
+            subtract_inside(row(s, i), a, i, s * CHUNK, CHUNK, outside)
 
         def quantise(name, src, width):
             codes = work.tile([P, width // PACK], U32, name=name + "_codes", align_bytes=64)
@@ -269,39 +269,11 @@ def tile_list_transit_cauchy_step_kernel(
             nc.vector.quantize_mx(out=codes[:].bitcast(FP8X4), scales=scales[:], in_=src)
             return codes, scales
 
-        model = {}
+        x_first, res_bank = {}, {}
 
-        def stage_one(g, x_ops):
+        def turned_residual(g, x_ops):
             cols = slice(g * P, (g + 1) * P)
-            model[g] = psum.tile([P, PACK, P], F32, name="model", tag="m_bank", bufs=4)
-            for t in range(PACK):
-                for a in range(PASSES):
-                    nc.tensor.matmul_mx(
-                        out=model[g][:, t, :],
-                        lhsT=w4_w[:, 2 * (a * H + t * P) : 2 * (a * H + (t + 1) * P)].bitcast(FP4X4),
-                        lhsT_scale=w4_sc[:, a * H + t * P : a * H + (t + 1) * P],
-                        rhs=words_of(a, g),
-                        rhs_scale=v_sc[a][:, cols],
-                        start=(t == 0 and a == 0),
-                        stop=False,
-                    )
-            for a in range(PASSES):
-                for t in range(PACK):
-                    nc.tensor.matmul_mx(
-                        out=model[g][:, t, :],
-                        lhsT=wb_codes[:, a * H + t * P : a * H + (t + 1) * P].bitcast(FP8X4),
-                        lhsT_scale=wb_sc[:, a * H + t * P : a * H + (t + 1) * P],
-                        rhs=x_ops[a][0].bitcast(FP8X4),
-                        rhs_scale=x_ops[a][1],
-                        start=False,
-                        stop=(a == PASSES - 1 and t == PACK - 1),
-                    )
-
-        res_bank = {}
-
-        def stage_one_turned(g, x_ops):
-            cols = slice(g * P, (g + 1) * P)
-            turned = psum.tile([P, H], F32, name="turned", tag="m_bank", bufs=4)
+            turned = psum.tile([P, H], F32, name="turned", tag="m_bank", bufs=BANKS)
             for a in range(PASSES):
                 nc.tensor.matmul_mx(
                     out=turned[:],
@@ -317,25 +289,30 @@ def tile_list_transit_cauchy_step_kernel(
                     out=turned[:],
                     lhsT=x_ops[a][0].bitcast(FP8X4),
                     lhsT_scale=x_ops[a][1],
-                    rhs=wb_codes[:, a * H : (a + 1) * H].bitcast(FP8X4),
+                    rhs=wb_codes[a][:].bitcast(FP8X4),
                     rhs_scale=wb_sc[:, a * H : (a + 1) * H],
                     start=False,
                     stop=(a == PASSES - 1),
                 )
-            negated = work.tile([P, H], F32, name="negated", tag="xb0%d" % (g % 2), align_bytes=64)
+            negated = work.tile([P, H], F32, name="negated", tag="xb0%d" % (g % UNITS), align_bytes=64)
             nc.scalar.activation(negated[:], turned[:], ACT.Copy, scale=-1.0)
-            c, u = divmod(g, UNITS)
-            res_bank[g] = psum.tile([P, PACK, P], F32, name="res_bank", tag="o_bank", bufs=4)
-            for n, src in enumerate((flux_woven(c)[:, u * H : (u + 1) * H], negated[:])):
+            res_bank[g] = psum.tile([P, PACK, P], F32, name="res_bank", tag="o_bank", bufs=BANKS)
+            for term, src in enumerate((flux_laid(g), negated[:])):
                 for t in range(PACK):
                     nc.tensor.matmul(
                         res_bank[g][:, t, :],
                         lhsT=src[:, t * P : (t + 1) * P],
                         rhs=ident[:],
                         is_transpose=True,
-                        start=(n == 0 and t == 0),
-                        stop=(n == 1 and t == PACK - 1),
+                        start=(term == 0 and t == 0),
+                        stop=(term == 1 and t == PACK - 1),
                     )
+
+        def finish_model(c):
+            x_second = quantise("x1%d" % (c % 2), xb[c, 1][:], CHUNK * PACK)
+            for u in range(UNITS):
+                cols = slice(u * P, (u + 1) * P)
+                turned_residual(c * UNITS + u, [(cd[:, cols], sc[:, cols]) for cd, sc in (x_first[c], x_second)])
 
         def square_turned(c):
             res_sq = work.tile([P, PACK, CHUNK], F32, name="res_sq", tag="res_sq", align_bytes=64)
@@ -343,43 +320,77 @@ def tile_list_transit_cauchy_step_kernel(
                 nc.scalar.activation(res_sq[:, :, u * P : (u + 1) * P], res_bank[c * UNITS + u][:], ACT.Square)
             return res_sq
 
-        def influence_turned(c, inv):
+        def psi_turned(c, inv):
             psi_b = work.tile([P, CHUNK * PACK], BF16, name="psi_b", align_bytes=64, bufs=2)
             for u in range(UNITS):
                 cols = slice(u * H, (u + 1) * H)
                 nc.vector.tensor_tensor(
-                    psi_b[:, cols].rearrange("p (j t) -> p j t", t=PACK),
-                    res_bank[c * UNITS + u][:].rearrange("p t j -> p j t"),
-                    inv[:, cols].rearrange("p (j t) -> p j t", t=PACK),
+                    psi_b[:, cols].rearrange("m (j t) -> m j t", t=PACK),
+                    res_bank[c * UNITS + u][:].rearrange("m t j -> m j t"),
+                    inv[:, cols].rearrange("m (j t) -> m j t", t=PACK),
                     ALU.mult,
                 )
             return psi_b
 
-        def residual(g, tag, piece):
-            res = work.tile([P, P * PACK], F32, name="res", tag=tag, align_bytes=64)
-            c, u = divmod(g, UNITS)
+        model = {}
+
+        def direct_model(g, x_ops):
+            cols = slice(g * P, (g + 1) * P)
+            model[g] = psum.tile([P, PACK, P], F32, name="model", tag="m_bank", bufs=BANKS)
+            for t in range(PACK):
+                for a in range(PASSES):
+                    nc.tensor.matmul_mx(
+                        out=model[g][:, t, :],
+                        lhsT=w4_w[:, 2 * (a * H + t * P) : 2 * (a * H + (t + 1) * P)].bitcast(FP4X4),
+                        lhsT_scale=w4_sc[:, a * H + t * P : a * H + (t + 1) * P],
+                        rhs=words_of(a, g),
+                        rhs_scale=v_sc[a][:, cols],
+                        start=(t == 0 and a == 0),
+                        stop=False,
+                    )
+            for a in range(PASSES):
+                for t in range(PACK):
+                    nc.tensor.matmul_mx(
+                        out=model[g][:, t, :],
+                        lhsT=wb_codes[a][:, t * P : (t + 1) * P].bitcast(FP8X4),
+                        lhsT_scale=wb_sc[:, a * H + t * P : a * H + (t + 1) * P],
+                        rhs=x_ops[a][0].bitcast(FP8X4),
+                        rhs_scale=x_ops[a][1],
+                        start=False,
+                        stop=(a == PASSES - 1 and t == PACK - 1),
+                    )
+
+        def direct_residual(g, tag, piece):
+            res = work.tile([P, H], F32, name="res", tag=tag, align_bytes=64)
             for o in range(0, P, piece):
                 cols = slice(o * PACK, (o + piece) * PACK)
                 nc.vector.tensor_tensor(
-                    res[:, cols].rearrange("p (j t) -> p j t", t=PACK),
-                    flux_woven(c)[:, u * H : (u + 1) * H][:, cols].rearrange("p (j t) -> p j t", t=PACK),
-                    model[g][:, :, o : o + piece].rearrange("p t j -> p j t"),
+                    res[:, cols].rearrange("m (j t) -> m j t", t=PACK),
+                    flux_laid(g)[:, cols].rearrange("m (j t) -> m j t", t=PACK),
+                    model[g][:, :, o : o + piece].rearrange("m t j -> m j t"),
                     ALU.subtract,
                 )
             return res
 
-        def square(res, n, tag, piece=P):
-            res_sq = work.tile([P, PACK, n], F32, name="res_sq", tag=tag, align_bytes=64)
-            for o in range(0, n, piece):
+        def square_direct(res, tag):
+            res_sq = work.tile([P, PACK, P], F32, name="res_sq", tag=tag, align_bytes=64)
+            for o in range(0, P, TAIL_PIECE):
                 nc.scalar.activation(
-                    res_sq[:, :, o : o + piece].rearrange("p t (c e) -> p c t e", e=RUN),
-                    by_runs(res[:, o * PACK : (o + piece) * PACK]),
+                    res_sq[:, :, o : o + TAIL_PIECE].rearrange("m t (c e) -> m c t e", e=RUN),
+                    by_runs(res[:, o * PACK : (o + TAIL_PIECE) * PACK]),
                     ACT.Square,
                 )
             return res_sq
 
-        def invert(res_sq, n, root, tag, piece):
-            inv_root = root.rearrange("p (t j) -> p t j", t=PACK)
+        def psi_direct(res, inv, piece):
+            psi_b = work.tile([P, H], BF16, name="psi_b", align_bytes=64, bufs=2)
+            for o in range(0, H, piece * PACK):
+                cols = slice(o, o + piece * PACK)
+                nc.vector.tensor_tensor(psi_b[:, cols], res[:, cols], inv[:, cols], ALU.mult)
+            return psi_b
+
+        def invert(res_sq, n, room, tag, piece):
+            inv_root = room.rearrange("m (t j) -> m t j", t=PACK)
             for o in range(0, n, piece):
                 for t in range(PACK):
                     nc.scalar.activation(
@@ -392,163 +403,140 @@ def tile_list_transit_cauchy_step_kernel(
             for o in range(0, n, piece):
                 nc.scalar.activation(
                     by_runs(inv[:, o * PACK : (o + piece) * PACK]),
-                    inv_root[:, :, o : o + piece].rearrange("p t (c e) -> p c t e", e=RUN),
+                    inv_root[:, :, o : o + piece].rearrange("m t (c e) -> m c t e", e=RUN),
                     ACT.Square,
                 )
             return inv
 
-        def influence(res, inv, n, piece):
-            psi_b = work.tile([P, n * PACK], BF16, name="psi_b", align_bytes=64, bufs=2)
-            for o in range(0, n * PACK, piece * PACK):
-                cols = slice(o, o + piece * PACK)
-                nc.vector.tensor_tensor(psi_b[:, cols], res[:, cols], inv[:, cols], ALU.mult)
-            return psi_b
+        out_rows = out.rearrange("(a p i) j -> a p i j", a=PASSES, i=PACK)
 
-        def back_through_wb(psi_q, j0, n, on_vector, tag, per_bank=2):
+        def second_product(psi_q, j0, n, tags, per_bank, on_vector):
             psi_codes, psi_sc = psi_q
-            for b in range(PASSES * PACK // per_bank):
-                if b * per_bank % PACK == 0:
-                    staged = work.tile([P, PACK, n], F32, name="staged", tag=tag[b * per_bank // PACK], align_bytes=64)
-                back = psum.tile([P, per_bank, n], F32, name="back", tag="o_bank", bufs=4)
+            for first in range(0, PASSES * PACK, per_bank):
+                a = first // PACK
+                if first % PACK == 0:
+                    staged = work.tile([P, PACK, n], F32, name="staged", tag=tags[a], align_bytes=64)
+                back = psum.tile([P, per_bank, n], F32, name="back", tag="o_bank", bufs=BANKS)
                 for e in range(per_bank):
-                    m = b * per_bank + e
+                    b = first + e
                     nc.tensor.matmul_mx(
                         out=back[:, e, :],
-                        lhsT=wt_codes[:, m * P : (m + 1) * P].bitcast(FP8X4),
-                        lhsT_scale=wt_sc[:, m * P : (m + 1) * P],
+                        lhsT=wt_codes[:, b * P : (b + 1) * P].bitcast(FP8X4),
+                        lhsT_scale=wt_sc[:, b * P : (b + 1) * P],
                         rhs=psi_codes[:].bitcast(FP8X4),
                         rhs_scale=psi_sc[:],
                         start=True,
                         stop=True,
                     )
                 for e in range(per_bank):
-                    m = b * per_bank + e
-                    factor = step_t[:, m // PACK, m % PACK : m % PACK + 1]
-                    if b in on_vector:
-                        nc.vector.tensor_scalar(staged[:, m % PACK, :], back[:, e, :], factor, None, ALU.mult)
+                    i = (first + e) % PACK
+                    factor = step_t[:, a, i : i + 1]
+                    if first // per_bank in on_vector:
+                        nc.vector.tensor_scalar(staged[:, i, :], back[:, e, :], factor, None, ALU.mult)
                     else:
-                        nc.scalar.activation(staged[:, m % PACK, :], back[:, e, :], ACT.Copy, scale=factor)
-                if (b + 1) * per_bank % PACK == 0:
-                    a = b * per_bank // PACK
+                        nc.scalar.activation(staged[:, i, :], back[:, e, :], ACT.Copy, scale=factor)
+                if (first + per_bank) % PACK == 0:
                     nc.sync.dma_start(out=out_rows[a, :, :, j0 : j0 + n], in_=staged[:])
 
-        x_first = {}
-
-        def quantise_second_pass(c):
-            second = quantise("x1%d" % (c % 2), xb[c, 1][:], CHUNK * PACK)
-            for u in range(UNITS):
-                cols = slice(u * P, (u + 1) * P)
-                (stage_one_turned if c in TURNED else stage_one)(c * UNITS + u, [(codes[:, cols], scales[:, cols]) for codes, scales in (x_first[c], second)])
-
-        last = EARLY
-        res, res_sq, inv, psi, psi_q = {}, {}, {}, {}, {}
         spare = work.tile([P, 3 * CHUNK], F32, name="spare", tag="oe0", align_bytes=64)
-        for c in range(EARLY):
+        for c in range(LAST):
             x_first[c] = quantise("x0%d" % c, xb[c, 0][:], CHUNK * PACK)
-        for c in range(EARLY):
-            (turn_flux if c in TURNED else weave_flux)(c)
-        weave_flux(3)
+        for g in range(LAST * UNITS):
+            turn_flux(g)
 
-        def chunk_influence(c):
-            return influence_turned(c, inv[c]) if c in TURNED else influence(res[c], inv[c], CHUNK)
-
-        def straddle(k):
-            return lanes[k][:, CHUNK // 2 : 3 * CHUNK // 2]
-
-        ahead = work.tile([P, 3 * CHUNK], F32, name="ahead", tag="oe1", align_bytes=64)
+        ahead = work.tile([P, 3 * CHUNK], F32, name="ahead", tag="ahead", align_bytes=64)
+        outside_0 = [spare[:, i * CHUNK : (i + 1) * CHUNK] for i in range(3)] + [across_rows(1)]
+        outside_1 = [ahead[:, i * CHUNK : (i + 1) * CHUNK] for i in range(3)] + [across_rows(2)]
         for i in range(PACK):
-            room = spare[:, i * CHUNK : (i + 1) * CHUNK] if i < 3 else straddle(1)
-            pick_outside(1, 0, i, room)
-            pick_outside(1, 1, i, ahead[:, i * CHUNK : (i + 1) * CHUNK] if i < 3 else straddle(2))
-            subtract_inside(quarter(0, i), 1, i, 0, CHUNK, room)
-        xb[0, 1] = work.tile([P, CHUNK * PACK], BF16, name="xb", tag="xb10", align_bytes=64)
-        weave_lane(0, xb[0, 1][:])
-        for k in range(1, EARLY + 1):
-            a = 1 if k < EARLY else 0
-            if k == 1:
-                room = [ahead[:, 0:CHUNK], ahead[:, CHUNK : 2 * CHUNK]]
-            elif k == 2:
-                room = later
-            else:
-                room = room_next
-                for i in range(2):
-                    pick_outside(a, k, i, room[i])
-            for i in range(2):
-                subtract_inside(quarter(k, i), a, i, k * CHUNK, CHUNK, room[i])
-            quantise_second_pass(k - 1)
-            if k == 1:
-                gather_words(0, 1, "xb10")
-            if k == 1:
-                room = [ahead[:, 2 * CHUNK : 3 * CHUNK], straddle(2)]
-                later = [quarter(0, 0), quarter(0, 1)]
-                for i in range(2):
-                    pick_outside(1, 2, i, later[i])
-            else:
-                room = [quarter(k - 1, 0), quarter(k - 1, 1)]
-                for i in range(2):
-                    pick_outside(a, k, 2 + i, room[i])
-                room_next = [straddle(k - 1), homes[k - 1][:, 3 * CHUNK // 2 : 5 * CHUNK // 2]]
-            if k - 1 in TURNED:
-                res_sq[k - 1] = square_turned(k - 1)
-            else:
-                res[k - 1] = residual((k - 1) * UNITS, CHUNK, "mid%d" % (k % 2))
-                res_sq[k - 1] = square(res[k - 1], CHUNK, "res_sq")
-            subtract_inside(quarter(k, 2), a, 2, k * CHUNK, CHUNK, room[0])
-            if k >= 2:
-                psi[k - 2] = chunk_influence(k - 2)
-            subtract_inside(quarter(k, 3), a, 3, k * CHUNK, CHUNK, room[1])
-            if k == 1:
-                wt_codes = work.tile([P, K], U32, name="wt_codes", tag="oe1", align_bytes=64)
-                nc.vector.quantize_mx(out=wt_codes[:].bitcast(FP8X4), scales=wt_sc[:], in_=wt_both[:])
-                gather_words(1, 1, "oe0")
-            if k >= 2:
-                psi_q[k - 2] = quantise("psi%d" % (k % 2), psi[k - 2][:], CHUNK * PACK)
-            xb[k, a] = work.tile([P, CHUNK * PACK], BF16, name="xb", tag="xb01" if k < last else "xb11", align_bytes=64)
-            weave_lane(k, xb[k, a][:])
-            inv[k - 1] = invert(res_sq[k - 1], CHUNK, root_room(k - 1), "mid%d" % (2 + k % 2), P)
-            if k == 2:
-                back_through_wb(psi_q[0], 0, CHUNK, (), ["xf_early", "big0"])
+            pick_outside(1, 0, i, outside_0[i])
+            pick_outside(1, 1, i, outside_1[i])
+            subtract_row(0, 1, i, outside_0[i])
+        weave_rows(nc.scalar.copy, 0, 1, "xb10")
+        for g in range(LAST * UNITS, (LAST + 1) * UNITS):
+            weave(nc.scalar.copy, flux_laid(g), flux_unit(g))
 
-        j_last = last * CHUNK
-        got = list(room)
+        for i in range(2):
+            subtract_row(1, 1, i, outside_1[i])
+        finish_model(0)
+        gather_words(0, 1, "xb10")
+        outside_2 = [row(0, 0), row(0, 1), row(1, 0), row(1, 1)]
+        for i in range(2):
+            pick_outside(1, 2, i, outside_2[i])
+        res_sq = square_turned(0)
+        for i in range(2, PACK):
+            subtract_row(1, 1, i, outside_1[i])
+        wt_codes = work.tile([P, K], U32, name="wt_codes", tag="ahead", align_bytes=64)
+        nc.vector.quantize_mx(out=wt_codes[:].bitcast(FP8X4), scales=wt_sc[:], in_=wt_both[:])
+        gather_words(1, 1, "oe0")
+        weave_rows(nc.scalar.copy, 1, 1, "xb01")
+        inv_0 = invert(res_sq, CHUNK, root_room(0), "mid3", P)
+
+        for i in range(2):
+            subtract_row(2, 1, i, outside_2[i])
+        finish_model(1)
+        for i in range(2, PACK):
+            pick_outside(1, 2, i, outside_2[i])
+        res_sq = square_turned(1)
+        subtract_row(2, 1, 2, outside_2[2])
+        psi_0 = psi_turned(0, inv_0)
+        subtract_row(2, 1, 3, outside_2[3])
+        psi_q0 = quantise("psi0", psi_0[:], CHUNK * PACK)
+        weave_rows(nc.scalar.copy, 2, 1, "xb01")
+        inv_1 = invert(res_sq, CHUNK, root_room(1), "mid2", P)
+        second_product(psi_q0, 0, CHUNK, ["xf_early", "big0"], 2, ())
+
+        outside_3 = [across_rows(1), lanes[1][:, 3 * CHUNK // 2 : 5 * CHUNK // 2], row(2, 0), row(2, 1)]
+        for i in range(2):
+            pick_outside(0, LAST, i, outside_3[i])
+        for i in range(2):
+            subtract_row(LAST, 0, i, outside_3[i])
+        finish_model(2)
+        for i in range(2, PACK):
+            pick_outside(0, LAST, i, outside_3[i])
+        res_sq = square_turned(2)
+        subtract_row(LAST, 0, 2, outside_3[2])
+        psi_1 = psi_turned(1, inv_1)
+        subtract_row(LAST, 0, 3, outside_3[3])
+        psi_q1 = quantise("psi1", psi_1[:], CHUNK * PACK)
+        weave_rows(nc.vector.tensor_copy, LAST, 0, "xb11")
+        inv_2 = invert(res_sq, CHUNK, root_room(2), "mid3", P)
+
+        outside_4 = [row(2, 0), row(2, 1), row(LAST, 0), row(LAST, 1)]
         for i in (1, 0):
-            pick_outside(1, last, i, got[i])
-        codes0, scales0 = quantise("x00", xb[last, 0][:], CHUNK * PACK)
-        got = got + [quarter(last, 0), quarter(last, 1)]
+            pick_outside(1, LAST, i, outside_4[i])
+        x_first[LAST] = quantise("x00", xb[LAST, 0][:], CHUNK * PACK)
         for i in (3, 2):
-            pick_outside(1, last, i, got[i])
-        xb_unit = {}
+            pick_outside(1, LAST, i, outside_4[i])
+        j_last = LAST * CHUNK
+        unit_a, unit_b = LAST * UNITS, LAST * UNITS + 1
 
-        def unit_subtract(u, xf, which):
-            for i in which:
-                subtract_inside(xf[:, i, :], 1, i, j_last + u * P, P, got[i][:, u * P : (u + 1) * P])
+        def gather_unit(u, room, engine_copy):
+            rows = room.rearrange("p (i j) -> p i j", i=PACK)
+            for i in range(PACK):
+                subtract_inside(rows[:, i, :], 1, i, j_last + u * P, P, outside_4[i][:, u * P : (u + 1) * P])
+            woven = work.tile([P, P * PACK], BF16, name="xb_unit", tag="xb0%d" % (1 + u), align_bytes=64)
+            weave(engine_copy, woven[:], rows)
+            return woven
 
-        def unit_weave(u, xf, copy):
-            xb_unit[u] = work.tile([P, P * PACK], BF16, name="xb_unit", tag="xb0%d" % (1 + u), align_bytes=64)
-            weave(copy, xb_unit[u][:], xf)
-
-        def unit_quantise(u):
-            codes1, scales1 = quantise("x0%d" % (1 + u), xb_unit[u][:], P * PACK)
+        def finish_unit_model(u, woven):
+            codes, scales = quantise("x0%d" % (1 + u), woven[:], P * PACK)
             cols = slice(u * P, (u + 1) * P)
-            stage_one(last * UNITS + u, [(codes0[:, cols], scales0[:, cols]), (codes1[:], scales1[:])])
+            first_codes, first_scales = x_first[LAST]
+            direct_model(LAST * UNITS + u, [(first_codes[:, cols], first_scales[:, cols]), (codes[:], scales[:])])
 
-        xf_a = lanes[last][:, pitch : pitch + 2 * CHUNK].rearrange("p (t j) -> p t j", t=PACK)
-        xf_b = end_lane[:, 2 * CHUNK : 4 * CHUNK].rearrange("p (t j) -> p t j", t=PACK)
-        unit_subtract(0, xf_a, range(PACK))
-        unit_weave(0, xf_a, nc.scalar.copy)
-        back_through_wb(psi_q[1], CHUNK, CHUNK, (), ["big2", "big3"])
-        psi[2] = chunk_influence(2)
-        unit_quantise(0)
-        psi_q[2] = quantise("psi0", psi[2][:], CHUNK * PACK)
-        unit_subtract(1, xf_b, range(PACK))
-        unit_weave(1, xf_b, nc.vector.tensor_copy)
-        res_a = residual(last * UNITS, "mid0", P)
-        unit_quantise(1)
-        inv_a = invert(square(res_a, P, "res_sq", P // 2), P, lanes[0][:, 0 : PACK * P], "mid2", P // 2)
-        res_b = residual(last * UNITS + 1, "xb12", P // 2)
-        inv_b = invert(square(res_b, P, "xb11", P // 2), P, lanes[0][:, PACK * P : 2 * PACK * P], "xb01", P // 2)
-        psi_qa = quantise("psi1", influence(res_a, inv_a, P, P)[:], P * PACK)
-        psi_qb = quantise("psi2", influence(res_b, inv_b, P, P // 2)[:], P * PACK)
-        back_through_wb(psi_q[2], 2 * CHUNK, CHUNK, (0, 1, 2, 3), ["xf_early", "big0"])
-        back_through_wb(psi_qa, j_last, P, (), ["big1", "xb13"], 4)
-        back_through_wb(psi_qb, j_last + P, P, (0, 2), ["big2", "big3"], 2)
+        woven_a = gather_unit(0, lanes[LAST][:, second_pair : second_pair + H], nc.scalar.copy)
+        second_product(psi_q1, CHUNK, CHUNK, ["big2", "big3"], 2, ())
+        psi_2 = psi_turned(2, inv_2)
+        finish_unit_model(0, woven_a)
+        psi_q2 = quantise("psi0", psi_2[:], CHUNK * PACK)
+        woven_b = gather_unit(1, end_lane[:, H : 2 * H], nc.vector.tensor_copy)
+        res_a = direct_residual(unit_a, "mid0", P)
+        finish_unit_model(1, woven_b)
+        inv_a = invert(square_direct(res_a, "res_sq"), P, lanes[0][:, 0:H], "mid2", TAIL_PIECE)
+        res_b = direct_residual(unit_b, "xb12", TAIL_PIECE)
+        inv_b = invert(square_direct(res_b, "xb11"), P, lanes[0][:, H : 2 * H], "xb01", TAIL_PIECE)
+        psi_qa = quantise("psi1", psi_direct(res_a, inv_a, P)[:], H)
+        psi_qb = quantise("psi2", psi_direct(res_b, inv_b, TAIL_PIECE)[:], H)
+        second_product(psi_q2, 2 * CHUNK, CHUNK, ["xf_early", "big0"], 2, (0, 1, 2, 3))
+        second_product(psi_qa, j_last, P, ["big1", "xb13"], PACK, ())
+        second_product(psi_qb, j_last + P, P, ["big2", "big3"], 2, (0, 2))

@@ -25,9 +25,6 @@ UNITS = CHUNK // P
 HALF = S // 2
 PER_COL = 16
 RUN = 4
-LAST = S // CHUNK - 1
-BANKS = 4
-TAIL_PIECE = P // 2
 
 
 def tile_list_transit_cauchy_step_kernel(
@@ -42,6 +39,12 @@ def tile_list_transit_cauchy_step_kernel(
         def entries(lst, j0, n):
             return lst[:, j0 // PER_COL : (j0 + n) // PER_COL]
 
+        def sbuf(shape, dtype, name, tag=None):
+            return work.tile(shape, dtype, name=name, tag=tag or name, align_bytes=64)
+
+        def bank(shape, name, b):
+            return psum.tile(shape, F32, name=name, tag="bank%d" % b)
+
         x_rows = xT.rearrange("(a p i) t -> a i p t", a=PASSES, i=PACK)
         planes, wb_raw, flux_sb, tab_w = {}, {}, {}, {}
 
@@ -50,21 +53,19 @@ def tile_list_transit_cauchy_step_kernel(
             nc.sync.dma_start(out=planes[a, i][:], in_=x_rows[a, i])
 
         def load_wb(a):
-            wb_raw[a] = work.tile([P, PACK * H], F32, name="wb_raw", tag="big%d" % a, align_bytes=64)
+            wb_raw[a] = sbuf([P, PACK * H], F32, "wb_raw", "big%d" % a)
             nc.sync.dma_start(
                 out=wb_raw[a][:], in_=wb[a * P * PACK : (a + 1) * P * PACK, :].rearrange("(p i) r -> p (i r)", i=PACK)
             )
 
-        def load_flux(c, chunks, tag):
-            rows = work.tile([P, PACK, chunks * CHUNK], F32, name="flux_sb", tag=tag, align_bytes=64)
+        def load_flux(c, tag):
+            flux_sb[c] = sbuf([P, PACK, CHUNK], F32, "flux_sb", tag)
             nc.sync.dma_start(
-                out=rows[:], in_=flux[:, c * CHUNK : (c + chunks) * CHUNK].rearrange("(m t) j -> m t j", t=PACK)
+                out=flux_sb[c][:], in_=flux[:, c * CHUNK : (c + 1) * CHUNK].rearrange("(m t) j -> m t j", t=PACK)
             )
-            for d in range(chunks):
-                flux_sb[c + d] = rows[:, :, d * CHUNK : (d + 1) * CHUNK]
 
         def load_tab(a):
-            tab_w[a] = work.tile([P, T], I32, name="tab_w", tag="big%d" % (2 + a), align_bytes=64)
+            tab_w[a] = keep.tile([P, T], I32, name="tab_w%d" % a, align_bytes=64)
             nc.sync.dma_start(out=tab_w[a][:], in_=tab_words[a].rearrange("p t i -> p (t i)").bitcast(I32))
 
         idx = keep.tile([P, S // PER_COL], U16, name="idx")
@@ -112,52 +113,59 @@ def tile_list_transit_cauchy_step_kernel(
                 )
 
         load_wb(1)
-        move_scale_rows(0)
         load_plane(0, 3)
         load_tab(0)
-        move_scale_rows(1)
-        load_tab(1)
-        load_flux(0, 2, "big0")
         load_plane(1, 0)
+        move_scale_rows(0)
+        load_tab(1)
+        move_scale_rows(1)
         load_plane(1, 1)
         load_plane(1, 2)
-        load_flux(2, 1, "big1")
         load_plane(1, 3)
-        load_flux(LAST, 1, "flux3")
+        load_flux(0, "flux0")
         var_t = keep.tile([P, PACK], F32, name="var_t")
         nc.sync.dma_start(out=var_t[:], in_=var.rearrange("(m t) -> m t", t=PACK))
+        load_flux(1, "flux1")
         step_t = keep.tile([P, PASSES, PACK], F32, name="step_t")
         nc.sync.dma_start(out=step_t[:], in_=step.rearrange("(a p i) -> p a i", a=PASSES, i=PACK))
+        load_flux(2, "big0")
+        load_flux(3, "big1")
 
         def by_runs(woven):
             return woven.rearrange("p (c e t) -> p c t e", e=RUN, t=PACK)
 
-        def weave(engine_copy, woven, rows):
-            engine_copy(by_runs(woven), rows.rearrange("p t (c e) -> p c t e", e=RUN))
+        def weave(engine_copy, rows, n, tag):
+            woven = sbuf([P, n * PACK], BF16, "xb", tag)
+            engine_copy(by_runs(woven[:]), rows.rearrange("p t (c e) -> p c t e", e=RUN))
+            return woven
 
-        n_early = LAST * CHUNK
-        pieces = [(0, 2 * CHUNK), (2 * CHUNK, CHUNK)]
-        xf_early = work.tile([P, PACK, n_early], F32, name="xf_early", align_bytes=64)
-        for i in range(PACK):
-            outside = work.tile([P, n_early], F32, name="outside_early", tag="oe%d" % (i % 2), align_bytes=64)
-            for j0, n in pieces:
-                nc.vector.tensor_copy(outside[:, j0 : j0 + n], planes[0, i][:].indirect(entries(idx3, j0, n)))
-            for j0, n in pieces:
-                nc.vector.tensor_tensor(
-                    xf_early[:, i, j0 : j0 + n],
-                    planes[0, i][:].indirect(entries(idx2, j0, n)),
-                    outside[:, j0 : j0 + n],
-                    ALU.subtract,
-                )
+        def pick(dst, a, i, j0, n):
+            nc.vector.tensor_copy(dst, planes[a, i][:].indirect(entries(idx3, j0, n)))
 
-        wb_codes = [
-            work.tile([P, H], U32, name="wb_codes", tag=tag, align_bytes=64) for tag in ("wb_codes0", "oe1")
-        ]
+        def subtract(dst, a, i, j0, n, outside):
+            nc.vector.tensor_tensor(dst, planes[a, i][:].indirect(entries(idx2, j0, n)), outside, ALU.subtract)
+
+        def quantise(name, src, width):
+            codes = sbuf([P, width // PACK], U32, name + "_codes")
+            scales = sbuf([P, width // PACK], U8, name + "_sc")
+            nc.vector.quantize_mx(out=codes[:].bitcast(FP8X4), scales=scales[:], in_=src)
+            return codes, scales
+
+        v_words = {}
+
+        def gather_words(a, j0, n, dst):
+            nc.vector.tensor_copy(dst, tab_w[a][:].bitcast(U32).indirect(entries(idx, j0, n)))
+            for o in range(0, n, P):
+                v_words[a, (j0 + o) // P] = dst[:, o : o + P]
+
+        wb_codes = [sbuf([P, H], U32, "wb_codes%d" % a) for a in range(PASSES)]
         wb_sc = keep.tile([P, PASSES * H], U8, name="wb_sc", align_bytes=64)
         wt_sc = keep.tile([P, K], U8, name="wt_sc", align_bytes=64)
-        wt_both = work.tile([P, PASSES * H * PACK], BF16, name="wt_both", tag="mid2", align_bytes=64)
-        for a in range(PASSES):
-            wb_b = work.tile([P, H * PACK], BF16, name="wb_b", tag="mid%d" % a, align_bytes=64)
+        wt_both = sbuf([P, PASSES * H * PACK], BF16, "wt_both", "mid2")
+        wt_codes = sbuf([P, K], U32, "wt_codes")
+
+        def prepare_wb(a):
+            wb_b = sbuf([P, H * PACK], BF16, "wb_b", "mid%d" % a)
             nc.scalar.copy(
                 wb_b[:].rearrange("p (t m i) -> p m t i", t=PACK, i=PACK),
                 wb_raw[a][:].rearrange("p (i m t) -> p m t i", i=PACK, t=PACK),
@@ -168,261 +176,97 @@ def tile_list_transit_cauchy_step_kernel(
             pairs = wb_b[:].bitcast(F32)
             wt_b = wt_both[:, a * H * PACK : (a + 1) * H * PACK]
             for u in range(2):
-                bank = psum.tile([P, PACK, P], F32, name="wt_bank", tag="o_bank", bufs=BANKS)
+                turned = bank([P, PACK, P], "wt_bank", 4 + 2 * a + u)
                 for t in range(PACK):
-                    nc.tensor.transpose(bank[:, t, :], pairs[:, 2 * P * t + u : 2 * P * (t + 1) : 2], ident[:])
+                    nc.tensor.transpose(turned[:, t, :], pairs[:, 2 * P * t + u : 2 * P * (t + 1) : 2], ident[:])
                 nc.scalar.copy(
                     wt_b[:, u * 2 * H : (u + 1) * 2 * H].rearrange("m (e p t) -> m e p t", e=2, t=PACK),
-                    bank[:].rearrange("m t p -> m (t p)").bitcast(BF16).rearrange("m (t p e) -> m e p t", t=PACK, e=2),
+                    turned[:].rearrange("m t p -> m (t p)").bitcast(BF16).rearrange("m (t p e) -> m e p t", t=PACK, e=2),
                 )
 
         w4_w = keep.tile([P, PASSES * 2 * H], U8, name="w4_w", align_bytes=64)
         w4_sc = keep.tile([P, PASSES * H], U8, name="w4_sc", align_bytes=64)
-        nc.vector.tensor_copy(
-            w4_w[:].bitcast(U16).rearrange("p (a t m) -> p a t m", a=PASSES, t=PACK),
-            w4_raw[:].rearrange("p a c -> p (a c)").bitcast(U16).rearrange("p (a m t) -> p a t m", a=PASSES, t=PACK),
-        )
-        nc.vector.tensor_copy(
-            w4_sc[:].rearrange("p (a t m) -> p a t m", a=PASSES, t=PACK),
-            w4_sc_raw[:].rearrange("p (a m t) -> p a t m", a=PASSES, t=PACK),
-        )
 
-        v_words = {}
-
-        def gather_words(a, h, tag):
-            v_words[a, h] = work.tile([P, HALF], U32, name="v_words", tag=tag, align_bytes=64)
-            nc.vector.tensor_copy(v_words[a, h][:], tab_w[a][:].bitcast(U32).indirect(entries(idx, h * HALF, HALF)))
-
-        def words_of(a, g):
-            h, o = divmod(g * P, HALF)
-            return v_words[a, h][:, o : o + P].bitcast(FP8X4)
-
-        for a in range(PASSES):
-            gather_words(a, 0, "words%d" % a)
-
-        xb = {}
-        for c in range(LAST):
-            xb[c, 0] = work.tile([P, CHUNK * PACK], BF16, name="xb", tag="xb0%d" % c, align_bytes=64)
-            weave(nc.scalar.copy, xb[c, 0][:], xf_early[:, :, c * CHUNK : (c + 1) * CHUNK])
-
-        second_pair = 9 * CHUNK // 2
-        lanes = [keep.tile([P, 10 * CHUNK], F32, name="lane%d" % s, align_bytes=64) for s in range(1, LAST + 1)]
-        lanes.insert(0, keep.tile([P, PACK * CHUNK], F32, name="lane0", align_bytes=64))
-        end_lane = keep.tile([P, 2 * PACK * CHUNK], F32, name="end_lane", align_bytes=64)
-        row_lane = [lanes[1], lanes[1], lanes[2], lanes[3]]
-        first_pair = [2 * CHUNK, 0, 0, 0]
-
-        def row(s, i):
-            o = (first_pair[s] if i < 2 else second_pair) + (i % 2) * CHUNK
-            return row_lane[s][:, o : o + CHUNK]
-
-        def across_rows(s):
-            return lanes[s][:, CHUNK // 2 : 3 * CHUNK // 2]
-
-        def flux_room(c):
-            if c == 0:
-                return lanes[0][:, :]
-            if c == LAST:
-                return end_lane[:, PACK * CHUNK : 2 * PACK * CHUNK]
-            return lanes[c + 1][:, 2 * CHUNK : 6 * CHUNK]
-
-        def root_room(c):
-            if c == LAST - 1:
-                return end_lane[:, 0 : PACK * CHUNK]
-            return lanes[c + 2][:, 6 * CHUNK : 10 * CHUNK]
-
-        def weave_rows(engine_copy, s, a, tag):
-            xb[s, a] = work.tile([P, CHUNK * PACK], BF16, name="xb", tag=tag, align_bytes=64)
-            pitch = second_pair - first_pair[s]
-            both = row_lane[s][:, first_pair[s] : first_pair[s] + 2 * pitch].rearrange("p (u x) -> p u x", u=2)
-            engine_copy(
-                xb[s, a][:].rearrange("p (c e u v) -> p c u v e", e=RUN, u=2, v=2),
-                both[:, :, 0 : 2 * CHUNK].rearrange("p u (v c e) -> p c u v e", v=2, e=RUN),
+        def reorder_w4():
+            nc.vector.tensor_copy(
+                w4_w[:].bitcast(U16).rearrange("p (a t m) -> p a t m", a=PASSES, t=PACK),
+                w4_raw[:].rearrange("p a c -> p (a c)").bitcast(U16).rearrange("p (a m t) -> p a t m", a=PASSES, t=PACK),
+            )
+            nc.vector.tensor_copy(
+                w4_sc[:].rearrange("p (a t m) -> p a t m", a=PASSES, t=PACK),
+                w4_sc_raw[:].rearrange("p (a m t) -> p a t m", a=PASSES, t=PACK),
             )
 
-        def flux_unit(g):
-            c, u = divmod(g, UNITS)
-            return flux_sb[c][:, :, u * P : (u + 1) * P]
+        model, x_q = {}, {}
 
-        def flux_laid(g):
-            c, u = divmod(g, UNITS)
-            return flux_room(c)[:, u * H : (u + 1) * H]
-
-        def turn_flux(g):
-            bank = psum.tile([P, PACK, P], F32, name="flux_bank", tag="o_bank", bufs=BANKS)
-            for t in range(PACK):
-                nc.tensor.transpose(bank[:, t, :], flux_unit(g)[:, t, :], ident[:])
-            nc.scalar.copy(flux_laid(g), bank[:].rearrange("j t m -> j (t m)"))
-
-        def pick_outside(a, c, i, room):
-            nc.vector.tensor_copy(room, planes[a, i][:].indirect(entries(idx3, c * CHUNK, CHUNK)))
-
-        def subtract_inside(dst, a, i, j0, n, outside):
-            nc.vector.tensor_tensor(dst, planes[a, i][:].indirect(entries(idx2, j0, n)), outside, ALU.subtract)
-
-        def subtract_row(s, a, i, outside):
-            subtract_inside(row(s, i), a, i, s * CHUNK, CHUNK, outside)
-
-        def quantise(name, src, width):
-            codes = work.tile([P, width // PACK], U32, name=name + "_codes", align_bytes=64)
-            scales = work.tile([P, width // PACK], U8, name=name + "_sc", align_bytes=64)
-            nc.vector.quantize_mx(out=codes[:].bitcast(FP8X4), scales=scales[:], in_=src)
-            return codes, scales
-
-        x_first, res_bank = {}, {}
-
-        def turned_residual(g, x_ops):
+        def model_pass(g, kind, a, start, stop):
             cols = slice(g * P, (g + 1) * P)
-            turned = psum.tile([P, H], F32, name="turned", tag="m_bank", bufs=BANKS)
-            for a in range(PASSES):
-                nc.tensor.matmul_mx(
-                    out=turned[:],
-                    lhsT=words_of(a, g),
-                    lhsT_scale=v_sc[a][:, cols],
-                    rhs=w4_w[:, 2 * a * H : 2 * (a + 1) * H].bitcast(FP4X4),
-                    rhs_scale=w4_sc[:, a * H : (a + 1) * H],
-                    start=(a == 0),
-                    stop=False,
-                )
-            for a in range(PASSES):
-                nc.tensor.matmul_mx(
-                    out=turned[:],
-                    lhsT=x_ops[a][0].bitcast(FP8X4),
-                    lhsT_scale=x_ops[a][1],
-                    rhs=wb_codes[a][:].bitcast(FP8X4),
-                    rhs_scale=wb_sc[:, a * H : (a + 1) * H],
-                    start=False,
-                    stop=(a == PASSES - 1),
-                )
-            negated = work.tile([P, H], F32, name="negated", tag="xb0%d" % (g % UNITS), align_bytes=64)
-            nc.scalar.activation(negated[:], turned[:], ACT.Copy, scale=-1.0)
-            res_bank[g] = psum.tile([P, PACK, P], F32, name="res_bank", tag="o_bank", bufs=BANKS)
-            for term, src in enumerate((flux_laid(g), negated[:])):
-                for t in range(PACK):
-                    nc.tensor.matmul(
-                        res_bank[g][:, t, :],
-                        lhsT=src[:, t * P : (t + 1) * P],
-                        rhs=ident[:],
-                        is_transpose=True,
-                        start=(term == 0 and t == 0),
-                        stop=(term == 1 and t == PACK - 1),
-                    )
-
-        def finish_model(c):
-            x_second = quantise("x1%d" % (c % 2), xb[c, 1][:], CHUNK * PACK)
-            for u in range(UNITS):
-                cols = slice(u * P, (u + 1) * P)
-                turned_residual(c * UNITS + u, [(cd[:, cols], sc[:, cols]) for cd, sc in (x_first[c], x_second)])
-
-        def square_turned(c):
-            res_sq = work.tile([P, PACK, CHUNK], F32, name="res_sq", tag="res_sq", align_bytes=64)
-            for u in range(UNITS):
-                nc.scalar.activation(res_sq[:, :, u * P : (u + 1) * P], res_bank[c * UNITS + u][:], ACT.Square)
-            return res_sq
-
-        def psi_turned(c, inv):
-            psi_b = work.tile([P, CHUNK * PACK], BF16, name="psi_b", align_bytes=64, bufs=2)
-            for u in range(UNITS):
-                cols = slice(u * H, (u + 1) * H)
-                nc.vector.tensor_tensor(
-                    psi_b[:, cols].rearrange("m (j t) -> m j t", t=PACK),
-                    res_bank[c * UNITS + u][:].rearrange("m t j -> m j t"),
-                    inv[:, cols].rearrange("m (j t) -> m j t", t=PACK),
-                    ALU.mult,
-                )
-            return psi_b
-
-        model = {}
-
-        def direct_model(g, x_ops):
-            cols = slice(g * P, (g + 1) * P)
-            model[g] = psum.tile([P, PACK, P], F32, name="model", tag="m_bank", bufs=BANKS)
             for t in range(PACK):
-                for a in range(PASSES):
-                    nc.tensor.matmul_mx(
-                        out=model[g][:, t, :],
-                        lhsT=w4_w[:, 2 * (a * H + t * P) : 2 * (a * H + (t + 1) * P)].bitcast(FP4X4),
-                        lhsT_scale=w4_sc[:, a * H + t * P : a * H + (t + 1) * P],
-                        rhs=words_of(a, g),
-                        rhs_scale=v_sc[a][:, cols],
-                        start=(t == 0 and a == 0),
-                        stop=False,
-                    )
-            for a in range(PASSES):
-                for t in range(PACK):
-                    nc.tensor.matmul_mx(
-                        out=model[g][:, t, :],
-                        lhsT=wb_codes[a][:, t * P : (t + 1) * P].bitcast(FP8X4),
-                        lhsT_scale=wb_sc[:, a * H + t * P : a * H + (t + 1) * P],
-                        rhs=x_ops[a][0].bitcast(FP8X4),
-                        rhs_scale=x_ops[a][1],
-                        start=False,
-                        stop=(a == PASSES - 1 and t == PACK - 1),
-                    )
-
-        def direct_residual(g, tag, piece):
-            res = work.tile([P, H], F32, name="res", tag=tag, align_bytes=64)
-            for o in range(0, P, piece):
-                cols = slice(o * PACK, (o + piece) * PACK)
-                nc.vector.tensor_tensor(
-                    res[:, cols].rearrange("m (j t) -> m j t", t=PACK),
-                    flux_laid(g)[:, cols].rearrange("m (j t) -> m j t", t=PACK),
-                    model[g][:, :, o : o + piece].rearrange("m t j -> m j t"),
-                    ALU.subtract,
+                w_cols = slice(a * H + t * P, a * H + (t + 1) * P)
+                if kind == "table":
+                    lhs, lhs_sc = w4_w[:, 2 * w_cols.start : 2 * w_cols.stop].bitcast(FP4X4), w4_sc[:, w_cols]
+                    rhs, rhs_sc = v_words[a, g], v_sc[a][:, cols]
+                else:
+                    lhs, lhs_sc = wb_codes[a][:, t * P : (t + 1) * P].bitcast(FP8X4), wb_sc[:, w_cols]
+                    rhs, rhs_sc = x_q[a, g]
+                nc.tensor.matmul_mx(
+                    out=model[g][:, t, :],
+                    lhsT=lhs,
+                    lhsT_scale=lhs_sc,
+                    rhs=rhs.bitcast(FP8X4),
+                    rhs_scale=rhs_sc,
+                    start=(start and t == 0),
+                    stop=(stop and t == PACK - 1),
                 )
-            return res
 
-        def square_direct(res, tag):
-            res_sq = work.tile([P, PACK, P], F32, name="res_sq", tag=tag, align_bytes=64)
-            for o in range(0, P, TAIL_PIECE):
-                nc.scalar.activation(
-                    res_sq[:, :, o : o + TAIL_PIECE].rearrange("m t (c e) -> m c t e", e=RUN),
-                    by_runs(res[:, o * PACK : (o + TAIL_PIECE) * PACK]),
-                    ACT.Square,
-                )
-            return res_sq
+        def open_model(g, b, passes):
+            model[g] = bank([P, PACK, P], "model", b)
+            for k, (kind, a) in enumerate(passes):
+                model_pass(g, kind, a, k == 0, False)
 
-        def psi_direct(res, inv, piece):
-            psi_b = work.tile([P, H], BF16, name="psi_b", align_bytes=64, bufs=2)
-            for o in range(0, H, piece * PACK):
-                cols = slice(o, o + piece * PACK)
-                nc.vector.tensor_tensor(psi_b[:, cols], res[:, cols], inv[:, cols], ALU.mult)
-            return psi_b
+        def quantise_x(a, g0, woven, n, name):
+            codes, scales = quantise(name, woven[:], n * PACK)
+            for u in range(n // P):
+                x_q[a, g0 + u] = (codes[:, u * P : (u + 1) * P], scales[:, u * P : (u + 1) * P])
 
-        def invert(res_sq, n, room, tag, piece):
-            inv_root = room.rearrange("m (t j) -> m t j", t=PACK)
-            for o in range(0, n, piece):
-                for t in range(PACK):
-                    nc.scalar.activation(
-                        inv_root[:, t, o : o + piece],
-                        res_sq[:, t, o : o + piece],
-                        ACT.Abs_reciprocal_sqrt,
-                        bias=var_t[:, t : t + 1],
-                    )
-            inv = work.tile([P, n * PACK], F32, name="inv", tag=tag, align_bytes=64)
-            for o in range(0, n, piece):
-                nc.scalar.activation(
-                    by_runs(inv[:, o * PACK : (o + piece) * PACK]),
-                    inv_root[:, :, o : o + piece].rearrange("m t (c e) -> m c t e", e=RUN),
-                    ACT.Square,
-                )
-            return inv
+        def weave_flux(dst, c, j0, n):
+            nc.scalar.copy(by_runs(dst), flux_sb[c][:, :, j0 : j0 + n].rearrange("p t (c e) -> p c t e", e=RUN))
+
+        def residual(res, laid, g, o, n):
+            nc.vector.tensor_tensor(
+                res.rearrange("m (j t) -> m j t", t=PACK),
+                laid.rearrange("m (j t) -> m j t", t=PACK),
+                model[g][:, :, o : o + n].rearrange("m t j -> m j t"),
+                ALU.subtract,
+            )
+
+        def square(res_sq, res):
+            nc.scalar.activation(res_sq.rearrange("m t (c e) -> m c t e", e=RUN), by_runs(res), ACT.Square)
+
+        def root(room, res_sq):
+            for t in range(PACK):
+                nc.scalar.activation(room[:, t, :], res_sq[:, t, :], ACT.Abs_reciprocal_sqrt, bias=var_t[:, t : t + 1])
+
+        def invert(inv, inv_root):
+            nc.scalar.activation(by_runs(inv), inv_root.rearrange("m t (c e) -> m c t e", e=RUN), ACT.Square)
 
         out_rows = out.rearrange("(a p i) j -> a p i j", a=PASSES, i=PACK)
 
-        def second_product(psi_q, j0, n, tags, per_bank, on_vector):
+        def second_product(psi_q, j0, n, tags, banks, on_vector):
             psi_codes, psi_sc = psi_q
-            for first in range(0, PASSES * PACK, per_bank):
+            per_bank = PASSES * PACK // len(banks)
+            for k, b in enumerate(banks):
+                first = k * per_bank
                 a = first // PACK
                 if first % PACK == 0:
-                    staged = work.tile([P, PACK, n], F32, name="staged", tag=tags[a], align_bytes=64)
-                back = psum.tile([P, per_bank, n], F32, name="back", tag="o_bank", bufs=BANKS)
+                    staged = sbuf([P, PACK, n], F32, "staged", tags[a])
+                back = bank([P, per_bank, n], "back", b)
                 for e in range(per_bank):
-                    b = first + e
+                    cols = slice((first + e) * P, (first + e + 1) * P)
                     nc.tensor.matmul_mx(
                         out=back[:, e, :],
-                        lhsT=wt_codes[:, b * P : (b + 1) * P].bitcast(FP8X4),
-                        lhsT_scale=wt_sc[:, b * P : (b + 1) * P],
+                        lhsT=wt_codes[:, cols].bitcast(FP8X4),
+                        lhsT_scale=wt_sc[:, cols],
                         rhs=psi_codes[:].bitcast(FP8X4),
                         rhs_scale=psi_sc[:],
                         start=True,
@@ -431,112 +275,205 @@ def tile_list_transit_cauchy_step_kernel(
                 for e in range(per_bank):
                     i = (first + e) % PACK
                     factor = step_t[:, a, i : i + 1]
-                    if first // per_bank in on_vector:
+                    if k in on_vector:
                         nc.vector.tensor_scalar(staged[:, i, :], back[:, e, :], factor, None, ALU.mult)
                     else:
                         nc.scalar.activation(staged[:, i, :], back[:, e, :], ACT.Copy, scale=factor)
                 if (first + per_bank) % PACK == 0:
                     nc.sync.dma_start(out=out_rows[a, :, :, j0 : j0 + n], in_=staged[:])
-
-        spare = work.tile([P, 3 * CHUNK], F32, name="spare", tag="oe0", align_bytes=64)
-        for c in range(LAST):
-            x_first[c] = quantise("x0%d" % c, xb[c, 0][:], CHUNK * PACK)
-        for g in range(LAST * UNITS):
-            turn_flux(g)
-
-        ahead = work.tile([P, 3 * CHUNK], F32, name="ahead", tag="ahead", align_bytes=64)
-        outside_0 = [spare[:, i * CHUNK : (i + 1) * CHUNK] for i in range(3)] + [across_rows(1)]
-        outside_1 = [ahead[:, i * CHUNK : (i + 1) * CHUNK] for i in range(3)] + [across_rows(2)]
+        early = 3 * CHUNK
+        xa0 = sbuf([P, PACK, early], F32, "xa0")
+        oe = sbuf([P, 2, early], F32, "oe")
         for i in range(PACK):
-            pick_outside(1, 0, i, outside_0[i])
-            pick_outside(1, 1, i, outside_1[i])
-            subtract_row(0, 1, i, outside_0[i])
-        weave_rows(nc.scalar.copy, 0, 1, "xb10")
-        for g in range(LAST * UNITS, (LAST + 1) * UNITS):
-            weave(nc.scalar.copy, flux_laid(g), flux_unit(g))
+            for j0, n in ((0, HALF), (HALF, CHUNK)):
+                pick(oe[:, i % 2, j0 : j0 + n], 0, i, j0, n)
+            for j0, n in ((0, HALF), (HALF, CHUNK)):
+                subtract(xa0[:, i, j0 : j0 + n], 0, i, j0, n, oe[:, i % 2, j0 : j0 + n])
+        for a in range(PASSES):
+            prepare_wb(a)
+        reorder_w4()
+        words_a = sbuf([P, PASSES, HALF], U32, "words_a")
+        gather_words(0, 0, HALF, words_a[:, 0, :])
+        woven_a = weave(nc.scalar.copy, xa0[:, :, 0:HALF], HALF, "xb_a")
+        woven_b = weave(nc.scalar.copy, xa0[:, :, HALF:], CHUNK, "xb_b")
+        xf = sbuf([P, PACK, CHUNK], F32, "xf")
+        ring = [sbuf([P, PACK, CHUNK], F32, "ring%d" % s) for s in range(1)]
+        o_0 = sbuf([P, PACK, CHUNK], F32, "o_0")
 
-        for i in range(2):
-            subtract_row(1, 1, i, outside_1[i])
-        finish_model(0)
-        gather_words(0, 1, "xb10")
-        outside_2 = [row(0, 0), row(0, 1), row(1, 0), row(1, 1)]
-        for i in range(2):
-            pick_outside(1, 2, i, outside_2[i])
-        res_sq = square_turned(0)
-        for i in range(2, PACK):
-            subtract_row(1, 1, i, outside_1[i])
-        wt_codes = work.tile([P, K], U32, name="wt_codes", tag="ahead", align_bytes=64)
+        def plane_arrives(i):
+            pick(o_0[:, i, :], 1, i, 0, CHUNK)
+            pick(ring[0][:, i, :], 1, i, CHUNK, CHUNK)
+            subtract(xf[:, i, :], 1, i, 0, CHUNK, o_0[:, i, :])
+
+        plane_arrives(0)
+        quantise_x(0, 0, woven_a, HALF, "x0a")
+        gather_words(1, 0, HALF, words_a[:, 1, :])
+        quantise_x(0, 4, woven_b, CHUNK, "x0b")
         nc.vector.quantize_mx(out=wt_codes[:].bitcast(FP8X4), scales=wt_sc[:], in_=wt_both[:])
-        gather_words(1, 1, "oe0")
-        weave_rows(nc.scalar.copy, 1, 1, "xb01")
-        inv_0 = invert(res_sq, CHUNK, root_room(0), "mid3", P)
+        plane_arrives(1)
+        three = [("table", 0), ("x", 0), ("table", 1)]
+        for g in range(2 * UNITS):
+            open_model(g, g, three)
+        plane_arrives(2)
+        plane_arrives(3)
 
-        for i in range(2):
-            subtract_row(2, 1, i, outside_2[i])
-        finish_model(1)
-        for i in range(2, PACK):
-            pick_outside(1, 2, i, outside_2[i])
-        res_sq = square_turned(1)
-        subtract_row(2, 1, 2, outside_2[2])
-        psi_0 = psi_turned(0, inv_0)
-        subtract_row(2, 1, 3, outside_2[3])
-        psi_q0 = quantise("psi0", psi_0[:], CHUNK * PACK)
-        weave_rows(nc.scalar.copy, 2, 1, "xb01")
-        inv_1 = invert(res_sq, CHUNK, root_room(1), "mid2", P)
-        second_product(psi_q0, 0, CHUNK, ["xf_early", "big0"], 2, ())
 
-        outside_3 = [across_rows(1), lanes[1][:, 3 * CHUNK // 2 : 5 * CHUNK // 2], row(2, 0), row(2, 1)]
-        for i in range(2):
-            pick_outside(0, LAST, i, outside_3[i])
-        for i in range(2):
-            subtract_row(LAST, 0, i, outside_3[i])
-        finish_model(2)
-        for i in range(2, PACK):
-            pick_outside(0, LAST, i, outside_3[i])
-        res_sq = square_turned(2)
-        subtract_row(LAST, 0, 2, outside_3[2])
-        psi_1 = psi_turned(1, inv_1)
-        subtract_row(LAST, 0, 3, outside_3[3])
-        psi_q1 = quantise("psi1", psi_1[:], CHUNK * PACK)
-        weave_rows(nc.vector.tensor_copy, LAST, 0, "xb11")
-        inv_2 = invert(res_sq, CHUNK, root_room(2), "mid3", P)
+        def flat(tile):
+            return tile[:].rearrange("p a b -> p (a b)")
 
-        outside_4 = [row(2, 0), row(2, 1), row(LAST, 0), row(LAST, 1)]
-        for i in (1, 0):
-            pick_outside(1, LAST, i, outside_4[i])
-        x_first[LAST] = quantise("x00", xb[LAST, 0][:], CHUNK * PACK)
-        for i in (3, 2):
-            pick_outside(1, LAST, i, outside_4[i])
-        j_last = LAST * CHUNK
-        unit_a, unit_b = LAST * UNITS, LAST * UNITS + 1
+        laid = [sbuf([P, PACK, CHUNK], F32, "laid", "mid%d" % s) for s in range(2)]
+        res_room = [sbuf([P, PACK, CHUNK], F32, "res%d" % s) for s in range(2)]
+        inv_room = [sbuf([P, PACK, CHUNK], F32, "inv%d" % s) for s in range(2)]
 
-        def gather_unit(u, room, engine_copy):
-            rows = room.rearrange("p (i j) -> p i j", i=PACK)
+        def finish(c, woven):
+            quantise_x(1, c * UNITS, woven, CHUNK, "x1%d" % (c % 2))
+            for u in range(UNITS):
+                model_pass(c * UNITS + u, "x", 1, False, True)
+
+        def residual_chunk(c):
+            for u in range(UNITS):
+                cols = slice(u * H, (u + 1) * H)
+                residual(flat(res_room[c % 2])[:, cols], flat(laid[c % 2])[:, cols], c * UNITS + u, 0, P)
+
+        def lay_flux(c, u):
+            weave_flux(flat(laid[c % 2])[:, u * H : (u + 1) * H], c, u * P, P)
+
+        def roots(c):
+            res_sq = sbuf([P, PACK, CHUNK], F32, "res_sq", "sq")
+            inv_root = sbuf([P, PACK, CHUNK], F32, "inv_root", "root")
+            for u in range(UNITS):
+                square(res_sq[:, :, u * P : (u + 1) * P], flat(res_room[c % 2])[:, u * H : (u + 1) * H])
+            root(inv_root[:], res_sq)
+            return inv_root
+
+        def inverses(c, inv_root):
+            for u in range(UNITS):
+                invert(flat(inv_room[c % 2])[:, u * H : (u + 1) * H], inv_root[:, :, u * P : (u + 1) * P])
+
+        def psi_chunk(c, engines, tag):
+            psi_b = sbuf([P, CHUNK * PACK], BF16, "psi_b", tag)
+            for u in range(UNITS):
+                cols = slice(u * H, (u + 1) * H)
+                engines[u].tensor_tensor(psi_b[:, cols], flat(res_room[c % 2])[:, cols], flat(inv_room[c % 2])[:, cols], ALU.mult)
+            return psi_b
+
+        j1, j2, j3 = CHUNK, 2 * CHUNK, 3 * CHUNK
+        backs = [4, 5, 6, 7]
+
+        def subtract_rows(a, j0, outside, tag):
+            rows = sbuf([P, PACK, CHUNK], F32, "rows", tag)
             for i in range(PACK):
-                subtract_inside(rows[:, i, :], 1, i, j_last + u * P, P, outside_4[i][:, u * P : (u + 1) * P])
-            woven = work.tile([P, P * PACK], BF16, name="xb_unit", tag="xb0%d" % (1 + u), align_bytes=64)
-            weave(engine_copy, woven[:], rows)
-            return woven
+                subtract(rows[:, i, :], a, i, j0, CHUNK, outside[i])
+            return rows
 
-        def finish_unit_model(u, woven):
-            codes, scales = quantise("x0%d" % (1 + u), woven[:], P * PACK)
-            cols = slice(u * P, (u + 1) * P)
-            first_codes, first_scales = x_first[LAST]
-            direct_model(LAST * UNITS + u, [(first_codes[:, cols], first_scales[:, cols]), (codes[:], scales[:])])
-
-        woven_a = gather_unit(0, lanes[LAST][:, second_pair : second_pair + H], nc.scalar.copy)
-        second_product(psi_q1, CHUNK, CHUNK, ["big2", "big3"], 2, ())
-        psi_2 = psi_turned(2, inv_2)
-        finish_unit_model(0, woven_a)
+        woven = weave(nc.scalar.copy, xf[:], CHUNK, "xb0")
+        lay_flux(0, 0)
+        lay_flux(0, 1)
+        lay_flux(1, 0)
+        lay_flux(1, 1)
+        words_2 = sbuf([P, PASSES, CHUNK], U32, "words_b", "o_0")
+        gather_words(0, j2, CHUNK, words_2[:, 0, :])
+        gather_words(1, j2, CHUNK, words_2[:, 1, :])
+        finish(0, woven)
+        outside_2 = [ring[0][:, 0, :], ring[0][:, 1, :], xf[:, 0, :], xf[:, 1, :]]
+        pick(outside_2[2], 1, 2, j2, CHUNK)
+        pick(outside_2[3], 1, 3, j2, CHUNK)
+        residual_chunk(0)
+        rows = subtract_rows(1, j1, [ring[0][:, i, :] for i in range(PACK)], "x10_codes")
+        inv_root = roots(0)
+        woven = weave(nc.scalar.copy, rows[:], CHUNK, "xb1")
+        inverses(0, inv_root)
+        lay_flux(2, 0)
+        lay_flux(2, 1)
+        for i in range(2):
+            pick(outside_2[i], 1, i, j2, CHUNK)
+        finish(1, woven)
+        outside_3 = [inv_room[0][:, 0, :], inv_room[0][:, 2, :], rows[:, 0, :], rows[:, 1, :]]
+        pick(outside_3[2], 0, 2, j3, CHUNK)
+        pick(outside_3[3], 0, 3, j3, CHUNK)
+        psi_0 = psi_chunk(0, (nc.gpsimd, nc.gpsimd), "xb1")
+        residual_chunk(1)
+        for g in (4, 5):
+            open_model(g, g - 4, three)
+        rows = subtract_rows(1, j2, outside_2, "x11_codes")
+        psi_q0 = quantise("psi0", psi_0[:], CHUNK * PACK)
+        inv_root = roots(1)
+        woven = weave(nc.scalar.copy, rows[:], CHUNK, "xb0")
+        inverses(1, inv_root)
+        second_product(psi_q0, 0, CHUNK, ["mid2", "st1"], backs, ())
+        for i in range(2):
+            pick(outside_3[i], 0, i, j3, CHUNK)
+        quantise_x(1, 4, woven, CHUNK, "x12")
+        for g in (4, 5):
+            model_pass(g, "x", 1, False, True)
+        outside_4 = [inv_room[1][:, 0, :], inv_room[1][:, 2, :], rows[:, 0, :], rows[:, 1, :]]
+        pick(outside_4[2], 1, 2, j3, CHUNK)
+        pick(outside_4[3], 1, 3, j3, CHUNK)
+        psi_1 = psi_chunk(1, (nc.gpsimd, nc.gpsimd), "xb0")
+        residual_chunk(2)
+        rows = subtract_rows(0, j3, outside_3, "x12_codes")
+        psi_q1 = quantise("psi1", psi_1[:], CHUNK * PACK)
+        inv_root = roots(2)
+        woven = weave(nc.scalar.copy, rows[:], CHUNK, "xb1")
+        inverses(2, inv_root)
+        second_product(psi_q1, CHUNK, CHUNK, ["flux0", "flux1"], backs, ())
+        lay_flux(3, 0)
+        lay_flux(3, 1)
+        for i in range(2):
+            pick(outside_4[i], 1, i, j3, CHUNK)
+        quantise_x(0, 6, woven, CHUNK, "x0b")
+        rows = sbuf([P, UNITS, PACK, P], F32, "rows", "x12_codes")
+        for i in range(PACK):
+            subtract(rows[:, 0, i, :], 1, i, j3, P, outside_4[i][:, 0:P])
+        words_3 = sbuf([P, PASSES, CHUNK], U32, "words_b", "sq")
+        gather_words(0, j3, CHUNK, words_3[:, 0, :])
+        gather_words(1, j3, CHUNK, words_3[:, 1, :])
+        for g in (6, 7):
+            open_model(g, g - 4, [("x", 0), ("table", 0), ("table", 1)])
+        woven_a = weave(nc.vector.tensor_copy, rows[:, 0, :, :], P, "xb_a")
+        psi_2 = psi_chunk(2, (nc.gpsimd, nc.vector), "xb1")
+        quantise_x(1, 6, woven_a, P, "x10")
+        model_pass(6, "x", 1, False, True)
         psi_q2 = quantise("psi0", psi_2[:], CHUNK * PACK)
-        woven_b = gather_unit(1, end_lane[:, H : 2 * H], nc.vector.tensor_copy)
-        res_a = direct_residual(unit_a, "mid0", P)
-        finish_unit_model(1, woven_b)
-        inv_a = invert(square_direct(res_a, "res_sq"), P, lanes[0][:, 0:H], "mid2", TAIL_PIECE)
-        res_b = direct_residual(unit_b, "xb12", TAIL_PIECE)
-        inv_b = invert(square_direct(res_b, "xb11"), P, lanes[0][:, H : 2 * H], "xb01", TAIL_PIECE)
-        psi_qa = quantise("psi1", psi_direct(res_a, inv_a, P)[:], H)
-        psi_qb = quantise("psi2", psi_direct(res_b, inv_b, TAIL_PIECE)[:], H)
-        second_product(psi_q2, 2 * CHUNK, CHUNK, ["xf_early", "big0"], 2, (0, 1, 2, 3))
-        second_product(psi_qa, j_last, P, ["big1", "xb13"], PACK, ())
-        second_product(psi_qb, j_last + P, P, ["big2", "big3"], 2, (0, 2))
+        half = P // 2
+        res = flat(res_room[1])
+        rows_b = sbuf([P, PACK, P], F32, "rows_b", "xb_a")
+        for i in range(2):
+            subtract(rows_b[:, i, :], 1, i, j3 + P, P, outside_4[i][:, P:])
+        residual(res[:, 0:H], flat(laid[1])[:, 0:H], 6, 0, P)
+        for i in range(2, PACK):
+            subtract(rows_b[:, i, :], 1, i, j3 + P, P, outside_4[i][:, P:])
+
+        def invert_unit(u, tags):
+            res_sq = sbuf([P, PACK, P], F32, "res_sq", tags[0])
+            inv_root = sbuf([P, PACK, P], F32, "inv_root", tags[1])
+            inv = sbuf([P, H], F32, "inv", tags[2])
+            for o in (0, half):
+                square(res_sq[:, :, o : o + half], res[:, u * H + o * PACK : u * H + (o + half) * PACK])
+            for o in (0, half):
+                root(inv_root[:, :, o : o + half], res_sq[:, :, o : o + half])
+            for o in (0, half):
+                invert(inv[:, o * PACK : (o + half) * PACK], inv_root[:, :, o : o + half])
+            return inv
+
+        def psi_unit(u, inv, tag, piece):
+            psi_b = sbuf([P, H], BF16, "psi_b", tag)
+            for o in range(0, H, piece):
+                cols = slice(o, o + piece)
+                nc.vector.tensor_tensor(psi_b[:, cols], res[:, u * H : (u + 1) * H][:, cols], inv[:, cols], ALU.mult)
+            return psi_b
+
+        inv_a = invert_unit(0, ("sq", "root", "ring0"))
+        woven_b = weave(nc.vector.tensor_copy, rows_b[:], P, "xb_b")
+        quantise_x(1, 7, woven_b, P, "x0a")
+        model_pass(7, "x", 1, False, True)
+        psi_a = psi_unit(0, inv_a, "xb0", H)
+        for o in (0, half):
+            cols = slice(H + o * PACK, H + (o + half) * PACK)
+            residual(res[:, cols], flat(laid[1])[:, cols], 7, o, half)
+        psi_qa = quantise("tq0", psi_a[:], H)
+        inv_b = invert_unit(1, ("oe", "xa0", "xf"))
+        psi_qb = quantise("tq1", psi_unit(1, inv_b, "xb_a", H // 2)[:], H)
+        second_product(psi_q2, j2, CHUNK, ["mid2", "st1"], backs, (0, 1, 2, 3))
+        second_product(psi_qa, j3, P, ["flux0", "flux1"], [0, 1], ())
+        second_product(psi_qb, j3 + P, P, ["big0", "big1"], backs, (0, 2))

@@ -119,17 +119,17 @@ def tile_list_transit_cauchy_step_kernel(
         move_scale_rows(0)
         load_tab(1)
         move_scale_rows(1)
+        load_flux(2, "big0")
         load_plane(1, 1)
-        load_plane(1, 2)
-        load_plane(1, 3)
         load_flux(0, "flux0")
+        load_plane(1, 2)
+        load_flux(1, "flux1")
+        load_plane(1, 3)
+        load_flux(3, "big1")
         var_t = keep.tile([P, PACK], F32, name="var_t")
         nc.sync.dma_start(out=var_t[:], in_=var.rearrange("(m t) -> m t", t=PACK))
-        load_flux(1, "flux1")
         step_t = keep.tile([P, PASSES, PACK], F32, name="step_t")
         nc.sync.dma_start(out=step_t[:], in_=step.rearrange("(a p i) -> p a i", a=PASSES, i=PACK))
-        load_flux(2, "big0")
-        load_flux(3, "big1")
 
         def by_runs(woven):
             return woven.rearrange("p (c e t) -> p c t e", e=RUN, t=PACK)
@@ -199,7 +199,7 @@ def tile_list_transit_cauchy_step_kernel(
 
         model, x_q = {}, {}
 
-        def model_pass(g, kind, a, start, stop):
+        def direct_pass(g, kind, a, start, stop):
             cols = slice(g * P, (g + 1) * P)
             for t in range(PACK):
                 w_cols = slice(a * H + t * P, a * H + (t + 1) * P)
@@ -218,6 +218,27 @@ def tile_list_transit_cauchy_step_kernel(
                     start=(start and t == 0),
                     stop=(stop and t == PACK - 1),
                 )
+
+        def turned_pass(g, kind, a, start, stop):
+            cols = slice(g * P, (g + 1) * P)
+            if kind == "table":
+                lhs, lhs_sc = v_words[a, g], v_sc[a][:, cols]
+                rhs, rhs_sc = w4_w[:, 2 * a * H : 2 * (a + 1) * H].bitcast(FP4X4), w4_sc[:, a * H : (a + 1) * H]
+            else:
+                lhs, lhs_sc = x_q[a, g]
+                rhs, rhs_sc = wb_codes[a][:].bitcast(FP8X4), wb_sc[:, a * H : (a + 1) * H]
+            nc.tensor.matmul_mx(
+                out=model[g][:].rearrange("j t m -> j (t m)"),
+                lhsT=lhs.bitcast(FP8X4),
+                lhsT_scale=lhs_sc,
+                rhs=rhs,
+                rhs_scale=rhs_sc,
+                start=start,
+                stop=stop,
+            )
+
+        def model_pass(g, kind, a, start, stop):
+            (turned_pass if g // UNITS in (0, 1, 2) else direct_pass)(g, kind, a, start, stop)
 
         def open_model(g, b, passes):
             model[g] = bank([P, PACK, P], "model", b)
@@ -296,14 +317,17 @@ def tile_list_transit_cauchy_step_kernel(
         gather_words(0, 0, HALF, words_a[:, 0, :])
         woven_a = weave(nc.scalar.copy, xa0[:, :, 0:HALF], HALF, "xb_a")
         woven_b = weave(nc.scalar.copy, xa0[:, :, HALF:], CHUNK, "xb_b")
-        xf = sbuf([P, PACK, CHUNK], F32, "xf")
-        ring = [sbuf([P, PACK, CHUNK], F32, "ring%d" % s) for s in range(1)]
-        o_0 = sbuf([P, PACK, CHUNK], F32, "o_0")
+        xf = [sbuf([P, PACK, CHUNK], F32, "xf%d" % c) for c in range(2)]
+        o_1 = sbuf([P, PACK, CHUNK], F32, "o_1")
+        o_2 = sbuf([P, 2, CHUNK], F32, "o_2")
 
         def plane_arrives(i):
-            pick(o_0[:, i, :], 1, i, 0, CHUNK)
-            pick(ring[0][:, i, :], 1, i, CHUNK, CHUNK)
-            subtract(xf[:, i, :], 1, i, 0, CHUNK, o_0[:, i, :])
+            for c in range(2):
+                pick(o_1[:, 2 * (i % 2) + c, :], 1, i, c * CHUNK, CHUNK)
+            if i < 2:
+                pick(o_2[:, i, :], 1, i, 2 * CHUNK, CHUNK)
+            for c in range(2):
+                subtract(xf[c][:, i, :], 1, i, c * CHUNK, CHUNK, o_1[:, 2 * (i % 2) + c, :])
 
         plane_arrives(0)
         quantise_x(0, 0, woven_a, HALF, "x0a")
@@ -314,6 +338,9 @@ def tile_list_transit_cauchy_step_kernel(
         three = [("table", 0), ("x", 0), ("table", 1)]
         for g in range(2 * UNITS):
             open_model(g, g, three)
+        words_2 = sbuf([P, PASSES, CHUNK], U32, "words_2")
+        for a in range(PASSES):
+            gather_words(a, 2 * CHUNK, CHUNK, words_2[:, a, :])
         plane_arrives(2)
         plane_arrives(3)
 
@@ -321,8 +348,8 @@ def tile_list_transit_cauchy_step_kernel(
         def flat(tile):
             return tile[:].rearrange("p a b -> p (a b)")
 
-        laid = [sbuf([P, PACK, CHUNK], F32, "laid", "mid%d" % s) for s in range(2)]
-        res_room = [sbuf([P, PACK, CHUNK], F32, "res%d" % s) for s in range(2)]
+        laid = [sbuf([P, PACK, CHUNK], F32, "laid", tag) for tag in ("mid0", "mid1", "res0", "xa0")]
+        res_room = [None, None]
         inv_room = [sbuf([P, PACK, CHUNK], F32, "inv%d" % s) for s in range(2)]
 
         def finish(c, woven):
@@ -330,31 +357,74 @@ def tile_list_transit_cauchy_step_kernel(
             for u in range(UNITS):
                 model_pass(c * UNITS + u, "x", 1, False, True)
 
+        res_bank = {}
+
+        def turned_residual(c):
+            for u in range(UNITS):
+                g = c * UNITS + u
+                negated = sbuf([P, H], F32, "negated", "neg%d" % u)
+                nc.scalar.activation(negated[:], model[g][:].rearrange("j t m -> j (t m)"), ACT.Copy, scale=-1.0)
+                res_bank[g] = bank([P, PACK, P], "res_bank", 4 + 2 * (c % 2) + u)
+                for term, src in enumerate((flat(laid[c])[:, u * H : (u + 1) * H], negated[:])):
+                    for t in range(PACK):
+                        nc.tensor.matmul(
+                            res_bank[g][:, t, :],
+                            lhsT=src[:, t * P : (t + 1) * P],
+                            rhs=ident[:],
+                            is_transpose=True,
+                            start=(term == 0 and t == 0),
+                            stop=(term == 1 and t == PACK - 1),
+                        )
+
         def residual_chunk(c):
+            if c in (0, 1, 2):
+                return turned_residual(c)
             for u in range(UNITS):
                 cols = slice(u * H, (u + 1) * H)
-                residual(flat(res_room[c % 2])[:, cols], flat(laid[c % 2])[:, cols], c * UNITS + u, 0, P)
+                residual(flat(res_room[c % 2])[:, cols], flat(laid[c])[:, cols], c * UNITS + u, 0, P)
 
         def lay_flux(c, u):
-            weave_flux(flat(laid[c % 2])[:, u * H : (u + 1) * H], c, u * P, P)
+            if c in (0, 1, 2):
+                turned = bank([P, PACK, P], "flux_bank", (4, 6, 6)[c] + u)
+                for t in range(PACK):
+                    nc.tensor.transpose(turned[:, t, :], flux_sb[c][:, t, u * P : (u + 1) * P], ident[:])
+                nc.scalar.copy(flat(laid[c])[:, u * H : (u + 1) * H], turned[:].rearrange("j t m -> j (t m)"))
+                return
+            weave_flux(flat(laid[c])[:, u * H : (u + 1) * H], c, u * P, P)
 
-        def roots(c):
-            res_sq = sbuf([P, PACK, CHUNK], F32, "res_sq", "sq")
-            inv_root = sbuf([P, PACK, CHUNK], F32, "inv_root", "root")
+        def squares(c):
+            res_sq = sbuf([P, PACK, CHUNK], F32, "res_sq", "sq%d" % (c % 2))
             for u in range(UNITS):
-                square(res_sq[:, :, u * P : (u + 1) * P], flat(res_room[c % 2])[:, u * H : (u + 1) * H])
+                nc.scalar.activation(res_sq[:, :, u * P : (u + 1) * P], res_bank[c * UNITS + u][:], ACT.Square)
+            return res_sq
+
+        def roots_of(c, res_sq):
+            inv_root = sbuf([P, PACK, CHUNK], F32, "inv_root", ("root0", "root1", "xf1")[c])
             root(inv_root[:], res_sq)
             return inv_root
+
+        def roots(c):
+            return roots_of(c, squares(c))
 
         def inverses(c, inv_root):
             for u in range(UNITS):
                 invert(flat(inv_room[c % 2])[:, u * H : (u + 1) * H], inv_root[:, :, u * P : (u + 1) * P])
 
-        def psi_chunk(c, engines, tag):
+        def psi_chunk(c, tag):
             psi_b = sbuf([P, CHUNK * PACK], BF16, "psi_b", tag)
             for u in range(UNITS):
                 cols = slice(u * H, (u + 1) * H)
-                engines[u].tensor_tensor(psi_b[:, cols], flat(res_room[c % 2])[:, cols], flat(inv_room[c % 2])[:, cols], ALU.mult)
+                if c in (0, 1, 2):
+                    nc.vector.tensor_tensor(
+                        psi_b[:, cols].rearrange("m (j t) -> m j t", t=PACK),
+                        res_bank[c * UNITS + u][:].rearrange("m t j -> m j t"),
+                        flat(inv_room[c % 2])[:, cols].rearrange("m (j t) -> m j t", t=PACK),
+                        ALU.mult,
+                    )
+                else:
+                    nc.vector.tensor_tensor(
+                        psi_b[:, cols], flat(res_room[c % 2])[:, cols], flat(inv_room[c % 2])[:, cols], ALU.mult
+                    )
             return psi_b
 
         j1, j2, j3 = CHUNK, 2 * CHUNK, 3 * CHUNK
@@ -366,83 +436,76 @@ def tile_list_transit_cauchy_step_kernel(
                 subtract(rows[:, i, :], a, i, j0, CHUNK, outside[i])
             return rows
 
-        woven = weave(nc.scalar.copy, xf[:], CHUNK, "xb0")
-        lay_flux(0, 0)
-        lay_flux(0, 1)
-        lay_flux(1, 0)
-        lay_flux(1, 1)
-        words_2 = sbuf([P, PASSES, CHUNK], U32, "words_b", "o_0")
-        gather_words(0, j2, CHUNK, words_2[:, 0, :])
-        gather_words(1, j2, CHUNK, words_2[:, 1, :])
-        finish(0, woven)
-        outside_2 = [ring[0][:, 0, :], ring[0][:, 1, :], xf[:, 0, :], xf[:, 1, :]]
-        pick(outside_2[2], 1, 2, j2, CHUNK)
-        pick(outside_2[3], 1, 3, j2, CHUNK)
+        for c in (2, 0, 1):
+            lay_flux(c, 0)
+            lay_flux(c, 1)
+        woven_0 = weave(nc.scalar.copy, xf[0][:], CHUNK, "xb0")
+        woven_1 = weave(nc.scalar.copy, xf[1][:], CHUNK, "xb1")
+        outside = [o_2[:, 0, :], o_2[:, 1, :], o_1[:, 2, :], xf[0][:, 0, :]]
+        pick(outside[2], 1, 2, j2, CHUNK)
+        finish(0, woven_0)
+        pick(outside[3], 1, 3, j2, CHUNK)
+        finish(1, woven_1)
         residual_chunk(0)
-        rows = subtract_rows(1, j1, [ring[0][:, i, :] for i in range(PACK)], "x10_codes")
-        inv_root = roots(0)
-        woven = weave(nc.scalar.copy, rows[:], CHUNK, "xb1")
-        inverses(0, inv_root)
-        lay_flux(2, 0)
-        lay_flux(2, 1)
-        for i in range(2):
-            pick(outside_2[i], 1, i, j2, CHUNK)
-        finish(1, woven)
-        outside_3 = [inv_room[0][:, 0, :], inv_room[0][:, 2, :], rows[:, 0, :], rows[:, 1, :]]
-        pick(outside_3[2], 0, 2, j3, CHUNK)
-        pick(outside_3[3], 0, 3, j3, CHUNK)
-        psi_0 = psi_chunk(0, (nc.gpsimd, nc.gpsimd), "xb1")
         residual_chunk(1)
+        for i in range(PACK):
+            subtract(xf[1][:, i, :], 1, i, j2, CHUNK, outside[i])
+        root_0 = roots(0)
+        outside = [o_2[:, 1, :], o_1[:, 2, :], xf[1][:, 0, :], xf[1][:, 1, :]]
+        pick(outside[0], 0, 0, j3, CHUNK)
+        woven = weave(nc.vector.tensor_copy, xf[1][:], CHUNK, "xb0")
+        pick(outside[1], 0, 1, j3, CHUNK)
         for g in (4, 5):
             open_model(g, g - 4, three)
-        rows = subtract_rows(1, j2, outside_2, "x11_codes")
+        finish(2, woven)
+        pick(outside[2], 0, 2, j3, CHUNK)
+        pick(outside[3], 0, 3, j3, CHUNK)
+        words_3 = sbuf([P, PASSES, CHUNK], U32, "words_3", "xb0")
+        for a in range(PASSES):
+            gather_words(a, j3, CHUNK, words_3[:, a, :])
+        sq_1 = squares(1)
+        inverses(0, root_0)
+        root_1 = roots_of(1, sq_1)
+        psi_0 = psi_chunk(0, "psi_b")
+        rows = sbuf([P, PACK, CHUNK], F32, "rows", "root0")
+        subtract(rows[:, 0, :], 0, 0, j3, CHUNK, outside[0])
         psi_q0 = quantise("psi0", psi_0[:], CHUNK * PACK)
-        inv_root = roots(1)
-        woven = weave(nc.scalar.copy, rows[:], CHUNK, "xb0")
-        inverses(1, inv_root)
-        second_product(psi_q0, 0, CHUNK, ["mid2", "st1"], backs, ())
-        for i in range(2):
-            pick(outside_3[i], 0, i, j3, CHUNK)
-        quantise_x(1, 4, woven, CHUNK, "x12")
-        for g in (4, 5):
-            model_pass(g, "x", 1, False, True)
-        outside_4 = [inv_room[1][:, 0, :], inv_room[1][:, 2, :], rows[:, 0, :], rows[:, 1, :]]
-        pick(outside_4[2], 1, 2, j3, CHUNK)
-        pick(outside_4[3], 1, 3, j3, CHUNK)
-        psi_1 = psi_chunk(1, (nc.gpsimd, nc.gpsimd), "xb0")
+        for i in range(1, PACK):
+            subtract(rows[:, i, :], 0, i, j3, CHUNK, outside[i])
+        inverses(1, root_1)
         residual_chunk(2)
-        rows = subtract_rows(0, j3, outside_3, "x12_codes")
+        outside_4 = [inv_room[0][:, 0, :], inv_room[0][:, 2, :], inv_room[1][:, 0, :], inv_room[1][:, 2, :]]
+        pick(outside_4[0], 1, 0, j3, CHUNK)
+        woven = weave(nc.vector.tensor_copy, rows[:], CHUNK, "xb1")
+        pick(outside_4[1], 1, 1, j3, CHUNK)
+        quantise_x(0, 6, woven, CHUNK, "x0b")
+        root_2 = roots(2)
+        inv_room[0] = sbuf([P, PACK, CHUNK], F32, "inv_late", "o_1")
+        inverses(2, root_2)
+        second_product(psi_q0, 0, CHUNK, ["mid2", "oe"], [2, 3, 0, 1], ())
+        psi_1 = psi_chunk(1, "psi_b")
+        pick(outside_4[2], 1, 2, j3, CHUNK)
         psi_q1 = quantise("psi1", psi_1[:], CHUNK * PACK)
-        inv_root = roots(2)
-        woven = weave(nc.scalar.copy, rows[:], CHUNK, "xb1")
-        inverses(2, inv_root)
-        second_product(psi_q1, CHUNK, CHUNK, ["flux0", "flux1"], backs, ())
+        pick(outside_4[3], 1, 3, j3, CHUNK)
         lay_flux(3, 0)
         lay_flux(3, 1)
-        for i in range(2):
-            pick(outside_4[i], 1, i, j3, CHUNK)
-        quantise_x(0, 6, woven, CHUNK, "x0b")
-        rows = sbuf([P, UNITS, PACK, P], F32, "rows", "x12_codes")
+        for g in (6, 7):
+            open_model(g, g - 4, [("table", 0), ("table", 1), ("x", 0)])
+        second_product(psi_q1, CHUNK, CHUNK, ["flux0", "flux1"], [0, 1, 6, 7], ())
+        rows = sbuf([P, UNITS, PACK, P], F32, "rows", "xf1")
         for i in range(PACK):
             subtract(rows[:, 0, i, :], 1, i, j3, P, outside_4[i][:, 0:P])
-        words_3 = sbuf([P, PASSES, CHUNK], U32, "words_b", "sq")
-        gather_words(0, j3, CHUNK, words_3[:, 0, :])
-        gather_words(1, j3, CHUNK, words_3[:, 1, :])
-        for g in (6, 7):
-            open_model(g, g - 4, [("x", 0), ("table", 0), ("table", 1)])
+        subtract(rows[:, 1, 0, :], 1, 0, j3 + P, P, outside_4[0][:, P:])
         woven_a = weave(nc.vector.tensor_copy, rows[:, 0, :, :], P, "xb_a")
-        psi_2 = psi_chunk(2, (nc.gpsimd, nc.vector), "xb1")
+        subtract(rows[:, 1, 1, :], 1, 1, j3 + P, P, outside_4[1][:, P:])
         quantise_x(1, 6, woven_a, P, "x10")
         model_pass(6, "x", 1, False, True)
-        psi_q2 = quantise("psi0", psi_2[:], CHUNK * PACK)
         half = P // 2
-        res = flat(res_room[1])
-        rows_b = sbuf([P, PACK, P], F32, "rows_b", "xb_a")
-        for i in range(2):
-            subtract(rows_b[:, i, :], 1, i, j3 + P, P, outside_4[i][:, P:])
-        residual(res[:, 0:H], flat(laid[1])[:, 0:H], 6, 0, P)
-        for i in range(2, PACK):
-            subtract(rows_b[:, i, :], 1, i, j3 + P, P, outside_4[i][:, P:])
+        res = flat(sbuf([P, PACK, CHUNK], F32, "res_room", "sq1"))
+        subtract(rows[:, 1, 2, :], 1, 2, j3 + P, P, outside_4[2][:, P:])
+        subtract(rows[:, 1, 3, :], 1, 3, j3 + P, P, outside_4[3][:, P:])
+        residual(res[:, 0:H], flat(laid[3])[:, 0:H], 6, 0, P)
+        rows_b = rows[:, 1, :, :]
 
         def invert_unit(u, tags):
             res_sq = sbuf([P, PACK, P], F32, "res_sq", tags[0])
@@ -463,17 +526,18 @@ def tile_list_transit_cauchy_step_kernel(
                 nc.vector.tensor_tensor(psi_b[:, cols], res[:, u * H : (u + 1) * H][:, cols], inv[:, cols], ALU.mult)
             return psi_b
 
-        inv_a = invert_unit(0, ("sq", "root", "ring0"))
-        woven_b = weave(nc.vector.tensor_copy, rows_b[:], P, "xb_b")
+        inv_a = invert_unit(0, ("sq0", "root0", "xf0"))
+        woven_b = weave(nc.vector.tensor_copy, rows_b, P, "xb_b")
+        psi_2 = psi_chunk(2, "xb1")
         quantise_x(1, 7, woven_b, P, "x0a")
         model_pass(7, "x", 1, False, True)
-        psi_a = psi_unit(0, inv_a, "xb0", H)
+        psi_q2 = quantise("psi0", psi_2[:], CHUNK * PACK)
         for o in (0, half):
             cols = slice(H + o * PACK, H + (o + half) * PACK)
-            residual(res[:, cols], flat(laid[1])[:, cols], 7, o, half)
-        psi_qa = quantise("tq0", psi_a[:], H)
-        inv_b = invert_unit(1, ("oe", "xa0", "xf"))
+            residual(res[:, cols], flat(laid[3])[:, cols], 7, o, half)
+        psi_qa = quantise("tq0", psi_unit(0, inv_a, "xb0", H)[:], H)
+        inv_b = invert_unit(1, ("o_2", "mid0", "root1"))
         psi_qb = quantise("tq1", psi_unit(1, inv_b, "xb_a", H // 2)[:], H)
-        second_product(psi_q2, j2, CHUNK, ["mid2", "st1"], backs, (0, 1, 2, 3))
-        second_product(psi_qa, j3, P, ["flux0", "flux1"], [0, 1], ())
-        second_product(psi_qb, j3 + P, P, ["big0", "big1"], backs, (0, 2))
+        second_product(psi_q2, j2, CHUNK, ["mid2", "root0"], [4, 5, 6, 7], (0, 1, 2, 3))
+        second_product(psi_qa, j3, P, ["mid1", "res0"], [2, 0], ())
+        second_product(psi_qb, j3 + P, P, ["big0", "big1"], [3, 1, 4, 5], (0, 2))

@@ -162,6 +162,7 @@ def tile_list_transit_cauchy_step_kernel(
         wb_sc = keep.tile([P, PASSES * H], U8, name="wb_sc", align_bytes=64)
         wt_sc = keep.tile([P, K], U8, name="wt_sc", align_bytes=64)
         wt_both = sbuf([P, PASSES * H * PACK], BF16, "wt_both", "mid2")
+
         wt_codes = sbuf([P, K], U32, "wt_codes")
 
         def prepare_wb(a):
@@ -273,7 +274,7 @@ def tile_list_transit_cauchy_step_kernel(
 
         out_rows = out.rearrange("(a p i) j -> a p i j", a=PASSES, i=PACK)
 
-        def second_product(psi_q, j0, n, tags, banks, on_vector):
+        def second_product(psi_q, j0, n, tags, banks, on_vector, rows_a_store=PACK):
             psi_codes, psi_sc = psi_q
             per_bank = PASSES * PACK // len(banks)
             for k, b in enumerate(banks):
@@ -300,8 +301,10 @@ def tile_list_transit_cauchy_step_kernel(
                         nc.vector.tensor_scalar(staged[:, i, :], back[:, e, :], factor, None, ALU.mult)
                     else:
                         nc.scalar.activation(staged[:, i, :], back[:, e, :], ACT.Copy, scale=factor)
-                if (first + per_bank) % PACK == 0:
-                    nc.sync.dma_start(out=out_rows[a, :, :, j0 : j0 + n], in_=staged[:])
+                done = first % PACK + per_bank
+                if done % rows_a_store == 0:
+                    rows_done = slice(done - rows_a_store, done)
+                    nc.sync.dma_start(out=out_rows[a, :, rows_done, j0 : j0 + n], in_=staged[:, rows_done, :])
         early = 3 * CHUNK
         xa0 = sbuf([P, PACK, early], F32, "xa0")
         oe = sbuf([P, 2, early], F32, "oe")
@@ -319,13 +322,10 @@ def tile_list_transit_cauchy_step_kernel(
         woven_b = weave(nc.scalar.copy, xa0[:, :, HALF:], CHUNK, "xb_b")
         xf = [sbuf([P, PACK, CHUNK], F32, "xf%d" % c) for c in range(2)]
         o_1 = sbuf([P, PACK, CHUNK], F32, "o_1")
-        o_2 = sbuf([P, 2, CHUNK], F32, "o_2")
 
         def plane_arrives(i):
             for c in range(2):
                 pick(o_1[:, 2 * (i % 2) + c, :], 1, i, c * CHUNK, CHUNK)
-            if i < 2:
-                pick(o_2[:, i, :], 1, i, 2 * CHUNK, CHUNK)
             for c in range(2):
                 subtract(xf[c][:, i, :], 1, i, c * CHUNK, CHUNK, o_1[:, 2 * (i % 2) + c, :])
 
@@ -338,9 +338,6 @@ def tile_list_transit_cauchy_step_kernel(
         three = [("table", 0), ("x", 0), ("table", 1)]
         for g in range(2 * UNITS):
             open_model(g, g, three)
-        words_2 = sbuf([P, PASSES, CHUNK], U32, "words_2")
-        for a in range(PASSES):
-            gather_words(a, 2 * CHUNK, CHUNK, words_2[:, a, :])
         plane_arrives(2)
         plane_arrives(3)
 
@@ -362,7 +359,7 @@ def tile_list_transit_cauchy_step_kernel(
         def turned_residual(c):
             for u in range(UNITS):
                 g = c * UNITS + u
-                negated = sbuf([P, H], F32, "negated", "neg%d" % u)
+                negated = sbuf([P, H], F32, "negated", "neg%d" % (g % 3))
                 nc.scalar.activation(negated[:], model[g][:].rearrange("j t m -> j (t m)"), ACT.Copy, scale=-1.0)
                 res_bank[g] = bank([P, PACK, P], "res_bank", 4 + 2 * (c % 2) + u)
                 for term, src in enumerate((flat(laid[c])[:, u * H : (u + 1) * H], negated[:])):
@@ -441,28 +438,30 @@ def tile_list_transit_cauchy_step_kernel(
             lay_flux(c, 1)
         woven_0 = weave(nc.scalar.copy, xf[0][:], CHUNK, "xb0")
         woven_1 = weave(nc.scalar.copy, xf[1][:], CHUNK, "xb1")
-        outside = [o_2[:, 0, :], o_2[:, 1, :], o_1[:, 2, :], xf[0][:, 0, :]]
+        outside = [xf[0][:, 1, :], xf[0][:, 2, :], o_1[:, 2, :], xf[0][:, 0, :]]
         pick(outside[2], 1, 2, j2, CHUNK)
         finish(0, woven_0)
         pick(outside[3], 1, 3, j2, CHUNK)
+        pick(outside[0], 1, 0, j2, CHUNK)
         finish(1, woven_1)
+        pick(outside[1], 1, 1, j2, CHUNK)
         residual_chunk(0)
+        sq_0 = squares(0)
         residual_chunk(1)
         for i in range(PACK):
             subtract(xf[1][:, i, :], 1, i, j2, CHUNK, outside[i])
-        root_0 = roots(0)
-        outside = [o_2[:, 1, :], o_1[:, 2, :], xf[1][:, 0, :], xf[1][:, 1, :]]
-        pick(outside[0], 0, 0, j3, CHUNK)
-        woven = weave(nc.vector.tensor_copy, xf[1][:], CHUNK, "xb0")
-        pick(outside[1], 0, 1, j3, CHUNK)
+        root_0 = roots_of(0, sq_0)
+        words_2 = sbuf([P, PASSES, CHUNK], U32, "words_2", "o_1")
+        gather_words(0, j2, CHUNK, words_2[:, 0, :])
+        woven = weave(nc.scalar.copy, xf[1][:], CHUNK, "xb0")
+        gather_words(1, j2, CHUNK, words_2[:, 1, :])
+        outside = [xf[0][:, 2, :], xf[0][:, 0, :], xf[1][:, 0, :], xf[1][:, 1, :]]
+        quantise_x(1, 4, woven, CHUNK, "x10")
         for g in (4, 5):
-            open_model(g, g - 4, three)
-        finish(2, woven)
-        pick(outside[2], 0, 2, j3, CHUNK)
-        pick(outside[3], 0, 3, j3, CHUNK)
-        words_3 = sbuf([P, PASSES, CHUNK], U32, "words_3", "xb0")
-        for a in range(PASSES):
-            gather_words(a, j3, CHUNK, words_3[:, a, :])
+            open_model(g, g - 4, [("x", 0), ("x", 1), ("table", 0)])
+            model_pass(g, "table", 1, False, True)
+        for i in range(PACK):
+            pick(outside[i], 0, i, j3, CHUNK)
         sq_1 = squares(1)
         inverses(0, root_0)
         root_1 = roots_of(1, sq_1)
@@ -476,22 +475,25 @@ def tile_list_transit_cauchy_step_kernel(
         residual_chunk(2)
         outside_4 = [inv_room[0][:, 0, :], inv_room[0][:, 2, :], inv_room[1][:, 0, :], inv_room[1][:, 2, :]]
         pick(outside_4[0], 1, 0, j3, CHUNK)
-        woven = weave(nc.vector.tensor_copy, rows[:], CHUNK, "xb1")
+        woven = weave(nc.scalar.copy, rows[:], CHUNK, "root1")
         pick(outside_4[1], 1, 1, j3, CHUNK)
         quantise_x(0, 6, woven, CHUNK, "x0b")
         root_2 = roots(2)
         inv_room[0] = sbuf([P, PACK, CHUNK], F32, "inv_late", "o_1")
         inverses(2, root_2)
-        second_product(psi_q0, 0, CHUNK, ["mid2", "oe"], [2, 3, 0, 1], ())
+        second_product(psi_q0, 0, CHUNK, ["mid2", "oe"], [2, 3, 0, 1], (), 2)
         psi_1 = psi_chunk(1, "psi_b")
         pick(outside_4[2], 1, 2, j3, CHUNK)
         psi_q1 = quantise("psi1", psi_1[:], CHUNK * PACK)
         pick(outside_4[3], 1, 3, j3, CHUNK)
+        words_3 = sbuf([P, PASSES, CHUNK], U32, "words_3", "psi_b")
+        for a in range(PASSES):
+            gather_words(a, j3, CHUNK, words_3[:, a, :])
         lay_flux(3, 0)
         lay_flux(3, 1)
         for g in (6, 7):
-            open_model(g, g - 4, [("table", 0), ("table", 1), ("x", 0)])
-        second_product(psi_q1, CHUNK, CHUNK, ["flux0", "flux1"], [0, 1, 6, 7], ())
+            open_model(g, g - 4, [("x", 0), ("table", 0), ("table", 1)])
+        second_product(psi_q1, CHUNK, CHUNK, ["flux0", "flux1"], [6, 7, 0, 1], (), 2)
         rows = sbuf([P, UNITS, PACK, P], F32, "rows", "xf1")
         for i in range(PACK):
             subtract(rows[:, 0, i, :], 1, i, j3, P, outside_4[i][:, 0:P])
@@ -536,8 +538,8 @@ def tile_list_transit_cauchy_step_kernel(
             cols = slice(H + o * PACK, H + (o + half) * PACK)
             residual(res[:, cols], flat(laid[3])[:, cols], 7, o, half)
         psi_qa = quantise("tq0", psi_unit(0, inv_a, "xb0", H)[:], H)
-        inv_b = invert_unit(1, ("o_2", "mid0", "root1"))
+        inv_b = invert_unit(1, ("neg0", "mid0", "neg1"))
         psi_qb = quantise("tq1", psi_unit(1, inv_b, "xb_a", H // 2)[:], H)
-        second_product(psi_q2, j2, CHUNK, ["mid2", "root0"], [4, 5, 6, 7], (0, 1, 2, 3))
+        second_product(psi_q2, j2, CHUNK, ["mid2", "oe"], [4, 5, 6, 7], (0, 1, 2, 3), 2)
         second_product(psi_qa, j3, P, ["mid1", "res0"], [2, 0], ())
-        second_product(psi_qb, j3 + P, P, ["big0", "big1"], [3, 1, 4, 5], (0, 2))
+        second_product(psi_qb, j3 + P, P, ["big0", "big1"], [3, 1, 4, 5], (0, 2), 2)

@@ -163,8 +163,6 @@ def tile_list_transit_cauchy_step_kernel(
         wt_sc = keep.tile([P, K], U8, name="wt_sc", align_bytes=64)
         wt_both = sbuf([P, PASSES * H * PACK], BF16, "wt_both", "mid2")
 
-        wt_codes = sbuf([P, K], U32, "wt_codes")
-
         def prepare_wb(a):
             wb_b = sbuf([P, H * PACK], BF16, "wb_b", "mid%d" % a)
             nc.scalar.copy(
@@ -333,7 +331,6 @@ def tile_list_transit_cauchy_step_kernel(
         quantise_x(0, 0, woven_a, HALF, "x0a")
         gather_words(1, 0, HALF, words_a[:, 1, :])
         quantise_x(0, 4, woven_b, CHUNK, "x0b")
-        nc.vector.quantize_mx(out=wt_codes[:].bitcast(FP8X4), scales=wt_sc[:], in_=wt_both[:])
         plane_arrives(1)
         three = [("table", 0), ("x", 0), ("table", 1)]
         for g in range(2 * UNITS):
@@ -462,6 +459,8 @@ def tile_list_transit_cauchy_step_kernel(
             model_pass(g, "table", 1, False, True)
         for i in range(PACK):
             pick(outside[i], 0, i, j3, CHUNK)
+        wt_codes = sbuf([P, K], U32, "wt_codes", "x11_codes")
+        nc.vector.quantize_mx(out=wt_codes[:].bitcast(FP8X4), scales=wt_sc[:], in_=wt_both[:])
         sq_1 = squares(1)
         inverses(0, root_0)
         root_1 = roots_of(1, sq_1)
@@ -481,7 +480,7 @@ def tile_list_transit_cauchy_step_kernel(
         root_2 = roots(2)
         inv_room[0] = sbuf([P, PACK, CHUNK], F32, "inv_late", "o_1")
         inverses(2, root_2)
-        second_product(psi_q0, 0, CHUNK, ["mid2", "oe"], [2, 3, 0, 1], (), 2)
+        second_product(psi_q0, 0, CHUNK, ["mid2", "oe"], [2, 3, 0, 1], ())
         psi_1 = psi_chunk(1, "psi_b")
         pick(outside_4[2], 1, 2, j3, CHUNK)
         psi_q1 = quantise("psi1", psi_1[:], CHUNK * PACK)
@@ -493,7 +492,7 @@ def tile_list_transit_cauchy_step_kernel(
         lay_flux(3, 1)
         for g in (6, 7):
             open_model(g, g - 4, [("x", 0), ("table", 0), ("table", 1)])
-        second_product(psi_q1, CHUNK, CHUNK, ["flux0", "flux1"], [6, 7, 0, 1], (), 2)
+        second_product(psi_q1, CHUNK, CHUNK, ["flux0", "flux1"], [6, 7, 0, 1], ())
         rows = sbuf([P, UNITS, PACK, P], F32, "rows", "xf1")
         for i in range(PACK):
             subtract(rows[:, 0, i, :], 1, i, j3, P, outside_4[i][:, 0:P])
@@ -542,4 +541,4 @@ def tile_list_transit_cauchy_step_kernel(
         psi_qb = quantise("tq1", psi_unit(1, inv_b, "xb_a", H // 2)[:], H)
         second_product(psi_q2, j2, CHUNK, ["mid2", "oe"], [4, 5, 6, 7], (0, 1, 2, 3), 2)
         second_product(psi_qa, j3, P, ["mid1", "res0"], [2, 0], ())
-        second_product(psi_qb, j3 + P, P, ["big0", "big1"], [3, 1, 4, 5], (0, 2), 2)
+        second_product(psi_qb, j3 + P, P, ["big0", "big1"], [3, 1, 4, 5], (0, 2), 4)

@@ -21,10 +21,10 @@ P = 128
 PACK = 4
 PASSES = K // (P * PACK)
 CHUNK = 256
-UNITS = CHUNK // P
 HALF = S // 2
 PER_COL = 16
 RUN = 4
+PAIR = 2
 
 
 def tile_list_transit_cauchy_step_kernel(
@@ -44,6 +44,9 @@ def tile_list_transit_cauchy_step_kernel(
 
         def bank(shape, name, b):
             return psum.tile(shape, F32, name=name, tag="bank%d" % b)
+
+        def flat(ap):
+            return ap.rearrange("p a b -> p (a b)")
 
         x_rows = xT.rearrange("(a p i) t -> a i p t", a=PASSES, i=PACK)
         planes, wb_raw, flux_sb, tab_w = {}, {}, {}, {}
@@ -72,7 +75,7 @@ def tile_list_transit_cauchy_step_kernel(
         idx2 = keep.tile([P, S // PER_COL], U16, name="idx2")
         idx3 = keep.tile([P, S // PER_COL], U16, name="idx3")
         tab_sc = keep.tile([P, T], U8, name="tab_sc")
-        w4_sc_raw = keep.tile([P, PASSES * H], U8, name="w4_sc_raw", align_bytes=64)
+        w4_sc_raw = sbuf([P, PASSES * H], U8, "w4_sc_raw")
         v_sc = [keep.tile([P, S], U8, name="v_sc%d" % a, align_bytes=64) for a in range(PASSES)]
         nc.vector.memset(tab_sc[32:64, :].bitcast(I32), 0)
         nc.vector.memset(tab_sc[64:128, :].bitcast(I32), 0)
@@ -85,25 +88,7 @@ def tile_list_transit_cauchy_step_kernel(
         ident = keep.tile([P, P], F32, name="ident")
         make_identity(nc, ident[:])
 
-        nc.sync.dma_start(idx[:], offs)
-        nc.sync.dma_start(
-            out=tab_sc[0:32, :].bitcast(I32), in_=tab_scales.rearrange("a q t -> (a q) t").bitcast(I32)
-        )
-        load_plane(0, 0)
-        nc.sync.dma_start(idx3[:], offs3)
-        nc.sync.dma_start(idx2[:], offs2)
-        load_plane(0, 1)
-        load_wb(0)
-        load_plane(0, 2)
-        w4_raw = keep.tile([P, PASSES, 2 * H], U8, name="w4_raw", align_bytes=64)
-        nc.sync.dma_start(out=w4_raw[:].bitcast(I32), in_=w4_words.rearrange("a p c -> p a c").bitcast(I32))
-        for q in range(4):
-            nc.sync.dma_start(
-                out=w4_sc_raw[32 * q : 32 * q + 4, :].bitcast(I32).rearrange("p (a c) -> p a c", a=PASSES),
-                in_=w4_scales[:, 4 * q : 4 * q + 4, :].rearrange("a s c -> s a c").bitcast(I32),
-            )
         picked_sc = keep.tile([P, S], U8, name="picked_sc")
-        nc.vector.tensor_copy(picked_sc[:], tab_sc[:].indirect(idx[:]))
 
         def move_scale_rows(a):
             for q in range(4):
@@ -112,31 +97,46 @@ def tile_list_transit_cauchy_step_kernel(
                     out=v_sc[a][32 * q : 32 * q + 4, :].bitcast(I32), in_=picked_sc[row : row + 4, :].bitcast(I32)
                 )
 
+        nc.sync.dma_start(idx[:], offs)
+        nc.sync.dma_start(
+            out=tab_sc[0:32, :].bitcast(I32), in_=tab_scales.rearrange("a q t -> (a q) t").bitcast(I32)
+        )
+        load_plane(0, 0)
+        nc.sync.dma_start(idx3[:], offs3)
+        nc.sync.dma_start(idx2[:], offs2)
+        nc.vector.tensor_copy(picked_sc[:], tab_sc[:].indirect(idx[:]))
+        load_plane(0, 1)
+        load_wb(0)
+        load_plane(0, 2)
+        for q in range(4):
+            nc.sync.dma_start(
+                out=w4_sc_raw[32 * q : 32 * q + 4, :].bitcast(I32).rearrange("p (a c) -> p a c", a=PASSES),
+                in_=w4_scales[:, 4 * q : 4 * q + 4, :].rearrange("a s c -> s a c").bitcast(I32),
+            )
         load_wb(1)
         load_plane(0, 3)
-        load_tab(0)
-        load_plane(1, 0)
         move_scale_rows(0)
-        load_tab(1)
+        w4_raw = sbuf([P, PASSES, 2 * H], U8, "w4_raw")
+        nc.sync.dma_start(out=w4_raw[:].bitcast(I32), in_=w4_words.rearrange("a p c -> p a c").bitcast(I32))
+        load_plane(1, 0)
+        load_tab(0)
         move_scale_rows(1)
-        load_flux(2, "big0")
         load_plane(1, 1)
-        load_flux(0, "flux0")
         load_plane(1, 2)
-        load_flux(1, "flux1")
+        load_tab(1)
         load_plane(1, 3)
-        load_flux(3, "big1")
         var_t = keep.tile([P, PACK], F32, name="var_t")
         nc.sync.dma_start(out=var_t[:], in_=var.rearrange("(m t) -> m t", t=PACK))
         step_t = keep.tile([P, PASSES, PACK], F32, name="step_t")
         nc.sync.dma_start(out=step_t[:], in_=step.rearrange("(a p i) -> p a i", a=PASSES, i=PACK))
 
-        def by_runs(woven):
-            return woven.rearrange("p (c e t) -> p c t e", e=RUN, t=PACK)
-
-        def weave(engine_copy, rows, n, tag):
-            woven = sbuf([P, n * PACK], BF16, "xb", tag)
-            engine_copy(by_runs(woven[:]), rows.rearrange("p t (c e) -> p c t e", e=RUN))
+        def weave(engine_copy, pieces, n, tag):
+            woven = sbuf([P, len(pieces) * n * PACK], BF16, "xb", tag)
+            for k, rows in enumerate(pieces):
+                engine_copy(
+                    woven[:, k * n * PACK : (k + 1) * n * PACK].rearrange("p (c e t) -> p c t e", e=RUN, t=PACK),
+                    rows.rearrange("p t (c e) -> p c t e", e=RUN),
+                )
             return woven
 
         def pick(dst, a, i, j0, n):
@@ -145,141 +145,180 @@ def tile_list_transit_cauchy_step_kernel(
         def subtract(dst, a, i, j0, n, outside):
             nc.vector.tensor_tensor(dst, planes[a, i][:].indirect(entries(idx2, j0, n)), outside, ALU.subtract)
 
-        def quantise(name, src, width):
-            codes = sbuf([P, width // PACK], U32, name + "_codes")
-            scales = sbuf([P, width // PACK], U8, name + "_sc")
+        def quantise(name, src, width, tag=None, scale_tag=None):
+            codes = sbuf([P, width // PACK], U32, name + "_codes", tag)
+            scales = sbuf([P, width // PACK], U8, name + "_sc", scale_tag)
             nc.vector.quantize_mx(out=codes[:].bitcast(FP8X4), scales=scales[:], in_=src)
             return codes, scales
 
-        v_words = {}
+        v_words, x_q = {}, {}
 
-        def gather_words(a, j0, n, dst):
-            nc.vector.tensor_copy(dst, tab_w[a][:].bitcast(U32).indirect(entries(idx, j0, n)))
+        def gather_words(a, j0, n, tag):
+            words = sbuf([P, n], U32, "words", tag)
+            nc.vector.tensor_copy(words[:], tab_w[a][:].bitcast(U32).indirect(entries(idx, j0, n)))
             for o in range(0, n, P):
-                v_words[a, (j0 + o) // P] = dst[:, o : o + P]
+                v_words[a, j0 + o] = words[:, o:n]
 
-        wb_codes = [sbuf([P, H], U32, "wb_codes%d" % a) for a in range(PASSES)]
-        wb_sc = keep.tile([P, PASSES * H], U8, name="wb_sc", align_bytes=64)
-        wt_sc = keep.tile([P, K], U8, name="wt_sc", align_bytes=64)
-        wt_both = sbuf([P, PASSES * H * PACK], BF16, "wt_both", "mid2")
+        def quantise_x(a, j0, woven, n, name, tag=None, scale_tag=None):
+            codes, scales = quantise(name, woven[:], n * PACK, tag, scale_tag)
+            for o in range(0, n, P):
+                x_q[a, j0 + o] = (codes[:, o:n], scales[:, o:n])
 
-        def prepare_wb(a):
+        wb_q, wt_b, wt_q = {}, {}, {}
+
+        def prepare_wb(a, scale_tag, turned_tag):
             wb_b = sbuf([P, H * PACK], BF16, "wb_b", "mid%d" % a)
             nc.scalar.copy(
                 wb_b[:].rearrange("p (t m i) -> p m t i", t=PACK, i=PACK),
                 wb_raw[a][:].rearrange("p (i m t) -> p m t i", i=PACK, t=PACK),
             )
-            nc.vector.quantize_mx(
-                out=wb_codes[a][:].bitcast(FP8X4), scales=wb_sc[:, a * H : (a + 1) * H], in_=wb_b[:]
-            )
+            wb_q[a] = quantise("wb%d" % a, wb_b[:], H * PACK, None, scale_tag)
             pairs = wb_b[:].bitcast(F32)
-            wt_b = wt_both[:, a * H * PACK : (a + 1) * H * PACK]
+            wt_b[a] = sbuf([P, H * PACK], BF16, "wt_b", turned_tag)
             for u in range(2):
                 turned = bank([P, PACK, P], "wt_bank", 4 + 2 * a + u)
                 for t in range(PACK):
                     nc.tensor.transpose(turned[:, t, :], pairs[:, 2 * P * t + u : 2 * P * (t + 1) : 2], ident[:])
                 nc.scalar.copy(
-                    wt_b[:, u * 2 * H : (u + 1) * 2 * H].rearrange("m (e p t) -> m e p t", e=2, t=PACK),
-                    turned[:].rearrange("m t p -> m (t p)").bitcast(BF16).rearrange("m (t p e) -> m e p t", t=PACK, e=2),
+                    wt_b[a][:, u * 2 * H : (u + 1) * 2 * H].rearrange("m (e p t) -> m e p t", e=2, t=PACK),
+                    flat(turned[:]).bitcast(BF16).rearrange("m (t p e) -> m e p t", t=PACK, e=2),
                 )
 
-        w4_w = keep.tile([P, PASSES * 2 * H], U8, name="w4_w", align_bytes=64)
-        w4_sc = keep.tile([P, PASSES * H], U8, name="w4_sc", align_bytes=64)
-
-        def reorder_w4():
-            nc.vector.tensor_copy(
+        def reorder_w4(tag):
+            w4_w = sbuf([P, PASSES * 2 * H], U8, "w4_w")
+            nc.scalar.copy(
                 w4_w[:].bitcast(U16).rearrange("p (a t m) -> p a t m", a=PASSES, t=PACK),
-                w4_raw[:].rearrange("p a c -> p (a c)").bitcast(U16).rearrange("p (a m t) -> p a t m", a=PASSES, t=PACK),
+                flat(w4_raw[:]).bitcast(U16).rearrange("p (a m t) -> p a t m", a=PASSES, t=PACK),
             )
+            w4_sc = sbuf([P, PASSES * H], U8, "w4_sc", tag)
             nc.vector.tensor_copy(
                 w4_sc[:].rearrange("p (a t m) -> p a t m", a=PASSES, t=PACK),
                 w4_sc_raw[:].rearrange("p (a m t) -> p a t m", a=PASSES, t=PACK),
             )
+            return w4_w, w4_sc
 
-        model, x_q = {}, {}
+        def weights(kind, a, c0, n):
+            cols = slice(a * H + c0, a * H + c0 + n)
+            if kind == "table":
+                return w4_w[:, 2 * cols.start : 2 * cols.stop].bitcast(FP4X4), w4_sc[:, cols]
+            codes, scales = wb_q[a]
+            return codes[:, c0 : c0 + n].bitcast(FP8X4), scales[:, c0 : c0 + n]
 
-        def direct_pass(g, kind, a, start, stop):
-            cols = slice(g * P, (g + 1) * P)
+        def columns(kind, a, j0, n):
+            if kind == "table":
+                return v_words[a, j0][:, 0:n].bitcast(FP8X4), v_sc[a][:, j0 : j0 + n]
+            codes, scales = x_q[a, j0]
+            return codes[:, 0:n].bitcast(FP8X4), scales[:, 0:n]
+
+        def direct_pass(banks, kind, a, j0, n, start, stop):
+            per_bank = PACK // len(banks)
+            rhs, rhs_sc = columns(kind, a, j0, n)
             for t in range(PACK):
-                w_cols = slice(a * H + t * P, a * H + (t + 1) * P)
-                if kind == "table":
-                    lhs, lhs_sc = w4_w[:, 2 * w_cols.start : 2 * w_cols.stop].bitcast(FP4X4), w4_sc[:, w_cols]
-                    rhs, rhs_sc = v_words[a, g], v_sc[a][:, cols]
-                else:
-                    lhs, lhs_sc = wb_codes[a][:, t * P : (t + 1) * P].bitcast(FP8X4), wb_sc[:, w_cols]
-                    rhs, rhs_sc = x_q[a, g]
+                lhs, lhs_sc = weights(kind, a, t * P, P)
                 nc.tensor.matmul_mx(
-                    out=model[g][:, t, :],
+                    out=banks[t // per_bank][:, t % per_bank, :],
                     lhsT=lhs,
                     lhsT_scale=lhs_sc,
-                    rhs=rhs.bitcast(FP8X4),
+                    rhs=rhs,
                     rhs_scale=rhs_sc,
-                    start=(start and t == 0),
-                    stop=(stop and t == PACK - 1),
+                    start=(start and t % per_bank == 0),
+                    stop=(stop and t % per_bank == per_bank - 1),
                 )
 
-        def turned_pass(g, kind, a, start, stop):
-            cols = slice(g * P, (g + 1) * P)
-            if kind == "table":
-                lhs, lhs_sc = v_words[a, g], v_sc[a][:, cols]
-                rhs, rhs_sc = w4_w[:, 2 * a * H : 2 * (a + 1) * H].bitcast(FP4X4), w4_sc[:, a * H : (a + 1) * H]
-            else:
-                lhs, lhs_sc = x_q[a, g]
-                rhs, rhs_sc = wb_codes[a][:].bitcast(FP8X4), wb_sc[:, a * H : (a + 1) * H]
-            nc.tensor.matmul_mx(
-                out=model[g][:].rearrange("j t m -> j (t m)"),
-                lhsT=lhs.bitcast(FP8X4),
-                lhsT_scale=lhs_sc,
-                rhs=rhs,
-                rhs_scale=rhs_sc,
-                start=start,
-                stop=stop,
-            )
+        def turned_pass(banks, kind, a, j0, start, stop):
+            rhs, rhs_sc = weights(kind, a, 0, H)
+            for u, model in enumerate(banks):
+                lhs, lhs_sc = columns(kind, a, j0 + u * P, P)
+                nc.tensor.matmul_mx(
+                    out=model[:], lhsT=lhs, lhsT_scale=lhs_sc, rhs=rhs, rhs_scale=rhs_sc, start=start, stop=stop
+                )
 
-        def model_pass(g, kind, a, start, stop):
-            (turned_pass if g // UNITS in (0, 1, 2) else direct_pass)(g, kind, a, start, stop)
+        def lay_flux(c, banks, tag):
+            laid = sbuf([P, 2, H], F32, "laid", tag)
+            for u, b in enumerate(banks):
+                turned = bank([P, PACK, P], "flux_bank", b)
+                for t in range(PACK):
+                    nc.tensor.transpose(turned[:, t, :], flux_sb[c][:, t, u * P : (u + 1) * P], ident[:])
+                nc.scalar.copy(laid[:, u, :], flat(turned[:]))
+            return laid
 
-        def open_model(g, b, passes):
-            model[g] = bank([P, PACK, P], "model", b)
-            for k, (kind, a) in enumerate(passes):
-                model_pass(g, kind, a, k == 0, False)
+        def turned_residual(models, laid, banks):
+            res_banks = []
+            for u, model in enumerate(models):
+                negated = sbuf([P, H], F32, "negated", "neg%d" % u)
+                nc.scalar.activation(negated[:], model[:], ACT.Copy, scale=-1.0)
+                res = bank([P, PACK, P], "res_bank", banks[u])
+                for term, src in enumerate((laid[:, u, :], negated[:])):
+                    for t in range(PACK):
+                        nc.tensor.matmul(
+                            res[:, t, :],
+                            lhsT=src[:, t * P : (t + 1) * P],
+                            rhs=ident[:],
+                            is_transpose=True,
+                            start=(term == 0 and t == 0),
+                            stop=(term == 1 and t == PACK - 1),
+                        )
+                res_banks.append(res)
+            return res_banks
 
-        def quantise_x(a, g0, woven, n, name):
-            codes, scales = quantise(name, woven[:], n * PACK)
-            for u in range(n // P):
-                x_q[a, g0 + u] = (codes[:, u * P : (u + 1) * P], scales[:, u * P : (u + 1) * P])
+        def direct_residual(models, flux_rows, n, tag):
+            res = sbuf([P, PACK, n], F32, "res", tag)
+            per_bank = PACK // len(models)
+            for b, model in enumerate(models):
+                rows = slice(b * per_bank, (b + 1) * per_bank)
+                nc.vector.tensor_tensor(res[:, rows, :], flux_rows[:, rows, :], model[:], ALU.subtract)
+            return res
 
-        def weave_flux(dst, c, j0, n):
-            nc.scalar.copy(by_runs(dst), flux_sb[c][:, :, j0 : j0 + n].rearrange("p t (c e) -> p c t e", e=RUN))
+        def square_rows(pairs, n, tag):
+            dst = sbuf([P, PACK, n], F32, "squared", tag)
+            for k, src in enumerate(pairs):
+                nc.scalar.activation(dst[:, 2 * k : 2 * k + 2, :], src, ACT.Square)
+            return dst
 
-        def residual(res, laid, g, o, n):
-            nc.vector.tensor_tensor(
-                res.rearrange("m (j t) -> m j t", t=PACK),
-                laid.rearrange("m (j t) -> m j t", t=PACK),
-                model[g][:, :, o : o + n].rearrange("m t j -> m j t"),
-                ALU.subtract,
-            )
+        def pairs_of(rows):
+            return [rows[:, 0:2, :], rows[:, 2:4, :]]
 
-        def square(res_sq, res):
-            nc.scalar.activation(res_sq.rearrange("m t (c e) -> m c t e", e=RUN), by_runs(res), ACT.Square)
+        def square_banks(res_banks, tag):
+            dst = sbuf([P, PACK, CHUNK], F32, "squared", tag)
+            for u, res in enumerate(res_banks):
+                nc.scalar.activation(dst[:, :, u * P : (u + 1) * P], res[:], ACT.Square)
+            return dst
 
-        def root(room, res_sq):
+        def roots(res_sq, n, tags):
+            pairs = [sbuf([P, 2, n], F32, "inv_root", tag) for tag in tags]
             for t in range(PACK):
-                nc.scalar.activation(room[:, t, :], res_sq[:, t, :], ACT.Abs_reciprocal_sqrt, bias=var_t[:, t : t + 1])
+                nc.scalar.activation(
+                    pairs[t // 2][:, t % 2, :], res_sq[:, t, :], ACT.Abs_reciprocal_sqrt, bias=var_t[:, t : t + 1]
+                )
+            return [pair[:] for pair in pairs]
 
-        def invert(inv, inv_root):
-            nc.scalar.activation(by_runs(inv), inv_root.rearrange("m t (c e) -> m c t e", e=RUN), ACT.Square)
+        def influence(pieces, n, tag):
+            psi_b = sbuf([P, len(pieces) * n * PACK], BF16, "psi_b", tag)
+            for k, (res, inv) in enumerate(pieces):
+                nc.vector.tensor_tensor(
+                    psi_b[:, k * n * PACK : (k + 1) * n * PACK].rearrange("m (c e t) -> m c t e", e=PAIR, t=PACK),
+                    res.rearrange("m t (c e) -> m c t e", e=PAIR),
+                    inv.rearrange("m t (c e) -> m c t e", e=PAIR),
+                    ALU.mult,
+                )
+            return psi_b
+
+        def square_units(pairs, tags):
+            units = [sbuf([P, PACK, P], F32, "squared", tag) for tag in tags]
+            for k, src in enumerate(pairs):
+                for u, dst in enumerate(units):
+                    nc.scalar.activation(dst[:, 2 * k : 2 * k + 2, :], src[:, :, u * P : (u + 1) * P], ACT.Square)
+            return units
 
         out_rows = out.rearrange("(a p i) j -> a p i j", a=PASSES, i=PACK)
 
-        def second_product(psi_q, j0, n, tags, banks, on_vector, rows_a_store=PACK):
+        def second_product(psi_q, j0, n, a, tag, banks, on_vector=(), rows_a_store=PACK):
             psi_codes, psi_sc = psi_q
-            per_bank = PASSES * PACK // len(banks)
+            wt_codes, wt_sc = wt_q[a]
+            per_bank = PACK // len(banks)
+            staged = sbuf([P, PACK, n], F32, "staged", tag)
             for k, b in enumerate(banks):
                 first = k * per_bank
-                a = first // PACK
-                if first % PACK == 0:
-                    staged = sbuf([P, PACK, n], F32, "staged", tags[a])
                 back = bank([P, per_bank, n], "back", b)
                 for e in range(per_bank):
                     cols = slice((first + e) * P, (first + e + 1) * P)
@@ -303,242 +342,172 @@ def tile_list_transit_cauchy_step_kernel(
                 if done % rows_a_store == 0:
                     rows_done = slice(done - rows_a_store, done)
                     nc.sync.dma_start(out=out_rows[a, :, rows_done, j0 : j0 + n], in_=staged[:, rows_done, :])
-        early = 3 * CHUNK
-        xa0 = sbuf([P, PACK, early], F32, "xa0")
-        oe = sbuf([P, 2, early], F32, "oe")
-        for i in range(PACK):
-            for j0, n in ((0, HALF), (HALF, CHUNK)):
-                pick(oe[:, i % 2, j0 : j0 + n], 0, i, j0, n)
-            for j0, n in ((0, HALF), (HALF, CHUNK)):
-                subtract(xa0[:, i, j0 : j0 + n], 0, i, j0, n, oe[:, i % 2, j0 : j0 + n])
-        for a in range(PASSES):
-            prepare_wb(a)
-        reorder_w4()
-        words_a = sbuf([P, PASSES, HALF], U32, "words_a")
-        gather_words(0, 0, HALF, words_a[:, 0, :])
-        woven_a = weave(nc.scalar.copy, xa0[:, :, 0:HALF], HALF, "xb_a")
-        woven_b = weave(nc.scalar.copy, xa0[:, :, HALF:], CHUNK, "xb_b")
-        xf = [sbuf([P, PACK, CHUNK], F32, "xf%d" % c) for c in range(2)]
-        o_1 = sbuf([P, PACK, CHUNK], F32, "o_1")
-
-        def plane_arrives(i):
-            for c in range(2):
-                pick(o_1[:, 2 * (i % 2) + c, :], 1, i, c * CHUNK, CHUNK)
-            for c in range(2):
-                subtract(xf[c][:, i, :], 1, i, c * CHUNK, CHUNK, o_1[:, 2 * (i % 2) + c, :])
-
-        plane_arrives(0)
-        quantise_x(0, 0, woven_a, HALF, "x0a")
-        gather_words(1, 0, HALF, words_a[:, 1, :])
-        quantise_x(0, 4, woven_b, CHUNK, "x0b")
-        plane_arrives(1)
-        three = [("table", 0), ("x", 0), ("table", 1)]
-        for g in range(2 * UNITS):
-            open_model(g, g, three)
-        plane_arrives(2)
-        plane_arrives(3)
-
-
-        def flat(tile):
-            return tile[:].rearrange("p a b -> p (a b)")
-
-        laid = [sbuf([P, PACK, CHUNK], F32, "laid", tag) for tag in ("mid0", "mid1", "res0", "xa0")]
-        res_room = [None, None]
-        inv_room = [sbuf([P, PACK, CHUNK], F32, "inv%d" % s) for s in range(2)]
-
-        def finish(c, woven):
-            quantise_x(1, c * UNITS, woven, CHUNK, "x1%d" % (c % 2))
-            for u in range(UNITS):
-                model_pass(c * UNITS + u, "x", 1, False, True)
-
-        res_bank = {}
-
-        def turned_residual(c):
-            for u in range(UNITS):
-                g = c * UNITS + u
-                negated = sbuf([P, H], F32, "negated", "neg%d" % (g % 3))
-                nc.scalar.activation(negated[:], model[g][:].rearrange("j t m -> j (t m)"), ACT.Copy, scale=-1.0)
-                res_bank[g] = bank([P, PACK, P], "res_bank", 4 + 2 * (c % 2) + u)
-                for term, src in enumerate((flat(laid[c])[:, u * H : (u + 1) * H], negated[:])):
-                    for t in range(PACK):
-                        nc.tensor.matmul(
-                            res_bank[g][:, t, :],
-                            lhsT=src[:, t * P : (t + 1) * P],
-                            rhs=ident[:],
-                            is_transpose=True,
-                            start=(term == 0 and t == 0),
-                            stop=(term == 1 and t == PACK - 1),
-                        )
-
-        def residual_chunk(c):
-            if c in (0, 1, 2):
-                return turned_residual(c)
-            for u in range(UNITS):
-                cols = slice(u * H, (u + 1) * H)
-                residual(flat(res_room[c % 2])[:, cols], flat(laid[c])[:, cols], c * UNITS + u, 0, P)
-
-        def lay_flux(c, u):
-            if c in (0, 1, 2):
-                turned = bank([P, PACK, P], "flux_bank", (4, 6, 6)[c] + u)
-                for t in range(PACK):
-                    nc.tensor.transpose(turned[:, t, :], flux_sb[c][:, t, u * P : (u + 1) * P], ident[:])
-                nc.scalar.copy(flat(laid[c])[:, u * H : (u + 1) * H], turned[:].rearrange("j t m -> j (t m)"))
-                return
-            weave_flux(flat(laid[c])[:, u * H : (u + 1) * H], c, u * P, P)
-
-        def squares(c):
-            res_sq = sbuf([P, PACK, CHUNK], F32, "res_sq", "sq%d" % (c % 2))
-            for u in range(UNITS):
-                nc.scalar.activation(res_sq[:, :, u * P : (u + 1) * P], res_bank[c * UNITS + u][:], ACT.Square)
-            return res_sq
-
-        def roots_of(c, res_sq):
-            inv_root = sbuf([P, PACK, CHUNK], F32, "inv_root", ("root0", "root1", "xf1")[c])
-            root(inv_root[:], res_sq)
-            return inv_root
-
-        def roots(c):
-            return roots_of(c, squares(c))
-
-        def inverses(c, inv_root):
-            for u in range(UNITS):
-                invert(flat(inv_room[c % 2])[:, u * H : (u + 1) * H], inv_root[:, :, u * P : (u + 1) * P])
-
-        def psi_chunk(c, tag):
-            psi_b = sbuf([P, CHUNK * PACK], BF16, "psi_b", tag)
-            for u in range(UNITS):
-                cols = slice(u * H, (u + 1) * H)
-                if c in (0, 1, 2):
-                    nc.vector.tensor_tensor(
-                        psi_b[:, cols].rearrange("m (j t) -> m j t", t=PACK),
-                        res_bank[c * UNITS + u][:].rearrange("m t j -> m j t"),
-                        flat(inv_room[c % 2])[:, cols].rearrange("m (j t) -> m j t", t=PACK),
-                        ALU.mult,
-                    )
-                else:
-                    nc.vector.tensor_tensor(
-                        psi_b[:, cols], flat(res_room[c % 2])[:, cols], flat(inv_room[c % 2])[:, cols], ALU.mult
-                    )
-            return psi_b
 
         j1, j2, j3 = CHUNK, 2 * CHUNK, 3 * CHUNK
-        backs = [4, 5, 6, 7]
 
-        def subtract_rows(a, j0, outside, tag):
-            rows = sbuf([P, PACK, CHUNK], F32, "rows", tag)
+        def room(tag, count=1):
+            picked = sbuf([P, count, CHUNK], F32, "picked", tag)
+            return [picked[:, k, :] for k in range(count)]
+
+        def picks(a, i, rooms):
+            for c in range(2):
+                pick(rooms[c], a, i, c * CHUNK, CHUNK)
+
+        def subtractions(rows, a, i, rooms):
+            for c in range(2):
+                subtract(rows[c][:, i, :], a, i, c * CHUNK, CHUNK, rooms[c])
+
+        def plane_arrives(rows, a, i, rooms):
+            picks(a, i, rooms)
+            subtractions(rows, a, i, rooms)
+
+        rows_0 = [sbuf([P, PACK, CHUNK], F32, "rows_0", "xa%d" % c) for c in range(2)]
+        rows_1 = [sbuf([P, PACK, CHUNK], F32, "rows_1", "xc%d" % c) for c in range(2)]
+        ahead = []
+
+        def pick_ahead(i, tag):
+            both = sbuf([P, 2, CHUNK], F32, "ahead", tag)
+            pick(flat(both[:]), 0, i, HALF, HALF)
+            ahead.append(both)
+
+        for i, tags in enumerate((("slot_a", "ahead1"), ("slot_a", "ahead2"), ("slot_u", "slot_b"))):
+            rooms = room(tags[0]) + room(tags[1])
+            picks(0, i, rooms)
+            pick_ahead(i, "ahead%d" % i)
+            subtractions(rows_0, 0, i, rooms)
+        prepare_wb(0, "slot_u", "wt_b0")
+        plane_arrives(rows_0, 0, 3, room("slot_w") + room("slot_v"))
+        woven = [weave(nc.scalar.copy, [rows_0[c][:]], CHUNK, "xb_a%d" % c) for c in range(2)]
+        w4_w, w4_sc = reorder_w4("slot_w")
+        prepare_wb(1, "slot_v", "wt_b1")
+        plane_arrives(rows_1, 1, 0, room("slot_a") + room("w4_sc_raw"))
+        quantise_x(0, 0, woven[0], CHUNK, "x00", "xa1", "slot_a")
+        quantise_x(0, j1, woven[1], CHUNK, "x01", "xa0", "w4_sc_raw")
+        gather_words(0, 0, HALF, "slot_b")
+        model_0 = [bank([P, 2, CHUNK], "model", b) for b in (0, 1)]
+        model_1 = [bank([P, H], "model", b) for b in (2, 3)]
+        for k, kind in enumerate(("x", "table")):
+            direct_pass(model_0, kind, 0, 0, CHUNK, k == 0, False)
+            turned_pass(model_1, kind, 0, j1, k == 0, False)
+        load_flux(1, "xa1")
+        load_flux(0, "xa0")
+        load_flux(2, "slot_b")
+        for i in (1, 2):
+            plane_arrives(rows_1, 1, i, room("xb_a0") + room("xb_a1"))
+        gather_words(1, 0, HALF, "xb_a0")
+        direct_pass(model_0, "table", 1, 0, CHUNK, False, False)
+        turned_pass(model_1, "table", 1, j1, False, False)
+        load_flux(3, "xb_a0")
+        plane_arrives(rows_1, 1, 3, room("xb_a1") + room("slot_a"))
+        woven_0 = weave(nc.scalar.copy, [rows_1[0][:]], CHUNK, "xb0")
+        woven_1 = weave(nc.scalar.copy, [rows_1[1][:]], CHUNK, "xb1")
+        pick_ahead(3, "xb_a1")
+        quantise_x(1, 0, woven_0, CHUNK, "x10", "wt0_codes")
+        direct_pass(model_0, "x", 1, 0, CHUNK, False, True)
+        spare = room("xc0")
+        pick(spare[0], 1, 0, j2, CHUNK)
+        quantise_x(1, j1, woven_1, CHUNK, "x11")
+        turned_pass(model_1, "x", 1, j1, False, True)
+        laid_1 = lay_flux(1, (6, 7), "xc1")
+        res_0 = direct_residual(model_0, flux_sb[0], CHUNK, "res0")
+        sq_0 = square_rows(pairs_of(res_0), CHUNK, "sq0")
+        res_1 = turned_residual(model_1, laid_1, (4, 5))
+        outside = [both[:, 0, :] for both in ahead]
+        rows = sbuf([P, PACK, CHUNK], F32, "rows", "xa0")
+        for i in range(PACK):
+            subtract(rows[:, i, :], 0, i, j2, CHUNK, outside[i])
+        wt_q[0] = quantise("wt0", wt_b[0][:], H * PACK)
+        wt_q[1] = quantise("wt1", wt_b[1][:], H * PACK, "xc1")
+        root_0 = roots(sq_0, CHUNK, ("root0a", "root0b"))
+        inv_0 = square_rows(root_0, CHUNK, "inv0")
+        sq_1 = square_banks(res_1, "sq1")
+        laid_2 = lay_flux(2, (6, 7), "sq0")
+        woven = weave(nc.scalar.copy, [rows[:]], CHUNK, "root0a")
+        outside = spare + outside[0:3]
+        for i in range(1, PACK):
+            pick(outside[i], 1, i, j2, CHUNK)
+        psi_0 = influence([(res_0[:], inv_0[:])], CHUNK, "psi_b0")
+        gather_words(0, HALF, HALF, "root0b")
+        psi_q0 = quantise("psi0", psi_0[:], CHUNK * PACK)
+        quantise_x(0, j2, woven, CHUNK, "x02")
+        model_2 = [bank([P, H], "model", b) for b in (2, 3)]
+        turned_pass(model_2, "table", 0, j2, True, False)
+        turned_pass(model_2, "x", 0, j2, False, False)
+        rows = sbuf([P, PACK, CHUNK], F32, "rows", "res0")
+        for i in range(PACK):
+            subtract(rows[:, i, :], 1, i, j2, CHUNK, outside[i])
+        root_1 = roots(sq_1, CHUNK, ("root1a", "root1b"))
+        inv_1 = square_rows(root_1, CHUNK, "inv1")
+        second_product(psi_q0, 0, CHUNK, 0, "sq1", [0, 1])
+        woven = weave(nc.scalar.copy, [rows[:]], CHUNK, "root1a")
+        second_product(psi_q0, 0, CHUNK, 1, "big0", [6, 7])
+        psi_1 = influence([(res_1[u][:], inv_1[:, :, u * P : (u + 1) * P]) for u in range(2)], P, "psi_b1")
+        gather_words(1, j2, CHUNK, "root1b")
+        psi_q1 = quantise("psi1", psi_1[:], CHUNK * PACK)
+        turned_pass(model_2, "table", 1, j2, False, False)
+        quantise_x(1, j2, woven, CHUNK, "x11")
+        turned_pass(model_2, "x", 1, j2, False, True)
+        outside = [both[:, 1, :] for both in ahead]
+        gather_words(1, j3, CHUNK, "res0")
+        rows = sbuf([P, PACK, CHUNK], F32, "rows", "root1a")
+        for i in range(PACK):
+            subtract(rows[:, i, :], 0, i, j3, CHUNK, outside[i])
+        res_2 = turned_residual(model_2, laid_2, (6, 7))
+        units = (j3, j3 + P)
+        sq_2 = square_banks(res_2, "sq0")
+        woven = [weave(nc.scalar.copy, [rows[:, :, u * P : (u + 1) * P]], P, "neg%d" % u) for u in range(2)]
+        root_2 = roots(sq_2, CHUNK, ("root0a", "root1b"))
+        inv_2 = square_units(root_2, ("inv0", "mid1"))
+        second_product(psi_q1, j1, CHUNK, 0, "big1", [0, 1])
+        second_product(psi_q1, j1, CHUNK, 1, "wt_b0", [4, 5])
+        models = [bank([P, PACK, P], "model", b) for b in (2, 3)]
+
+        def unit_picks(u):
             for i in range(PACK):
-                subtract(rows[:, i, :], a, i, j0, CHUNK, outside[i])
+                pick(outside[i][:, u * P : (u + 1) * P], 1, i, units[u], P)
+
+        def unit_rows(u, tag):
+            rows = sbuf([P, PACK, P], F32, "rows", tag)
+            for i in range(PACK):
+                subtract(rows[:, i, :], 1, i, units[u], P, outside[i][:, u * P : (u + 1) * P])
             return rows
 
-        for c in (2, 0, 1):
-            lay_flux(c, 0)
-            lay_flux(c, 1)
-        woven_0 = weave(nc.scalar.copy, xf[0][:], CHUNK, "xb0")
-        woven_1 = weave(nc.scalar.copy, xf[1][:], CHUNK, "xb1")
-        outside = [xf[0][:, 1, :], xf[0][:, 2, :], o_1[:, 2, :], xf[0][:, 0, :]]
-        pick(outside[2], 1, 2, j2, CHUNK)
-        finish(0, woven_0)
-        pick(outside[3], 1, 3, j2, CHUNK)
-        pick(outside[0], 1, 0, j2, CHUNK)
-        finish(1, woven_1)
-        pick(outside[1], 1, 1, j2, CHUNK)
-        residual_chunk(0)
-        sq_0 = squares(0)
-        residual_chunk(1)
-        for i in range(PACK):
-            subtract(xf[1][:, i, :], 1, i, j2, CHUNK, outside[i])
-        root_0 = roots_of(0, sq_0)
-        words_2 = sbuf([P, PASSES, CHUNK], U32, "words_2", "o_1")
-        gather_words(0, j2, CHUNK, words_2[:, 0, :])
-        woven = weave(nc.scalar.copy, xf[1][:], CHUNK, "xb0")
-        gather_words(1, j2, CHUNK, words_2[:, 1, :])
-        outside = [xf[0][:, 2, :], xf[0][:, 0, :], xf[1][:, 0, :], xf[1][:, 1, :]]
-        quantise_x(1, 4, woven, CHUNK, "x10")
-        for g in (4, 5):
-            open_model(g, g - 4, [("x", 0), ("x", 1), ("table", 0)])
-            model_pass(g, "table", 1, False, True)
-        for i in range(PACK):
-            pick(outside[i], 0, i, j3, CHUNK)
-        wt_codes = sbuf([P, K], U32, "wt_codes", "x11_codes")
-        nc.vector.quantize_mx(out=wt_codes[:].bitcast(FP8X4), scales=wt_sc[:], in_=wt_both[:])
-        sq_1 = squares(1)
-        inverses(0, root_0)
-        root_1 = roots_of(1, sq_1)
-        psi_0 = psi_chunk(0, "psi_b")
-        rows = sbuf([P, PACK, CHUNK], F32, "rows", "root0")
-        subtract(rows[:, 0, :], 0, 0, j3, CHUNK, outside[0])
-        psi_q0 = quantise("psi0", psi_0[:], CHUNK * PACK)
-        for i in range(1, PACK):
-            subtract(rows[:, i, :], 0, i, j3, CHUNK, outside[i])
-        inverses(1, root_1)
-        residual_chunk(2)
-        outside_4 = [inv_room[0][:, 0, :], inv_room[0][:, 2, :], inv_room[1][:, 0, :], inv_room[1][:, 2, :]]
-        pick(outside_4[0], 1, 0, j3, CHUNK)
-        woven = weave(nc.scalar.copy, rows[:], CHUNK, "root1")
-        pick(outside_4[1], 1, 1, j3, CHUNK)
-        quantise_x(0, 6, woven, CHUNK, "x0b")
-        root_2 = roots(2)
-        inv_room[0] = sbuf([P, PACK, CHUNK], F32, "inv_late", "o_1")
-        inverses(2, root_2)
-        second_product(psi_q0, 0, CHUNK, ["mid2", "oe"], [2, 3, 0, 1], ())
-        psi_1 = psi_chunk(1, "psi_b")
-        pick(outside_4[2], 1, 2, j3, CHUNK)
-        psi_q1 = quantise("psi1", psi_1[:], CHUNK * PACK)
-        pick(outside_4[3], 1, 3, j3, CHUNK)
-        words_3 = sbuf([P, PASSES, CHUNK], U32, "words_3", "psi_b")
-        for a in range(PASSES):
-            gather_words(a, j3, CHUNK, words_3[:, a, :])
-        lay_flux(3, 0)
-        lay_flux(3, 1)
-        for g in (6, 7):
-            open_model(g, g - 4, [("x", 0), ("table", 0), ("table", 1)])
-        second_product(psi_q1, CHUNK, CHUNK, ["flux0", "flux1"], [6, 7, 0, 1], ())
-        rows = sbuf([P, UNITS, PACK, P], F32, "rows", "xf1")
-        for i in range(PACK):
-            subtract(rows[:, 0, i, :], 1, i, j3, P, outside_4[i][:, 0:P])
-        subtract(rows[:, 1, 0, :], 1, 0, j3 + P, P, outside_4[0][:, P:])
-        woven_a = weave(nc.vector.tensor_copy, rows[:, 0, :, :], P, "xb_a")
-        subtract(rows[:, 1, 1, :], 1, 1, j3 + P, P, outside_4[1][:, P:])
-        quantise_x(1, 6, woven_a, P, "x10")
-        model_pass(6, "x", 1, False, True)
-        half = P // 2
-        res = flat(sbuf([P, PACK, CHUNK], F32, "res_room", "sq1"))
-        subtract(rows[:, 1, 2, :], 1, 2, j3 + P, P, outside_4[2][:, P:])
-        subtract(rows[:, 1, 3, :], 1, 3, j3 + P, P, outside_4[3][:, P:])
-        residual(res[:, 0:H], flat(laid[3])[:, 0:H], 6, 0, P)
-        rows_b = rows[:, 1, :, :]
+        def close_unit(u, rows, tag, name):
+            quantise_x(1, units[u], weave(nc.vector.tensor_copy, [rows[:]], P, tag), P, name)
+            direct_pass(models[u : u + 1], "x", 1, units[u], P, False, True)
 
         def invert_unit(u, tags):
-            res_sq = sbuf([P, PACK, P], F32, "res_sq", tags[0])
-            inv_root = sbuf([P, PACK, P], F32, "inv_root", tags[1])
-            inv = sbuf([P, H], F32, "inv", tags[2])
-            for o in (0, half):
-                square(res_sq[:, :, o : o + half], res[:, u * H + o * PACK : u * H + (o + half) * PACK])
-            for o in (0, half):
-                root(inv_root[:, :, o : o + half], res_sq[:, :, o : o + half])
-            for o in (0, half):
-                invert(inv[:, o * PACK : (o + half) * PACK], inv_root[:, :, o : o + half])
-            return inv
+            res = direct_residual(models[u : u + 1], flux_sb[3][:, :, u * P : (u + 1) * P], P, tags[0])
+            return res, square_rows(roots(square_rows(pairs_of(res), P, tags[1]), P, tags[2:4]), P, tags[4])
 
-        def psi_unit(u, inv, tag, piece):
-            psi_b = sbuf([P, H], BF16, "psi_b", tag)
-            for o in range(0, H, piece):
-                cols = slice(o, o + piece)
-                nc.vector.tensor_tensor(psi_b[:, cols], res[:, u * H : (u + 1) * H][:, cols], inv[:, cols], ALU.mult)
-            return psi_b
-
-        inv_a = invert_unit(0, ("sq0", "root0", "xf0"))
-        woven_b = weave(nc.vector.tensor_copy, rows_b, P, "xb_b")
-        psi_2 = psi_chunk(2, "xb1")
-        quantise_x(1, 7, woven_b, P, "x0a")
-        model_pass(7, "x", 1, False, True)
+        for a in range(PASSES):
+            for u in range(2):
+                direct_pass(models[u : u + 1], "table", a, units[u], P, a == 0, False)
+        unit_picks(0)
+        quantise_x(0, units[0], woven[0], P, "x06")
+        direct_pass(models[0:1], "x", 0, units[0], P, False, False)
+        rows_a = unit_rows(0, "neg0")
+        quantise_x(0, units[1], woven[1], P, "x07")
+        close_unit(0, rows_a, "xb1", "x11")
+        direct_pass(models[1:2], "x", 0, units[1], P, False, False)
+        second = sbuf([P, PACK, P], F32, "second", "neg1")
+        outside = [second[:, i, :] for i in range(PACK)]
+        for i in range(PACK):
+            pick(outside[i], 1, i, units[1], P)
+        psi_2 = influence([(res_2[u][:], inv_2[u][:]) for u in range(2)], P, "psi_b1")
+        res_a, inv_a = invert_unit(0, ("inv0", "xc0", "xa1", "xa0", "wt_b1"))
+        rows_b = sbuf([P, PACK, P], F32, "rows_b", "mid1")
+        subtract(rows_b[:, 0, :], 1, 0, units[1], P, outside[0])
         psi_q2 = quantise("psi0", psi_2[:], CHUNK * PACK)
-        for o in (0, half):
-            cols = slice(H + o * PACK, H + (o + half) * PACK)
-            residual(res[:, cols], flat(laid[3])[:, cols], 7, o, half)
-        psi_qa = quantise("tq0", psi_unit(0, inv_a, "xb0", H)[:], H)
-        inv_b = invert_unit(1, ("neg0", "mid0", "neg1"))
-        psi_qb = quantise("tq1", psi_unit(1, inv_b, "xb_a", H // 2)[:], H)
-        second_product(psi_q2, j2, CHUNK, ["mid2", "oe"], [4, 5, 6, 7], (0, 1, 2, 3), 2)
-        second_product(psi_qa, j3, P, ["mid1", "res0"], [2, 0], ())
-        second_product(psi_qb, j3 + P, P, ["big0", "big1"], [3, 1, 4, 5], (0, 2), 4)
+        for i in range(1, PACK):
+            subtract(rows_b[:, i, :], 1, i, units[1], P, outside[i])
+        second_product(psi_q2, j2, CHUNK, 0, "inv1", [0, 1], (), 2)
+        close_unit(1, rows_b, "xb0", "x02")
+        res_b, inv_b = invert_unit(1, ("mid0", "neg0", "slot_a", "slot_b", "root1a"))
+        psi_qa = quantise("tq0", influence([(res_a[:], inv_a[:])], P, "psi_b0")[:], H)
+        psi_qb = quantise("tq1", influence([(res_b[:], inv_b[:])], P, "xb_a1")[:], H)
+        second_product(psi_q2, j2, CHUNK, 1, "big0", [4, 5], (0, 1), 2)
+        second_product(psi_qa, j3, P, 0, "sq0", [6], (0,))
+        second_product(psi_qa, j3, P, 1, "sq1", [7])
+        second_product(psi_qb, j3 + P, P, 0, "big1", [2, 0], (0,), 2)
+        second_product(psi_qb, j3 + P, P, 1, "wt_b0", [3, 1], (0,), 2)

@@ -61,11 +61,13 @@ def tile_list_transit_cauchy_step_kernel(
                 out=wb_raw[a][:], in_=wb[a * P * PACK : (a + 1) * P * PACK, :].rearrange("(p i) r -> p (i r)", i=PACK)
             )
 
-        def load_flux(c, tag):
-            flux_sb[c] = sbuf([P, PACK, CHUNK], F32, "flux_sb", tag)
+        def load_flux(c0, count, tag):
+            rows = sbuf([P, PACK, count * CHUNK], F32, "flux_sb", tag)
             nc.sync.dma_start(
-                out=flux_sb[c][:], in_=flux[:, c * CHUNK : (c + 1) * CHUNK].rearrange("(m t) j -> m t j", t=PACK)
+                out=rows[:], in_=flux[:, c0 * CHUNK : (c0 + count) * CHUNK].rearrange("(m t) j -> m t j", t=PACK)
             )
+            for k in range(count):
+                flux_sb[c0 + k] = rows[:, :, k * CHUNK : (k + 1) * CHUNK]
 
         def load_tab(a):
             tab_w[a] = keep.tile([P, T], I32, name="tab_w%d" % a, align_bytes=64)
@@ -123,6 +125,7 @@ def tile_list_transit_cauchy_step_kernel(
         move_scale_rows(1)
         load_plane(1, 1)
         load_plane(1, 2)
+        load_flux(0, 2, "big0")
         load_tab(1)
         load_plane(1, 3)
         var_t = keep.tile([P, PACK], F32, name="var_t")
@@ -137,6 +140,14 @@ def tile_list_transit_cauchy_step_kernel(
                     woven[:, k * n * PACK : (k + 1) * n * PACK].rearrange("p (c e t) -> p c t e", e=RUN, t=PACK),
                     rows.rearrange("p t (c e) -> p c t e", e=RUN),
                 )
+            return woven
+
+        def pool_copy(dst, src):
+            nc.gpsimd.tensor_scalar(dst, src, 1.0, 0.0, ALU.mult, ALU.add)
+
+        def pool_weave(rows, n, tag):
+            woven = sbuf([P, n * PACK], BF16, "xb", tag)
+            pool_copy(woven[:].rearrange("p (j t) -> p j t", t=PACK), rows.rearrange("p t j -> p j t"))
             return woven
 
         def pick(dst, a, i, j0, n):
@@ -164,9 +175,10 @@ def tile_list_transit_cauchy_step_kernel(
             for o in range(0, n, P):
                 x_q[a, j0 + o] = (codes[:, o:n], scales[:, o:n])
 
-        wb_q, wt_b, wt_q = {}, {}, {}
+        wb_q = {}
+        wt_both = sbuf([P, PASSES * H * PACK], BF16, "wt_both")
 
-        def prepare_wb(a, scale_tag, turned_tag):
+        def prepare_wb(a, scale_tag):
             wb_b = sbuf([P, H * PACK], BF16, "wb_b", "mid%d" % a)
             nc.scalar.copy(
                 wb_b[:].rearrange("p (t m i) -> p m t i", t=PACK, i=PACK),
@@ -174,13 +186,13 @@ def tile_list_transit_cauchy_step_kernel(
             )
             wb_q[a] = quantise("wb%d" % a, wb_b[:], H * PACK, None, scale_tag)
             pairs = wb_b[:].bitcast(F32)
-            wt_b[a] = sbuf([P, H * PACK], BF16, "wt_b", turned_tag)
+            wt_b = wt_both[:, a * H * PACK : (a + 1) * H * PACK]
             for u in range(2):
                 turned = bank([P, PACK, P], "wt_bank", 4 + 2 * a + u)
                 for t in range(PACK):
                     nc.tensor.transpose(turned[:, t, :], pairs[:, 2 * P * t + u : 2 * P * (t + 1) : 2], ident[:])
                 nc.scalar.copy(
-                    wt_b[a][:, u * 2 * H : (u + 1) * 2 * H].rearrange("m (e p t) -> m e p t", e=2, t=PACK),
+                    wt_b[:, u * 2 * H : (u + 1) * 2 * H].rearrange("m (e p t) -> m e p t", e=2, t=PACK),
                     flat(turned[:]).bitcast(BF16).rearrange("m (t p e) -> m e p t", t=PACK, e=2),
                 )
 
@@ -242,10 +254,10 @@ def tile_list_transit_cauchy_step_kernel(
                 nc.scalar.copy(laid[:, u, :], flat(turned[:]))
             return laid
 
-        def turned_residual(models, laid, banks):
+        def turned_residual(models, laid, banks, first=0):
             res_banks = []
             for u, model in enumerate(models):
-                negated = sbuf([P, H], F32, "negated", "neg%d" % u)
+                negated = sbuf([P, H], F32, "negated", "neg%d" % (first + u))
                 nc.scalar.activation(negated[:], model[:], ACT.Copy, scale=-1.0)
                 res = bank([P, PACK, P], "res_bank", banks[u])
                 for term, src in enumerate((laid[:, u, :], negated[:])):
@@ -314,11 +326,11 @@ def tile_list_transit_cauchy_step_kernel(
 
         def second_product(psi_q, j0, n, a, tag, banks, on_vector=(), rows_a_store=PACK):
             psi_codes, psi_sc = psi_q
-            wt_codes, wt_sc = wt_q[a]
+            wt_codes, wt_sc = wt_q
             per_bank = PACK // len(banks)
             staged = sbuf([P, PACK, n], F32, "staged", tag)
             for k, b in enumerate(banks):
-                first = k * per_bank
+                first = a * PACK + k * per_bank
                 back = bank([P, per_bank, n], "back", b)
                 for e in range(per_bank):
                     cols = slice((first + e) * P, (first + e + 1) * P)
@@ -375,102 +387,99 @@ def tile_list_transit_cauchy_step_kernel(
             picks(0, i, rooms)
             pick_ahead(i, "ahead%d" % i)
             subtractions(rows_0, 0, i, rooms)
-        prepare_wb(0, "slot_u", "wt_b0")
+        prepare_wb(0, "slot_u")
         plane_arrives(rows_0, 0, 3, room("slot_w") + room("slot_v"))
         woven = [weave(nc.scalar.copy, [rows_0[c][:]], CHUNK, "xb_a%d" % c) for c in range(2)]
+        prepare_wb(1, "slot_v")
         w4_w, w4_sc = reorder_w4("slot_w")
-        prepare_wb(1, "slot_v", "wt_b1")
         plane_arrives(rows_1, 1, 0, room("slot_a") + room("w4_sc_raw"))
         quantise_x(0, 0, woven[0], CHUNK, "x00", "xa1", "slot_a")
         quantise_x(0, j1, woven[1], CHUNK, "x01", "xa0", "w4_sc_raw")
         gather_words(0, 0, HALF, "slot_b")
-        model_0 = [bank([P, 2, CHUNK], "model", b) for b in (0, 1)]
+        model_0 = [bank([P, H], "model", b) for b in (0, 1)]
         model_1 = [bank([P, H], "model", b) for b in (2, 3)]
         for k, kind in enumerate(("x", "table")):
-            direct_pass(model_0, kind, 0, 0, CHUNK, k == 0, False)
+            turned_pass(model_0, kind, 0, 0, k == 0, False)
             turned_pass(model_1, kind, 0, j1, k == 0, False)
-        load_flux(1, "xa1")
-        load_flux(0, "xa0")
-        load_flux(2, "slot_b")
+        load_flux(2, 1, "slot_b")
         for i in (1, 2):
             plane_arrives(rows_1, 1, i, room("xb_a0") + room("xb_a1"))
-        gather_words(1, 0, HALF, "xb_a0")
-        direct_pass(model_0, "table", 1, 0, CHUNK, False, False)
+        pick_ahead(3, "xb_a0")
+        wt_q = quantise("wt", wt_both[:], PASSES * H * PACK, "xa1")
+        gather_words(1, 0, HALF, "xb_a1")
+        turned_pass(model_0, "table", 1, 0, False, False)
         turned_pass(model_1, "table", 1, j1, False, False)
-        load_flux(3, "xb_a0")
-        plane_arrives(rows_1, 1, 3, room("xb_a1") + room("slot_a"))
+        load_flux(3, 1, "xb_a1")
+        laid_0 = lay_flux(0, (4, 5), "mid0")
+        laid_1 = lay_flux(1, (6, 7), "mid1")
+        plane_arrives(rows_1, 1, 3, room("wt_both", 2))
         woven_0 = weave(nc.scalar.copy, [rows_1[0][:]], CHUNK, "xb0")
-        woven_1 = weave(nc.scalar.copy, [rows_1[1][:]], CHUNK, "xb1")
-        pick_ahead(3, "xb_a1")
-        quantise_x(1, 0, woven_0, CHUNK, "x10", "wt0_codes")
-        direct_pass(model_0, "x", 1, 0, CHUNK, False, True)
-        spare = room("xc0")
-        pick(spare[0], 1, 0, j2, CHUNK)
+        woven_1 = pool_weave(rows_1[1][:], CHUNK, "xb1")
+        gather_words(0, HALF, HALF, "wt_both")
+        quantise_x(1, 0, woven_0, CHUNK, "x10")
+        turned_pass(model_0, "x", 1, 0, False, True)
         quantise_x(1, j1, woven_1, CHUNK, "x11")
         turned_pass(model_1, "x", 1, j1, False, True)
-        laid_1 = lay_flux(1, (6, 7), "xc1")
-        res_0 = direct_residual(model_0, flux_sb[0], CHUNK, "res0")
-        sq_0 = square_rows(pairs_of(res_0), CHUNK, "sq0")
-        res_1 = turned_residual(model_1, laid_1, (4, 5))
+        gather_words(1, j2, CHUNK, "xb0")
+        res_0 = turned_residual(model_0, laid_0, (4, 5))
+        res_1 = turned_residual(model_1, laid_1, (6, 7), 2)
+        sq_0 = square_banks(res_0, "sq0")
         outside = [both[:, 0, :] for both in ahead]
-        rows = sbuf([P, PACK, CHUNK], F32, "rows", "xa0")
+        rows = sbuf([P, PACK, CHUNK], F32, "rows", "xb1")
         for i in range(PACK):
             subtract(rows[:, i, :], 0, i, j2, CHUNK, outside[i])
-        wt_q[0] = quantise("wt0", wt_b[0][:], H * PACK)
-        wt_q[1] = quantise("wt1", wt_b[1][:], H * PACK, "xc1")
+        woven = pool_weave(rows[:], CHUNK, "xg0")
         root_0 = roots(sq_0, CHUNK, ("root0a", "root0b"))
-        inv_0 = square_rows(root_0, CHUNK, "inv0")
+        inv_0 = square_units(root_0, ("inv0", "res0"))
         sq_1 = square_banks(res_1, "sq1")
-        laid_2 = lay_flux(2, (6, 7), "sq0")
-        woven = weave(nc.scalar.copy, [rows[:]], CHUNK, "root0a")
-        outside = spare + outside[0:3]
-        for i in range(1, PACK):
+        root_1 = roots(sq_1, CHUNK, ("root1a", "root1b"))
+        inv_1 = square_units(root_1, ("inv1", "xc1"))
+        laid_2 = lay_flux(2, (2, 3), "sq0")
+        for i in range(PACK):
             pick(outside[i], 1, i, j2, CHUNK)
-        psi_0 = influence([(res_0[:], inv_0[:])], CHUNK, "psi_b0")
-        gather_words(0, HALF, HALF, "root0b")
-        psi_q0 = quantise("psi0", psi_0[:], CHUNK * PACK)
         quantise_x(0, j2, woven, CHUNK, "x02")
-        model_2 = [bank([P, H], "model", b) for b in (2, 3)]
+        model_2 = [bank([P, H], "model", b) for b in (0, 1)]
         turned_pass(model_2, "table", 0, j2, True, False)
+        turned_pass(model_2, "table", 1, j2, False, False)
         turned_pass(model_2, "x", 0, j2, False, False)
-        rows = sbuf([P, PACK, CHUNK], F32, "rows", "res0")
+        rows = sbuf([P, PACK, CHUNK], F32, "rows", "xb1")
         for i in range(PACK):
             subtract(rows[:, i, :], 1, i, j2, CHUNK, outside[i])
-        root_1 = roots(sq_1, CHUNK, ("root1a", "root1b"))
-        inv_1 = square_rows(root_1, CHUNK, "inv1")
-        second_product(psi_q0, 0, CHUNK, 0, "sq1", [0, 1])
-        woven = weave(nc.scalar.copy, [rows[:]], CHUNK, "root1a")
-        second_product(psi_q0, 0, CHUNK, 1, "big0", [6, 7])
-        psi_1 = influence([(res_1[u][:], inv_1[:, :, u * P : (u + 1) * P]) for u in range(2)], P, "psi_b1")
-        gather_words(1, j2, CHUNK, "root1b")
-        psi_q1 = quantise("psi1", psi_1[:], CHUNK * PACK)
-        turned_pass(model_2, "table", 1, j2, False, False)
-        quantise_x(1, j2, woven, CHUNK, "x11")
+        woven = pool_weave(rows[:], CHUNK, "xg1")
+        psi_0 = influence([(res_0[u][:], inv_0[u][:]) for u in range(2)], P, "psi_b0")
+        gather_words(1, j3, CHUNK, "root0b")
+        quantise_x(1, j2, woven, CHUNK, "x11", None, "inv0")
         turned_pass(model_2, "x", 1, j2, False, True)
-        outside = [both[:, 1, :] for both in ahead]
-        gather_words(1, j3, CHUNK, "res0")
-        rows = sbuf([P, PACK, CHUNK], F32, "rows", "root1a")
-        for i in range(PACK):
-            subtract(rows[:, i, :], 0, i, j3, CHUNK, outside[i])
+        psi_q0 = quantise("psi0", psi_0[:], CHUNK * PACK)
+        psi_1 = influence([(res_1[u][:], inv_1[u][:]) for u in range(2)], P, "psi_b1")
+        psi_q1 = quantise("psi1", psi_1[:], CHUNK * PACK)
+        second_product(psi_q0, 0, CHUNK, 0, "root1a", [2, 3])
         res_2 = turned_residual(model_2, laid_2, (6, 7))
         units = (j3, j3 + P)
+        outside = [both[:, 1, :] for both in ahead]
+        rows = sbuf([P, PACK, CHUNK], F32, "rows", "inv1")
+        for i in range(PACK):
+            subtract(rows[:, i, :], 0, i, j3, CHUNK, outside[i])
+        woven = pool_weave(rows[:], CHUNK, "xg0")
         sq_2 = square_banks(res_2, "sq0")
-        woven = [weave(nc.scalar.copy, [rows[:, :, u * P : (u + 1) * P]], P, "neg%d" % u) for u in range(2)]
-        root_2 = roots(sq_2, CHUNK, ("root0a", "root1b"))
-        inv_2 = square_units(root_2, ("inv0", "mid1"))
-        second_product(psi_q1, j1, CHUNK, 0, "big1", [0, 1])
-        second_product(psi_q1, j1, CHUNK, 1, "wt_b0", [4, 5])
-        models = [bank([P, PACK, P], "model", b) for b in (2, 3)]
+        root_2 = roots(sq_2, CHUNK, ("root0a", "sq1"))
+        inv_2 = square_units(root_2, ("res0", "mid1"))
+        second_product(psi_q0, 0, CHUNK, 1, "big0", [4, 5])
+        second_product(psi_q1, j1, CHUNK, 0, "big1", [2, 3])
+        second_product(psi_q1, j1, CHUNK, 1, "mid0", [4, 5])
+        models = [bank([P, PACK, P], "model", b) for b in (0, 1)]
+        for a in range(PASSES):
+            for u in range(2):
+                direct_pass(models[u : u + 1], "table", a, units[u], P, a == 0, False)
+        for i in range(PACK):
+            pick(outside[i], 1, i, j3, CHUNK)
+        quantise_x(0, j3, woven, CHUNK, "x02")
+        for u in range(2):
+            direct_pass(models[u : u + 1], "x", 0, units[u], P, False, False)
 
-        def unit_picks(u):
-            for i in range(PACK):
-                pick(outside[i][:, u * P : (u + 1) * P], 1, i, units[u], P)
-
-        def unit_rows(u, tag):
-            rows = sbuf([P, PACK, P], F32, "rows", tag)
-            for i in range(PACK):
+        def unit_rows(u, rows, planes_now):
+            for i in planes_now:
                 subtract(rows[:, i, :], 1, i, units[u], P, outside[i][:, u * P : (u + 1) * P])
-            return rows
 
         def close_unit(u, rows, tag, name):
             quantise_x(1, units[u], weave(nc.vector.tensor_copy, [rows[:]], P, tag), P, name)
@@ -480,34 +489,21 @@ def tile_list_transit_cauchy_step_kernel(
             res = direct_residual(models[u : u + 1], flux_sb[3][:, :, u * P : (u + 1) * P], P, tags[0])
             return res, square_rows(roots(square_rows(pairs_of(res), P, tags[1]), P, tags[2:4]), P, tags[4])
 
-        for a in range(PASSES):
-            for u in range(2):
-                direct_pass(models[u : u + 1], "table", a, units[u], P, a == 0, False)
-        unit_picks(0)
-        quantise_x(0, units[0], woven[0], P, "x06")
-        direct_pass(models[0:1], "x", 0, units[0], P, False, False)
-        rows_a = unit_rows(0, "neg0")
-        quantise_x(0, units[1], woven[1], P, "x07")
-        close_unit(0, rows_a, "xb1", "x11")
-        direct_pass(models[1:2], "x", 0, units[1], P, False, False)
-        second = sbuf([P, PACK, P], F32, "second", "neg1")
-        outside = [second[:, i, :] for i in range(PACK)]
-        for i in range(PACK):
-            pick(outside[i], 1, i, units[1], P)
+        rows_a = sbuf([P, PACK, P], F32, "rows_a", "inv1")
+        unit_rows(0, rows_a, range(PACK))
         psi_2 = influence([(res_2[u][:], inv_2[u][:]) for u in range(2)], P, "psi_b1")
-        res_a, inv_a = invert_unit(0, ("inv0", "xc0", "xa1", "xa0", "wt_b1"))
-        rows_b = sbuf([P, PACK, P], F32, "rows_b", "mid1")
-        subtract(rows_b[:, 0, :], 1, 0, units[1], P, outside[0])
+        close_unit(0, rows_a, "res0", "x11")
         psi_q2 = quantise("psi0", psi_2[:], CHUNK * PACK)
-        for i in range(1, PACK):
-            subtract(rows_b[:, i, :], 1, i, units[1], P, outside[i])
-        second_product(psi_q2, j2, CHUNK, 0, "inv1", [0, 1], (), 2)
-        close_unit(1, rows_b, "xb0", "x02")
-        res_b, inv_b = invert_unit(1, ("mid0", "neg0", "slot_a", "slot_b", "root1a"))
+        rows_b = sbuf([P, PACK, P], F32, "rows_b", "mid1")
+        unit_rows(1, rows_b, range(PACK))
+        second_product(psi_q2, j2, CHUNK, 0, "sq0", [2, 3], (), 2)
+        res_a, inv_a = invert_unit(0, ("neg0", "xc0", "neg2", "neg3", "slot_a"))
+        close_unit(1, rows_b, "neg1", "x10")
+        res_b, inv_b = invert_unit(1, ("xb1", "xc1", "xb0", "slot_b", "xg1"))
         psi_qa = quantise("tq0", influence([(res_a[:], inv_a[:])], P, "psi_b0")[:], H)
-        psi_qb = quantise("tq1", influence([(res_b[:], inv_b[:])], P, "xb_a1")[:], H)
+        psi_qb = quantise("tq1", influence([(res_b[:], inv_b[:])], P, "xb_a0")[:], H)
         second_product(psi_q2, j2, CHUNK, 1, "big0", [4, 5], (0, 1), 2)
-        second_product(psi_qa, j3, P, 0, "sq0", [6], (0,))
+        second_product(psi_qa, j3, P, 0, "root1a", [6], (0,))
         second_product(psi_qa, j3, P, 1, "sq1", [7])
-        second_product(psi_qb, j3 + P, P, 0, "big1", [2, 0], (0,), 2)
-        second_product(psi_qb, j3 + P, P, 1, "wt_b0", [3, 1], (0,), 2)
+        second_product(psi_qb, j3 + P, P, 0, "big1", [0, 2], (0,), 2)
+        second_product(psi_qb, j3 + P, P, 1, "wt_both", [1, 3], (0,), 2)

@@ -51,8 +51,8 @@ def tile_list_transit_cauchy_step_kernel(
         x_rows = xT.rearrange("(a p i) t -> a i p t", a=PASSES, i=PACK)
         planes, wb_raw, flux_sb, tab_w = {}, {}, {}, {}
 
-        def load_plane(a, i):
-            planes[a, i] = keep.tile([P, T], F32, name="plane%d%d" % (a, i), align_bytes=64)
+        def load_plane(a, i, tag=None):
+            planes[a, i] = sbuf([P, T], F32, "plane%d%d" % (a, i), tag)
             nc.sync.dma_start(out=planes[a, i][:], in_=x_rows[a, i])
 
         def load_wb(a):
@@ -63,14 +63,23 @@ def tile_list_transit_cauchy_step_kernel(
 
         def load_flux(c0, count, tag):
             rows = sbuf([P, PACK, count * CHUNK], F32, "flux_sb", tag)
-            nc.sync.dma_start(
-                out=rows[:], in_=flux[:, c0 * CHUNK : (c0 + count) * CHUNK].rearrange("(m t) j -> m t j", t=PACK)
-            )
+            for o in range(0, count * CHUNK, HALF):
+                cols = slice(o, min(o + HALF, count * CHUNK))
+                nc.sync.dma_start(
+                    out=rows[:, :, cols],
+                    in_=flux[:, c0 * CHUNK + cols.start : c0 * CHUNK + cols.stop].rearrange("(m t) j -> m t j", t=PACK),
+                )
             for k in range(count):
                 flux_sb[c0 + k] = rows[:, :, k * CHUNK : (k + 1) * CHUNK]
 
-        def load_tab(a):
-            tab_w[a] = keep.tile([P, T], I32, name="tab_w%d" % a, align_bytes=64)
+        def load_flux_by_slot(c, tag):
+            flux_sb[c] = sbuf([P, PACK, CHUNK], F32, "flux_sb", tag)
+            by_slot = flux[:, c * CHUNK : (c + 1) * CHUNK].rearrange("(g t e) j -> t g e j", t=PACK, e=PACK)
+            for t in range(PACK):
+                nc.sync.dma_start(out=flux_sb[c][:, t, :], in_=by_slot[t])
+
+        def load_tab(a, tag=None):
+            tab_w[a] = sbuf([P, T], I32, "tab_w%d" % a, tag)
             nc.sync.dma_start(out=tab_w[a][:], in_=tab_words[a].rearrange("p t i -> p (t i)").bitcast(I32))
 
         idx = keep.tile([P, S // PER_COL], U16, name="idx")
@@ -125,11 +134,9 @@ def tile_list_transit_cauchy_step_kernel(
         move_scale_rows(1)
         load_plane(1, 1)
         load_plane(1, 2)
-        load_flux(0, 2, "big0")
-        load_tab(1)
-        load_plane(1, 3)
-        var_t = keep.tile([P, PACK], F32, name="var_t")
-        nc.sync.dma_start(out=var_t[:], in_=var.rearrange("(m t) -> m t", t=PACK))
+        var_t = keep.tile([P, PACK, 8], F32, name="var_t", align_bytes=64)
+        for t in range(PACK):
+            nc.sync.dma_start(out=var_t[:, t, 0:1], in_=var.rearrange("(g t e) -> t g e", t=PACK, e=PACK)[t])
         step_t = keep.tile([P, PASSES, PACK], F32, name="step_t")
         nc.sync.dma_start(out=step_t[:], in_=step.rearrange("(a p i) -> p a i", a=PASSES, i=PACK))
 
@@ -164,9 +171,11 @@ def tile_list_transit_cauchy_step_kernel(
 
         v_words, x_q = {}, {}
 
-        def gather_words(a, j0, n, tag):
+        def gather_words(a, j0, n, tag, piece=None):
             words = sbuf([P, n], U32, "words", tag)
-            nc.vector.tensor_copy(words[:], tab_w[a][:].bitcast(U32).indirect(entries(idx, j0, n)))
+            for o in range(0, n, piece or n):
+                part = slice(o, o + (piece or n))
+                nc.vector.tensor_copy(words[:, part], tab_w[a][:].bitcast(U32).indirect(entries(idx, j0 + o, piece or n)))
             for o in range(0, n, P):
                 v_words[a, j0 + o] = words[:, o:n]
 
@@ -181,8 +190,8 @@ def tile_list_transit_cauchy_step_kernel(
         def prepare_wb(a, scale_tag):
             wb_b = sbuf([P, H * PACK], BF16, "wb_b", "mid%d" % a)
             nc.scalar.copy(
-                wb_b[:].rearrange("p (t m i) -> p m t i", t=PACK, i=PACK),
-                wb_raw[a][:].rearrange("p (i m t) -> p m t i", i=PACK, t=PACK),
+                wb_b[:].rearrange("p (t g e i) -> p g t e i", t=PACK, e=PACK, i=PACK),
+                wb_raw[a][:].rearrange("p (i g t e) -> p g t e i", i=PACK, t=PACK, e=PACK),
             )
             wb_q[a] = quantise("wb%d" % a, wb_b[:], H * PACK, None, scale_tag)
             pairs = wb_b[:].bitcast(F32)
@@ -196,16 +205,16 @@ def tile_list_transit_cauchy_step_kernel(
                     flat(turned[:]).bitcast(BF16).rearrange("m (t p e) -> m e p t", t=PACK, e=2),
                 )
 
-        def reorder_w4(tag):
+        def reorder_w4():
             w4_w = sbuf([P, PASSES * 2 * H], U8, "w4_w")
             nc.scalar.copy(
-                w4_w[:].bitcast(U16).rearrange("p (a t m) -> p a t m", a=PASSES, t=PACK),
-                flat(w4_raw[:]).bitcast(U16).rearrange("p (a m t) -> p a t m", a=PASSES, t=PACK),
+                w4_w[:].bitcast(U32).rearrange("p (a t g w) -> p a t g w", a=PASSES, t=PACK, w=2),
+                flat(w4_raw[:]).bitcast(U32).rearrange("p (a g t w) -> p a t g w", a=PASSES, t=PACK, w=2),
             )
-            w4_sc = sbuf([P, PASSES * H], U8, "w4_sc", tag)
-            nc.vector.tensor_copy(
-                w4_sc[:].rearrange("p (a t m) -> p a t m", a=PASSES, t=PACK),
-                w4_sc_raw[:].rearrange("p (a m t) -> p a t m", a=PASSES, t=PACK),
+            w4_sc = sbuf([P, PASSES * H], U8, "w4_sc")
+            nc.scalar.copy(
+                w4_sc[:].bitcast(U32).rearrange("p (a t g) -> p a t g", a=PASSES, t=PACK),
+                w4_sc_raw[:].bitcast(U32).rearrange("p (a g t) -> p a t g", a=PASSES, t=PACK),
             )
             return w4_w, w4_sc
 
@@ -251,7 +260,10 @@ def tile_list_transit_cauchy_step_kernel(
                 turned = bank([P, PACK, P], "flux_bank", b)
                 for t in range(PACK):
                     nc.tensor.transpose(turned[:, t, :], flux_sb[c][:, t, u * P : (u + 1) * P], ident[:])
-                nc.scalar.copy(laid[:, u, :], flat(turned[:]))
+                nc.scalar.copy(
+                    laid[:, u, :].rearrange("j (t g e) -> j t g e", t=PACK, e=PACK),
+                    turned[:].rearrange("j e (g t) -> j t g e", t=PACK),
+                )
             return laid
 
         def turned_residual(models, laid, banks, first=0):
@@ -300,7 +312,7 @@ def tile_list_transit_cauchy_step_kernel(
             pairs = [sbuf([P, 2, n], F32, "inv_root", tag) for tag in tags]
             for t in range(PACK):
                 nc.scalar.activation(
-                    pairs[t // 2][:, t % 2, :], res_sq[:, t, :], ACT.Abs_reciprocal_sqrt, bias=var_t[:, t : t + 1]
+                    pairs[t // 2][:, t % 2, :], res_sq[:, t, :], ACT.Abs_reciprocal_sqrt, bias=var_t[:, t, 0:1]
                 )
             return [pair[:] for pair in pairs]
 
@@ -361,19 +373,14 @@ def tile_list_transit_cauchy_step_kernel(
             picked = sbuf([P, count, CHUNK], F32, "picked", tag)
             return [picked[:, k, :] for k in range(count)]
 
-        def picks(a, i, rooms):
+        def plane_arrives(rows, a, i, rooms):
             for c in range(2):
                 pick(rooms[c], a, i, c * CHUNK, CHUNK)
-
-        def subtractions(rows, a, i, rooms):
             for c in range(2):
                 subtract(rows[c][:, i, :], a, i, c * CHUNK, CHUNK, rooms[c])
 
-        def plane_arrives(rows, a, i, rooms):
-            picks(a, i, rooms)
-            subtractions(rows, a, i, rooms)
-
-        rows_0 = [sbuf([P, PACK, CHUNK], F32, "rows_0", "xa%d" % c) for c in range(2)]
+        rows_0 = sbuf([P, PACK, HALF], F32, "rows_0", "xa")
+        halves_0 = [rows_0[:, :, c * CHUNK : (c + 1) * CHUNK] for c in range(2)]
         rows_1 = [sbuf([P, PACK, CHUNK], F32, "rows_1", "xc%d" % c) for c in range(2)]
         ahead = []
 
@@ -382,50 +389,54 @@ def tile_list_transit_cauchy_step_kernel(
             pick(flat(both[:]), 0, i, HALF, HALF)
             ahead.append(both)
 
-        for i, tags in enumerate((("slot_a", "ahead1"), ("slot_a", "ahead2"), ("slot_u", "slot_b"))):
-            rooms = room(tags[0]) + room(tags[1])
-            picks(0, i, rooms)
+        for i, tag in enumerate(("ahead1", "ahead2", "slot_u")):
+            picked = sbuf([P, HALF], F32, "picked", tag)
+            pick(picked[:], 0, i, 0, HALF)
             pick_ahead(i, "ahead%d" % i)
-            subtractions(rows_0, 0, i, rooms)
-        prepare_wb(0, "slot_u")
-        plane_arrives(rows_0, 0, 3, room("slot_w") + room("slot_v"))
-        woven = [weave(nc.scalar.copy, [rows_0[c][:]], CHUNK, "xb_a%d" % c) for c in range(2)]
+            subtract(rows_0[:, i, :], 0, i, 0, HALF, picked[:])
+        prepare_wb(0, None)
+        plane_arrives(halves_0, 0, 3, room("slot_w") + room("slot_v"))
+        woven = weave(nc.scalar.copy, [rows_0[:]], HALF, "xb_a")
+        w4_w, w4_sc = reorder_w4()
+        load_flux(0, 3, "w4_raw")
         prepare_wb(1, "slot_v")
-        w4_w, w4_sc = reorder_w4("slot_w")
-        plane_arrives(rows_1, 1, 0, room("slot_a") + room("w4_sc_raw"))
-        quantise_x(0, 0, woven[0], CHUNK, "x00", "xa1", "slot_a")
-        quantise_x(0, j1, woven[1], CHUNK, "x01", "xa0", "w4_sc_raw")
+        plane_arrives(rows_1, 1, 0, room("slot_a") + room("slot_w"))
+        quantise_x(0, 0, woven[:, 0 : CHUNK * PACK], CHUNK, "x00", None, "slot_a")
+        quantise_x(0, j1, woven[:, CHUNK * PACK :], CHUNK, "x01", None, "slot_w")
         gather_words(0, 0, HALF, "slot_b")
         model_0 = [bank([P, H], "model", b) for b in (0, 1)]
         model_1 = [bank([P, H], "model", b) for b in (2, 3)]
         for k, kind in enumerate(("x", "table")):
             turned_pass(model_0, kind, 0, 0, k == 0, False)
             turned_pass(model_1, kind, 0, j1, k == 0, False)
-        load_flux(2, 1, "slot_b")
-        for i in (1, 2):
-            plane_arrives(rows_1, 1, i, room("xb_a0") + room("xb_a1"))
-        pick_ahead(3, "xb_a0")
-        wt_q = quantise("wt", wt_both[:], PASSES * H * PACK, "xa1")
-        gather_words(1, 0, HALF, "xb_a1")
-        turned_pass(model_0, "table", 1, 0, False, False)
-        turned_pass(model_1, "table", 1, j1, False, False)
-        load_flux(3, 1, "xb_a1")
-        laid_0 = lay_flux(0, (4, 5), "mid0")
+        load_plane(1, 3, "x00_codes")
+        load_tab(1, "x01_codes")
+        load_flux_by_slot(3, "slot_b")
+        plane_arrives(rows_1, 1, 1, room("xa") + room("xb_a"))
+        pick_ahead(3, "xa")
+        plane_arrives(rows_1, 1, 2, room("slot_w", 2))
+        wt_q = quantise("wt", wt_both[:], PASSES * H * PACK, "xb_a", "slot_a")
+        gather_words(0, j2, CHUNK, "slot_w")
+        laid_0 = lay_flux(0, (4, 5), "big1")
         laid_1 = lay_flux(1, (6, 7), "mid1")
-        plane_arrives(rows_1, 1, 3, room("wt_both", 2))
-        woven_0 = weave(nc.scalar.copy, [rows_1[0][:]], CHUNK, "xb0")
-        woven_1 = pool_weave(rows_1[1][:], CHUNK, "xb1")
-        gather_words(0, HALF, HALF, "wt_both")
+        laid_2 = lay_flux(2, (4, 5), "big0")
+        plane_arrives(rows_1, 1, 3, room("w4_raw", 2))
+        woven_0 = weave(nc.scalar.copy, [rows_1[0][:]], CHUNK, "wt_both")
+        woven_1 = weave(nc.scalar.copy, [rows_1[1][:]], CHUNK, "xb1")
+        gather_words(1, 0, HALF, "w4_raw", CHUNK)
+        turned_pass(model_0, "table", 1, 0, False, False)
         quantise_x(1, 0, woven_0, CHUNK, "x10")
         turned_pass(model_0, "x", 1, 0, False, True)
+        gather_words(0, j3, CHUNK, "xc0")
+        gather_words(1, j2, CHUNK, "wt_both")
         quantise_x(1, j1, woven_1, CHUNK, "x11")
-        turned_pass(model_1, "x", 1, j1, False, True)
-        gather_words(1, j2, CHUNK, "xb0")
-        res_0 = turned_residual(model_0, laid_0, (4, 5))
-        res_1 = turned_residual(model_1, laid_1, (6, 7), 2)
+        turned_pass(model_1, "x", 1, j1, False, False)
+        turned_pass(model_1, "table", 1, j1, False, True)
+        res_0 = turned_residual(model_0, laid_0, (6, 7))
+        res_1 = turned_residual(model_1, laid_1, (4, 5), 2)
         sq_0 = square_banks(res_0, "sq0")
         outside = [both[:, 0, :] for both in ahead]
-        rows = sbuf([P, PACK, CHUNK], F32, "rows", "xb1")
+        rows = sbuf([P, PACK, CHUNK], F32, "rows", "xc1")
         for i in range(PACK):
             subtract(rows[:, i, :], 0, i, j2, CHUNK, outside[i])
         woven = pool_weave(rows[:], CHUNK, "xg0")
@@ -433,8 +444,7 @@ def tile_list_transit_cauchy_step_kernel(
         inv_0 = square_units(root_0, ("inv0", "res0"))
         sq_1 = square_banks(res_1, "sq1")
         root_1 = roots(sq_1, CHUNK, ("root1a", "root1b"))
-        inv_1 = square_units(root_1, ("inv1", "xc1"))
-        laid_2 = lay_flux(2, (2, 3), "sq0")
+        inv_1 = square_units(root_1, ("inv1", "xb1"))
         for i in range(PACK):
             pick(outside[i], 1, i, j2, CHUNK)
         quantise_x(0, j2, woven, CHUNK, "x02")
@@ -442,19 +452,19 @@ def tile_list_transit_cauchy_step_kernel(
         turned_pass(model_2, "table", 0, j2, True, False)
         turned_pass(model_2, "table", 1, j2, False, False)
         turned_pass(model_2, "x", 0, j2, False, False)
-        rows = sbuf([P, PACK, CHUNK], F32, "rows", "xb1")
+        rows = sbuf([P, PACK, CHUNK], F32, "rows", "xc1")
         for i in range(PACK):
             subtract(rows[:, i, :], 1, i, j2, CHUNK, outside[i])
         woven = pool_weave(rows[:], CHUNK, "xg1")
         psi_0 = influence([(res_0[u][:], inv_0[u][:]) for u in range(2)], P, "psi_b0")
         gather_words(1, j3, CHUNK, "root0b")
-        quantise_x(1, j2, woven, CHUNK, "x11", None, "inv0")
-        turned_pass(model_2, "x", 1, j2, False, True)
         psi_q0 = quantise("psi0", psi_0[:], CHUNK * PACK)
+        quantise_x(1, j2, woven, CHUNK, "x11", None, "res0")
+        turned_pass(model_2, "x", 1, j2, False, True)
         psi_1 = influence([(res_1[u][:], inv_1[u][:]) for u in range(2)], P, "psi_b1")
         psi_q1 = quantise("psi1", psi_1[:], CHUNK * PACK)
-        second_product(psi_q0, 0, CHUNK, 0, "root1a", [2, 3])
         res_2 = turned_residual(model_2, laid_2, (6, 7))
+        second_product(psi_q0, 0, CHUNK, 0, "root1a", [2, 3])
         units = (j3, j3 + P)
         outside = [both[:, 1, :] for both in ahead]
         rows = sbuf([P, PACK, CHUNK], F32, "rows", "inv1")
@@ -463,10 +473,10 @@ def tile_list_transit_cauchy_step_kernel(
         woven = pool_weave(rows[:], CHUNK, "xg0")
         sq_2 = square_banks(res_2, "sq0")
         root_2 = roots(sq_2, CHUNK, ("root0a", "sq1"))
-        inv_2 = square_units(root_2, ("res0", "mid1"))
-        second_product(psi_q0, 0, CHUNK, 1, "big0", [4, 5])
+        inv_2 = square_units(root_2, ("inv0", "mid1"))
+        second_product(psi_q0, 0, CHUNK, 1, "w4_raw", [4, 5])
         second_product(psi_q1, j1, CHUNK, 0, "big1", [2, 3])
-        second_product(psi_q1, j1, CHUNK, 1, "mid0", [4, 5])
+        second_product(psi_q1, j1, CHUNK, 1, "xb0", [4, 5])
         models = [bank([P, PACK, P], "model", b) for b in (0, 1)]
         for a in range(PASSES):
             for u in range(2):
@@ -492,18 +502,21 @@ def tile_list_transit_cauchy_step_kernel(
         rows_a = sbuf([P, PACK, P], F32, "rows_a", "inv1")
         unit_rows(0, rows_a, range(PACK))
         psi_2 = influence([(res_2[u][:], inv_2[u][:]) for u in range(2)], P, "psi_b1")
-        close_unit(0, rows_a, "res0", "x11")
+        close_unit(0, rows_a, "inv0", "x11")
         psi_q2 = quantise("psi0", psi_2[:], CHUNK * PACK)
         rows_b = sbuf([P, PACK, P], F32, "rows_b", "mid1")
         unit_rows(1, rows_b, range(PACK))
         second_product(psi_q2, j2, CHUNK, 0, "sq0", [2, 3], (), 2)
-        res_a, inv_a = invert_unit(0, ("neg0", "xc0", "neg2", "neg3", "slot_a"))
-        close_unit(1, rows_b, "neg1", "x10")
-        res_b, inv_b = invert_unit(1, ("xb1", "xc1", "xb0", "slot_b", "xg1"))
+        res_a, inv_a = invert_unit(0, ("neg0", "mid0", "neg2", "neg3", "wt_both"))
+        close_unit(1, rows_b, "x11_codes", "x10")
+        idle = bank([P, H], "idle", 2)
+        for k in range(2):
+            turned_pass([idle], "x", 1, units[1], True, True)
+        res_b, inv_b = invert_unit(1, ("xb1", "big0", "neg1", "root1b", "xg1"))
         psi_qa = quantise("tq0", influence([(res_a[:], inv_a[:])], P, "psi_b0")[:], H)
-        psi_qb = quantise("tq1", influence([(res_b[:], inv_b[:])], P, "xb_a0")[:], H)
-        second_product(psi_q2, j2, CHUNK, 1, "big0", [4, 5], (0, 1), 2)
-        second_product(psi_qa, j3, P, 0, "root1a", [6], (0,))
+        psi_qb = quantise("tq1", influence([(res_b[:], inv_b[:])], P, "xg0")[:], H)
+        second_product(psi_q2, j2, CHUNK, 1, "w4_raw", [4, 5], (0, 1), 2)
+        second_product(psi_qa, j3, P, 0, "root1a", [6])
         second_product(psi_qa, j3, P, 1, "sq1", [7])
         second_product(psi_qb, j3 + P, P, 0, "big1", [0, 2], (0,), 2)
-        second_product(psi_qb, j3 + P, P, 1, "wt_both", [1, 3], (0,), 2)
+        second_product(psi_qb, j3 + P, P, 1, "xb0", [1, 3], (0,), 2)

@@ -285,12 +285,11 @@ def tile_list_transit_cauchy_step_kernel(
                 res_banks.append(res)
             return res_banks
 
-        def direct_residual(models, flux_rows, n, tag):
+        def direct_residual(model, flux_rows, n, tag, pieces):
             res = sbuf([P, PACK, n], F32, "res", tag)
-            per_bank = PACK // len(models)
-            for b, model in enumerate(models):
-                rows = slice(b * per_bank, (b + 1) * per_bank)
-                nc.vector.tensor_tensor(res[:, rows, :], flux_rows[:, rows, :], model[:], ALU.subtract)
+            for t0 in range(0, PACK, PACK // pieces):
+                rows = slice(t0, t0 + PACK // pieces)
+                nc.vector.tensor_tensor(res[:, rows, :], flux_rows[:, rows, :], model[:, rows, :], ALU.subtract)
             return res
 
         def square_rows(pairs, n, tag):
@@ -463,8 +462,9 @@ def tile_list_transit_cauchy_step_kernel(
         turned_pass(model_2, "x", 1, j2, False, True)
         psi_1 = influence([(res_1[u][:], inv_1[u][:]) for u in range(2)], P, "psi_b1")
         psi_q1 = quantise("psi1", psi_1[:], CHUNK * PACK)
-        res_2 = turned_residual(model_2, laid_2, (6, 7))
         second_product(psi_q0, 0, CHUNK, 0, "root1a", [2, 3])
+        res_2 = turned_residual(model_2, laid_2, (6, 7))
+        second_product(psi_q0, 0, CHUNK, 1, "w4_raw", [4, 5])
         units = (j3, j3 + P)
         outside = [both[:, 1, :] for both in ahead]
         rows = sbuf([P, PACK, CHUNK], F32, "rows", "inv1")
@@ -474,9 +474,8 @@ def tile_list_transit_cauchy_step_kernel(
         sq_2 = square_banks(res_2, "sq0")
         root_2 = roots(sq_2, CHUNK, ("root0a", "sq1"))
         inv_2 = square_units(root_2, ("inv0", "mid1"))
-        second_product(psi_q0, 0, CHUNK, 1, "w4_raw", [4, 5])
-        second_product(psi_q1, j1, CHUNK, 0, "big1", [2, 3])
-        second_product(psi_q1, j1, CHUNK, 1, "xb0", [4, 5])
+        second_product(psi_q1, j1, CHUNK, 0, "big1", [2, 3], (), 2)
+        second_product(psi_q1, j1, CHUNK, 1, "xb0", [4, 5], (), 2)
         models = [bank([P, PACK, P], "model", b) for b in (0, 1)]
         for a in range(PASSES):
             for u in range(2):
@@ -496,7 +495,7 @@ def tile_list_transit_cauchy_step_kernel(
             direct_pass(models[u : u + 1], "x", 1, units[u], P, False, True)
 
         def invert_unit(u, tags):
-            res = direct_residual(models[u : u + 1], flux_sb[3][:, :, u * P : (u + 1) * P], P, tags[0])
+            res = direct_residual(models[u], flux_sb[3][:, :, u * P : (u + 1) * P], P, tags[0], 1 + u)
             return res, square_rows(roots(square_rows(pairs_of(res), P, tags[1]), P, tags[2:4]), P, tags[4])
 
         rows_a = sbuf([P, PACK, P], F32, "rows_a", "inv1")
@@ -516,6 +515,9 @@ def tile_list_transit_cauchy_step_kernel(
         psi_qa = quantise("tq0", influence([(res_a[:], inv_a[:])], P, "psi_b0")[:], H)
         psi_qb = quantise("tq1", influence([(res_b[:], inv_b[:])], P, "xg0")[:], H)
         second_product(psi_q2, j2, CHUNK, 1, "w4_raw", [4, 5], (0, 1), 2)
+        idle = bank([P, H], "idle", 5)
+        for k in range(2):
+            turned_pass([idle], "x", 1, units[1], True, True)
         second_product(psi_qa, j3, P, 0, "root1a", [6])
         second_product(psi_qa, j3, P, 1, "sq1", [7])
         second_product(psi_qb, j3 + P, P, 0, "big1", [0, 2], (0,), 2)

@@ -157,6 +157,26 @@ def tile_list_transit_cauchy_step_kernel(
             pool_copy(woven[:].rearrange("p (j t) -> p j t", t=PACK), rows.rearrange("p t j -> p j t"))
             return woven
 
+        def pool_difference(a, j0, outside, tags, woven_tag):
+            woven = sbuf([P, CHUNK * PACK], BF16, "xb", woven_tag)
+            for k, tag in enumerate(tags):
+                inside = sbuf([P, 2, CHUNK], F32, "inside", tag)
+                for e in range(2):
+                    nc.vector.tensor_copy(inside[:, e, :], planes[a, 2 * k + e][:].indirect(entries(idx2, j0, CHUNK)))
+                nc.gpsimd.tensor_tensor(
+                    woven[:].rearrange("p (c e t) -> p c t e", e=PAIR, t=PACK)[:, :, 2 * k : 2 * k + 2, :],
+                    inside[:].rearrange("p t (c e) -> p c t e", e=PAIR),
+                    outside[:, 2 * k : 2 * k + 2, :].rearrange("p t (c e) -> p c t e", e=PAIR),
+                    ALU.subtract,
+                )
+            return woven
+
+        def pick_outside(tag, a, j0):
+            rows = sbuf([P, PACK, CHUNK], F32, "outside", tag)
+            for i in range(PACK):
+                pick(rows[:, i, :], a, i, j0, CHUNK)
+            return rows
+
         def pick(dst, a, i, j0, n):
             nc.vector.tensor_copy(dst, planes[a, i][:].indirect(entries(idx3, j0, n)))
 
@@ -381,17 +401,15 @@ def tile_list_transit_cauchy_step_kernel(
         rows_0 = sbuf([P, PACK, HALF], F32, "rows_0", "xa")
         halves_0 = [rows_0[:, :, c * CHUNK : (c + 1) * CHUNK] for c in range(2)]
         rows_1 = [sbuf([P, PACK, CHUNK], F32, "rows_1", "xc%d" % c) for c in range(2)]
-        ahead = []
+        ahead = sbuf([P, PACK, HALF], F32, "ahead")
 
-        def pick_ahead(i, tag):
-            both = sbuf([P, 2, CHUNK], F32, "ahead", tag)
-            pick(flat(both[:]), 0, i, HALF, HALF)
-            ahead.append(both)
+        def pick_ahead(i):
+            pick(ahead[:, i, :], 0, i, HALF, HALF)
 
-        for i, tag in enumerate(("ahead1", "ahead2", "slot_u")):
+        for i, tag in enumerate(("slot_u", "slot_t", "slot_u")):
             picked = sbuf([P, HALF], F32, "picked", tag)
             pick(picked[:], 0, i, 0, HALF)
-            pick_ahead(i, "ahead%d" % i)
+            pick_ahead(i)
             subtract(rows_0[:, i, :], 0, i, 0, HALF, picked[:])
         prepare_wb(0, None)
         plane_arrives(halves_0, 0, 3, room("slot_w") + room("slot_v"))
@@ -412,7 +430,7 @@ def tile_list_transit_cauchy_step_kernel(
         load_tab(1, "x01_codes")
         load_flux_by_slot(3, "slot_b")
         plane_arrives(rows_1, 1, 1, room("xa") + room("xb_a"))
-        pick_ahead(3, "xa")
+        pick_ahead(3)
         plane_arrives(rows_1, 1, 2, room("slot_w", 2))
         wt_q = quantise("wt", wt_both[:], PASSES * H * PACK, "xb_a", "slot_a")
         gather_words(0, j2, CHUNK, "slot_w")
@@ -434,31 +452,23 @@ def tile_list_transit_cauchy_step_kernel(
         res_0 = turned_residual(model_0, laid_0, (6, 7))
         res_1 = turned_residual(model_1, laid_1, (4, 5), 2)
         sq_0 = square_banks(res_0, "sq0")
-        outside = [both[:, 0, :] for both in ahead]
-        rows = sbuf([P, PACK, CHUNK], F32, "rows", "xc1")
-        for i in range(PACK):
-            subtract(rows[:, i, :], 0, i, j2, CHUNK, outside[i])
-        woven = pool_weave(rows[:], CHUNK, "xg0")
+        woven = pool_difference(0, j2, ahead[:, :, 0:CHUNK], ("xc1", "xb1"), "xg0")
         root_0 = roots(sq_0, CHUNK, ("root0a", "root0b"))
         inv_0 = square_units(root_0, ("inv0", "res0"))
         sq_1 = square_banks(res_1, "sq1")
         root_1 = roots(sq_1, CHUNK, ("root1a", "root1b"))
-        inv_1 = square_units(root_1, ("inv1", "xb1"))
-        for i in range(PACK):
-            pick(outside[i], 1, i, j2, CHUNK)
+        inv_1 = square_units(root_1, ("inv1", "slot_t"))
+        outside = pick_outside("x11_codes", 1, j2)
         quantise_x(0, j2, woven, CHUNK, "x02")
         model_2 = [bank([P, H], "model", b) for b in (0, 1)]
         turned_pass(model_2, "table", 0, j2, True, False)
         turned_pass(model_2, "table", 1, j2, False, False)
         turned_pass(model_2, "x", 0, j2, False, False)
-        rows = sbuf([P, PACK, CHUNK], F32, "rows", "xc1")
-        for i in range(PACK):
-            subtract(rows[:, i, :], 1, i, j2, CHUNK, outside[i])
-        woven = pool_weave(rows[:], CHUNK, "xg1")
+        woven = pool_difference(1, j2, outside[:], ("xb1", "xg0"), "xg1")
         psi_0 = influence([(res_0[u][:], inv_0[u][:]) for u in range(2)], P, "psi_b0")
         gather_words(1, j3, CHUNK, "root0b")
-        psi_q0 = quantise("psi0", psi_0[:], CHUNK * PACK)
-        quantise_x(1, j2, woven, CHUNK, "x11", None, "res0")
+        psi_q0 = quantise("psi0", psi_0[:], CHUNK * PACK, None, "x11_codes")
+        quantise_x(1, j2, woven, CHUNK, "x10", None, "res0")
         turned_pass(model_2, "x", 1, j2, False, True)
         psi_1 = influence([(res_1[u][:], inv_1[u][:]) for u in range(2)], P, "psi_b1")
         psi_q1 = quantise("psi1", psi_1[:], CHUNK * PACK)
@@ -466,11 +476,9 @@ def tile_list_transit_cauchy_step_kernel(
         res_2 = turned_residual(model_2, laid_2, (6, 7))
         second_product(psi_q0, 0, CHUNK, 1, "w4_raw", [4, 5])
         units = (j3, j3 + P)
-        outside = [both[:, 1, :] for both in ahead]
-        rows = sbuf([P, PACK, CHUNK], F32, "rows", "inv1")
-        for i in range(PACK):
-            subtract(rows[:, i, :], 0, i, j3, CHUNK, outside[i])
-        woven = pool_weave(rows[:], CHUNK, "xg0")
+        woven = pool_difference(0, j3, ahead[:, :, CHUNK:], ("inv1", "slot_t"), "xg0")
+        last = pick_outside("psi_b1", 1, j3)
+        outside = [last[:, i, :] for i in range(PACK)]
         sq_2 = square_banks(res_2, "sq0")
         root_2 = roots(sq_2, CHUNK, ("root0a", "sq1"))
         inv_2 = square_units(root_2, ("inv0", "mid1"))
@@ -480,8 +488,6 @@ def tile_list_transit_cauchy_step_kernel(
         for a in range(PASSES):
             for u in range(2):
                 direct_pass(models[u : u + 1], "table", a, units[u], P, a == 0, False)
-        for i in range(PACK):
-            pick(outside[i], 1, i, j3, CHUNK)
         quantise_x(0, j3, woven, CHUNK, "x02")
         for u in range(2):
             direct_pass(models[u : u + 1], "x", 0, units[u], P, False, False)
@@ -498,9 +504,9 @@ def tile_list_transit_cauchy_step_kernel(
             res = direct_residual(models[u], flux_sb[3][:, :, u * P : (u + 1) * P], P, tags[0], 1 + u)
             return res, square_rows(roots(square_rows(pairs_of(res), P, tags[1]), P, tags[2:4]), P, tags[4])
 
-        rows_a = sbuf([P, PACK, P], F32, "rows_a", "inv1")
+        rows_a = sbuf([P, PACK, P], F32, "rows_a", "slot_t")
         unit_rows(0, rows_a, range(PACK))
-        psi_2 = influence([(res_2[u][:], inv_2[u][:]) for u in range(2)], P, "psi_b1")
+        psi_2 = influence([(res_2[u][:], inv_2[u][:]) for u in range(2)], P, "xg1")
         close_unit(0, rows_a, "inv0", "x11")
         psi_q2 = quantise("psi0", psi_2[:], CHUNK * PACK)
         rows_b = sbuf([P, PACK, P], F32, "rows_b", "mid1")
@@ -511,9 +517,9 @@ def tile_list_transit_cauchy_step_kernel(
         idle = bank([P, H], "idle", 2)
         for k in range(2):
             turned_pass([idle], "x", 1, units[1], True, True)
-        res_b, inv_b = invert_unit(1, ("xb1", "big0", "neg1", "root1b", "xg1"))
+        res_b, inv_b = invert_unit(1, ("xb1", "big0", "neg1", "root1b", "xc1"))
         psi_qa = quantise("tq0", influence([(res_a[:], inv_a[:])], P, "psi_b0")[:], H)
-        psi_qb = quantise("tq1", influence([(res_b[:], inv_b[:])], P, "xg0")[:], H)
+        psi_qb = quantise("tq1", influence([(res_b[:], inv_b[:])], P, "inv1")[:], H)
         second_product(psi_q2, j2, CHUNK, 1, "w4_raw", [4, 5], (0, 1), 2)
         idle = bank([P, H], "idle", 5)
         for k in range(2):

@@ -335,6 +335,33 @@ def tile_list_transit_cauchy_step_kernel(
                 )
             return [pair[:] for pair in pairs]
 
+        def whole_roots(res_sq, tag):
+            room = sbuf([P, PACK, CHUNK], F32, "inv_root", tag)
+            for t in range(PACK):
+                nc.scalar.activation(room[:, t, :], res_sq[:, t, :], ACT.Abs_reciprocal_sqrt, bias=var_t[:, t, 0:1])
+            return room
+
+        def woven_squares(root, tags):
+            units = [sbuf([P, H], F32, "inv", tag) for tag in tags]
+            for u, dst in enumerate(units):
+                nc.scalar.activation(
+                    dst[:].rearrange("m (c e t) -> m c t e", e=RUN, t=PACK),
+                    root[:, :, u * P : (u + 1) * P].rearrange("m t (c e) -> m c t e", e=RUN),
+                    ACT.Square,
+                )
+            return units
+
+        def bank_influence(res_banks, inv, tag):
+            psi_b = sbuf([P, CHUNK * PACK], BF16, "psi_b", tag)
+            for u, res in enumerate(res_banks):
+                nc.vector.tensor_tensor(
+                    psi_b[:, u * H : (u + 1) * H].rearrange("m (j t) -> m j t", t=PACK),
+                    res[:].rearrange("m t j -> m j t"),
+                    inv[u][:].rearrange("m (j t) -> m j t", t=PACK),
+                    ALU.mult,
+                )
+            return psi_b
+
         def influence(pieces, n, tag):
             psi_b = sbuf([P, len(pieces) * n * PACK], BF16, "psi_b", tag)
             for k, (res, inv) in enumerate(pieces):
@@ -453,11 +480,9 @@ def tile_list_transit_cauchy_step_kernel(
         res_1 = turned_residual(model_1, laid_1, (4, 5), 2)
         sq_0 = square_banks(res_0, "sq0")
         woven = pool_difference(0, j2, ahead[:, :, 0:CHUNK], ("xc1", "xb1"), "xg0")
-        root_0 = roots(sq_0, CHUNK, ("root0a", "root0b"))
-        inv_0 = square_units(root_0, ("inv0", "res0"))
+        inv_0 = woven_squares(whole_roots(sq_0, "root0b"), ("inv0", "res0"))
         sq_1 = square_banks(res_1, "sq1")
-        root_1 = roots(sq_1, CHUNK, ("root1a", "root1b"))
-        inv_1 = square_units(root_1, ("inv1", "slot_t"))
+        inv_1 = woven_squares(whole_roots(sq_1, "root1a"), ("inv1", "slot_t"))
         outside = pick_outside("x11_codes", 1, j2)
         quantise_x(0, j2, woven, CHUNK, "x02")
         model_2 = [bank([P, H], "model", b) for b in (0, 1)]
@@ -465,12 +490,12 @@ def tile_list_transit_cauchy_step_kernel(
         turned_pass(model_2, "table", 1, j2, False, False)
         turned_pass(model_2, "x", 0, j2, False, False)
         woven = pool_difference(1, j2, outside[:], ("xb1", "xg0"), "xg1")
-        psi_0 = influence([(res_0[u][:], inv_0[u][:]) for u in range(2)], P, "psi_b0")
+        psi_0 = bank_influence(res_0, inv_0, "psi_b0")
         gather_words(1, j3, CHUNK, "root0b")
         psi_q0 = quantise("psi0", psi_0[:], CHUNK * PACK, None, "x11_codes")
         quantise_x(1, j2, woven, CHUNK, "x10", None, "res0")
         turned_pass(model_2, "x", 1, j2, False, True)
-        psi_1 = influence([(res_1[u][:], inv_1[u][:]) for u in range(2)], P, "psi_b1")
+        psi_1 = bank_influence(res_1, inv_1, "psi_b1")
         psi_q1 = quantise("psi1", psi_1[:], CHUNK * PACK)
         second_product(psi_q0, 0, CHUNK, 0, "root1a", [2, 3])
         res_2 = turned_residual(model_2, laid_2, (6, 7))
@@ -480,8 +505,7 @@ def tile_list_transit_cauchy_step_kernel(
         last = pick_outside("psi_b1", 1, j3)
         outside = [last[:, i, :] for i in range(PACK)]
         sq_2 = square_banks(res_2, "sq0")
-        root_2 = roots(sq_2, CHUNK, ("root0a", "sq1"))
-        inv_2 = square_units(root_2, ("inv0", "mid1"))
+        inv_2 = woven_squares(whole_roots(sq_2, "sq1"), ("inv0", "mid1"))
         second_product(psi_q1, j1, CHUNK, 0, "big1", [2, 3], (), 2)
         second_product(psi_q1, j1, CHUNK, 1, "xb0", [4, 5], (), 2)
         models = [bank([P, PACK, P], "model", b) for b in (0, 1)]
@@ -506,7 +530,7 @@ def tile_list_transit_cauchy_step_kernel(
 
         rows_a = sbuf([P, PACK, P], F32, "rows_a", "slot_t")
         unit_rows(0, rows_a, range(PACK))
-        psi_2 = influence([(res_2[u][:], inv_2[u][:]) for u in range(2)], P, "xg1")
+        psi_2 = bank_influence(res_2, inv_2, "xg1")
         close_unit(0, rows_a, "inv0", "x11")
         psi_q2 = quantise("psi0", psi_2[:], CHUNK * PACK)
         rows_b = sbuf([P, PACK, P], F32, "rows_b", "mid1")

@@ -21,10 +21,8 @@ P = 128
 PACK = 4
 PASSES = K // (P * PACK)
 CHUNK = 256
-HALF = S // 2
 PER_COL = 16
 RUN = 4
-PAIR = 2
 
 
 def tile_list_transit_cauchy_step_kernel(
@@ -49,10 +47,12 @@ def tile_list_transit_cauchy_step_kernel(
             return ap.rearrange("p a b -> p (a b)")
 
         x_rows = xT.rearrange("(a p i) t -> a i p t", a=PASSES, i=PACK)
-        planes, wb_raw, flux_sb, tab_w = {}, {}, {}, {}
+        flux_rows = flux.rearrange("(m t) j -> m t j", t=PACK)
+        out_rows = out.rearrange("(a p i) j -> a p i j", a=PASSES, i=PACK)
+        planes, wb_raw, tab_w = {}, {}, {}
 
-        def load_plane(a, i, tag=None):
-            planes[a, i] = sbuf([P, T], F32, "plane%d%d" % (a, i), tag)
+        def load_plane(a, i):
+            planes[a, i] = sbuf([P, T], F32, "plane%d%d" % (a, i))
             nc.sync.dma_start(out=planes[a, i][:], in_=x_rows[a, i])
 
         def load_wb(a):
@@ -61,25 +61,13 @@ def tile_list_transit_cauchy_step_kernel(
                 out=wb_raw[a][:], in_=wb[a * P * PACK : (a + 1) * P * PACK, :].rearrange("(p i) r -> p (i r)", i=PACK)
             )
 
-        def load_flux(c0, count, tag):
-            rows = sbuf([P, PACK, count * CHUNK], F32, "flux_sb", tag)
-            for o in range(0, count * CHUNK, HALF):
-                cols = slice(o, min(o + HALF, count * CHUNK))
-                nc.sync.dma_start(
-                    out=rows[:, :, cols],
-                    in_=flux[:, c0 * CHUNK + cols.start : c0 * CHUNK + cols.stop].rearrange("(m t) j -> m t j", t=PACK),
-                )
-            for k in range(count):
-                flux_sb[c0 + k] = rows[:, :, k * CHUNK : (k + 1) * CHUNK]
+        def load_flux(j0, n, tag):
+            rows = sbuf([P, PACK, n], F32, "flux_sb", tag)
+            nc.sync.dma_start(out=rows[:], in_=flux_rows[:, :, j0 : j0 + n])
+            return rows
 
-        def load_flux_by_slot(c, tag):
-            flux_sb[c] = sbuf([P, PACK, CHUNK], F32, "flux_sb", tag)
-            by_slot = flux[:, c * CHUNK : (c + 1) * CHUNK].rearrange("(g t e) j -> t g e j", t=PACK, e=PACK)
-            for t in range(PACK):
-                nc.sync.dma_start(out=flux_sb[c][:, t, :], in_=by_slot[t])
-
-        def load_tab(a, tag=None):
-            tab_w[a] = sbuf([P, T], I32, "tab_w%d" % a, tag)
+        def load_tab(a):
+            tab_w[a] = sbuf([P, T], I32, "tab_w%d" % a)
             nc.sync.dma_start(out=tab_w[a][:], in_=tab_words[a].rearrange("p t i -> p (t i)").bitcast(I32))
 
         idx = keep.tile([P, S // PER_COL], U16, name="idx")
@@ -108,116 +96,78 @@ def tile_list_transit_cauchy_step_kernel(
                     out=v_sc[a][32 * q : 32 * q + 4, :].bitcast(I32), in_=picked_sc[row : row + 4, :].bitcast(I32)
                 )
 
-        nc.sync.dma_start(idx[:], offs)
-        nc.sync.dma_start(
-            out=tab_sc[0:32, :].bitcast(I32), in_=tab_scales.rearrange("a q t -> (a q) t").bitcast(I32)
-        )
-        load_plane(0, 0)
-        nc.sync.dma_start(idx3[:], offs3)
-        nc.sync.dma_start(idx2[:], offs2)
-        nc.vector.tensor_copy(picked_sc[:], tab_sc[:].indirect(idx[:]))
-        load_plane(0, 1)
-        load_wb(0)
-        load_plane(0, 2)
-        for q in range(4):
-            nc.sync.dma_start(
-                out=w4_sc_raw[32 * q : 32 * q + 4, :].bitcast(I32).rearrange("p (a c) -> p a c", a=PASSES),
-                in_=w4_scales[:, 4 * q : 4 * q + 4, :].rearrange("a s c -> s a c").bitcast(I32),
-            )
-        load_wb(1)
-        load_plane(0, 3)
-        move_scale_rows(0)
-        w4_raw = sbuf([P, PASSES, 2 * H], U8, "w4_raw")
-        nc.sync.dma_start(out=w4_raw[:].bitcast(I32), in_=w4_words.rearrange("a p c -> p a c").bitcast(I32))
-        load_plane(1, 0)
-        load_tab(0)
-        move_scale_rows(1)
-        load_plane(1, 1)
-        load_plane(1, 2)
-        var_t = keep.tile([P, PACK, 8], F32, name="var_t", align_bytes=64)
-        for t in range(PACK):
-            nc.sync.dma_start(out=var_t[:, t, 0:1], in_=var.rearrange("(g t e) -> t g e", t=PACK, e=PACK)[t])
-        step_t = keep.tile([P, PASSES, PACK], F32, name="step_t")
-        nc.sync.dma_start(out=step_t[:], in_=step.rearrange("(a p i) -> p a i", a=PASSES, i=PACK))
-
-        def weave(engine_copy, pieces, n, tag):
-            woven = sbuf([P, len(pieces) * n * PACK], BF16, "xb", tag)
-            for k, rows in enumerate(pieces):
-                engine_copy(
-                    woven[:, k * n * PACK : (k + 1) * n * PACK].rearrange("p (c e t) -> p c t e", e=RUN, t=PACK),
-                    rows.rearrange("p t (c e) -> p c t e", e=RUN),
+        def load_w4_scales():
+            for q in range(4):
+                nc.sync.dma_start(
+                    out=w4_sc_raw[32 * q : 32 * q + 4, :].bitcast(I32).rearrange("p (a c) -> p a c", a=PASSES),
+                    in_=w4_scales[:, 4 * q : 4 * q + 4, :].rearrange("a s c -> s a c").bitcast(I32),
                 )
-            return woven
 
-        def pool_copy(dst, src):
-            nc.gpsimd.tensor_scalar(dst, src, 1.0, 0.0, ALU.mult, ALU.add)
+        def pick(dst, lst, a, i, j0, n):
+            nc.vector.tensor_copy(dst, planes[a, i][:].indirect(entries(lst, j0, n)))
 
-        def pool_weave(rows, n, tag):
-            woven = sbuf([P, n * PACK], BF16, "xb", tag)
-            pool_copy(woven[:].rearrange("p (j t) -> p j t", t=PACK), rows.rearrange("p t j -> p j t"))
-            return woven
-
-        def pool_difference(a, j0, outside, tags, woven_tag):
-            woven = sbuf([P, CHUNK * PACK], BF16, "xb", woven_tag)
-            for k, tag in enumerate(tags):
-                inside = sbuf([P, 2, CHUNK], F32, "inside", tag)
-                for e in range(2):
-                    nc.vector.tensor_copy(inside[:, e, :], planes[a, 2 * k + e][:].indirect(entries(idx2, j0, CHUNK)))
-                nc.gpsimd.tensor_tensor(
-                    woven[:].rearrange("p (c e t) -> p c t e", e=PAIR, t=PACK)[:, :, 2 * k : 2 * k + 2, :],
-                    inside[:].rearrange("p t (c e) -> p c t e", e=PAIR),
-                    outside[:, 2 * k : 2 * k + 2, :].rearrange("p t (c e) -> p c t e", e=PAIR),
-                    ALU.subtract,
-                )
-            return woven
-
-        def pick_outside(tag, a, j0):
-            rows = sbuf([P, PACK, CHUNK], F32, "outside", tag)
+        def pick_rows(lst, a, j0, n, tag):
+            rows = sbuf([P, PACK, n], F32, "rows", tag)
             for i in range(PACK):
-                pick(rows[:, i, :], a, i, j0, CHUNK)
+                pick(rows[:, i, :], lst, a, i, j0, n)
             return rows
 
-        def pick(dst, a, i, j0, n):
-            nc.vector.tensor_copy(dst, planes[a, i][:].indirect(entries(idx3, j0, n)))
+        def weave(dst, first, second, op, slots=slice(0, PACK)):
+            nc.gpsimd.tensor_tensor(
+                dst.rearrange("p (c e t) -> p c t e", e=RUN, t=PACK)[:, :, slots, :],
+                first.rearrange("p t (c e) -> p c t e", e=RUN),
+                second.rearrange("p t (c e) -> p c t e", e=RUN),
+                op,
+            )
 
-        def subtract(dst, a, i, j0, n, outside):
-            nc.vector.tensor_tensor(dst, planes[a, i][:].indirect(entries(idx2, j0, n)), outside, ALU.subtract)
-
-        def quantise(name, src, width, tag=None, scale_tag=None):
-            codes = sbuf([P, width // PACK], U32, name + "_codes", tag)
-            scales = sbuf([P, width // PACK], U8, name + "_sc", scale_tag)
+        def quantise(src, width, tag, scale_tag):
+            codes = sbuf([P, width // PACK], U32, "codes", tag)
+            scales = sbuf([P, width // PACK], U8, "scales", scale_tag)
             nc.vector.quantize_mx(out=codes[:].bitcast(FP8X4), scales=scales[:], in_=src)
             return codes, scales
 
-        v_words, x_q = {}, {}
+        v_words, x_q, wb_q = {}, {}, {}
 
-        def gather_words(a, j0, n, tag, piece=None):
+        def gather_words(a, j0, n, tag):
             words = sbuf([P, n], U32, "words", tag)
-            for o in range(0, n, piece or n):
-                part = slice(o, o + (piece or n))
-                nc.vector.tensor_copy(words[:, part], tab_w[a][:].bitcast(U32).indirect(entries(idx, j0 + o, piece or n)))
+            nc.vector.tensor_copy(words[:], tab_w[a][:].bitcast(U32).indirect(entries(idx, j0, n)))
             for o in range(0, n, P):
                 v_words[a, j0 + o] = words[:, o:n]
 
-        def quantise_x(a, j0, woven, n, name, tag=None, scale_tag=None):
-            codes, scales = quantise(name, woven[:], n * PACK, tag, scale_tag)
-            for o in range(0, n, P):
-                x_q[a, j0 + o] = (codes[:, o:n], scales[:, o:n])
+        def quantise_x(places, woven, tag, scale_tag, cut=None):
+            n = len(places) * P
+            codes = sbuf([P, n], U32, "codes", tag)
+            scales = sbuf([P, n], U8, "scales", scale_tag)
+            for part in (slice(0, cut), slice(cut, n)) if cut else (slice(0, n),):
+                nc.vector.quantize_mx(
+                    out=codes[:, part].bitcast(FP8X4),
+                    scales=scales[:, part],
+                    in_=woven[:, part.start * PACK : part.stop * PACK],
+                )
+            for k, place in enumerate(places):
+                x_q[place] = (codes[:, k * P : n], scales[:, k * P : n])
 
-        wb_q = {}
+        def units(a, j0, n):
+            return [(a, j) for j in range(j0, j0 + n, P)]
+
         wt_both = sbuf([P, PASSES * H * PACK], BF16, "wt_both")
 
-        def prepare_wb(a, scale_tag):
+        def weave_wb(a):
             wb_b = sbuf([P, H * PACK], BF16, "wb_b", "mid%d" % a)
             nc.scalar.copy(
-                wb_b[:].rearrange("p (t g e i) -> p g t e i", t=PACK, e=PACK, i=PACK),
-                wb_raw[a][:].rearrange("p (i g t e) -> p g t e i", i=PACK, t=PACK, e=PACK),
+                wb_b[:].rearrange("p (t m i) -> p m i t", t=PACK, i=PACK),
+                wb_raw[a][:].rearrange("p (i m t) -> p m i t", i=PACK, t=PACK),
             )
-            wb_q[a] = quantise("wb%d" % a, wb_b[:], H * PACK, None, scale_tag)
+            return wb_b
+
+        def quantise_wb(a, wb_b):
+            wb_q[a] = quantise(wb_b[:], H * PACK, "wb_codes%d" % a, "wb_sc%d" % a)
+
+        def turn_wb(a, wb_b):
             pairs = wb_b[:].bitcast(F32)
             wt_b = wt_both[:, a * H * PACK : (a + 1) * H * PACK]
             for u in range(2):
-                turned = bank([P, PACK, P], "wt_bank", 4 + 2 * a + u)
+                turned = bank([P, PACK, P], "wt_bank", 6 + u)
                 for t in range(PACK):
                     nc.tensor.transpose(turned[:, t, :], pairs[:, 2 * P * t + u : 2 * P * (t + 1) : 2], ident[:])
                 nc.scalar.copy(
@@ -225,18 +175,21 @@ def tile_list_transit_cauchy_step_kernel(
                     flat(turned[:]).bitcast(BF16).rearrange("m (t p e) -> m e p t", t=PACK, e=2),
                 )
 
-        def reorder_w4():
+        def reorder_w4_words():
             w4_w = sbuf([P, PASSES * 2 * H], U8, "w4_w")
             nc.scalar.copy(
-                w4_w[:].bitcast(U32).rearrange("p (a t g w) -> p a t g w", a=PASSES, t=PACK, w=2),
-                flat(w4_raw[:]).bitcast(U32).rearrange("p (a g t w) -> p a t g w", a=PASSES, t=PACK, w=2),
+                w4_w[:].bitcast(U16).rearrange("p (a t m) -> p a m t", a=PASSES, t=PACK),
+                flat(w4_raw[:]).bitcast(U16).rearrange("p (a m t) -> p a m t", a=PASSES, t=PACK),
             )
+            return w4_w
+
+        def reorder_w4_scales():
             w4_sc = sbuf([P, PASSES * H], U8, "w4_sc")
-            nc.scalar.copy(
-                w4_sc[:].bitcast(U32).rearrange("p (a t g) -> p a t g", a=PASSES, t=PACK),
-                w4_sc_raw[:].bitcast(U32).rearrange("p (a g t) -> p a t g", a=PASSES, t=PACK),
+            nc.gpsimd.tensor_copy(
+                w4_sc[:].rearrange("p (a t m) -> p a t m", a=PASSES, t=PACK),
+                w4_sc_raw[:].rearrange("p (a m t) -> p a t m", a=PASSES, t=PACK),
             )
-            return w4_w, w4_sc
+            return w4_sc
 
         def weights(kind, a, c0, n):
             cols = slice(a * H + c0, a * H + c0 + n)
@@ -251,7 +204,7 @@ def tile_list_transit_cauchy_step_kernel(
             codes, scales = x_q[a, j0]
             return codes[:, 0:n].bitcast(FP8X4), scales[:, 0:n]
 
-        def direct_pass(banks, kind, a, j0, n, start, stop):
+        def model_pass(banks, kind, a, j0, n, start=False, stop=False):
             per_bank = PACK // len(banks)
             rhs, rhs_sc = columns(kind, a, j0, n)
             for t in range(PACK):
@@ -266,127 +219,53 @@ def tile_list_transit_cauchy_step_kernel(
                     stop=(stop and t % per_bank == per_bank - 1),
                 )
 
-        def turned_pass(banks, kind, a, j0, start, stop):
-            rhs, rhs_sc = weights(kind, a, 0, H)
-            for u, model in enumerate(banks):
-                lhs, lhs_sc = columns(kind, a, j0 + u * P, P)
-                nc.tensor.matmul_mx(
-                    out=model[:], lhsT=lhs, lhsT_scale=lhs_sc, rhs=rhs, rhs_scale=rhs_sc, start=start, stop=stop
-                )
+        def model_banks(numbers, n):
+            return [bank([P, PACK // len(numbers), n], "model", b) for b in numbers]
 
-        def lay_flux(c, banks, tag):
-            laid = sbuf([P, 2, H], F32, "laid", tag)
-            for u, b in enumerate(banks):
-                turned = bank([P, PACK, P], "flux_bank", b)
-                for t in range(PACK):
-                    nc.tensor.transpose(turned[:, t, :], flux_sb[c][:, t, u * P : (u + 1) * P], ident[:])
-                nc.scalar.copy(
-                    laid[:, u, :].rearrange("j (t g e) -> j t g e", t=PACK, e=PACK),
-                    turned[:].rearrange("j e (g t) -> j t g e", t=PACK),
-                )
-            return laid
+        def slot_groups(count):
+            return [slice(t, t + PACK // count) for t in range(0, PACK, PACK // count)]
 
-        def turned_residual(models, laid, banks, first=0):
-            res_banks = []
-            for u, model in enumerate(models):
-                negated = sbuf([P, H], F32, "negated", "neg%d" % (first + u))
-                nc.scalar.activation(negated[:], model[:], ACT.Copy, scale=-1.0)
-                res = bank([P, PACK, P], "res_bank", banks[u])
-                for term, src in enumerate((laid[:, u, :], negated[:])):
-                    for t in range(PACK):
-                        nc.tensor.matmul(
-                            res[:, t, :],
-                            lhsT=src[:, t * P : (t + 1) * P],
-                            rhs=ident[:],
-                            is_transpose=True,
-                            start=(term == 0 and t == 0),
-                            stop=(term == 1 and t == PACK - 1),
-                        )
-                res_banks.append(res)
-            return res_banks
-
-        def direct_residual(model, flux_rows, n, tag, pieces):
+        def residual(banks, flux_sb, n, tag):
             res = sbuf([P, PACK, n], F32, "res", tag)
-            for t0 in range(0, PACK, PACK // pieces):
-                rows = slice(t0, t0 + PACK // pieces)
-                nc.vector.tensor_tensor(res[:, rows, :], flux_rows[:, rows, :], model[:, rows, :], ALU.subtract)
+            for model, rows in zip(banks, slot_groups(len(banks))):
+                nc.vector.tensor_tensor(res[:, rows, :], flux_sb[:, rows, :], model[:], ALU.subtract)
             return res
 
-        def square_rows(pairs, n, tag):
-            dst = sbuf([P, PACK, n], F32, "squared", tag)
-            for k, src in enumerate(pairs):
-                nc.scalar.activation(dst[:, 2 * k : 2 * k + 2, :], src, ACT.Square)
-            return dst
+        def copy_model(banks, n, tag):
+            model_sb = sbuf([P, PACK, n], F32, "model_sb", tag)
+            for model, rows in zip(banks, slot_groups(len(banks))):
+                nc.scalar.copy(model_sb[:, rows, :], model[:])
+            return model_sb
 
-        def pairs_of(rows):
-            return [rows[:, 0:2, :], rows[:, 2:4, :]]
-
-        def square_banks(res_banks, tag):
-            dst = sbuf([P, PACK, CHUNK], F32, "squared", tag)
-            for u, res in enumerate(res_banks):
-                nc.scalar.activation(dst[:, :, u * P : (u + 1) * P], res[:], ACT.Square)
-            return dst
-
-        def roots(res_sq, n, tags):
-            pairs = [sbuf([P, 2, n], F32, "inv_root", tag) for tag in tags]
+        def invert(res, n, tag):
+            inv = sbuf([P, PACK, n], F32, "inv", tag)
+            for rows in slot_groups(2):
+                nc.scalar.activation(inv[:, rows, :], res[:, rows, :], ACT.Square)
             for t in range(PACK):
-                nc.scalar.activation(
-                    pairs[t // 2][:, t % 2, :], res_sq[:, t, :], ACT.Abs_reciprocal_sqrt, bias=var_t[:, t, 0:1]
-                )
-            return [pair[:] for pair in pairs]
+                nc.scalar.activation(inv[:, t, :], inv[:, t, :], ACT.Abs_reciprocal_sqrt, bias=var_t[:, t : t + 1])
+            for rows in slot_groups(2):
+                nc.scalar.activation(inv[:, rows, :], inv[:, rows, :], ACT.Square)
+            return inv
 
-        def whole_roots(res_sq, tag):
-            room = sbuf([P, PACK, CHUNK], F32, "inv_root", tag)
-            for t in range(PACK):
-                nc.scalar.activation(room[:, t, :], res_sq[:, t, :], ACT.Abs_reciprocal_sqrt, bias=var_t[:, t, 0:1])
-            return room
-
-        def woven_squares(root, tags):
-            units = [sbuf([P, H], F32, "inv", tag) for tag in tags]
-            for u, dst in enumerate(units):
-                nc.scalar.activation(
-                    dst[:].rearrange("m (c e t) -> m c t e", e=RUN, t=PACK),
-                    root[:, :, u * P : (u + 1) * P].rearrange("m t (c e) -> m c t e", e=RUN),
-                    ACT.Square,
-                )
-            return units
-
-        def bank_influence(res_banks, inv, tag):
-            psi_b = sbuf([P, CHUNK * PACK], BF16, "psi_b", tag)
-            for u, res in enumerate(res_banks):
-                nc.vector.tensor_tensor(
-                    psi_b[:, u * H : (u + 1) * H].rearrange("m (j t) -> m j t", t=PACK),
-                    res[:].rearrange("m t j -> m j t"),
-                    inv[u][:].rearrange("m (j t) -> m j t", t=PACK),
-                    ALU.mult,
-                )
+        def pool_influence(res, inv, n, tag):
+            psi_b = sbuf([P, n * PACK], BF16, "psi_b", tag)
+            weave(psi_b[:], res[:], inv[:], ALU.mult)
             return psi_b
 
-        def influence(pieces, n, tag):
-            psi_b = sbuf([P, len(pieces) * n * PACK], BF16, "psi_b", tag)
-            for k, (res, inv) in enumerate(pieces):
-                nc.vector.tensor_tensor(
-                    psi_b[:, k * n * PACK : (k + 1) * n * PACK].rearrange("m (c e t) -> m c t e", e=PAIR, t=PACK),
-                    res.rearrange("m t (c e) -> m c t e", e=PAIR),
-                    inv.rearrange("m t (c e) -> m c t e", e=PAIR),
-                    ALU.mult,
-                )
+        def vector_influence(res, inv, n, tag):
+            psi_b = sbuf([P, n * PACK], BF16, "psi_b", tag)
+            nc.vector.tensor_tensor(
+                psi_b[:].rearrange("m (c e t) -> m c t e", e=RUN, t=PACK),
+                res[:].rearrange("m t (c e) -> m c t e", e=RUN),
+                inv[:].rearrange("m t (c e) -> m c t e", e=RUN),
+                ALU.mult,
+            )
             return psi_b
 
-        def square_units(pairs, tags):
-            units = [sbuf([P, PACK, P], F32, "squared", tag) for tag in tags]
-            for k, src in enumerate(pairs):
-                for u, dst in enumerate(units):
-                    nc.scalar.activation(dst[:, 2 * k : 2 * k + 2, :], src[:, :, u * P : (u + 1) * P], ACT.Square)
-            return units
-
-        out_rows = out.rearrange("(a p i) j -> a p i j", a=PASSES, i=PACK)
-
-        def second_product(psi_q, j0, n, a, tag, banks, on_vector=(), rows_a_store=PACK):
+        def second_product(psi_q, j0, n, a, staged, banks, on_vector=(), rows_a_store=PACK):
             psi_codes, psi_sc = psi_q
             wt_codes, wt_sc = wt_q
             per_bank = PACK // len(banks)
-            staged = sbuf([P, PACK, n], F32, "staged", tag)
             for k, b in enumerate(banks):
                 first = a * PACK + k * per_bank
                 back = bank([P, per_bank, n], "back", b)
@@ -413,142 +292,152 @@ def tile_list_transit_cauchy_step_kernel(
                     rows_done = slice(done - rows_a_store, done)
                     nc.sync.dma_start(out=out_rows[a, :, rows_done, j0 : j0 + n], in_=staged[:, rows_done, :])
 
+        def finish(psi_q, j0, n, tag, banks, on_vector=((), ()), rows_a_store=PACK):
+            staged = sbuf([P, PASSES, PACK, n], F32, "staged", tag)
+            for a in range(PASSES):
+                second_product(psi_q, j0, n, a, staged[:, a], banks[a], on_vector[a], rows_a_store)
+
         j1, j2, j3 = CHUNK, 2 * CHUNK, 3 * CHUNK
+        j_last, j_unit = j3, j3 + P
+        pairs_of_slots = slot_groups(2)
 
-        def room(tag, count=1):
-            picked = sbuf([P, count, CHUNK], F32, "picked", tag)
-            return [picked[:, k, :] for k in range(count)]
+        nc.sync.dma_start(idx[:], offs)
+        nc.sync.dma_start(
+            out=tab_sc[0:32, :].bitcast(I32), in_=tab_scales.rearrange("a q t -> (a q) t").bitcast(I32)
+        )
+        load_plane(0, 0)
+        nc.sync.dma_start(idx3[:], offs3)
+        nc.sync.dma_start(idx2[:], offs2)
+        nc.vector.tensor_copy(picked_sc[:], tab_sc[:].indirect(idx[:]))
+        load_w4_scales()
+        load_plane(0, 1)
+        load_wb(0)
+        load_plane(0, 2)
+        load_plane(0, 3)
+        w4_raw = sbuf([P, PASSES, 2 * H], U8, "w4_raw")
+        nc.sync.dma_start(out=w4_raw[:].bitcast(I32), in_=w4_words.rearrange("a p c -> p a c").bitcast(I32))
+        load_tab(0)
+        load_plane(1, 0)
+        move_scale_rows(0)
+        load_wb(1)
+        load_plane(1, 1)
+        load_plane(1, 2)
+        move_scale_rows(1)
+        load_tab(1)
+        load_plane(1, 3)
+        flux_0 = load_flux(0, CHUNK, "wt_codes")
+        var_t = keep.tile([P, PACK], F32, name="var_t")
+        nc.sync.dma_start(out=var_t[:], in_=var.rearrange("(m t) -> m t", t=PACK))
+        step_t = keep.tile([P, PASSES, PACK], F32, name="step_t")
+        nc.sync.dma_start(out=step_t[:], in_=step.rearrange("(a p i) -> p a i", a=PASSES, i=PACK))
+        flux_1 = load_flux(j1, CHUNK, "flux1")
+        flux_2 = load_flux(j2, CHUNK, "flux2")
+        flux_3 = load_flux(j3, CHUNK, "flux3")
 
-        def plane_arrives(rows, a, i, rooms):
-            for c in range(2):
-                pick(rooms[c], a, i, c * CHUNK, CHUNK)
-            for c in range(2):
-                subtract(rows[c][:, i, :], a, i, c * CHUNK, CHUNK, rooms[c])
+        w4_sc = reorder_w4_scales()
 
-        rows_0 = sbuf([P, PACK, HALF], F32, "rows_0", "xa")
-        halves_0 = [rows_0[:, :, c * CHUNK : (c + 1) * CHUNK] for c in range(2)]
-        rows_1 = [sbuf([P, PACK, CHUNK], F32, "rows_1", "xc%d" % c) for c in range(2)]
-        ahead = sbuf([P, PACK, HALF], F32, "ahead")
+        def pair_rooms(n, tag):
+            return [sbuf([P, 2, n], F32, "pair", side + tag) for side in ("out", "in")]
 
-        def pick_ahead(i):
-            pick(ahead[:, i, :], 0, i, HALF, HALF)
+        def pick_both(rooms, a, i, j0, n):
+            for room, lst in zip(rooms, (idx3, idx2)):
+                pick(room[:, i % 2, :], lst, a, i, j0, n)
 
-        for i, tag in enumerate(("slot_u", "slot_t", "slot_u")):
-            picked = sbuf([P, HALF], F32, "picked", tag)
-            pick(picked[:], 0, i, 0, HALF)
-            pick_ahead(i)
-            subtract(rows_0[:, i, :], 0, i, 0, HALF, picked[:])
-        prepare_wb(0, None)
-        plane_arrives(halves_0, 0, 3, room("slot_w") + room("slot_v"))
-        woven = weave(nc.scalar.copy, [rows_0[:]], HALF, "xb_a")
-        w4_w, w4_sc = reorder_w4()
-        load_flux(0, 3, "w4_raw")
-        prepare_wb(1, "slot_v")
-        plane_arrives(rows_1, 1, 0, room("slot_a") + room("slot_w"))
-        quantise_x(0, 0, woven[:, 0 : CHUNK * PACK], CHUNK, "x00", None, "slot_a")
-        quantise_x(0, j1, woven[:, CHUNK * PACK :], CHUNK, "x01", None, "slot_w")
-        gather_words(0, 0, HALF, "slot_b")
-        model_0 = [bank([P, H], "model", b) for b in (0, 1)]
-        model_1 = [bank([P, H], "model", b) for b in (2, 3)]
-        for k, kind in enumerate(("x", "table")):
-            turned_pass(model_0, kind, 0, 0, k == 0, False)
-            turned_pass(model_1, kind, 0, j1, k == 0, False)
-        load_plane(1, 3, "x00_codes")
-        load_tab(1, "x01_codes")
-        load_flux_by_slot(3, "slot_b")
-        plane_arrives(rows_1, 1, 1, room("xa") + room("xb_a"))
-        pick_ahead(3)
-        plane_arrives(rows_1, 1, 2, room("slot_w", 2))
-        wt_q = quantise("wt", wt_both[:], PASSES * H * PACK, "xb_a", "slot_a")
-        gather_words(0, j2, CHUNK, "slot_w")
-        laid_0 = lay_flux(0, (4, 5), "big1")
-        laid_1 = lay_flux(1, (6, 7), "mid1")
-        laid_2 = lay_flux(2, (4, 5), "big0")
-        plane_arrives(rows_1, 1, 3, room("w4_raw", 2))
-        woven_0 = weave(nc.scalar.copy, [rows_1[0][:]], CHUNK, "wt_both")
-        woven_1 = weave(nc.scalar.copy, [rows_1[1][:]], CHUNK, "xb1")
-        gather_words(1, 0, HALF, "w4_raw", CHUNK)
-        turned_pass(model_0, "table", 1, 0, False, False)
-        quantise_x(1, 0, woven_0, CHUNK, "x10")
-        turned_pass(model_0, "x", 1, 0, False, True)
-        gather_words(0, j3, CHUNK, "xc0")
-        gather_words(1, j2, CHUNK, "wt_both")
-        quantise_x(1, j1, woven_1, CHUNK, "x11")
-        turned_pass(model_1, "x", 1, j1, False, False)
-        turned_pass(model_1, "table", 1, j1, False, True)
-        res_0 = turned_residual(model_0, laid_0, (6, 7))
-        res_1 = turned_residual(model_1, laid_1, (4, 5), 2)
-        sq_0 = square_banks(res_0, "sq0")
-        woven = pool_difference(0, j2, ahead[:, :, 0:CHUNK], ("xc1", "xb1"), "xg0")
-        inv_0 = woven_squares(whole_roots(sq_0, "root0b"), ("inv0", "res0"))
-        sq_1 = square_banks(res_1, "sq1")
-        inv_1 = woven_squares(whole_roots(sq_1, "root1a"), ("inv1", "slot_t"))
-        outside = pick_outside("x11_codes", 1, j2)
-        quantise_x(0, j2, woven, CHUNK, "x02")
-        model_2 = [bank([P, H], "model", b) for b in (0, 1)]
-        turned_pass(model_2, "table", 0, j2, True, False)
-        turned_pass(model_2, "table", 1, j2, False, False)
-        turned_pass(model_2, "x", 0, j2, False, False)
-        woven = pool_difference(1, j2, outside[:], ("xb1", "xg0"), "xg1")
-        psi_0 = bank_influence(res_0, inv_0, "psi_b0")
-        gather_words(1, j3, CHUNK, "root0b")
-        psi_q0 = quantise("psi0", psi_0[:], CHUNK * PACK, None, "x11_codes")
-        quantise_x(1, j2, woven, CHUNK, "x10", None, "res0")
-        turned_pass(model_2, "x", 1, j2, False, True)
-        psi_1 = bank_influence(res_1, inv_1, "psi_b1")
-        psi_q1 = quantise("psi1", psi_1[:], CHUNK * PACK)
-        second_product(psi_q0, 0, CHUNK, 0, "root1a", [2, 3])
-        res_2 = turned_residual(model_2, laid_2, (6, 7))
-        second_product(psi_q0, 0, CHUNK, 1, "w4_raw", [4, 5])
-        units = (j3, j3 + P)
-        woven = pool_difference(0, j3, ahead[:, :, CHUNK:], ("inv1", "slot_t"), "xg0")
-        last = pick_outside("psi_b1", 1, j3)
-        outside = [last[:, i, :] for i in range(PACK)]
-        sq_2 = square_banks(res_2, "sq0")
-        inv_2 = woven_squares(whole_roots(sq_2, "sq1"), ("inv0", "mid1"))
-        second_product(psi_q1, j1, CHUNK, 0, "big1", [2, 3], (), 2)
-        second_product(psi_q1, j1, CHUNK, 1, "xb0", [4, 5], (), 2)
-        models = [bank([P, PACK, P], "model", b) for b in (0, 1)]
+        def pair_difference(dst, rooms, k):
+            weave(dst, rooms[1][:], rooms[0][:], ALU.subtract, pairs_of_slots[k])
+
+        woven_0 = sbuf([P, j3 * PACK], BF16, "woven0")
+        for k in range(2):
+            rooms = pair_rooms(j3, "0%d" % k)
+            for i in (2 * k, 2 * k + 1):
+                pick_both(rooms, 0, i, 0, j3)
+                if i == 2:
+                    wb_b = weave_wb(0)
+                    quantise_wb(0, wb_b)
+                    turn_wb(0, wb_b)
+            pair_difference(woven_0[:], rooms, k)
+        w4_w = reorder_w4_words()
+        gather_words(0, 0, j3, "words0")
+        rooms = pair_rooms(j2, "10")
+        pick_both(rooms, 1, 0, 0, j2)
+        wb_b = weave_wb(1)
+        turn_wb(1, wb_b)
+        pick_both(rooms, 1, 1, 0, j2)
+        quantise_x(units(0, 0, j3), woven_0[:], "big1", "x0_sc", j2)
+        quantise_wb(1, wb_b)
+        models = [model_banks((2 * c, 2 * c + 1), CHUNK) for c in range(3)]
+        for c in range(3):
+            model_pass(models[c], "table", 0, c * CHUNK, CHUNK, start=True)
+        for c in range(3):
+            model_pass(models[c], "x", 0, c * CHUNK, CHUNK)
+        woven_1 = sbuf([P, j2 * PACK], BF16, "woven1", "mid1")
+        pair_difference(woven_1[:], rooms, 0)
+        rooms = [pair_rooms(CHUNK, "11%d" % c) for c in range(2)]
+        for c in range(2):
+            pick_both(rooms[c], 1, 2, c * CHUNK, CHUNK)
+        gather_words(1, 0, j2, "words1")
+        for c in range(2):
+            model_pass(models[c], "table", 1, c * CHUNK, CHUNK)
+        halves = [woven_1[:, c * CHUNK * PACK : (c + 1) * CHUNK * PACK] for c in range(2)]
+        for c in range(2):
+            pick_both(rooms[c], 1, 3, c * CHUNK, CHUNK)
+            pair_difference(halves[c], rooms[c], 1)
+        quantise_x(units(1, 0, CHUNK), halves[0], "x1_codes", "x1_sc")
+        model_pass(models[0], "x", 1, 0, CHUNK, stop=True)
+        gather_words(1, j2, 2 * CHUNK, "in110")
+        quantise_x(units(1, j1, CHUNK), halves[1], "x1_codes", "x1c_sc")
+        model_pass(models[1], "x", 1, j1, CHUNK, stop=True)
+
+        res_0 = residual(models[0], flux_0, CHUNK, "mid0")
+        model_pass(models[2], "table", 1, j2, CHUNK)
+        model_1 = copy_model(models[1], CHUNK, "model1")
+        wt_q = quantise(wt_both[:], PASSES * H * PACK, "wt_codes", "wt_sc")
+        res_1 = sbuf([P, PACK, CHUNK], F32, "res", "res1")
+        nc.gpsimd.tensor_tensor(flat(res_1[:]), flat(flux_1[:]), flat(model_1[:]), ALU.subtract)
+        inv_0 = invert(res_0, CHUNK, "inv0")
+        both = sbuf([P, 2, PACK, CHUNK], F32, "rows", "wt_both")
+        for i in range(PACK):
+            pick(both[:, 0, i, :], idx3, 1, i, j2, CHUNK)
+            pick(both[:, 1, i, :], idx2, 1, i, j2, CHUNK)
+        inv_1 = invert(res_1, CHUNK, "inv1")
+        psi_q0 = quantise(pool_influence(res_0, inv_0, CHUNK, "handed")[:], CHUNK * PACK, "psi_codes0", "psi_sc0")
+        woven = sbuf([P, CHUNK * PACK], BF16, "woven", "handed")
+        weave(woven[:], both[:, 1], both[:, 0], ALU.subtract)
+        finish(psi_q0, 0, CHUNK, "big0", ((0, 1), (2, 3)))
+        outside = pick_rows(idx3, 0, j3, CHUNK, "inv0")
+        quantise_x(units(1, j2, CHUNK), woven[:], "x1b_codes", "x1b_sc")
+        model_pass(models[2], "x", 1, j2, CHUNK, stop=True)
+        psi_1 = pool_influence(res_1, inv_1, CHUNK, "handed")
+        gather_words(0, j3, CHUNK, "wt_both")
+        model_last, model_unit = model_banks((6,), P), model_banks((7,), P)
+        res_2 = residual(models[2], flux_2, CHUNK, "mid1")
         for a in range(PASSES):
-            for u in range(2):
-                direct_pass(models[u : u + 1], "table", a, units[u], P, a == 0, False)
-        quantise_x(0, j3, woven, CHUNK, "x02")
-        for u in range(2):
-            direct_pass(models[u : u + 1], "x", 0, units[u], P, False, False)
-
-        def unit_rows(u, rows, planes_now):
-            for i in planes_now:
-                subtract(rows[:, i, :], 1, i, units[u], P, outside[i][:, u * P : (u + 1) * P])
-
-        def close_unit(u, rows, tag, name):
-            quantise_x(1, units[u], weave(nc.vector.tensor_copy, [rows[:]], P, tag), P, name)
-            direct_pass(models[u : u + 1], "x", 1, units[u], P, False, True)
-
-        def invert_unit(u, tags):
-            res = direct_residual(models[u], flux_sb[3][:, :, u * P : (u + 1) * P], P, tags[0], 1 + u)
-            return res, square_rows(roots(square_rows(pairs_of(res), P, tags[1]), P, tags[2:4]), P, tags[4])
-
-        rows_a = sbuf([P, PACK, P], F32, "rows_a", "slot_t")
-        unit_rows(0, rows_a, range(PACK))
-        psi_2 = bank_influence(res_2, inv_2, "xg1")
-        close_unit(0, rows_a, "inv0", "x11")
-        psi_q2 = quantise("psi0", psi_2[:], CHUNK * PACK)
-        rows_b = sbuf([P, PACK, P], F32, "rows_b", "mid1")
-        unit_rows(1, rows_b, range(PACK))
-        second_product(psi_q2, j2, CHUNK, 0, "sq0", [2, 3], (), 2)
-        res_a, inv_a = invert_unit(0, ("neg0", "mid0", "neg2", "neg3", "wt_both"))
-        close_unit(1, rows_b, "x11_codes", "x10")
-        idle = bank([P, H], "idle", 2)
-        for k in range(2):
-            turned_pass([idle], "x", 1, units[1], True, True)
-        res_b, inv_b = invert_unit(1, ("xb1", "big0", "neg1", "root1b", "xc1"))
-        psi_qa = quantise("tq0", influence([(res_a[:], inv_a[:])], P, "psi_b0")[:], H)
-        psi_qb = quantise("tq1", influence([(res_b[:], inv_b[:])], P, "inv1")[:], H)
-        second_product(psi_q2, j2, CHUNK, 1, "w4_raw", [4, 5], (0, 1), 2)
-        idle = bank([P, H], "idle", 5)
-        for k in range(2):
-            turned_pass([idle], "x", 1, units[1], True, True)
-        second_product(psi_qa, j3, P, 0, "root1a", [6])
-        second_product(psi_qa, j3, P, 1, "sq1", [7])
-        second_product(psi_qb, j3 + P, P, 0, "big1", [0, 2], (0,), 2)
-        second_product(psi_qb, j3 + P, P, 1, "xb0", [1, 3], (0,), 2)
+            model_pass(model_unit, "table", a, j_unit, P, start=(a == 0))
+            model_pass(model_last, "table", a, j_last, P, start=(a == 0))
+        psi_q1 = quantise(psi_1[:], CHUNK * PACK, "flux2", "psi_sc1")
+        inside = pick_rows(idx2, 0, j3, CHUNK, "x1b_codes")
+        inv_2 = invert(res_2, CHUNK, "woven0")
+        finish(psi_q1, j1, CHUNK, "big1", ((0, 1), (2, 3)))
+        outside_1 = pick_rows(idx3, 1, j3, CHUNK, "inv1")
+        psi_q2 = quantise(pool_influence(res_2, inv_2, CHUNK, "handed")[:], CHUNK * PACK, "psi_codes0", "psi_sc0")
+        woven = sbuf([P, (CHUNK + P) * PACK], BF16, "woven", "handed")
+        weave(woven[:, 0 : CHUNK * PACK], inside[:], outside[:], ALU.subtract)
+        inside_1 = [pick_rows(idx2, 1, j0, P, tag) for j0, tag in ((j_unit, "woven0"), (j_last, "mid1"))]
+        weave(woven[:, CHUNK * PACK :], inside_1[0][:], outside_1[:, :, P:], ALU.subtract)
+        finish(psi_q2, j2, CHUNK, "big0", ((0, 1), (2, 3)))
+        quantise_x([(0, j_last), (0, j_unit), (1, j_unit)], woven[:], "x1_codes", "x1_sc")
+        woven = sbuf([P, P * PACK], BF16, "woven", "handed")
+        weave(woven[:], inside_1[1][:], outside_1[:, :, 0:P], ALU.subtract)
+        model_pass(model_unit, "x", 0, j_unit, P)
+        model_pass(model_unit, "x", 1, j_unit, P, stop=True)
+        model_pass(model_last, "x", 0, j_last, P)
+        quantise_x([(1, j_last)], woven[:], "psi_codes2", "psi_sc2")
+        model_pass(model_last, "x", 1, j_last, P, stop=True)
+        res_unit = residual(model_unit, flux_3[:, :, P:], P, "res1")
+        inv_unit = invert(res_unit, P, "inv0")
+        res_last = residual(model_last, flux_3[:, :, 0:P], P, "mid0")
+        inv_last = invert(res_last, P, "flux1")
+        psi_qu = quantise(vector_influence(res_unit, inv_unit, P, "handed")[:], H, "psi_codes1", "psi_sc1")
+        psi_ql = quantise(vector_influence(res_last, inv_last, P, "x1b_codes")[:], H, "psi_codes2", "psi_sc2")
+        finish(psi_qu, j_unit, P, "out10", ((4,), (5,)), ((), (0,)))
+        finish(psi_ql, j_last, P, "in10", ((0, 2), (1, 3)), ((0,), (0,)), 2)

@@ -112,8 +112,8 @@ def tile_list_transit_cauchy_step_kernel(
                 pick(rows[:, i, :], lst, a, i, j0, n)
             return rows
 
-        def weave(dst, first, second, op, slots=slice(0, PACK)):
-            nc.gpsimd.tensor_tensor(
+        def weave(dst, first, second, op, slots=slice(0, PACK), engine=nc.gpsimd):
+            engine.tensor_tensor(
                 dst.rearrange("p (c e t) -> p c t e", e=RUN, t=PACK)[:, :, slots, :],
                 first.rearrange("p t (c e) -> p c t e", e=RUN),
                 second.rearrange("p t (c e) -> p c t e", e=RUN),
@@ -247,19 +247,9 @@ def tile_list_transit_cauchy_step_kernel(
                 nc.scalar.activation(inv[:, rows, :], inv[:, rows, :], ACT.Square)
             return inv
 
-        def pool_influence(res, inv, n, tag):
+        def influence(res, inv, n, tag, engine):
             psi_b = sbuf([P, n * PACK], BF16, "psi_b", tag)
-            weave(psi_b[:], res[:], inv[:], ALU.mult)
-            return psi_b
-
-        def vector_influence(res, inv, n, tag):
-            psi_b = sbuf([P, n * PACK], BF16, "psi_b", tag)
-            nc.vector.tensor_tensor(
-                psi_b[:].rearrange("m (c e t) -> m c t e", e=RUN, t=PACK),
-                res[:].rearrange("m t (c e) -> m c t e", e=RUN),
-                inv[:].rearrange("m t (c e) -> m c t e", e=RUN),
-                ALU.mult,
-            )
+            weave(psi_b[:], res[:], inv[:], ALU.mult, engine=engine)
             return psi_b
 
         def second_product(psi_q, j0, n, a, staged, banks, on_vector=(), rows_a_store=PACK):
@@ -399,45 +389,63 @@ def tile_list_transit_cauchy_step_kernel(
         for i in range(PACK):
             pick(both[:, 0, i, :], idx3, 1, i, j2, CHUNK)
             pick(both[:, 1, i, :], idx2, 1, i, j2, CHUNK)
+
+        def pick_pair(lst, k, tag):
+            room = sbuf([P, 2, CHUNK], F32, "pair", tag)
+            for e in range(2):
+                pick(room[:, e, :], lst, 0, 2 * k + e, j3, CHUNK)
+            return room
+
+        out_low = pick_pair(idx3, 0, "x1_codes")
         inv_1 = invert(res_1, CHUNK, "inv1")
-        psi_q0 = quantise(pool_influence(res_0, inv_0, CHUNK, "handed")[:], CHUNK * PACK, "psi_codes0", "psi_sc0")
+        psi_q0 = quantise(influence(res_0, inv_0, CHUNK, "handed", nc.gpsimd)[:], CHUNK * PACK, "psi_codes0", "psi_sc0")
         woven = sbuf([P, CHUNK * PACK], BF16, "woven", "handed")
         weave(woven[:], both[:, 1], both[:, 0], ALU.subtract)
         finish(psi_q0, 0, CHUNK, "big0", ((0, 1), (2, 3)))
-        outside = pick_rows(idx3, 0, j3, CHUNK, "inv0")
+        in_low = pick_pair(idx2, 0, "inv0")
+        out_high = pick_pair(idx3, 1, "mid0")
         quantise_x(units(1, j2, CHUNK), woven[:], "x1b_codes", "x1b_sc")
         model_pass(models[2], "x", 1, j2, CHUNK, stop=True)
-        psi_1 = pool_influence(res_1, inv_1, CHUNK, "handed")
+        psi_1 = influence(res_1, inv_1, CHUNK, "handed", nc.gpsimd)
         gather_words(0, j3, CHUNK, "wt_both")
         model_last, model_unit = model_banks((6,), P), model_banks((7,), P)
         res_2 = residual(models[2], flux_2, CHUNK, "mid1")
         for a in range(PASSES):
             model_pass(model_unit, "table", a, j_unit, P, start=(a == 0))
             model_pass(model_last, "table", a, j_last, P, start=(a == 0))
+        in_high = pick_pair(idx2, 1, "x1b_codes")
         psi_q1 = quantise(psi_1[:], CHUNK * PACK, "flux2", "psi_sc1")
-        inside = pick_rows(idx2, 0, j3, CHUNK, "x1b_codes")
         inv_2 = invert(res_2, CHUNK, "woven0")
-        finish(psi_q1, j1, CHUNK, "big1", ((0, 1), (2, 3)))
-        outside_1 = pick_rows(idx3, 1, j3, CHUNK, "inv1")
-        psi_q2 = quantise(pool_influence(res_2, inv_2, CHUNK, "handed")[:], CHUNK * PACK, "psi_codes0", "psi_sc0")
         woven = sbuf([P, (CHUNK + P) * PACK], BF16, "woven", "handed")
-        weave(woven[:, 0 : CHUNK * PACK], inside[:], outside[:], ALU.subtract)
-        inside_1 = [pick_rows(idx2, 1, j0, P, tag) for j0, tag in ((j_unit, "woven0"), (j_last, "mid1"))]
-        weave(woven[:, CHUNK * PACK :], inside_1[0][:], outside_1[:, :, P:], ALU.subtract)
-        finish(psi_q2, j2, CHUNK, "big0", ((0, 1), (2, 3)))
+        pair_difference(woven[:, 0 : CHUNK * PACK], (out_low, in_low), 0)
+        pair_difference(woven[:, 0 : CHUNK * PACK], (out_high, in_high), 1)
+        finish(psi_q1, j1, CHUNK, "big1", ((0, 1), (2, 3)))
+        outside = sbuf([P, PACK, P], F32, "rows", "inv1")
+        inside = sbuf([P, PACK, P], F32, "rows", "res1")
+        for i in range(PACK):
+            pick(outside[:, i, :], idx3, 1, i, j_unit, P)
+            pick(inside[:, i, :], idx2, 1, i, j_unit, P)
+        weave(woven[:, CHUNK * PACK :], inside[:], outside[:], ALU.subtract)
+        outside = pick_rows(idx3, 1, j_last, P, "inv0")
         quantise_x([(0, j_last), (0, j_unit), (1, j_unit)], woven[:], "x1_codes", "x1_sc")
-        woven = sbuf([P, P * PACK], BF16, "woven", "handed")
-        weave(woven[:], inside_1[1][:], outside_1[:, :, 0:P], ALU.subtract)
+        psi_2 = influence(res_2, inv_2, CHUNK, "handed", nc.gpsimd)
         model_pass(model_unit, "x", 0, j_unit, P)
         model_pass(model_unit, "x", 1, j_unit, P, stop=True)
         model_pass(model_last, "x", 0, j_last, P)
+        inside = pick_rows(idx2, 1, j_last, P, "res1")
+        res_unit = residual(model_unit, flux_3[:, :, P:], P, "model1")
+        inv_unit = invert(res_unit, P, "in111")
+        psi_q2 = quantise(psi_2[:], CHUNK * PACK, "x1_codes", "psi_sc0")
+        woven = sbuf([P, P * PACK], BF16, "woven", "handed")
+        weave(woven[:], inside[:], outside[:], ALU.subtract, engine=nc.vector)
+        second = sbuf([P, PASSES, PACK, CHUNK], F32, "staged", "wt_both")
+        second_product(psi_q2, j2, CHUNK, 0, second[:, 0], (0, 1), (), 2)
         quantise_x([(1, j_last)], woven[:], "psi_codes2", "psi_sc2")
         model_pass(model_last, "x", 1, j_last, P, stop=True)
-        res_unit = residual(model_unit, flux_3[:, :, P:], P, "res1")
-        inv_unit = invert(res_unit, P, "inv0")
-        res_last = residual(model_last, flux_3[:, :, 0:P], P, "mid0")
-        inv_last = invert(res_last, P, "flux1")
-        psi_qu = quantise(vector_influence(res_unit, inv_unit, P, "handed")[:], H, "psi_codes1", "psi_sc1")
-        psi_ql = quantise(vector_influence(res_last, inv_last, P, "x1b_codes")[:], H, "psi_codes2", "psi_sc2")
-        finish(psi_qu, j_unit, P, "out10", ((4,), (5,)), ((), (0,)))
+        psi_qu = quantise(influence(res_unit, inv_unit, P, "handed", nc.vector)[:], H, "psi_codes1", "psi_sc1")
+        res_last = residual(model_last, flux_3[:, :, 0:P], P, "out110")
+        inv_last = invert(res_last, P, "out111")
+        second_product(psi_q2, j2, CHUNK, 1, second[:, 1], (2, 3), (0, 1), 2)
+        finish(psi_qu, j_unit, P, "out10", ((4,), (5,)), ((0,), ()))
+        psi_ql = quantise(influence(res_last, inv_last, P, "x1b_codes", nc.vector)[:], H, "psi_codes2", "psi_sc2")
         finish(psi_ql, j_last, P, "in10", ((0, 2), (1, 3)), ((0,), (0,)), 2)

@@ -106,6 +106,9 @@ def tile_list_transit_cauchy_step_kernel(
         def pick(dst, lst, a, i, j0, n):
             nc.vector.tensor_copy(dst, planes[a, i][:].indirect(entries(lst, j0, n)))
 
+        def subtract(dst, a, i, j0, n, outside):
+            nc.vector.tensor_tensor(dst, planes[a, i][:].indirect(entries(idx2, j0, n)), outside, ALU.subtract)
+
         def pick_rows(lst, a, j0, n, tag):
             rows = sbuf([P, PACK, n], F32, "rows", tag)
             for i in range(PACK):
@@ -237,50 +240,65 @@ def tile_list_transit_cauchy_step_kernel(
                 nc.scalar.copy(model_sb[:, rows, :], model[:])
             return model_sb
 
-        def invert(res, n, tag):
+        def invert(res, n, tag, groups=1):
             inv = sbuf([P, PACK, n], F32, "inv", tag)
-            for rows in slot_groups(2):
-                nc.scalar.activation(inv[:, rows, :], res[:, rows, :], ACT.Square)
-            for t in range(PACK):
-                nc.scalar.activation(inv[:, t, :], inv[:, t, :], ACT.Abs_reciprocal_sqrt, bias=var_t[:, t : t + 1])
-            for rows in slot_groups(2):
-                nc.scalar.activation(inv[:, rows, :], inv[:, rows, :], ACT.Square)
+            for group in slot_groups(groups):
+                halves = [slice(t, t + 2) for t in range(group.start, group.stop, 2)]
+                for rows in halves:
+                    nc.scalar.activation(inv[:, rows, :], res[:, rows, :], ACT.Square)
+                for t in range(group.start, group.stop):
+                    nc.scalar.activation(inv[:, t, :], inv[:, t, :], ACT.Abs_reciprocal_sqrt, bias=var_t[:, t : t + 1])
+                for rows in halves:
+                    nc.scalar.activation(inv[:, rows, :], inv[:, rows, :], ACT.Square)
             return inv
+
+        def pool_residual(model_sb, flux_sb, n, tag, groups):
+            res = sbuf([P, PACK, n], F32, "res", tag)
+            for rows in slot_groups(groups):
+                nc.gpsimd.tensor_tensor(res[:, rows, :], flux_sb[:, rows, :], model_sb[:, rows, :], ALU.subtract)
+            return res
 
         def influence(res, inv, n, tag, engine):
             psi_b = sbuf([P, n * PACK], BF16, "psi_b", tag)
             weave(psi_b[:], res[:], inv[:], ALU.mult, engine=engine)
             return psi_b
 
-        def second_product(psi_q, j0, n, a, staged, banks, on_vector=(), rows_a_store=PACK):
+        def second_matmuls(psi_q, n, a, banks):
             psi_codes, psi_sc = psi_q
             wt_codes, wt_sc = wt_q
             per_bank = PACK // len(banks)
-            for k, b in enumerate(banks):
-                first = a * PACK + k * per_bank
-                back = bank([P, per_bank, n], "back", b)
-                for e in range(per_bank):
-                    cols = slice((first + e) * P, (first + e + 1) * P)
-                    nc.tensor.matmul_mx(
-                        out=back[:, e, :],
-                        lhsT=wt_codes[:, cols].bitcast(FP8X4),
-                        lhsT_scale=wt_sc[:, cols],
-                        rhs=psi_codes[:].bitcast(FP8X4),
-                        rhs_scale=psi_sc[:],
-                        start=True,
-                        stop=True,
-                    )
-                for e in range(per_bank):
-                    i = (first + e) % PACK
-                    factor = step_t[:, a, i : i + 1]
-                    if k in on_vector:
-                        nc.vector.tensor_scalar(staged[:, i, :], back[:, e, :], factor, None, ALU.mult)
-                    else:
-                        nc.scalar.activation(staged[:, i, :], back[:, e, :], ACT.Copy, scale=factor)
-                done = first % PACK + per_bank
-                if done % rows_a_store == 0:
-                    rows_done = slice(done - rows_a_store, done)
-                    nc.sync.dma_start(out=out_rows[a, :, rows_done, j0 : j0 + n], in_=staged[:, rows_done, :])
+            backs = [bank([P, per_bank, n], "back", b) for b in banks]
+            for i in range(PACK):
+                cols = slice((a * PACK + i) * P, (a * PACK + i + 1) * P)
+                nc.tensor.matmul_mx(
+                    out=backs[i // per_bank][:, i % per_bank, :],
+                    lhsT=wt_codes[:, cols].bitcast(FP8X4),
+                    lhsT_scale=wt_sc[:, cols],
+                    rhs=psi_codes[:].bitcast(FP8X4),
+                    rhs_scale=psi_sc[:],
+                    start=True,
+                    stop=True,
+                )
+            return backs
+
+        def scale_and_store(backs, j0, n, a, staged, k, on_vector, rows_a_store):
+            per_bank = PACK // len(backs)
+            for e in range(per_bank):
+                i = k * per_bank + e
+                factor = step_t[:, a, i : i + 1]
+                if on_vector:
+                    nc.vector.tensor_scalar(staged[:, i, :], backs[k][:, e, :], factor, None, ALU.mult)
+                else:
+                    nc.scalar.activation(staged[:, i, :], backs[k][:, e, :], ACT.Copy, scale=factor)
+            done = (k + 1) * per_bank
+            if done % rows_a_store == 0:
+                rows_done = slice(done - rows_a_store, done)
+                nc.sync.dma_start(out=out_rows[a, :, rows_done, j0 : j0 + n], in_=staged[:, rows_done, :])
+
+        def second_product(psi_q, j0, n, a, staged, banks, on_vector=(), rows_a_store=PACK):
+            backs = second_matmuls(psi_q, n, a, banks)
+            for k in range(len(banks)):
+                scale_and_store(backs, j0, n, a, staged, k, k in on_vector, rows_a_store)
 
         def finish(psi_q, j0, n, tag, banks, on_vector=((), ()), rows_a_store=PACK):
             staged = sbuf([P, PASSES, PACK, n], F32, "staged", tag)
@@ -315,7 +333,7 @@ def tile_list_transit_cauchy_step_kernel(
         move_scale_rows(1)
         load_tab(1)
         load_plane(1, 3)
-        flux_0 = load_flux(0, CHUNK, "wt_codes")
+        flux_0 = load_flux(0, CHUNK, "flux0")
         var_t = keep.tile([P, PACK], F32, name="var_t")
         nc.sync.dma_start(out=var_t[:], in_=var.rearrange("(m t) -> m t", t=PACK))
         step_t = keep.tile([P, PASSES, PACK], F32, name="step_t")
@@ -362,33 +380,27 @@ def tile_list_transit_cauchy_step_kernel(
             model_pass(models[c], "x", 0, c * CHUNK, CHUNK)
         woven_1 = sbuf([P, j2 * PACK], BF16, "woven1", "mid1")
         pair_difference(woven_1[:], rooms, 0)
-        rooms = [pair_rooms(CHUNK, "11%d" % c) for c in range(2)]
-        for c in range(2):
-            pick_both(rooms[c], 1, 2, c * CHUNK, CHUNK)
+        outside = [sbuf([P, j2], F32, "outside", "out1%d" % i) for i in (2, 3)]
+        apart = sbuf([P, 2, j2], F32, "apart")
+        pick(outside[0][:], idx3, 1, 2, 0, j2)
         gather_words(1, 0, j2, "words1")
         for c in range(2):
             model_pass(models[c], "table", 1, c * CHUNK, CHUNK)
+        pick(outside[1][:], idx3, 1, 3, 0, j2)
+        subtract(apart[:, 0, :], 1, 2, 0, j2, outside[0][:])
+        for c in range(2):
+            cols = slice(c * CHUNK, (c + 1) * CHUNK)
+            subtract(apart[:, 1, cols], 1, 3, cols.start, CHUNK, outside[1][:, cols])
         halves = [woven_1[:, c * CHUNK * PACK : (c + 1) * CHUNK * PACK] for c in range(2)]
         for c in range(2):
-            pick_both(rooms[c], 1, 3, c * CHUNK, CHUNK)
-            pair_difference(halves[c], rooms[c], 1)
-        quantise_x(units(1, 0, CHUNK), halves[0], "x1_codes", "x1_sc")
-        model_pass(models[0], "x", 1, 0, CHUNK, stop=True)
-        gather_words(1, j2, 2 * CHUNK, "in110")
-        quantise_x(units(1, j1, CHUNK), halves[1], "x1_codes", "x1c_sc")
-        model_pass(models[1], "x", 1, j1, CHUNK, stop=True)
-
-        res_0 = residual(models[0], flux_0, CHUNK, "mid0")
-        model_pass(models[2], "table", 1, j2, CHUNK)
-        model_1 = copy_model(models[1], CHUNK, "model1")
-        wt_q = quantise(wt_both[:], PASSES * H * PACK, "wt_codes", "wt_sc")
-        res_1 = sbuf([P, PACK, CHUNK], F32, "res", "res1")
-        nc.gpsimd.tensor_tensor(flat(res_1[:]), flat(flux_1[:]), flat(model_1[:]), ALU.subtract)
-        inv_0 = invert(res_0, CHUNK, "inv0")
-        both = sbuf([P, 2, PACK, CHUNK], F32, "rows", "wt_both")
-        for i in range(PACK):
-            pick(both[:, 0, i, :], idx3, 1, i, j2, CHUNK)
-            pick(both[:, 1, i, :], idx2, 1, i, j2, CHUNK)
+            nc.scalar.copy(
+                halves[c].rearrange("p (c e t) -> p c t e", e=RUN, t=PACK)[:, :, 2:4, :],
+                apart[:, :, c * CHUNK : (c + 1) * CHUNK].rearrange("p t (c e) -> p c t e", e=RUN),
+            )
+        for c, tag in enumerate(("x1_codes", "x1c_codes")):
+            quantise_x(units(1, c * CHUNK, CHUNK), halves[c], tag, "x1_sc%d" % c)
+            model_pass(models[c], "x", 1, c * CHUNK, CHUNK, stop=True)
+        wt_q = quantise(wt_both[:], PASSES * H * PACK, "apart", "wt_sc")
 
         def pick_pair(lst, k, tag):
             room = sbuf([P, 2, CHUNK], F32, "pair", tag)
@@ -396,56 +408,74 @@ def tile_list_transit_cauchy_step_kernel(
                 pick(room[:, e, :], lst, 0, 2 * k + e, j3, CHUNK)
             return room
 
-        out_low = pick_pair(idx3, 0, "x1_codes")
+        model_0 = copy_model(models[0], CHUNK, "model0")
+        model_1 = copy_model(models[1], CHUNK, "handed")
+        res_0 = pool_residual(model_0, flux_0, CHUNK, "mid0", 2)
+        res_1 = pool_residual(model_1, flux_1, CHUNK, "res1", 1)
+        inv_0 = invert(res_0, CHUNK, "inv0", 2)
+        both = sbuf([P, 2, PACK, CHUNK], F32, "rows", "x1_codes")
+        for i in range(PACK):
+            pick(both[:, 0, i, :], idx3, 1, i, j2, CHUNK)
+            pick(both[:, 1, i, :], idx2, 1, i, j2, CHUNK)
+        gather_words(1, j2, 2 * CHUNK, "wt_both")
+        model_pass(models[2], "table", 1, j2, CHUNK)
+        out_low = pick_pair(idx3, 0, "x1c_codes")
         inv_1 = invert(res_1, CHUNK, "inv1")
-        psi_q0 = quantise(influence(res_0, inv_0, CHUNK, "handed", nc.gpsimd)[:], CHUNK * PACK, "psi_codes0", "psi_sc0")
         woven = sbuf([P, CHUNK * PACK], BF16, "woven", "handed")
         weave(woven[:], both[:, 1], both[:, 0], ALU.subtract)
-        finish(psi_q0, 0, CHUNK, "big0", ((0, 1), (2, 3)))
-        in_low = pick_pair(idx2, 0, "inv0")
-        out_high = pick_pair(idx3, 1, "mid0")
         quantise_x(units(1, j2, CHUNK), woven[:], "x1b_codes", "x1b_sc")
         model_pass(models[2], "x", 1, j2, CHUNK, stop=True)
-        psi_1 = influence(res_1, inv_1, CHUNK, "handed", nc.gpsimd)
-        gather_words(0, j3, CHUNK, "wt_both")
-        model_last, model_unit = model_banks((6,), P), model_banks((7,), P)
+        psi_early = sbuf([P, j2 * PACK], BF16, "psi_b", "handed")
+        weave(psi_early[:, 0 : CHUNK * PACK], res_0[:], inv_0[:], ALU.mult)
+        weave(psi_early[:, CHUNK * PACK :], res_1[:], inv_1[:], ALU.mult)
+        in_low = pick_pair(idx2, 0, "x1_codes")
         res_2 = residual(models[2], flux_2, CHUNK, "mid1")
-        for a in range(PASSES):
-            model_pass(model_unit, "table", a, j_unit, P, start=(a == 0))
-            model_pass(model_last, "table", a, j_last, P, start=(a == 0))
-        in_high = pick_pair(idx2, 1, "x1b_codes")
-        psi_q1 = quantise(psi_1[:], CHUNK * PACK, "flux2", "psi_sc1")
         inv_2 = invert(res_2, CHUNK, "woven0")
+        out_high = pick_pair(idx3, 1, "x1b_codes")
+        in_high = pick_pair(idx2, 1, "flux2")
+        psi_q0 = quantise(psi_early[:], j2 * PACK, "psi_codes0", "psi_sc0")
+        for a in range(PASSES):
+            staged = sbuf([P, PACK, j2], F32, "staged", "big%d" % a)
+            second_product(psi_q0, 0, j2, a, staged[:], (0, 1, 2, 3), (), 2)
         woven = sbuf([P, (CHUNK + P) * PACK], BF16, "woven", "handed")
         pair_difference(woven[:, 0 : CHUNK * PACK], (out_low, in_low), 0)
         pair_difference(woven[:, 0 : CHUNK * PACK], (out_high, in_high), 1)
-        finish(psi_q1, j1, CHUNK, "big1", ((0, 1), (2, 3)))
-        outside = sbuf([P, PACK, P], F32, "rows", "inv1")
-        inside = sbuf([P, PACK, P], F32, "rows", "res1")
+        gather_words(0, j3, CHUNK, "res1")
+        model_last, model_unit = model_banks((6,), P), model_banks((7,), P)
+        for a in range(PASSES):
+            model_pass(model_unit, "table", a, j_unit, P, start=(a == 0))
+            model_pass(model_last, "table", a, j_last, P, start=(a == 0))
+        both = sbuf([P, 2, PACK, P], F32, "rows", "inv1")
+        outside, inside = both[:, 0], both[:, 1]
         for i in range(PACK):
             pick(outside[:, i, :], idx3, 1, i, j_unit, P)
             pick(inside[:, i, :], idx2, 1, i, j_unit, P)
-        weave(woven[:, CHUNK * PACK :], inside[:], outside[:], ALU.subtract)
-        outside = pick_rows(idx3, 1, j_last, P, "inv0")
-        quantise_x([(0, j_last), (0, j_unit), (1, j_unit)], woven[:], "x1_codes", "x1_sc")
-        psi_2 = influence(res_2, inv_2, CHUNK, "handed", nc.gpsimd)
+        psi_2 = influence(res_2, inv_2, CHUNK, "model0", nc.gpsimd)
+        weave(woven[:, CHUNK * PACK :], inside, outside, ALU.subtract)
+        outside_last = pick_rows(idx3, 1, j_last, P, "x1_codes")
+        inside = pick_rows(idx2, 1, j_last, P, "x1c_codes")
+        quantise_x([(0, j_last), (0, j_unit), (1, j_unit)], woven[:], "unit_codes", "x1_sc0")
         model_pass(model_unit, "x", 0, j_unit, P)
         model_pass(model_unit, "x", 1, j_unit, P, stop=True)
         model_pass(model_last, "x", 0, j_last, P)
-        inside = pick_rows(idx2, 1, j_last, P, "res1")
-        res_unit = residual(model_unit, flux_3[:, :, P:], P, "model1")
-        inv_unit = invert(res_unit, P, "in111")
-        psi_q2 = quantise(psi_2[:], CHUNK * PACK, "x1_codes", "psi_sc0")
+        outside = outside_last
+        psi_q2 = quantise(psi_2[:], CHUNK * PACK, "psi_codes1", "psi_sc1")
         woven = sbuf([P, P * PACK], BF16, "woven", "handed")
         weave(woven[:], inside[:], outside[:], ALU.subtract, engine=nc.vector)
-        second = sbuf([P, PASSES, PACK, CHUNK], F32, "staged", "wt_both")
-        second_product(psi_q2, j2, CHUNK, 0, second[:, 0], (0, 1), (), 2)
         quantise_x([(1, j_last)], woven[:], "psi_codes2", "psi_sc2")
         model_pass(model_last, "x", 1, j_last, P, stop=True)
-        psi_qu = quantise(influence(res_unit, inv_unit, P, "handed", nc.vector)[:], H, "psi_codes1", "psi_sc1")
-        res_last = residual(model_last, flux_3[:, :, 0:P], P, "out110")
-        inv_last = invert(res_last, P, "out111")
-        second_product(psi_q2, j2, CHUNK, 1, second[:, 1], (2, 3), (0, 1), 2)
-        finish(psi_qu, j_unit, P, "out10", ((4,), (5,)), ((0,), ()))
-        psi_ql = quantise(influence(res_last, inv_last, P, "x1b_codes", nc.vector)[:], H, "psi_codes2", "psi_sc2")
+        res_unit = residual(model_unit, flux_3[:, :, P:], P, "res1")
+        res_last = residual(model_last, flux_3[:, :, 0:P], P, "out13")
+        inv_unit = invert(res_unit, P, "out12")
+        inv_last = invert(res_last, P, "flux0")
+        second = sbuf([P, PASSES, PACK, CHUNK], F32, "staged", "wt_both")
+        second_product(psi_q2, j2, CHUNK, 0, second[:, 0], (0, 1), (0, 1), 2)
+        psi_u = influence(res_unit, inv_unit, P, "model0", nc.vector)
+        back_2 = second_matmuls(psi_q2, CHUNK, 1, (2, 3))
+        scale_and_store(back_2, j2, CHUNK, 1, second[:, 1], 0, True, 2)
+        psi_qu = quantise(psi_u[:], H, "psi_codes0", "psi_sc0")
+        scale_and_store(back_2, j2, CHUNK, 1, second[:, 1], 1, True, 2)
+        psi_l = influence(res_last, inv_last, P, "x1b_codes", nc.vector)
+        finish(psi_qu, j_unit, P, "out10", ((4,), (5,)))
+        psi_ql = quantise(psi_l[:], H, "psi_codes2", "psi_sc2")
         finish(psi_ql, j_last, P, "in10", ((0, 2), (1, 3)), ((0,), (0,)), 2)

@@ -380,17 +380,20 @@ def tile_list_transit_cauchy_step_kernel(
             model_pass(models[c], "x", 0, c * CHUNK, CHUNK)
         woven_1 = sbuf([P, j2 * PACK], BF16, "woven1", "mid1")
         pair_difference(woven_1[:], rooms, 0)
-        outside = [sbuf([P, j2], F32, "outside", "out1%d" % i) for i in (2, 3)]
+        third = [sbuf([P, j2], F32, "third", side + "12") for side in ("out", "in")]
+        for room, lst in zip(third, (idx3, idx2)):
+            pick(room[:], lst, 1, 2, 0, j2)
         apart = sbuf([P, 2, j2], F32, "apart")
-        pick(outside[0][:], idx3, 1, 2, 0, j2)
+        nc.gpsimd.tensor_tensor(apart[:, 0, :], third[1][:], third[0][:], ALU.subtract)
         gather_words(1, 0, j2, "words1")
         for c in range(2):
             model_pass(models[c], "table", 1, c * CHUNK, CHUNK)
-        pick(outside[1][:], idx3, 1, 3, 0, j2)
-        subtract(apart[:, 0, :], 1, 2, 0, j2, outside[0][:])
+        outside = sbuf([P, j2], F32, "outside", "out13")
+        for c in range(2):
+            pick(outside[:, c * CHUNK : (c + 1) * CHUNK], idx3, 1, 3, c * CHUNK, CHUNK)
         for c in range(2):
             cols = slice(c * CHUNK, (c + 1) * CHUNK)
-            subtract(apart[:, 1, cols], 1, 3, cols.start, CHUNK, outside[1][:, cols])
+            subtract(apart[:, 1, cols], 1, 3, cols.start, CHUNK, outside[:, cols])
         halves = [woven_1[:, c * CHUNK * PACK : (c + 1) * CHUNK * PACK] for c in range(2)]
         for c in range(2):
             nc.scalar.copy(
@@ -420,7 +423,7 @@ def tile_list_transit_cauchy_step_kernel(
         gather_words(1, j2, 2 * CHUNK, "wt_both")
         model_pass(models[2], "table", 1, j2, CHUNK)
         out_low = pick_pair(idx3, 0, "x1c_codes")
-        inv_1 = invert(res_1, CHUNK, "inv1")
+        inv_1 = invert(res_1, CHUNK, "out00")
         woven = sbuf([P, CHUNK * PACK], BF16, "woven", "handed")
         weave(woven[:], both[:, 1], both[:, 0], ALU.subtract)
         quantise_x(units(1, j2, CHUNK), woven[:], "x1b_codes", "x1b_sc")
@@ -445,7 +448,7 @@ def tile_list_transit_cauchy_step_kernel(
         for a in range(PASSES):
             model_pass(model_unit, "table", a, j_unit, P, start=(a == 0))
             model_pass(model_last, "table", a, j_last, P, start=(a == 0))
-        both = sbuf([P, 2, PACK, P], F32, "rows", "inv1")
+        both = sbuf([P, 2, PACK, P], F32, "rows", "out00")
         outside, inside = both[:, 0], both[:, 1]
         for i in range(PACK):
             pick(outside[:, i, :], idx3, 1, i, j_unit, P)
@@ -459,23 +462,23 @@ def tile_list_transit_cauchy_step_kernel(
         model_pass(model_unit, "x", 1, j_unit, P, stop=True)
         model_pass(model_last, "x", 0, j_last, P)
         outside = outside_last
-        psi_q2 = quantise(psi_2[:], CHUNK * PACK, "psi_codes1", "psi_sc1")
         woven = sbuf([P, P * PACK], BF16, "woven", "handed")
         weave(woven[:], inside[:], outside[:], ALU.subtract, engine=nc.vector)
         quantise_x([(1, j_last)], woven[:], "psi_codes2", "psi_sc2")
         model_pass(model_last, "x", 1, j_last, P, stop=True)
         res_unit = residual(model_unit, flux_3[:, :, P:], P, "res1")
+        psi_q2 = quantise(psi_2[:], CHUNK * PACK, "psi_codes2", "psi_sc1")
         res_last = residual(model_last, flux_3[:, :, 0:P], P, "out13")
-        inv_unit = invert(res_unit, P, "out12")
+        inv_unit = invert(res_unit, P, "in12")
         inv_last = invert(res_last, P, "flux0")
         second = sbuf([P, PASSES, PACK, CHUNK], F32, "staged", "wt_both")
         second_product(psi_q2, j2, CHUNK, 0, second[:, 0], (0, 1), (0, 1), 2)
-        psi_u = influence(res_unit, inv_unit, P, "model0", nc.vector)
+        psi_u = influence(res_unit, inv_unit, P, "handed", nc.vector)
         back_2 = second_matmuls(psi_q2, CHUNK, 1, (2, 3))
         scale_and_store(back_2, j2, CHUNK, 1, second[:, 1], 0, True, 2)
         psi_qu = quantise(psi_u[:], H, "psi_codes0", "psi_sc0")
         scale_and_store(back_2, j2, CHUNK, 1, second[:, 1], 1, True, 2)
         psi_l = influence(res_last, inv_last, P, "x1b_codes", nc.vector)
         finish(psi_qu, j_unit, P, "out10", ((4,), (5,)))
-        psi_ql = quantise(psi_l[:], H, "psi_codes2", "psi_sc2")
+        psi_ql = quantise(psi_l[:], H, "psi_codes1", "psi_sc2")
         finish(psi_ql, j_last, P, "in10", ((0, 2), (1, 3)), ((0,), (0,)), 2)

@@ -23,6 +23,7 @@ PASSES = K // (P * PACK)
 CHUNK = 256
 PER_COL = 16
 RUN = 4
+POOL_RUN = 8
 
 
 def tile_list_transit_cauchy_step_kernel(
@@ -116,10 +117,11 @@ def tile_list_transit_cauchy_step_kernel(
             return rows
 
         def weave(dst, first, second, op, slots=slice(0, PACK), engine=nc.gpsimd):
+            run = POOL_RUN if engine is nc.gpsimd else RUN
             engine.tensor_tensor(
-                dst.rearrange("p (c e t) -> p c t e", e=RUN, t=PACK)[:, :, slots, :],
-                first.rearrange("p t (c e) -> p c t e", e=RUN),
-                second.rearrange("p t (c e) -> p c t e", e=RUN),
+                dst.rearrange("p (c e t) -> p c t e", e=run, t=PACK)[:, :, slots, :],
+                first.rearrange("p t (c e) -> p c t e", e=run),
+                second.rearrange("p t (c e) -> p c t e", e=run),
                 op,
             )
 

@@ -415,9 +415,9 @@ def tile_list_transit_cauchy_step_kernel(
 
         model_0 = copy_model(models[0], CHUNK, "model0")
         model_1 = copy_model(models[1], CHUNK, "handed")
-        res_0 = pool_residual(model_0, flux_0, CHUNK, "mid0", 2)
+        res_0 = pool_residual(model_0, flux_0, CHUNK, "mid0", 1)
         res_1 = pool_residual(model_1, flux_1, CHUNK, "res1", 1)
-        inv_0 = invert(res_0, CHUNK, "inv0", 2)
+        inv_0 = invert(res_0, CHUNK, "inv0")
         both = sbuf([P, 2, PACK, CHUNK], F32, "rows", "x1_codes")
         for i in range(PACK):
             pick(both[:, 0, i, :], idx3, 1, i, j2, CHUNK)
@@ -438,44 +438,38 @@ def tile_list_transit_cauchy_step_kernel(
         inv_2 = invert(res_2, CHUNK, "woven0")
         out_high = pick_pair(idx3, 1, "x1b_codes")
         in_high = pick_pair(idx2, 1, "flux2")
+        gather_words(0, j3, CHUNK, "mid0")
         psi_q0 = quantise(psi_early[:], j2 * PACK, "psi_codes0", "psi_sc0")
         for a in range(PASSES):
             staged = sbuf([P, PACK, j2], F32, "staged", "big%d" % a)
             second_product(psi_q0, 0, j2, a, staged[:], (0, 1, 2, 3), (), 2)
-        woven = sbuf([P, (CHUNK + P) * PACK], BF16, "woven", "handed")
-        pair_difference(woven[:, 0 : CHUNK * PACK], (out_low, in_low), 0)
-        pair_difference(woven[:, 0 : CHUNK * PACK], (out_high, in_high), 1)
-        gather_words(0, j3, CHUNK, "res1")
+        psi_2 = influence(res_2, inv_2, CHUNK, "handed", nc.gpsimd)
+        woven = sbuf([P, CHUNK * PACK], BF16, "woven", "woven0")
+        pair_difference(woven[:], (out_low, in_low), 0)
+        pair_difference(woven[:], (out_high, in_high), 1)
         model_last, model_unit = model_banks((6,), P), model_banks((7,), P)
+        tail_units = ((model_unit, j_unit), (model_last, j_last))
         for a in range(PASSES):
-            model_pass(model_unit, "table", a, j_unit, P, start=(a == 0))
-            model_pass(model_last, "table", a, j_last, P, start=(a == 0))
-        both = sbuf([P, 2, PACK, P], F32, "rows", "out00")
-        outside, inside = both[:, 0], both[:, 1]
-        for i in range(PACK):
-            pick(outside[:, i, :], idx3, 1, i, j_unit, P)
-            pick(inside[:, i, :], idx2, 1, i, j_unit, P)
-        psi_2 = influence(res_2, inv_2, CHUNK, "model0", nc.gpsimd)
-        weave(woven[:, CHUNK * PACK :], inside, outside, ALU.subtract)
-        outside_last = pick_rows(idx3, 1, j_last, P, "x1_codes")
-        inside = pick_rows(idx2, 1, j_last, P, "x1c_codes")
-        quantise_x([(0, j_last), (0, j_unit), (1, j_unit)], woven[:], "unit_codes", "x1_sc0")
-        model_pass(model_unit, "x", 0, j_unit, P)
-        model_pass(model_unit, "x", 1, j_unit, P, stop=True)
-        model_pass(model_last, "x", 0, j_last, P)
-        outside = outside_last
-        woven = sbuf([P, P * PACK], BF16, "woven", "handed")
+            for model, j0 in tail_units:
+                model_pass(model, "table", a, j0, P, start=(a == 0))
+        outside = pick_rows(idx3, 1, j3, CHUNK, "out00")
+        inside = pick_rows(idx2, 1, j3, CHUNK, "res1")
+        quantise_x(units(0, j3, CHUNK), woven[:], "model0", "x1_sc0")
+        for model, j0 in tail_units:
+            model_pass(model, "x", 0, j0, P)
+        woven = sbuf([P, CHUNK * PACK], BF16, "woven", "x1b_codes")
         weave(woven[:], inside[:], outside[:], ALU.subtract, engine=nc.vector)
-        quantise_x([(1, j_last)], woven[:], "psi_codes2", "psi_sc2")
-        model_pass(model_last, "x", 1, j_last, P, stop=True)
-        res_unit = residual(model_unit, flux_3[:, :, P:], P, "res1")
+        quantise_x(units(1, j3, CHUNK), woven[:], "psi_codes2", "psi_sc2")
+        for model, j0 in tail_units:
+            model_pass(model, "x", 1, j0, P, stop=True)
+        res_unit = residual(model_unit, flux_3[:, :, P:], P, "mid1")
         psi_q2 = quantise(psi_2[:], CHUNK * PACK, "psi_codes2", "psi_sc1")
         res_last = residual(model_last, flux_3[:, :, 0:P], P, "out13")
         inv_unit = invert(res_unit, P, "in12")
         inv_last = invert(res_last, P, "flux0")
         second = sbuf([P, PASSES, PACK, CHUNK], F32, "staged", "wt_both")
         second_product(psi_q2, j2, CHUNK, 0, second[:, 0], (0, 1), (0, 1), 2)
-        psi_u = influence(res_unit, inv_unit, P, "handed", nc.vector)
+        psi_u = influence(res_unit, inv_unit, P, "x1_codes", nc.vector)
         back_2 = second_matmuls(psi_q2, CHUNK, 1, (2, 3))
         scale_and_store(back_2, j2, CHUNK, 1, second[:, 1], 0, True, 2)
         psi_qu = quantise(psi_u[:], H, "psi_codes0", "psi_sc0")

@@ -367,7 +367,7 @@ def tile_list_transit_cauchy_step_kernel(
                     turn_wb(0, wb_b)
             pair_difference(woven_0[:], rooms, k)
         w4_w = reorder_w4_words()
-        gather_words(0, 0, j3, "words0")
+        gather_words(0, 0, j2, "words0")
         rooms = pair_rooms(j2, "10")
         pick_both(rooms, 1, 0, 0, j2)
         wb_b = weave_wb(1)
@@ -376,10 +376,10 @@ def tile_list_transit_cauchy_step_kernel(
         quantise_x(units(0, 0, j3), woven_0[:], "big1", "x0_sc", j2)
         quantise_wb(1, wb_b)
         models = [model_banks((2 * c, 2 * c + 1), CHUNK) for c in range(3)]
-        for c in range(3):
+        for c in range(2):
             model_pass(models[c], "table", 0, c * CHUNK, CHUNK, start=True)
         for c in range(3):
-            model_pass(models[c], "x", 0, c * CHUNK, CHUNK)
+            model_pass(models[c], "x", 0, c * CHUNK, CHUNK, start=(c == 2))
         woven_1 = sbuf([P, j2 * PACK], BF16, "woven1", "mid1")
         pair_difference(woven_1[:], rooms, 0)
         third = [sbuf([P, j2], F32, "third", side + "12") for side in ("out", "in")]
@@ -398,7 +398,7 @@ def tile_list_transit_cauchy_step_kernel(
             subtract(apart[:, 1, cols], 1, 3, cols.start, CHUNK, outside[:, cols])
         halves = [woven_1[:, c * CHUNK * PACK : (c + 1) * CHUNK * PACK] for c in range(2)]
         for c in range(2):
-            nc.scalar.copy(
+            nc.vector.tensor_copy(
                 halves[c].rearrange("p (c e t) -> p c t e", e=RUN, t=PACK)[:, :, 2:4, :],
                 apart[:, :, c * CHUNK : (c + 1) * CHUNK].rearrange("p t (c e) -> p c t e", e=RUN),
             )
@@ -424,6 +424,8 @@ def tile_list_transit_cauchy_step_kernel(
             pick(both[:, 1, i, :], idx2, 1, i, j2, CHUNK)
         gather_words(1, j2, 2 * CHUNK, "wt_both")
         model_pass(models[2], "table", 1, j2, CHUNK)
+        gather_words(0, j2, CHUNK, "x1_sc1")
+        model_pass(models[2], "table", 0, j2, CHUNK)
         out_low = pick_pair(idx3, 0, "x1c_codes")
         inv_1 = invert(res_1, CHUNK, "out00")
         woven = sbuf([P, CHUNK * PACK], BF16, "woven", "handed")
@@ -443,10 +445,11 @@ def tile_list_transit_cauchy_step_kernel(
         for a in range(PASSES):
             staged = sbuf([P, PACK, j2], F32, "staged", "big%d" % a)
             second_product(psi_q0, 0, j2, a, staged[:], (0, 1, 2, 3), (), 2)
-        psi_2 = influence(res_2, inv_2, CHUNK, "handed", nc.gpsimd)
-        woven = sbuf([P, CHUNK * PACK], BF16, "woven", "woven0")
-        pair_difference(woven[:], (out_low, in_low), 0)
-        pair_difference(woven[:], (out_high, in_high), 1)
+        handed = sbuf([P, 3 * H], BF16, "handed")
+        psi_2, woven = [handed[:, 0:H]], handed[:, H:]
+        weave(psi_2[0], res_2[:, :, 0:P], inv_2[:, :, 0:P], ALU.mult)
+        pair_difference(woven, (out_low, in_low), 0)
+        pair_difference(woven, (out_high, in_high), 1)
         model_last, model_unit = model_banks((6,), P), model_banks((7,), P)
         tail_units = ((model_unit, j_unit), (model_last, j_last))
         for a in range(PASSES):
@@ -454,7 +457,7 @@ def tile_list_transit_cauchy_step_kernel(
                 model_pass(model, "table", a, j0, P, start=(a == 0))
         outside = pick_rows(idx3, 1, j3, CHUNK, "out00")
         inside = pick_rows(idx2, 1, j3, CHUNK, "res1")
-        quantise_x(units(0, j3, CHUNK), woven[:], "model0", "x1_sc0")
+        quantise_x(units(0, j3, CHUNK), woven, "model0", "x1_sc0")
         for model, j0 in tail_units:
             model_pass(model, "x", 0, j0, P)
         woven = sbuf([P, CHUNK * PACK], BF16, "woven", "x1b_codes")
@@ -462,8 +465,12 @@ def tile_list_transit_cauchy_step_kernel(
         quantise_x(units(1, j3, CHUNK), woven[:], "psi_codes2", "psi_sc2")
         for model, j0 in tail_units:
             model_pass(model, "x", 1, j0, P, stop=True)
-        res_unit = residual(model_unit, flux_3[:, :, P:], P, "mid1")
-        psi_q2 = quantise(psi_2[:], CHUNK * PACK, "psi_codes2", "psi_sc1")
+        psi_2.append(influence(res_2[:, :, P:], inv_2[:, :, P:], P, "x1b_codes", nc.vector)[:])
+        res_unit = residual(model_unit, flux_3[:, :, P:], P, "mid0")
+        psi_q2 = (sbuf([P, CHUNK], U32, "codes", "psi_codes2"), sbuf([P, CHUNK], U8, "scales", "psi_sc1"))
+        for u, half in enumerate(psi_2):
+            cols = slice(u * P, (u + 1) * P)
+            nc.vector.quantize_mx(out=psi_q2[0][:, cols].bitcast(FP8X4), scales=psi_q2[1][:, cols], in_=half)
         res_last = residual(model_last, flux_3[:, :, 0:P], P, "out13")
         inv_unit = invert(res_unit, P, "in12")
         inv_last = invert(res_last, P, "flux0")

@@ -482,6 +482,6 @@ def tile_list_transit_cauchy_step_kernel(
         psi_qu = quantise(psi_u[:], H, "psi_codes0", "psi_sc0")
         scale_and_store(back_2, j2, CHUNK, 1, second[:, 1], 1, True, 2)
         psi_l = influence(res_last, inv_last, P, "x1b_codes", nc.vector)
-        finish(psi_qu, j_unit, P, "out10", ((4,), (5,)))
+        finish(psi_qu, j_unit, P, "out10", ((4, 7), (5, 6)), ((), ()), 2)
         psi_ql = quantise(psi_l[:], H, "psi_codes1", "psi_sc2")
         finish(psi_ql, j_last, P, "in10", ((0, 2), (1, 3)), ((0,), (0,)), 2)

@@ -321,8 +321,8 @@ def tile_list_transit_cauchy_step_kernel(
         nc.vector.tensor_copy(picked_sc[:], tab_sc[:].indirect(idx[:]))
         load_w4_scales()
         load_plane(0, 1)
-        load_wb(0)
         load_plane(0, 2)
+        load_wb(0)
         load_plane(0, 3)
         w4_raw = sbuf([P, PASSES, 2 * H], U8, "w4_raw")
         nc.sync.dma_start(out=w4_raw[:].bitcast(I32), in_=w4_words.rearrange("a p c -> p a c").bitcast(I32))
@@ -361,7 +361,7 @@ def tile_list_transit_cauchy_step_kernel(
             rooms = pair_rooms(j3, "0%d" % k)
             for i in (2 * k, 2 * k + 1):
                 pick_both(rooms, 0, i, 0, j3)
-                if i == 2:
+                if i == 3:
                     wb_b = weave_wb(0)
                     quantise_wb(0, wb_b)
                     turn_wb(0, wb_b)

@@ -242,12 +242,15 @@ def tile_list_transit_cauchy_step_kernel(
                 nc.scalar.copy(model_sb[:, rows, :], model[:])
             return model_sb
 
-        def invert(res, n, tag, groups=1):
+        def invert(res, n, tag, groups=1, pool_squares=False):
             inv = sbuf([P, PACK, n], F32, "inv", tag)
             for group in slot_groups(groups):
                 halves = [slice(t, t + 2) for t in range(group.start, group.stop, 2)]
                 for rows in halves:
-                    nc.scalar.activation(inv[:, rows, :], res[:, rows, :], ACT.Square)
+                    if pool_squares:
+                        nc.gpsimd.tensor_tensor(inv[:, rows, :], res[:, rows, :], res[:, rows, :], ALU.mult)
+                    else:
+                        nc.scalar.activation(inv[:, rows, :], res[:, rows, :], ACT.Square)
                 for t in range(group.start, group.stop):
                     nc.scalar.activation(inv[:, t, :], inv[:, t, :], ACT.Abs_reciprocal_sqrt, bias=var_t[:, t : t + 1])
                 for rows in halves:
@@ -321,8 +324,8 @@ def tile_list_transit_cauchy_step_kernel(
         nc.vector.tensor_copy(picked_sc[:], tab_sc[:].indirect(idx[:]))
         load_w4_scales()
         load_plane(0, 1)
-        load_plane(0, 2)
         load_wb(0)
+        load_plane(0, 2)
         load_plane(0, 3)
         w4_raw = sbuf([P, PASSES, 2 * H], U8, "w4_raw")
         nc.sync.dma_start(out=w4_raw[:].bitcast(I32), in_=w4_words.rearrange("a p c -> p a c").bitcast(I32))
@@ -361,7 +364,7 @@ def tile_list_transit_cauchy_step_kernel(
             rooms = pair_rooms(j3, "0%d" % k)
             for i in (2 * k, 2 * k + 1):
                 pick_both(rooms, 0, i, 0, j3)
-                if i == 3:
+                if i == 2:
                     wb_b = weave_wb(0)
                     quantise_wb(0, wb_b)
                     turn_wb(0, wb_b)
@@ -450,21 +453,18 @@ def tile_list_transit_cauchy_step_kernel(
         weave(psi_2[0], res_2[:, :, 0:P], inv_2[:, :, 0:P], ALU.mult)
         pair_difference(woven, (out_low, in_low), 0)
         pair_difference(woven, (out_high, in_high), 1)
-        model_last, model_unit = model_banks((6,), P), model_banks((7,), P)
-        tail_units = ((model_unit, j_unit), (model_last, j_last))
+        model_3 = model_banks((6, 7), CHUNK)
+        model_last, model_unit = ([half[:, :, c0 : c0 + P] for half in model_3] for c0 in (0, P))
         for a in range(PASSES):
-            for model, j0 in tail_units:
-                model_pass(model, "table", a, j0, P, start=(a == 0))
+            model_pass(model_3, "table", a, j3, CHUNK, start=(a == 0))
         outside = pick_rows(idx3, 1, j3, CHUNK, "out00")
         inside = pick_rows(idx2, 1, j3, CHUNK, "res1")
         quantise_x(units(0, j3, CHUNK), woven, "model0", "x1_sc0")
-        for model, j0 in tail_units:
-            model_pass(model, "x", 0, j0, P)
+        model_pass(model_3, "x", 0, j3, CHUNK)
         woven = sbuf([P, CHUNK * PACK], BF16, "woven", "x1b_codes")
         weave(woven[:], inside[:], outside[:], ALU.subtract, engine=nc.vector)
         quantise_x(units(1, j3, CHUNK), woven[:], "psi_codes2", "psi_sc2")
-        for model, j0 in tail_units:
-            model_pass(model, "x", 1, j0, P, stop=True)
+        model_pass(model_3, "x", 1, j3, CHUNK, stop=True)
         psi_2.append(influence(res_2[:, :, P:], inv_2[:, :, P:], P, "x1b_codes", nc.vector)[:])
         res_unit = residual(model_unit, flux_3[:, :, P:], P, "mid0")
         psi_q2 = (sbuf([P, CHUNK], U32, "codes", "psi_codes2"), sbuf([P, CHUNK], U8, "scales", "psi_sc1"))
@@ -473,14 +473,14 @@ def tile_list_transit_cauchy_step_kernel(
             nc.vector.quantize_mx(out=psi_q2[0][:, cols].bitcast(FP8X4), scales=psi_q2[1][:, cols], in_=half)
         res_last = residual(model_last, flux_3[:, :, 0:P], P, "out13")
         inv_unit = invert(res_unit, P, "in12")
-        inv_last = invert(res_last, P, "flux0")
+        inv_last = invert(res_last, P, "flux0", pool_squares=True)
         second = sbuf([P, PASSES, PACK, CHUNK], F32, "staged", "wt_both")
         second_product(psi_q2, j2, CHUNK, 0, second[:, 0], (0, 1), (0, 1), 2)
         psi_u = influence(res_unit, inv_unit, P, "x1_codes", nc.vector)
         back_2 = second_matmuls(psi_q2, CHUNK, 1, (2, 3))
         scale_and_store(back_2, j2, CHUNK, 1, second[:, 1], 0, True, 2)
         psi_qu = quantise(psi_u[:], H, "psi_codes0", "psi_sc0")
-        scale_and_store(back_2, j2, CHUNK, 1, second[:, 1], 1, True, 2)
+        scale_and_store(back_2, j2, CHUNK, 1, second[:, 1], 1, False, 2)
         psi_l = influence(res_last, inv_last, P, "x1b_codes", nc.vector)
         finish(psi_qu, j_unit, P, "out10", ((4, 7), (5, 6)), ((), ()), 2)
         psi_ql = quantise(psi_l[:], H, "psi_codes1", "psi_sc2")

@@ -376,13 +376,13 @@ def tile_list_transit_cauchy_step_kernel(
         wb_b = weave_wb(1)
         turn_wb(1, wb_b)
         pick_both(rooms, 1, 1, 0, j2)
-        quantise_x(units(0, 0, j3), woven_0[:], "big1", "x0_sc", j2)
+        quantise_x(units(0, 0, j2), woven_0[:, 0 : j2 * PACK], "big1", "x0_sc")
         quantise_wb(1, wb_b)
         models = [model_banks((2 * c, 2 * c + 1), CHUNK) for c in range(3)]
         for c in range(2):
             model_pass(models[c], "table", 0, c * CHUNK, CHUNK, start=True)
-        for c in range(3):
-            model_pass(models[c], "x", 0, c * CHUNK, CHUNK, start=(c == 2))
+        for c in range(2):
+            model_pass(models[c], "x", 0, c * CHUNK, CHUNK)
         woven_1 = sbuf([P, j2 * PACK], BF16, "woven1", "mid1")
         pair_difference(woven_1[:], rooms, 0)
         third = [sbuf([P, j2], F32, "third", side + "12") for side in ("out", "in")]
@@ -408,7 +408,12 @@ def tile_list_transit_cauchy_step_kernel(
         for c, tag in enumerate(("x1_codes", "x1c_codes")):
             quantise_x(units(1, c * CHUNK, CHUNK), halves[c], tag, "x1_sc%d" % c)
             model_pass(models[c], "x", 1, c * CHUNK, CHUNK, stop=True)
-        wt_q = quantise(wt_both[:], PASSES * H * PACK, "apart", "wt_sc")
+        late_codes = sbuf([P, CHUNK + PASSES * H], U32, "late_codes", "apart")
+        late_scales = sbuf([P, CHUNK + PASSES * H], U8, "late_scales")
+        x_q[0, j2] = (late_codes[:, 0:CHUNK], late_scales[:, 0:CHUNK])
+        wt_q = (late_codes[:, CHUNK:], late_scales[:, CHUNK:])
+        for (codes, scales), src in ((x_q[0, j2], woven_0[:, j2 * PACK :]), (wt_q, wt_both[:])):
+            nc.vector.quantize_mx(out=codes.bitcast(FP8X4), scales=scales, in_=src)
 
         def pick_pair(lst, k, tag):
             room = sbuf([P, 2, CHUNK], F32, "pair", tag)
@@ -426,7 +431,8 @@ def tile_list_transit_cauchy_step_kernel(
             pick(both[:, 0, i, :], idx3, 1, i, j2, CHUNK)
             pick(both[:, 1, i, :], idx2, 1, i, j2, CHUNK)
         gather_words(1, j2, 2 * CHUNK, "wt_both")
-        model_pass(models[2], "table", 1, j2, CHUNK)
+        model_pass(models[2], "table", 1, j2, CHUNK, start=True)
+        model_pass(models[2], "x", 0, j2, CHUNK)
         gather_words(0, j2, CHUNK, "x1_sc1")
         model_pass(models[2], "table", 0, j2, CHUNK)
         out_low = pick_pair(idx3, 0, "x1c_codes")
@@ -447,7 +453,7 @@ def tile_list_transit_cauchy_step_kernel(
         psi_q0 = quantise(psi_early[:], j2 * PACK, "psi_codes0", "psi_sc0")
         for a in range(PASSES):
             staged = sbuf([P, PACK, j2], F32, "staged", "big%d" % a)
-            second_product(psi_q0, 0, j2, a, staged[:], (0, 1, 2, 3), (), 2)
+            second_product(psi_q0, 0, j2, a, staged[:], ((0, 1, 2, 3), (4, 5, 0, 1))[a], (), 2)
         handed = sbuf([P, 3 * H], BF16, "handed")
         psi_2, woven = [handed[:, 0:H]], handed[:, H:]
         weave(psi_2[0], res_2[:, :, 0:P], inv_2[:, :, 0:P], ALU.mult)

@@ -473,7 +473,7 @@ def tile_list_transit_cauchy_step_kernel(
         model_pass(model_3, "x", 1, j3, CHUNK, stop=True)
         psi_2.append(influence(res_2[:, :, P:], inv_2[:, :, P:], P, "x1b_codes", nc.vector)[:])
         res_unit = residual(model_unit, flux_3[:, :, P:], P, "mid0")
-        psi_q2 = (sbuf([P, CHUNK], U32, "codes", "psi_codes2"), sbuf([P, CHUNK], U8, "scales", "psi_sc1"))
+        psi_q2 = (sbuf([P, CHUNK], U32, "codes", "res1"), sbuf([P, CHUNK], U8, "scales", "psi_sc1"))
         for u, half in enumerate(psi_2):
             cols = slice(u * P, (u + 1) * P)
             nc.vector.quantize_mx(out=psi_q2[0][:, cols].bitcast(FP8X4), scales=psi_q2[1][:, cols], in_=half)

from contextlib import ExitStack

import concourse.mybir as mybir
from concourse.masks import make_identity

K, H, T, S = 1024, 512, 2048, 1024
FLOPS = 2 * (2 * K * H * S + H * K * S)

F32 = mybir.dt.float32
BF16 = mybir.dt.bfloat16
I32 = mybir.dt.int32
U32 = mybir.dt.uint32
U16 = mybir.dt.uint16
U8 = mybir.dt.uint8
FP8X4 = mybir.dt.float8_e4m3fn_x4
FP4X4 = mybir.dt.float4_e2m1fn_x4
ACT = mybir.ActivationFunctionType
ALU = mybir.AluOpType

P = 128
PACK = 4
PASSES = K // (P * PACK)
CHUNK = 256
PER_COL = 16
RUN = 4
POOL_RUN = 8


def tile_list_transit_cauchy_step_kernel(
    tc, tab_words, tab_scales, offs, xT, offs2, offs3, w4_words, w4_scales, wb, flux, var, step, out
):
    nc = tc.nc
    with ExitStack() as ctx:
        keep = ctx.enter_context(tc.tile_pool(name="keep", bufs=1))
        work = ctx.enter_context(tc.tile_pool(name="work", bufs=1))
        psum = ctx.enter_context(tc.psum_pool(name="psum", bufs=1))

        def entries(lst, j0, n):
            return lst[:, j0 // PER_COL : (j0 + n) // PER_COL]

        def sbuf(shape, dtype, name, tag=None):
            return work.tile(shape, dtype, name=name, tag=tag or name, align_bytes=64)

        def bank(shape, name, b):
            return psum.tile(shape, F32, name=name, tag="bank%d" % b)

        def flat(ap):
            return ap.rearrange("p a b -> p (a b)")

        x_rows = xT.rearrange("(a p i) t -> a i p t", a=PASSES, i=PACK)
        flux_rows = flux.rearrange("(m t) j -> m t j", t=PACK)
        out_rows = out.rearrange("(a p i) j -> a p i j", a=PASSES, i=PACK)
        planes, wb_raw, tab_w = {}, {}, {}

        def load_plane(a, i):
            planes[a, i] = sbuf([P, T], F32, "plane%d%d" % (a, i))
            nc.sync.dma_start(out=planes[a, i][:], in_=x_rows[a, i])

        def load_wb(a):
            wb_raw[a] = sbuf([P, PACK * H], F32, "wb_raw", "big%d" % a)
            nc.sync.dma_start(
                out=wb_raw[a][:], in_=wb[a * P * PACK : (a + 1) * P * PACK, :].rearrange("(p i) r -> p (i r)", i=PACK)
            )

        def load_flux(j0, n, tag):
            rows = sbuf([P, PACK, n], F32, "flux_sb", tag)
            nc.sync.dma_start(out=rows[:], in_=flux_rows[:, :, j0 : j0 + n])
            return rows

        def load_tab(a):
            tab_w[a] = sbuf([P, T], I32, "tab_w%d" % a)
            nc.sync.dma_start(out=tab_w[a][:], in_=tab_words[a].rearrange("p t i -> p (t i)").bitcast(I32))

        idx = keep.tile([P, S // PER_COL], U16, name="idx")
        idx2 = keep.tile([P, S // PER_COL], U16, name="idx2")
        idx3 = keep.tile([P, S // PER_COL], U16, name="idx3")
        tab_sc = keep.tile([P, T], U8, name="tab_sc")
        w4_sc_raw = sbuf([P, PASSES * H], U8, "w4_sc_raw")
        v_sc = [keep.tile([P, S], U8, name="v_sc%d" % a, align_bytes=64) for a in range(PASSES)]
        nc.vector.memset(tab_sc[32:64, :].bitcast(I32), 0)
        nc.vector.memset(tab_sc[64:128, :].bitcast(I32), 0)
        nc.gpsimd.memset(w4_sc_raw[:].bitcast(I32), 0)
        for a in range(PASSES):
            nc.gpsimd.memset(v_sc[a][:].bitcast(I32), 0)
        warm = keep.tile([P, 2], F32, name="warm")
        nc.vector.memset(warm[:, 0:1], 1.0)
        nc.scalar.activation(warm[:, 1:2], warm[:, 0:1], ACT.Abs_reciprocal_sqrt)
        ident = keep.tile([P, P], F32, name="ident")
        make_identity(nc, ident[:])

        picked_sc = keep.tile([P, S], U8, name="picked_sc")

        def move_scale_rows(a):
            for q in range(4):
                row = 16 * a + 4 * q
                nc.sync.dma_start(
                    out=v_sc[a][32 * q : 32 * q + 4, :].bitcast(I32), in_=picked_sc[row : row + 4, :].bitcast(I32)
                )

        def load_w4_scales():
            for q in range(4):
                nc.sync.dma_start(
                    out=w4_sc_raw[32 * q : 32 * q + 4, :].bitcast(I32).rearrange("p (a c) -> p a c", a=PASSES),
                    in_=w4_scales[:, 4 * q : 4 * q + 4, :].rearrange("a s c -> s a c").bitcast(I32),
                )

        def pick(dst, lst, a, i, j0, n):
            nc.vector.tensor_copy(dst, planes[a, i][:].indirect(entries(lst, j0, n)))

        def subtract(dst, a, i, j0, n, outside):
            nc.vector.tensor_tensor(dst, planes[a, i][:].indirect(entries(idx2, j0, n)), outside, ALU.subtract)

        def pick_rows(lst, a, j0, n, tag):
            rows = sbuf([P, PACK, n], F32, "rows", tag)
            for i in range(PACK):
                pick(rows[:, i, :], lst, a, i, j0, n)
            return rows

        def weave(dst, first, second, op, slots=slice(0, PACK), engine=nc.gpsimd):
            run = POOL_RUN if engine is nc.gpsimd else RUN
            engine.tensor_tensor(
                dst.rearrange("p (c e t) -> p c t e", e=run, t=PACK)[:, :, slots, :],
                first.rearrange("p t (c e) -> p c t e", e=run),
                second.rearrange("p t (c e) -> p c t e", e=run),
                op,
            )

        def quantise(src, width, tag, scale_tag):
            codes = sbuf([P, width // PACK], U32, "codes", tag)
            scales = sbuf([P, width // PACK], U8, "scales", scale_tag)
            nc.vector.quantize_mx(out=codes[:].bitcast(FP8X4), scales=scales[:], in_=src)
            return codes, scales

        v_words, x_q, wb_q = {}, {}, {}

        def gather_words(a, j0, n, tag):
            words = sbuf([P, n], U32, "words", tag)
            nc.vector.tensor_copy(words[:], tab_w[a][:].bitcast(U32).indirect(entries(idx, j0, n)))
            for o in range(0, n, P):
                v_words[a, j0 + o] = words[:, o:n]

        def quantise_x(places, woven, tag, scale_tag, cut=None):
            n = len(places) * P
            codes = sbuf([P, n], U32, "codes", tag)
            scales = sbuf([P, n], U8, "scales", scale_tag)
            for part in (slice(0, cut), slice(cut, n)) if cut else (slice(0, n),):
                nc.vector.quantize_mx(
                    out=codes[:, part].bitcast(FP8X4),
                    scales=scales[:, part],
                    in_=woven[:, part.start * PACK : part.stop * PACK],
                )
            for k, place in enumerate(places):
                x_q[place] = (codes[:, k * P : n], scales[:, k * P : n])

        def units(a, j0, n):
            return [(a, j) for j in range(j0, j0 + n, P)]

        wt_both = sbuf([P, PASSES * H * PACK], BF16, "wt_both")

        def weave_wb(a):
            wb_b = sbuf([P, H * PACK], BF16, "wb_b", "mid%d" % a)
            nc.scalar.copy(
                wb_b[:].rearrange("p (t m i) -> p m i t", t=PACK, i=PACK),
                wb_raw[a][:].rearrange("p (i m t) -> p m i t", i=PACK, t=PACK),
            )
            return wb_b

        def quantise_wb(a, wb_b):
            wb_q[a] = quantise(wb_b[:], H * PACK, "wb_codes%d" % a, "wb_sc%d" % a)

        def turn_wb(a, wb_b):
            pairs = wb_b[:].bitcast(F32)
            wt_b = wt_both[:, a * H * PACK : (a + 1) * H * PACK]
            for u in range(2):
                turned = bank([P, PACK, P], "wt_bank", 6 + u)
                for t in range(PACK):
                    nc.tensor.transpose(turned[:, t, :], pairs[:, 2 * P * t + u : 2 * P * (t + 1) : 2], ident[:])
                nc.scalar.copy(
                    wt_b[:, u * 2 * H : (u + 1) * 2 * H].rearrange("m (e p t) -> m e p t", e=2, t=PACK),
                    flat(turned[:]).bitcast(BF16).rearrange("m (t p e) -> m e p t", t=PACK, e=2),
                )

        def reorder_w4_words():
            w4_w = sbuf([P, PASSES * 2 * H], U8, "w4_w")
            nc.scalar.copy(
                w4_w[:].bitcast(U16).rearrange("p (a t m) -> p a m t", a=PASSES, t=PACK),
                flat(w4_raw[:]).bitcast(U16).rearrange("p (a m t) -> p a m t", a=PASSES, t=PACK),
            )
            return w4_w

        def reorder_w4_scales():
            w4_sc = sbuf([P, PASSES * H], U8, "w4_sc")
            nc.gpsimd.tensor_copy(
                w4_sc[:].rearrange("p (a t m) -> p a t m", a=PASSES, t=PACK),
                w4_sc_raw[:].rearrange("p (a m t) -> p a t m", a=PASSES, t=PACK),
            )
            return w4_sc

        def weights(kind, a, c0, n):
            cols = slice(a * H + c0, a * H + c0 + n)
            if kind == "table":
                return w4_w[:, 2 * cols.start : 2 * cols.stop].bitcast(FP4X4), w4_sc[:, cols]
            codes, scales = wb_q[a]
            return codes[:, c0 : c0 + n].bitcast(FP8X4), scales[:, c0 : c0 + n]

        def columns(kind, a, j0, n):
            if kind == "table":
                return v_words[a, j0][:, 0:n].bitcast(FP8X4), v_sc[a][:, j0 : j0 + n]
            codes, scales = x_q[a, j0]
            return codes[:, 0:n].bitcast(FP8X4), scales[:, 0:n]

        def model_pass(banks, kind, a, j0, n, start=False, stop=False):
            per_bank = PACK // len(banks)
            rhs, rhs_sc = columns(kind, a, j0, n)
            for t in range(PACK):
                lhs, lhs_sc = weights(kind, a, t * P, P)
                nc.tensor.matmul_mx(
                    out=banks[t // per_bank][:, t % per_bank, :],
                    lhsT=lhs,
                    lhsT_scale=lhs_sc,
                    rhs=rhs,
                    rhs_scale=rhs_sc,
                    start=(start and t % per_bank == 0),
                    stop=(stop and t % per_bank == per_bank - 1),
                )

        def model_banks(numbers, n):
            return [bank([P, PACK // len(numbers), n], "model", b) for b in numbers]

        def slot_groups(count):
            return [slice(t, t + PACK // count) for t in range(0, PACK, PACK // count)]

        def residual(banks, flux_sb, n, tag):
            res = sbuf([P, PACK, n], F32, "res", tag)
            for model, rows in zip(banks, slot_groups(len(banks))):
                nc.vector.tensor_tensor(res[:, rows, :], flux_sb[:, rows, :], model[:], ALU.subtract)
            return res

        def copy_model(banks, n, tag):
            model_sb = sbuf([P, PACK, n], F32, "model_sb", tag)
            for model, rows in zip(banks, slot_groups(len(banks))):
                nc.scalar.copy(model_sb[:, rows, :], model[:])
            return model_sb

        def invert(res, n, tag, groups=1, pool_squares=False):
            inv = sbuf([P, PACK, n], F32, "inv", tag)
            for group in slot_groups(groups):
                halves = [slice(t, t + 2) for t in range(group.start, group.stop, 2)]
                for rows in halves:
                    if pool_squares:
                        nc.gpsimd.tensor_tensor(inv[:, rows, :], res[:, rows, :], res[:, rows, :], ALU.mult)
                    else:
                        nc.scalar.activation(inv[:, rows, :], res[:, rows, :], ACT.Square)
                for t in range(group.start, group.stop):
                    nc.scalar.activation(inv[:, t, :], inv[:, t, :], ACT.Abs_reciprocal_sqrt, bias=var_t[:, t : t + 1])
                for rows in halves:
                    nc.scalar.activation(inv[:, rows, :], inv[:, rows, :], ACT.Square)
            return inv

        def pool_residual(model_sb, flux_sb, n, tag, groups):
            res = sbuf([P, PACK, n], F32, "res", tag)
            for rows in slot_groups(groups):
                nc.gpsimd.tensor_tensor(res[:, rows, :], flux_sb[:, rows, :], model_sb[:, rows, :], ALU.subtract)
            return res

        def influence(res, inv, n, tag, engine):
            psi_b = sbuf([P, n * PACK], BF16, "psi_b", tag)
            weave(psi_b[:], res[:], inv[:], ALU.mult, engine=engine)
            return psi_b

        def second_matmuls(psi_q, n, a, banks):
            psi_codes, psi_sc = psi_q
            wt_codes, wt_sc = wt_q
            per_bank = PACK // len(banks)
            backs = [bank([P, per_bank, n], "back", b) for b in banks]
            for i in range(PACK):
                cols = slice((a * PACK + i) * P, (a * PACK + i + 1) * P)
                nc.tensor.matmul_mx(
                    out=backs[i // per_bank][:, i % per_bank, :],
                    lhsT=wt_codes[:, cols].bitcast(FP8X4),
                    lhsT_scale=wt_sc[:, cols],
                    rhs=psi_codes[:].bitcast(FP8X4),
                    rhs_scale=psi_sc[:],
                    start=True,
                    stop=True,
                )
            return backs

        def scale_and_store(backs, j0, n, a, staged, k, on_vector, rows_a_store):
            per_bank = PACK // len(backs)
            for e in range(per_bank):
                i = k * per_bank + e
                factor = step_t[:, a, i : i + 1]
                if on_vector:
                    nc.vector.tensor_scalar(staged[:, i, :], backs[k][:, e, :], factor, None, ALU.mult)
                else:
                    nc.scalar.activation(staged[:, i, :], backs[k][:, e, :], ACT.Copy, scale=factor)
            done = (k + 1) * per_bank
            if done % rows_a_store == 0:
                rows_done = slice(done - rows_a_store, done)
                nc.sync.dma_start(out=out_rows[a, :, rows_done, j0 : j0 + n], in_=staged[:, rows_done, :])

        def second_product(psi_q, j0, n, a, staged, banks, on_vector=(), rows_a_store=PACK):
            backs = second_matmuls(psi_q, n, a, banks)
            for k in range(len(banks)):
                scale_and_store(backs, j0, n, a, staged, k, k in on_vector, rows_a_store)

        def finish(psi_q, j0, n, tag, banks, on_vector=((), ()), rows_a_store=PACK):
            staged = sbuf([P, PASSES, PACK, n], F32, "staged", tag)
            for a in range(PASSES):
                second_product(psi_q, j0, n, a, staged[:, a], banks[a], on_vector[a], rows_a_store)

        j1, j2, j3 = CHUNK, 2 * CHUNK, 3 * CHUNK
        j_last, j_unit = j3, j3 + P
        pairs_of_slots = slot_groups(2)

        nc.sync.dma_start(idx[:], offs)
        nc.sync.dma_start(
            out=tab_sc[0:32, :].bitcast(I32), in_=tab_scales.rearrange("a q t -> (a q) t").bitcast(I32)
        )
        load_plane(0, 0)
        nc.sync.dma_start(idx3[:], offs3)
        nc.sync.dma_start(idx2[:], offs2)
        nc.vector.tensor_copy(picked_sc[:], tab_sc[:].indirect(idx[:]))
        load_w4_scales()
        load_plane(0, 1)
        load_wb(0)
        load_plane(0, 2)
        load_plane(0, 3)
        w4_raw = sbuf([P, PASSES, 2 * H], U8, "w4_raw")
        nc.sync.dma_start(out=w4_raw[:].bitcast(I32), in_=w4_words.rearrange("a p c -> p a c").bitcast(I32))
        load_tab(0)
        load_plane(1, 0)
        move_scale_rows(0)
        load_wb(1)
        load_plane(1, 1)
        load_plane(1, 2)
        move_scale_rows(1)
        load_tab(1)
        load_plane(1, 3)
        flux_0 = load_flux(0, CHUNK, "flux0")
        var_t = keep.tile([P, PACK], F32, name="var_t")
        nc.sync.dma_start(out=var_t[:], in_=var.rearrange("(m t) -> m t", t=PACK))
        step_t = keep.tile([P, PASSES, PACK], F32, name="step_t")
        nc.sync.dma_start(out=step_t[:], in_=step.rearrange("(a p i) -> p a i", a=PASSES, i=PACK))
        flux_1 = load_flux(j1, CHUNK, "flux1")
        flux_2 = load_flux(j2, CHUNK, "flux2")
        flux_3 = load_flux(j3, CHUNK, "flux3")

        w4_sc = reorder_w4_scales()

        def pair_rooms(n, tag):
            return [sbuf([P, 2, n], F32, "pair", side + tag) for side in ("out", "in")]

        def pick_both(rooms, a, i, j0, n):
            for room, lst in zip(rooms, (idx3, idx2)):
                pick(room[:, i % 2, :], lst, a, i, j0, n)

        def pair_difference(dst, rooms, k):
            weave(dst, rooms[1][:], rooms[0][:], ALU.subtract, pairs_of_slots[k])

        woven_0 = sbuf([P, j3 * PACK], BF16, "woven0")
        for k in range(2):
            rooms = pair_rooms(j3, "0%d" % k)
            for i in (2 * k, 2 * k + 1):
                pick_both(rooms, 0, i, 0, j3)
                if i == 2:
                    wb_b = weave_wb(0)
                    quantise_wb(0, wb_b)
                    turn_wb(0, wb_b)
            pair_difference(woven_0[:], rooms, k)
        w4_w = reorder_w4_words()
        gather_words(0, 0, j2, "words0")
        rooms = pair_rooms(j2, "10")
        pick_both(rooms, 1, 0, 0, j2)
        wb_b = weave_wb(1)
        turn_wb(1, wb_b)
        pick_both(rooms, 1, 1, 0, j2)
        quantise_x(units(0, 0, j2), woven_0[:, 0 : j2 * PACK], "big1", "x0_sc")
        quantise_wb(1, wb_b)
        models = [model_banks((2 * c, 2 * c + 1), CHUNK) for c in range(3)]
        for c in range(2):
            model_pass(models[c], "table", 0, c * CHUNK, CHUNK, start=True)
        for c in range(2):
            model_pass(models[c], "x", 0, c * CHUNK, CHUNK)
        woven_1 = sbuf([P, j2 * PACK], BF16, "woven1", "mid1")
        pair_difference(woven_1[:], rooms, 0)
        third = [sbuf([P, j2], F32, "third", side + "12") for side in ("out", "in")]
        for room, lst in zip(third, (idx3, idx2)):
            pick(room[:], lst, 1, 2, 0, j2)
        apart = sbuf([P, 2, j2], F32, "apart")
        nc.gpsimd.tensor_tensor(apart[:, 0, :], third[1][:], third[0][:], ALU.subtract)
        gather_words(1, 0, j2, "words1")
        for c in range(2):
            model_pass(models[c], "table", 1, c * CHUNK, CHUNK)
        outside = sbuf([P, j2], F32, "outside", "out13")
        for c in range(2):
            pick(outside[:, c * CHUNK : (c + 1) * CHUNK], idx3, 1, 3, c * CHUNK, CHUNK)
        for c in range(2):
            cols = slice(c * CHUNK, (c + 1) * CHUNK)
            subtract(apart[:, 1, cols], 1, 3, cols.start, CHUNK, outside[:, cols])
        halves = [woven_1[:, c * CHUNK * PACK : (c + 1) * CHUNK * PACK] for c in range(2)]
        for c in range(2):
            nc.vector.tensor_copy(
                halves[c].rearrange("p (c e t) -> p c t e", e=RUN, t=PACK)[:, :, 2:4, :],
                apart[:, :, c * CHUNK : (c + 1) * CHUNK].rearrange("p t (c e) -> p c t e", e=RUN),
            )
        for c, tag in enumerate(("x1_codes", "x1c_codes")):
            quantise_x(units(1, c * CHUNK, CHUNK), halves[c], tag, "x1_sc%d" % c)
            model_pass(models[c], "x", 1, c * CHUNK, CHUNK, stop=True)
        late_codes = sbuf([P, CHUNK + PASSES * H], U32, "late_codes", "apart")
        late_scales = sbuf([P, CHUNK + PASSES * H], U8, "late_scales")
        x_q[0, j2] = (late_codes[:, 0:CHUNK], late_scales[:, 0:CHUNK])
        wt_q = (late_codes[:, CHUNK:], late_scales[:, CHUNK:])
        for (codes, scales), src in ((x_q[0, j2], woven_0[:, j2 * PACK :]), (wt_q, wt_both[:])):
            nc.vector.quantize_mx(out=codes.bitcast(FP8X4), scales=scales, in_=src)

        def pick_pair(lst, k, tag):
            room = sbuf([P, 2, CHUNK], F32, "pair", tag)
            for e in range(2):
                pick(room[:, e, :], lst, 0, 2 * k + e, j3, CHUNK)
            return room

        model_0 = copy_model(models[0], CHUNK, "model0")
        model_1 = copy_model(models[1], CHUNK, "handed")
        res_0 = pool_residual(model_0, flux_0, CHUNK, "mid0", 1)
        res_1 = pool_residual(model_1, flux_1, CHUNK, "res1", 1)
        inv_0 = invert(res_0, CHUNK, "inv0")
        both = sbuf([P, 2, PACK, CHUNK], F32, "rows", "x1_codes")
        for i in range(PACK):
            pick(both[:, 0, i, :], idx3, 1, i, j2, CHUNK)
            pick(both[:, 1, i, :], idx2, 1, i, j2, CHUNK)
        gather_words(1, j2, 2 * CHUNK, "wt_both")
        model_pass(models[2], "table", 1, j2, CHUNK, start=True)
        model_pass(models[2], "x", 0, j2, CHUNK)
        gather_words(0, j2, CHUNK, "x1_sc1")
        model_pass(models[2], "table", 0, j2, CHUNK)
        out_low = pick_pair(idx3, 0, "x1c_codes")
        inv_1 = invert(res_1, CHUNK, "out00")
        woven = sbuf([P, CHUNK * PACK], BF16, "woven", "handed")
        weave(woven[:], both[:, 1], both[:, 0], ALU.subtract)
        quantise_x(units(1, j2, CHUNK), woven[:], "x1b_codes", "x1b_sc")
        model_pass(models[2], "x", 1, j2, CHUNK, stop=True)
        psi_early = sbuf([P, j2 * PACK], BF16, "psi_b", "handed")
        weave(psi_early[:, 0 : CHUNK * PACK], res_0[:], inv_0[:], ALU.mult)
        weave(psi_early[:, CHUNK * PACK :], res_1[:], inv_1[:], ALU.mult)
        in_low = pick_pair(idx2, 0, "x1_codes")
        res_2 = residual(models[2], flux_2, CHUNK, "mid1")
        inv_2 = invert(res_2, CHUNK, "woven0")
        out_high = pick_pair(idx3, 1, "x1b_codes")
        in_high = pick_pair(idx2, 1, "flux2")
        gather_words(0, j3, CHUNK, "mid0")
        psi_q0 = quantise(psi_early[:], j2 * PACK, "psi_codes0", "psi_sc0")
        for a in range(PASSES):
            staged = sbuf([P, PACK, j2], F32, "staged", "big%d" % a)
            second_product(psi_q0, 0, j2, a, staged[:], ((0, 1, 2, 3), (4, 5, 0, 1))[a], (), 2)
        handed = sbuf([P, 3 * H], BF16, "handed")
        psi_2, woven = [handed[:, 0:H]], handed[:, H:]
        weave(psi_2[0], res_2[:, :, 0:P], inv_2[:, :, 0:P], ALU.mult)
        pair_difference(woven, (out_low, in_low), 0)
        pair_difference(woven, (out_high, in_high), 1)
        model_3 = model_banks((6, 7), CHUNK)
        model_last, model_unit = ([half[:, :, c0 : c0 + P] for half in model_3] for c0 in (0, P))
        for a in range(PASSES):
            model_pass(model_3, "table", a, j3, CHUNK, start=(a == 0))
        outside = pick_rows(idx3, 1, j3, CHUNK, "out00")
        inside = pick_rows(idx2, 1, j3, CHUNK, "res1")
        quantise_x(units(0, j3, CHUNK), woven, "model0", "x1_sc0")
        model_pass(model_3, "x", 0, j3, CHUNK)
        woven = sbuf([P, CHUNK * PACK], BF16, "woven", "x1b_codes")
        weave(woven[:], inside[:], outside[:], ALU.subtract, engine=nc.vector)
        quantise_x(units(1, j3, CHUNK), woven[:], "psi_codes2", "psi_sc2")
        model_pass(model_3, "x", 1, j3, CHUNK, stop=True)
        psi_2.append(influence(res_2[:, :, P:], inv_2[:, :, P:], P, "x1b_codes", nc.vector)[:])
        res_unit = residual(model_unit, flux_3[:, :, P:], P, "mid0")
        psi_q2 = (sbuf([P, CHUNK], U32, "codes", "res1"), sbuf([P, CHUNK], U8, "scales", "psi_sc1"))
        for u, half in enumerate(psi_2):
            cols = slice(u * P, (u + 1) * P)
            nc.vector.quantize_mx(out=psi_q2[0][:, cols].bitcast(FP8X4), scales=psi_q2[1][:, cols], in_=half)
        res_last = residual(model_last, flux_3[:, :, 0:P], P, "out13")
        inv_unit = invert(res_unit, P, "in12")
        inv_last = invert(res_last, P, "flux0", pool_squares=True)
        second = sbuf([P, PASSES, PACK, CHUNK], F32, "staged", "wt_both")
        second_product(psi_q2, j2, CHUNK, 0, second[:, 0], (0, 1), (0, 1), 2)
        psi_u = influence(res_unit, inv_unit, P, "x1_codes", nc.vector)
        back_2 = second_matmuls(psi_q2, CHUNK, 1, (2, 3))
        scale_and_store(back_2, j2, CHUNK, 1, second[:, 1], 0, True, 2)
        psi_qu = quantise(psi_u[:], H, "psi_codes0", "psi_sc0")
        scale_and_store(back_2, j2, CHUNK, 1, second[:, 1], 1, False, 2)
        psi_l = influence(res_last, inv_last, P, "x1b_codes", nc.vector)
        finish(psi_qu, j_unit, P, "out10", ((4, 7), (5, 6)), ((), ()), 2)
        psi_ql = quantise(psi_l[:], H, "psi_codes1", "psi_sc2")
        finish(psi_ql, j_last, P, "in10", ((0, 2), (1, 3)), ((0,), (0,)), 2)
